import numpy as np, ml_dtypes
CORES = [24,25,26,27,28,29,30,31]
N = 8
import mx_ref
BF = ml_dtypes.bfloat16
def entries(a):
    return np.ascontiguousarray(a.T).reshape(-1)
def table(e):
    return np.ascontiguousarray(np.reshape(e, (-1, 16)).T).astype(np.int32)
def gentries(a):
    return np.ascontiguousarray(a.reshape(8, 16, -1).transpose(0, 2, 1)).reshape(8, -1)
def gtable(e):
    e = np.asarray(e); return np.ascontiguousarray(e.reshape(8, -1, 16).transpose(0, 2, 1)).reshape(128, -1).astype(np.int32)
def gcols(t, e):
    v = np.concatenate([t.reshape(8, 16, -1, 4), np.zeros((8, 16, 1, 4), BF)], axis=2)
    return np.ascontiguousarray(np.stack([v[g][:, e[g]] for g in range(8)])).reshape(128, -1)
def tile(rs):
    return np.stack(rs, axis=2).reshape(128, -1).astype(BF)
def pick(q, e):
    c = np.concatenate([q[0].reshape(128, -1, 4), np.zeros((128, 1, 4), np.uint8)], axis=1); s = np.concatenate([q[1], np.ones((16, 1), np.uint8)], axis=1)
    return (np.ascontiguousarray(c[:, e].reshape(128, -1)), np.ascontiguousarray(s[:, e]))
def join(*qs):
    return (np.concatenate([q[0] for q in qs], axis=1), np.concatenate([q[1] for q in qs], axis=1))
def put(q, e, v):
    c, s = q[0].reshape(128, -1, 4).copy(), q[1].copy(); c[:, e] = v[0].reshape(128, -1, 4); s[:, e] = v[1]
    return (c.reshape(128, -1), s)
def pk(c, s):
    return (np.ascontiguousarray(c), mx_ref.live(s))
def emit(q):
    return q[0], q[1]
def packed(v, rng):
    q = [mx_ref.quantize(np.ascontiguousarray(v[r])) for r in range(N)]
    return np.stack([a for a, b in q]), np.stack([mx_ref.plane(b, rng) for a, b in q])
def values_of_codes():
    e, c = np.zeros((128, 128, 4), np.float32), np.zeros((128, 2, 4), np.uint8)
    e[np.arange(128), np.arange(128), 0] = 1
    c[:127, :, 0] = np.arange(256).reshape(2, 128).T[:127]
    return mx_ref.matmul(mx_ref.quantize(e.reshape(128, 512).astype(BF)), (c.reshape(128, 8), np.full((16, 2), 127, np.uint8))).T.reshape(-1).astype(np.float64)
CODE_VALUE, SCALE_VALUE = values_of_codes(), 2.0 ** (np.arange(256) - 127.0)
def decode(q):
    return (CODE_VALUE[q[0]].reshape(16, 8, -1, 4) * SCALE_VALUE[q[1]][:, None, :, None] + 0.0).reshape(128, -1).astype(np.float32)
def f(rng, *shape):
    return mx_ref.flush((rng.standard_normal(shape, dtype=np.float32) * np.exp2(rng.integers(-2, 3, shape[:-1] + (1,)))).astype(BF))
def wide(rng, *shape, cols=0):
    v = rng.standard_normal(shape, dtype=np.float32) * np.exp2(rng.integers(-12, 13, shape)).astype(np.float32)
    if cols: v *= np.repeat(np.exp2(rng.integers(-cols, cols + 1, shape[:-2] + (1, shape[-1] // 4))) * (rng.random(shape[:-2] + (1, shape[-1] // 4)) > 0.0625), 4, axis=-1).astype(np.float32)
    return mx_ref.flush(v.astype(BF))
C, K, M = 512, 64, 8
DIST = [1, 2, 4]
def big(v):
    v = v.astype(np.float32)
    v[np.abs(v) < np.float32(2.0 ** -16)] = 0
    return v.astype(BF)
def numbers_of(rng):
    return {"x": big(f(rng, N, 128, 4 * C)), "u": np.array(f(rng, N, 128, 512)), "v": np.array(f(rng, N, 128, 512))}
def trees(rng):
    j = np.arange(C)
    return np.maximum(j - 1 - np.floor(rng.random((N, C)) ** 3 * j).astype(np.int64), 0)
def flags(rng):
    a = (rng.random((N, 8, C)) < 0.5) * 1
    a[:, :, 0] = 1
    return a
def lists_of(e, a):
    return {"par": np.stack([table(e[r]) for r in range(N)]), "fl": np.stack([gtable(a[r]) for r in range(N)])}
def layers(rng):
    return big(f(rng, N, 128, 2048)).reshape(N, 8, 16, 4, 8, 16, 4)
def carry(w, parts, k):
    k = np.asarray(k, np.float32).astype(BF)
    w[:, :, :, :, :, parts] = 0
    for g in range(8):
        for i in parts:
            for b in range(4): w[:, g, i, b, g, i, b] = k[:, g]
    return w
def weights(rng, w):
    c, p = packed(np.ascontiguousarray(w).reshape(N, 128, 2048), rng)
    return {"wc": c, "ws": p}
def setup_inputs(rng):
    return {**numbers_of(rng), **lists_of(trees(rng), flags(rng)), **weights(rng, layers(rng))}
def setup_inputs_ties(rng):
    d = numbers_of(rng)
    first = int(rng.integers(N))
    ones = [(first + 1) % N, (first + 2) % N]
    x = d["x"].reshape(N, 8, 16, C, 4)
    for r in range(N):
        a = x[r][:, :8, :3].copy()
        a[:, :, 2] = 0
        x[r][:, :8] = a[:, :, rng.permutation(C) % 3]
    x[first, :, :8] = 0
    x[ones, :, :8] = 1
    u = d["u"].reshape(N, 8, 16, 128, 4)
    z = u.copy()
    u[:, :, :, ::16] = 0
    u[:, :, :, 1::16] = 0
    for g in range(8):
        for i in (16 * g, 16 * g + 1):
            u[:, g, :8, i] = z[:, g, :8, i]
            for r in ones: u[r, g, :8, i] = np.abs(z[r, g, :8, i])
    w = carry(layers(rng), list(range(8)), np.full((N, 8), 32.0))
    return {"x": x.reshape(N, 128, 4 * C), "u": u.reshape(N, 128, 512), "v": d["v"], **lists_of(trees(rng), flags(rng)), **weights(rng, w)}
def setup_inputs_near(rng):
    d = numbers_of(rng)
    x = np.zeros((N, 8, 16, C, 4), np.float32)
    a = (N, 8, 8, C, 4)
    x[:, :, 8:] = rng.choice([-1.0, 1.0], a) * (1.0 + (2 * rng.integers(0, 64, a) + 1) * 2.0 ** -7) * np.exp2(-rng.integers(8, 15, a).astype(np.float64))
    x[:, :, 8 + int(rng.integers(8)), :, int(rng.integers(4))] = np.where(np.arange(8) % 2 == 1, 1.75, 1.96875)[None, :, None]
    x[:, :, 8:] *= np.exp2(rng.integers(-1, 2, (N, 8, 1, C, 1)).astype(np.float32))
    u = d["u"].reshape(N, 128, 128, 4)
    u[:, :, ::16] = 0
    u[:, :, 1::16] = 0
    o = rng.permutation(N) % 2
    m = flags(rng)
    for r in range(N):
        k = 2.0 ** -30 if o[r] == 0 else 1.0
        s = rng.integers(-1, 2, (8, 2, C)) * k
        t = np.concatenate([1.125 * s, -1.25 * s], axis=1)
        for g in rng.permutation(8)[:4]:
            j = int(rng.integers(C))
            t[g, :2, j] = 2.0 ** 30 * rng.choice([-1.0, 1.0], 2)
            t[g, 2:, j] = 0
            m[r, g, j] = 1
        x[r, :, :4, :, 0] = t
        for h in range(0, 128, 16):
            for b in range(2):
                u[r, h + b, h + b, 0] = 1.125 * k
                u[r, h + 2 + b, h + b, 0] = k
    w = np.zeros((N, 8, 16, 4, 8, 16, 4), np.float32).astype(BF)
    w = carry(w, list(range(8)), np.full((N, 8), 32.0))
    w = carry(w, list(range(8, 16)), np.where(np.arange(8) % 2 == 1, 36.0, 32.0) * np.ones((N, 1)))
    return {"x": x.reshape(N, 128, 4 * C).astype(BF), "u": u.reshape(N, 128, 512), "v": d["v"], **lists_of(trees(rng), m), **weights(rng, w)}
def setup_inputs_chain(rng):
    d = numbers_of(rng)
    u = d["u"].reshape(N, 128, 128, 4)
    g = int(rng.integers(8))
    u[:, :, 16 * g:16 * g + 2] = 0
    d["u"] = u.reshape(N, 128, 512)
    o = rng.permutation(N) % 4
    e = np.stack([np.maximum(np.arange(C) - 1, 0)] * N)
    m = np.zeros((N, 8, C), np.int64)
    for r in range(N):
        if o[r] == 1: m[r, np.arange(8), rng.integers(1, C // 4, 8)] = 1
        if o[r] == 2:
            e[r] = 0
            m[r, rng.permutation(8)[:4]] = 1
        if o[r] == 3: m[r] = 1
    m[:, :, 0] = 1
    return {**d, **lists_of(e, m), **weights(rng, layers(rng))}
def setup_inputs_huge(rng):
    d = numbers_of(rng)
    c = rng.choice([-1.0, 1.0], (N, 8, 1, C, 1))
    c[int(rng.integers(N))] = -1
    x = c * (0.8 + 0.2 * rng.random((N, 8, 16, C, 4))) * 2.0 ** 30
    u = d["u"].reshape(N, 8, 16, 128, 4)
    u[:, :, :, ::16] = 0
    u[:, :, :, 1::16] = 0
    for g in range(8):
        for b in range(2):
            for h in rng.permutation(8)[:1 + 2 * ((g + b) % 4)]:
                u[:, h, :, 16 * g + b] = (2.0 ** 30 * (0.9 + 0.1 * rng.random((N, 16, 4)))).astype(np.float32).astype(BF)
    w = carry(np.zeros((N, 8, 16, 4, 8, 16, 4), np.float32).astype(BF), list(range(16)), 32.0 * rng.choice([-1.0, 1.0], (N, 8)))
    return {"x": x.astype(np.float32).reshape(N, 128, 4 * C).astype(BF), "u": u.reshape(N, 128, 512), "v": d["v"], **lists_of(trees(rng), flags(rng)), **weights(rng, w)}
def setup_inputs_spread(rng):
    d = setup_inputs(rng)
    d["x"] = big(wide(rng, N, 128, 4 * C, cols=6))
    return d
def check_inputs(d):
    b = []
    for k in ("x", "u", "v"):
        a = np.abs(d[k].astype(np.float32))
        if not (np.isfinite(a).all() and ((a == 0) | (a >= 2.0 ** -30) & (a <= 2.0 ** 30)).all()): b.append("a value of " + k)
    none, least, most = [emit(mx_ref.quantize(np.full((128, 16), k, np.float32).astype(BF)))[1][0, 0] for k in (0.0, 2.0 ** -30, 2.0 ** 30)]
    for r in range(N):
        e = entries(d["par"][r])
        if e[0] != 0 or ((e[1:] < 0) | (e[1:] >= np.arange(1, C))).any(): b.append("par: an entry out of range")
        m = gentries(d["fl"][r])
        if ((m != 0) & (m != 1)).any(): b.append("fl: an entry that is neither 0 nor 1")
        if (m[:, 0] != 1).any(): b.append("fl: column 0 isn't flagged in every group")
        if ((d["wc"][r] == 0x7F) | (d["wc"][r] == 0xFF)).any(): b.append("wc: a code that is no number")
        s = mx_ref.live(d["ws"][r])
        if ((s != none) & ((s < least) | (s > most))).any(): b.append("ws: a scale out of range")
    return b
def inherited(now, flag, up):
    a = np.where(flag == 1, np.arange(C), up[:, None])
    for i in range(9): a = np.take_along_axis(a, a, axis=2)
    return [gcols(now[r], a[r]) for r in range(N)]
def reference(x, u, v, par, fl, wc, ws):
    qu = [mx_ref.quantize(u[r]) for r in range(N)]
    lay = [pk(wc[r], ws[r]) for r in range(N)]
    now = [x[r] for r in range(N)]
    up = np.stack([entries(par[r]) for r in range(N)])
    flag = np.stack([gentries(fl[r]) for r in range(N)])
    for h in DIST:
        e = inherited(now, flag, up)
        sym, came, new = [], [], []
        for r in range(N):
            q = mx_ref.quantize(e[r])
            s = mx_ref.matmul(qu[r], q)
            sym.append(2 * (s[::16] > 0) + (s[1::16] > 0))
            k = pick(q, np.arange(0, C, M))
            t = tile([mx_ref.matmul(pick(lay[r], np.arange(128 * b, 128 * b + 128)), k) * np.float32(0.03125) for b in range(4)])
            came.append(decode(mx_ref.quantize(t)).astype(BF))
        for r in range(N):
            d = (r + h) % N
            key, lock = sym[d][:, ::M], sym[r]
            master = lock[:, up[r]]
            agree = (key[:, None] == lock[:, :, None]) | (key[:, None] == master[:, :, None])
            best = np.argmax(np.count_nonzero(agree, axis=0), axis=1)
            far = key[:, best]
            wanted = (far != lock) & (far != master)
            left = (far != lock) & (far == master)
            new.append(gcols(np.concatenate([now[r], came[d]], axis=1), np.where(wanted, C + best, np.arange(C))))
            flag[r] = np.where(wanted, 1, np.where(left, 0, flag[r]))
        now = new
    e = inherited(now, flag, up)
    y, ofl = np.zeros((N, 128, C), np.float32), np.zeros((N, 8, C), np.float32)
    oc, osc = np.zeros((N, 128, 4 * C), np.uint8), np.zeros((N, 16, C), np.uint8)
    for r in range(N):
        q = mx_ref.quantize(e[r])
        y[r] = mx_ref.matmul(mx_ref.quantize(v[r]), q)
        ofl[r] = flag[r]
        oc[r], osc[r] = emit(q)
    return {"y": y, "ofl": ofl, "oc": oc, "osc": osc}

@@ -1,0 +1,544 @@
+from concourse.mybir import dt, AluOpType, ActivationFunctionType
+
+A = AluOpType
+F = ActivationFunctionType
+DIST = [1, 2, 4]
+C, K = 512, 64
+PW = C + 3 * K
+F32, BF, I32, U16, U8, MX = "float32", "bfloat16", "int32", "uint16", "uint8", "float8_e4m3fn_x4"
+PIECES = [(0, 256, "vaaa"), (256, 384, "vvaa"), (384, 512, "vvaa")]
+PIECES_LAST = [(0, 256, "vvaa"), (256, 384, "vaaa"), (384, 512, "vvaa")]
+
+
+def _sb(n, d):
+    return ("sbuf", [128, n], d)
+
+
+SCRATCH = {
+    "parL": _sb(8, I32), "flr": _sb(256, I32), "xin": _sb(2048, BF), "ut": _sb(512, BF), "vt": _sb(512, BF),
+    "wq": _sb(512, MX), "wsc": _sb(512, U8), "uq": _sb(128, MX), "us": _sb(128, U8), "urq": _sb(128, MX), "urs": _sb(128, U8),
+    "vq": _sb(128, MX), "vs": _sb(128, U8), "one": _sb(516, BF), "eb": _sb(516, BF), "ebq": _sb(512, MX), "ebs": _sb(512, U8),
+    "pi": _sb(2, I32), "fi": _sb(16, I32), "ff": _sb(16, F32), "col": _sb(64, F32), "row": _sb(96, F32),
+    "lf": _sb(100, F32), "lu": _sb(100, U16), "jp": _sb(32, F32), "jfull": _sb(32, F32), "jcode": _sb(32, F32),
+    "vcon": _sb(128, F32), "horn": _sb(128, F32), "lane": _sb(64, F32),
+    "ptr": _sb(160, U16), "paru": _sb(8, U16),
+    "va": _sb(160, F32), "vb": _sb(160, F32), "vc": _sb(160, F32), "w8": _sb(136, F32), "w9": _sb(264, F32),
+    "tb": _sb(320, F32), "tc": _sb(288, F32), "kin": _sb(32, F32),
+    "yy": _sb(144, F32), "ei": _sb(48, I32), "ej": _sb(48, I32), "el": _sb(48, U16),
+    "in0": _sb(128, F32), "in1": _sb(128, F32), "flg": _sb(128, F32),
+    "pool": _sb(4 * PW, BF), "et": _sb(2048, BF), "eq": _sb(512, MX), "es": _sb(512, U8),
+    "kt": _sb(512, BF), "kq": _sb(128, MX), "ks": _sb(128, U8), "ht": _sb(512, BF),
+    "kb": _sb(128, BF), "kbt": _sb(128, BF), "rows": _sb(512, BF), "op": _sb(256, BF), "opt": _sb(256, BF),
+    "sm": _sb(64, F32), "m4": _sb(32, F32), "ix0": _sb(32, F32), "ixu": _sb(32, U16),
+    "xe": _sb(128, F32), "eqv": _sb(128, F32), "eq6": _sb(136, F32), "pa": _sb(128, F32), "tab": _sb(128, F32),
+    "ac0": _sb(128, F32), "ac1": _sb(128, F32),
+    "ci": _sb(64, I32), "yi": _sb(256, I32), "y2": _sb(128, F32), "y1": _sb(64, F32), "yt": _sb(64, F32),
+    "sc": _sb(64, F32), "ku": _sb(4, U16), "fw": _sb(64, F32), "fw9": _sb(576, F32), "fg": _sb(64, F32), "ft": _sb(64, F32),
+    "d0": _sb(32, F32), "d1": _sb(32, F32), "d2": _sb(32, F32), "d3": _sb(32, F32), "d4": _sb(32, F32), "d5": _sb(32, F32),
+    "yo": _sb(512, F32),
+    "ps": ("psum", [128, 4096], F32),
+}
+for _r in range(3):
+    SCRATCH["fs%d" % _r] = _sb(32, BF)
+    SCRATCH["fl%d" % _r] = _sb(32, BF)
+    SCRATCH["fin%d" % _r] = _sb(64, F32)
+    SCRATCH["hq%d" % _r] = _sb(192, MX)
+    SCRATCH["hs%d" % _r] = _sb(192, U8)
+
+SEMAPHORES = (["sv", "sa", "sp", "st", "l_par", "l_fl", "l_u", "l_x", "l_w", "l_v", "out", "sent"]
+              + ["af%d" % r for r in range(3)] + ["ah%d" % r for r in range(3)])
+ENG_SEM = {"v": "sv", "a": "sa", "p": "sp", "t": "st"}
+
+L_PJ, L_FJ, L_SEL, L_UREP, L_OWN, L_FSEL, L_FIN, L_KEY, L_REO, L_EXP, L_PS, L_PM, L_FIN2, L_REP = 0, 2, 4, 6, 14, 22, 26, 30, 32, 34, 42, 50, 58, 60
+CYC = 0.001
+
+
+def rank_program(g, core, T, topo):
+    rank = T.rank_of(core)
+    if rank is None:
+        return
+    n_ranks = len(T.cores)
+    ops = []
+    arrive = {}
+
+    def V(name, c0=0, c1=None, st=1, p0=0, p1=128):
+        if c1 is None:
+            c1 = T[name].shape[1]
+        ap = T[name][p0:p1, c0:c1:st] if st > 1 else T[name][p0:p1, c0:c1]
+        n = (c1 - c0 + st - 1) // st
+        if name == "ps":
+            return (ap, [("ps", 0, 128, c0 // 512 * 512, c0 // 512 * 512 + 512, 1)], n, False)
+        return (ap, [(name, p0, p1, c0, c1, st)], n, False)
+
+    def IND(w, o):
+        return (w[0].indirect(o[0]), w[1] + o[1], 16 * o[2], True)
+
+    def L(c, n):
+        return V("lu", c, c + n)
+
+    def LF(c, n=1):
+        return V("lf", c, c + n)
+
+    ncol = [0]
+
+    def newcol():
+        ncol[0] += 1
+        return V("col", ncol[0] - 1, ncol[0])
+
+    def fcol(c):
+        return V("ff", c, c + 1)
+
+    def op(eng, fn, outs, ins, cost, lat=0.0, sem=None, inc=1, ext=None, gives=None):
+        w = [f for v in outs for f in v[1]]
+        r = []
+        for v in ins:
+            if isinstance(v, tuple):
+                for f in v[1]:
+                    (w if f[0] == "ps" else r).append(f)
+        ops.append({"eng": eng, "fn": fn, "r": r, "w": w, "sem": sem or ENG_SEM[eng], "inc": inc, "dma": sem is not None,
+                    "ext": ext, "cost": cost, "lat": lat, "early": 0.0, "id": len(ops)})
+        if gives is not None:
+            arrive.setdefault(gives, []).append(len(ops) - 1)
+
+    def early(t):
+        ops[-1]["early"] = t
+
+    def ap(v):
+        return v[0] if isinstance(v, tuple) else v
+
+    def cc(v, k=1.0):
+        return 0.05 + 1.5 * CYC * v[2] if v[3] else max(64, k * v[2]) * CYC
+
+    def cp(o, i):
+        op("v", lambda: g.vector.tensor_copy(o[0], i[0]), [o], [i], cc(i))
+
+    def tt(o, a, b, alu, ext=None):
+        op("v", lambda: g.vector.tensor_tensor(o[0], a[0], b[0], alu), [o], [a, b], cc(a, 2), ext=ext)
+
+    def ts(o, a, s1, o0, s2=None, o1=None):
+        if o1 is None:
+            op("v", lambda: g.vector.tensor_scalar(o[0], a[0], ap(s1), None, o0), [o], [a, s1], cc(a))
+        else:
+            op("v", lambda: g.vector.tensor_scalar(o[0], a[0], ap(s1), ap(s2), o0, o1), [o], [a, s1, s2], cc(a))
+
+    def tr(o, i, k=1.0):
+        op("v", lambda: g.vector.transpose(o[0], i[0]), [o], [i], cc(i, k))
+
+    def ms(o, c):
+        op("v", lambda: g.vector.memset(o[0], c), [o], [], cc(o))
+
+    def scan(o, d0, d1, init, o0, o1):
+        op("v", lambda: g.vector.tensor_tensor_scan(o[0], d0[0], d1[0], init, o0, o1), [o], [d0, d1], cc(d0))
+
+    def act(o, i, func=None, scale=None, bias=None, ext=None):
+        kw = {}
+        if scale is not None:
+            kw["scale"] = ap(scale)
+        if bias is not None:
+            kw["bias"] = ap(bias)
+        fn = func if func is not None else (F.Identity if bias is not None else F.Copy)
+        op("a", lambda: g.scalar.activation(o[0], i[0], fn, **kw), [o], [i, scale, bias], cc(i) + 0.015, ext=ext)
+
+    POOL = (None, [("gpsimd", 0, 128, 0, 1, 1)])
+
+    def iota(o, pat, base, cm, flt=True):
+        if flt:
+            op("p", lambda: g.iota(o[0], pat, base, cm, allow_small_or_imprecise_dtypes=True), [o, POOL], [], 0.13 + 2 * CYC * o[2])
+        else:
+            op("p", lambda: g.iota(o[0], pat, base, cm), [o, POOL], [], 0.13 + 2 * CYC * o[2])
+
+    def quant(q, s, i):
+        op("v", lambda: g.vector.quantize_mx(q[0], s[0], i[0]), [q, s], [i], 0.015 + 0.26 * CYC * i[2])
+
+    def mm(o, lq, ls, rq, rs, ext=None):
+        op("t", lambda: g.tensor.matmul_mx(o[0], lq[0], ls[0], rq[0], rs[0], True, True), [o], [lq, ls, rq, rs], 0.7 * CYC * (rq[2] + 16), 0.05, ext=ext)
+
+    def dma(eng, o, i, sem, lat=1.8):
+        q = {"s": g.sync, "a": g.scalar, "p": g}[eng]
+        op(eng, lambda: q.dma_start(ap(o), ap(i)), [o] if isinstance(o, tuple) else [], [i], 0.06, lat, sem=sem, inc=16)
+
+    def u8(v):
+        return (v[0].bitcast(dt.uint8), v[1], v[2], False)
+
+    count = {}
+
+    def send(dst_core, o, i, rsem, lat):
+        rid, pid = topo.addr(dst_core)[:2]
+        m = topo.mask(core, dst_core)
+        n = len(topo.engines(core, dst_core))
+        count[rsem] = count.get(rsem, 0) + n
+        op("p", lambda: g.remote_dma(o[0], i[0], T.sem[rsem], T.sem["sent"], pid, rid, m), [], [i], 0.1, lat, sem="sent", inc=-n, gives=rsem)
+
+    for G in range(8):
+        a = G // 2
+        dma("s", V("parL", 0, 8, 1, 16 * G, 16 * G + 16), T.par[:, 8 * a:8 * a + 8], "l_par")
+    n = 0
+    for r in range(8):
+        for (d0, d1, s0) in ((0, 128 - 16 * r, 16 * r), (128 - 16 * r, 128, 0)):
+            if d1 > d0:
+                dma("a" if n < 11 else "s", V("flr", 32 * r, 32 * r + 32, 1, d0, d1), T.fl[s0:s0 + d1 - d0, :], "l_fl")
+                n += 1
+    dma("s", V("xin"), T.x[:, :], "l_x", 5.0)
+    dma("s", V("ut"), T.u[:, :], "l_u", 4.5)
+    dma("s", u8(V("wq")), T.wc[:, :], "l_w", 6.0)
+    dma("s", V("wsc"), T.ws[:, :], "l_w", 6.0)
+    dma("s", V("vt"), T.v[:, :], "l_v", 6.5)
+
+    iota(V("pi", 0, 1), [[0, 1]], 0, 1, False)
+    iota(V("row", 0, 16), [[0, 2], [1, 8]], 0, 0)
+    iota(V("jp"), [[32, 4], [0, 8]], 0, 1)
+    iota(V("row", 16, 24), [[16, 8]], 0, 0)
+    iota(V("row", 24, 32), [[0, 4], [64, 2]], 0, 0)
+    iota(V("row", 48, 84), [[0, 9], [-16, 4]], 63, 0)
+    RC, R16, R64, RREP = V("row", 0, 8), V("row", 16, 24), V("row", 24, 32), V("row", 48, 84)
+    RC2 = V("row", 0, 2)
+    P = V("pi", 0, 1)
+    ms(V("in0"), 0.0)
+    ms(V("lf", 0, 6), 0.0)
+    fields = [(0, 7), (2, 3), (0, 1), (3, 1), (4, 1), (5, 3), None, None, (0, 15), (0, 3), (1, 1), (2, 1), (5, 1), (6, 1), (0, 31)]
+    FQ7, FPH, FB0, FB3, FH, FA, FRHO, FT, FP, FP3, FB1, FB2, FA0, FA1, F31 = range(15)
+    ts(V("fi", 15, 16), P, 4, A.logical_shift_right)
+    tt(V("fi", FT, FT + 1), P, V("fi", 15, 16), A.subtract)
+    ts(V("fi", FRHO, FRHO + 1), V("fi", FT, FT + 1), 7, A.bitwise_and)
+    for i, sm_ in enumerate(fields):
+        if sm_ is not None:
+            ts(V("fi", i, i + 1), P, sm_[0], A.logical_shift_right, sm_[1], A.bitwise_and)
+    cp(V("ff", 0, 8), V("fi", 0, 8))
+    cp(V("ff", 8, 16), V("fi", 8, 16))
+    for nm in ("va", "vb", "vc"):
+        ms(V(nm, 0, 16), 0.0)
+        ms(V(nm, 144, 160), 0.0)
+
+    def lin(eng, x, s, b, out=None, func=None):
+        o = out if out is not None else newcol()
+        if eng == "a":
+            act(o, x, func, scale=s, bias=b)
+        else:
+            ts(o, x, s, A.mult, b, A.add)
+        return o
+
+    lin("v", fcol(FPH), 2.0, fcol(FH), LF(L_PJ))
+    c = lin("v", fcol(FA), 8.0, fcol(FH))
+    c = lin("v", fcol(FB3), 2.0, c)
+    c = lin("v", fcol(FRHO), 32.0, c)
+    lin("v", RC2, 4.0, c, LF(L_FJ, 2))
+    cp(V("lu", 0, 4), V("lf", 0, 4))
+    c = lin("a", fcol(FA), 98400.0, 1024.0)
+    lin("a", V("jp"), 1025.0, c, V("jfull"))
+    CB0 = lin("a", fcol(FA), -128.0, 8.0)
+    CB = lin("a", fcol(FA), -128.0, 519.0)
+    CX = lin("a", fcol(FB0), -1.0, fcol(FH), func=F.Abs)
+    c = lin("a", fcol(FH), -16.0, 1.0)
+    c = lin("a", fcol(FQ7), 16.0, c)
+    SEL = lin("a", CX, 144.0, c, LF(L_SEL))
+    cp(V("lu", 4, 6), V("lf", 4, 6))
+    ms(V("lf", 6, 100), 0.0)
+    c = lin("a", fcol(FA), 98304.0, 1024.0)
+    lin("a", V("jp"), 1024.0, c, V("jcode"))
+    lin("a", R16, 1.0, lin("a", fcol(FA), 128.0, fcol(FP)), LF(L_OWN, 8))
+    lin("a", R64, 1.0, lin("a", fcol(FPH), 16.0, fcol(FP3)), LF(L_UREP, 8))
+    CW = lin("a", fcol(FB0), -1.0, 2.0)
+    CW4 = lin("a", fcol(FB0), -4.0, 8.0)
+    C8 = lin("a", fcol(FA0), 100000.0, lin("a", fcol(FA), -128.0, 647.0 - 100000.0))
+    C9 = lin("a", fcol(FA1), 100000.0, 519.0 - 100000.0)
+    c = lin("a", lin("a", SEL, -1.0, 289.0), fcol(FB3), SEL)
+    c = lin("a", fcol(FH), 4.0, c)
+    s0 = lin("a", fcol(FA), 8.0, lin("a", c, 1.0, -1.0), LF(L_FSEL + 2))
+    lin("a", fcol(FA0), -16.0, lin("a", s0, 1.0, 8.0), LF(L_FSEL + 3))
+    lin("a", fcol(FA1), -32.0, lin("a", s0, 1.0, 16.0), LF(L_FSEL))
+    lin("a", fcol(FA), -8.0, lin("a", c, 1.0, 23.0), LF(L_FSEL + 1))
+    c = lin("a", lin("a", fcol(FB3), -1.0, fcol(FA0), func=F.Abs), 64.0, fcol(FQ7))
+    lin("a", fcol(FA1), 32.0, lin("a", c, 1.0, 32.0), LF(L_FIN))
+    lin("a", fcol(FA1), -32.0, lin("a", c, 1.0, 64.0), LF(L_FIN + 1))
+    c = lin("a", lin("a", fcol(FB0), -1.0, fcol(FB2), func=F.Abs), -1.0, fcol(FA0), func=F.Abs)
+    lin("a", c, 64.0, lin("a", lin("a", fcol(FB1), -1.0, fcol(FA1), func=F.Abs), 32.0, 40.0), LF(L_FIN + 2))
+    lin("a", RC2, 0.0, lin("a", fcol(FP), 8.0, 0.0), LF(L_KEY, 2))
+    cp(V("lu", 6, 32), V("lf", 6, 32))
+    lin("a", RC2, 4.0, lin("a", fcol(FP3), 8.0, fcol(FPH)), LF(L_REO, 2))
+    lin("a", RC, 1.0, lin("a", CX, 16.0, lin("a", fcol(FB1), 8.0, 0.0)), LF(L_EXP, 8))
+    lin("a", R16, 1.0, lin("a", fcol(FPH), 4.0, 3.0), LF(L_PS, 8))
+    lin("a", R16, 1.0, lin("a", fcol(FP3), 4.0, -125.0), V("row", 32, 40))
+    c = lin("a", lin("a", fcol(FP3), -1.0, fcol(FPH), func=F.Abs), 1.0, 0.0, func=F.Sign)
+    lin("a", V("row", 32, 40), c, 128.0, LF(L_PM, 8))
+    lin("a", RC2, 8.0, fcol(FQ7), LF(L_FIN2, 2))
+    lin("a", RREP, 1.0, lin("a", fcol(FP), -1.0, 0.0), LF(L_REP, 36))
+    cp(V("lu", 32, 100), V("lf", 32, 100))
+    early(2.0)
+    iota(V("w8"), [[0, 136]], 0, 0)
+    iota(V("w9"), [[0, 264]], 0, 0)
+    iota(V("ht", 256, 512), [[0, 256]], 0, 0)
+    iota(V("vcon"), [[0, 8], [4, 4], [0, 4]], 0, 0)
+    iota(V("horn"), [[0, 128]], 64, 0)
+    iota(V("horn", 0, 128, 4), [[0, 32]], 0, 0)
+    iota(V("lane"), [[0, 64]], 1, 0)
+    iota(V("lane", 15, 64, 16), [[0, 4]], -1024, 0)
+    iota(V("eq6", 128, 136), [[0, 8]], 0, 0)
+    iota(V("in1"), [[0, 128]], 0, 0)
+    for r in range(3):
+        iota(V("fin%d" % r, 1, 64, 2), [[32, 2], [0, 16]], C + K * r, 0)
+        act(V("fin%d" % r, 1, 64, 2), V("fin%d" % r, 1, 64, 2), bias=fcol(F31))
+    iota(V("one"), [[0, 516]], 1, 0)
+    op("p", lambda: g.affine_select(T.eb[:, :], T.one[:, :], [[-1, 516]], A.is_equal, 0.0, 3, 4), [V("eb"), POOL], [V("one")], 1.2)
+    for b in range(4):
+        quant(V("ebq", 128 * b, 128 * b + 128), V("ebs", 128 * b, 128 * b + 128), V("eb", 3 - b, 515 - b))
+        early(6.0)
+    for t in range(4):
+        act(V("pool", PW * t, PW * t + C), V("xin", t, 2048, 4))
+    quant(V("uq"), V("us"), V("ut"))
+    op("v", lambda: g.vector.tensor_copy(T.urq[:, :].bitcast(dt.uint32), T.uq[:, :].bitcast(dt.uint32).indirect(T.lu[:, L_UREP:L_UREP + 8])),
+       [V("urq")], [V("uq"), L(L_UREP, 8)], 0.25)
+    op("a", lambda: g.scalar.activation(T.urs[:, :], T.us[:, :].indirect(T.lu[:, L_UREP:L_UREP + 8]), F.Copy), [V("urs")], [V("us"), L(L_UREP, 8)], 0.25)
+    quant(V("vq"), V("vs"), V("vt"))
+    early(6.0)
+
+    ts(V("in0", 1, 128, 8), IND(V("parL"), L(L_PJ, 1)), -1.0, A.mult, 511.0, A.add)
+    tt(V("in0", 0, 128, 4), IND(V("flr"), L(L_FJ, 2)), V("jfull"), A.mult)
+    ts(V("ptr", 0, 8), V("parL"), CB0, A.add)
+    cp(V("paru"), V("parL"))
+
+    def both(src, tb="tb"):
+        tr(V(tb, 0, 128), V(src, 16, 144))
+        tr(V(tb, 128, 288), V(src, 0, 160))
+
+    def pointer(src, k, bias):
+        tb = "tc" if k % 2 else "tb"
+        both(src, tb)
+        ts(V("ptr", 16 * k, 16 * k + 16), IND(V(tb, 0, 288), L(L_SEL, 1)), -1.0, A.mult, bias, A.add)
+
+    def step(o, w, own, lst, c0, c1, end):
+        tt(V(o, 16 + c0, 16 + c1), IND(V(w, 8, 16 + end), V("ptr", 16 * lst + c0 // 16, 16 * lst + c1 // 16)), V(own, 16 + c0, 16 + c1), A.max)
+
+    def inherit(r):
+        first, last = r == 0, r == 3
+        src = V("in%d" % (r % 2))
+        tr(V("va", 16, 144), src)
+        tr(V("vb", 16, 144), src)
+        if last:
+            act(V("flg"), V("vb", 16, 144), F.Sign)
+            for a in range(4):
+                dma("s", T.ofl[:, 128 * a:128 * a + 128], (T.flg[32 * a:32 * a + 32:4, :], V("flg")[1]), "out")
+        old, cur, nxt = "va", "vb", "vc"
+        for k in range(7):
+            for (c0, c1) in (((0, 128),) if first else ((0, 64), (64, 128))):
+                step(nxt, cur, old, max(k - 1, 0), c0, c1, c1)
+            old, cur, nxt = cur, nxt, old
+            if first and (k < 5 or k == 6):
+                pointer(cur, min(k + 1, 6), CB)
+        for c0 in (32, 64, 96):
+            step(cur, cur, cur, 6, c0, c0 + 32, c0)
+        (act if first else cp)(V("w8", 8, 136, 1, 32, 64), V(cur, 16, 144, 1, 0, 32))
+        act(V("w8", 8, 136, 1, 96, 128), V(cur, 16, 144, 1, 64, 96))
+        act(V("w9", 8, 136, 1, 64, 96), V(cur, 16, 144, 1, 0, 32))
+        act(V("w9", 8, 136, 1, 96, 128), V(cur, 16, 144, 1, 0, 32))
+        if first:
+            pointer(cur, 8, C8)
+        tt(V(old, 16, 144), IND(V("w8"), V("ptr", 128, 136)), V(cur, 16, 144), A.max)
+        old, cur = cur, old
+        (act if first else cp)(V("w9", 136, 264, 1, 64, 96), V(cur, 16, 144, 1, 32, 64))
+        act(V("w9", 136, 264, 1, 96, 128), V(cur, 16, 144, 1, 32, 64))
+        if first:
+            pointer(cur, 9, C9)
+        tt(V(old, 16, 144), IND(V("w9"), V("ptr", 144, 152)), V(cur, 16, 144), A.max)
+        old, cur = cur, old
+        if not last:
+            act(V("kin"), IND(V(cur, 16, 144), L(L_KEY, 2)))
+        both(cur)
+        if not last:
+            tr(V("tb", 288, 320), V("kin"))
+        cp(V("yy", 0, 64), IND(V("tb"), L(L_FSEL, 4)))
+        cp(V("yy", 64, 96, 1, 64, 128), V("yy", 0, 32, 1, 0, 64))
+        act(V("yy", 64, 96, 1, 0, 64), V("yy", 0, 32, 1, 64, 128))
+        for a in range(4):
+            b = a ^ 1
+            (cp if a >= 2 else act)(V("yy", 96, 144, 1, 32 * b, 32 * b + 32), V("yy", 48, 96, 1, 32 * a, 32 * a + 32))
+        cp(V("ei"), IND(V("yy"), L(L_FIN, 3)))
+        ts(V("ej"), V("ei"), 1023, A.bitwise_and)
+        cp(V("el"), V("ej"))
+
+    def plane(eng, r, dst, t, c0, c1, l0):
+        w = IND(V("pool", PW * t, PW * t + C + K * r), V("el", l0, l0 + (c1 - c0) // 16))
+        (cp if eng == "v" else act)(V(dst, 4 * c0 + t, 4 * c1, 4), w)
+
+    def pieces(r, parts, sq, ss):
+        for i, (c0, c1, engs) in enumerate(parts):
+            for t in range(4):
+                plane(engs[t], r, "et", t, c0, c1, c0 // 16)
+            quant(V("eq", c0, c1), V("es", c0, c1), V("et", 4 * c0, 4 * c1))
+            mm(V("ps", 512 * i, 512 * i + c1 - c0), V(sq), V(ss), V("eq", c0, c1), V("es", c0, c1))
+
+    def symbols(r):
+        dst = T.cores[(rank - DIST[r]) % n_ranks]
+        for t in range(4):
+            plane("v" if t < 2 else "a", r, "kt", t, 0, 128, 32)
+        quant(V("kq"), V("ks"), V("kt"))
+        mm(V("ps", 1536, 1664), V("urq"), V("urs"), V("kq"), V("ks"))
+        for b in range(4):
+            mm(V("ps", 2048 + 512 * b, 2176 + 512 * b), V("wq", 128 * b, 128 * b + 128), V("wsc", 128 * b, 128 * b + 128), V("kq"), V("ks"))
+        ts(V("kb"), V("ps", 1536, 1664), 0.0, A.is_gt, CW4, A.mult)
+        tr(V("kbt"), V("kb"), 0.5)
+        tt(V("fs%d" % r), V("kbt", 0, 128, 4), V("kbt", 1, 128, 4), A.add)
+        send(dst, V("fl%d" % r), V("fs%d" % r), "af%d" % r, 2.5)
+        pieces(r, PIECES, "urq", "urs")
+        for i, (c0, c1, engs) in enumerate(PIECES):
+            ts(V("rows", c0, c1), V("ps", 512 * i, 512 * i + c1 - c0), 0.0, A.is_gt, CW, A.mult)
+        for b in range(4):
+            act(V("ht", b, 256, 4), V("ps", 2048 + 512 * b, 2048 + 512 * b + K), scale=0.03125)
+        act(V("op", 0, 128), IND(V("rows"), L(L_OWN, 8)), scale=4.0)
+        cp(V("op", 128, 256), IND(V("rows"), V("paru")))
+        hq, hs = "hq%d" % r, "hs%d" % r
+        quant(V(hq, 64, 192), V(hs, 64, 192), V("ht"))
+        send(dst, u8(V(hq, 0, 64)), u8(V(hq, 64, 128)), "ah%d" % r, 7.0)
+        send(dst, V(hs, 0, 64), V(hs, 64, 128), "ah%d" % r, 7.0)
+        tr(V("opt"), V("op"), 0.5)
+        tt(V("sm"), V("opt", 0, 256, 4), V("opt", 1, 256, 4), A.add)
+        act(V("m4"), V("sm", 32, 64), scale=4.0)
+        tt(V("ix0"), V("sm", 0, 32), V("sm", 32, 64), A.add)
+        cp(V("ixu"), IND(V("ix0"), L(L_REO, 2)))
+
+    def choose(r):
+        fl, fin = "fl%d" % r, "fin%d" % r
+        tt(V("xe"), IND(V(fl), L(L_EXP, 8)), V("vcon"), A.is_equal, ext="af%d" % r)
+        act(V(fin, 0, 64, 2), IND(V(fl), L(L_FIN2, 2)), ext="af%d" % r)
+        scan(V("eqv"), V("horn"), V("xe"), 0.0, A.mult, A.add)
+        act(V("eq6", 0, 128), V("eqv"), scale=64.0)
+        act(V("pa"), IND(V("eqv"), L(L_PS, 8)), scale=64.0)
+        tr(V("fw"), V(fin))
+        early(1.0)
+        tt(V("tab"), IND(V("eq6"), L(L_PM, 8)), V("pa"), A.add)
+        act(V("fw9"), IND(V("fw"), L(L_REP, 36)))
+        hq, hs = "hq%d" % r, "hs%d" % r
+        for b in range(4):
+            mm(V("ps", 2048 + 512 * b, 2176 + 512 * b), V("ebq", 128 * b, 128 * b + 128), V("ebs", 128 * b, 128 * b + 128),
+               V(hq, 0, 128), V(hs, 0, 128), ext="ah%d" % r)
+        for b in range(4):
+            act(V("pool", PW * b + C + K * r, PW * b + C + K * r + K), V("ps", 2048 + 512 * b, 2048 + 512 * b + K))
+            early(1.5)
+        half = float(sum((3 - t) * 8 * 64 ** (3 - t) for t in range(4)))
+        for i in range(4):
+            for c in range(2):
+                k = 2 * i + c
+                w = IND(V("tab", 16 * k, 16 * k + 16), V("ixu", 4 * k, 4 * k + 4))
+                o = V("ac%d" % (i % 2), 64 * c, 64 * c + 64)
+                if i == 0:
+                    ts(o, w, half, A.add)
+                else:
+                    tt(o, w, V("ac%d" % (1 - i % 2), 64 * c, 64 * c + 64), A.add)
+        tt(V("ci"), V("ac1", 0, 64), V("ac1", 64, 128), A.add)
+        for t in range(4):
+            ts(V("yi", 64 * t, 64 * t + 64), V("ci"), 6 * (3 - t), A.logical_shift_right, 63 * 16, A.bitwise_and)
+        for c in range(2):
+            tt(V("y2", 64 * c, 64 * c + 64), V("yi", 128 * c, 128 * c + 64), V("yi", 128 * c + 64, 128 * c + 128), A.max)
+        tt(V("y1"), V("y2", 0, 64), V("y2", 64, 128), A.max)
+        tr(V("yt"), V("y1"))
+        scan(V("sc"), V("yt"), V("lane"), 0.0, A.max, A.add)
+        ts(V("ku"), V("sc", 15, 64, 16), 1024.0, A.add)
+        cp(V("fg"), IND(V("fw9"), V("ku")))
+        tr(V("ft"), V("fg"))
+        f4, kc = V("ft", 0, 64, 2), V("ft", 1, 64, 2)
+        old, new = V("in%d" % (r % 2), 0, 128, 4), V("in%d" % (1 - r % 2), 0, 128, 4)
+        tt(V("d0"), f4, V("m4"), A.not_equal)
+        tt(V("d1"), kc, V("jcode"), A.add)
+        tt(V("d2"), f4, V("sm", 0, 32), A.is_equal)
+        tt(V("d3"), V("d0"), V("d1"), A.mult)
+        tt(V("d4"), old, V("d3"), A.subtract)
+        tt(V("d5"), V("d4"), V("d2"), A.mult)
+        tt(new, V("d5"), V("d3"), A.add)
+
+    for r in range(3):
+        inherit(r)
+        symbols(r)
+        choose(r)
+    inherit(3)
+    pieces(3, PIECES_LAST, "vq", "vs")
+    for i, (c0, c1, engs) in enumerate(PIECES_LAST):
+        dma("s", T.oc[:, 4 * c0:4 * c1], u8(V("eq", c0, c1)), "out", 2.2)
+        (act if i == 0 else cp)(V("yo", c0, c1), V("ps", 512 * i, 512 * i + c1 - c0))
+        dma("a" if i == 1 else "s", T.y[:, c0:c1], V("yo", c0, c1), "out", 2.2)
+    for k in range(4):
+        dma("a" if k % 2 else "s", T.osc[4 * k:4 * k + 4, :], V("es", 0, 512, 1, 32 * k, 32 * k + 4), "out")
+
+    def meet(x, y):
+        if x[1] >= y[2] or y[1] >= x[2] or x[3] >= y[4] or y[3] >= x[4]:
+            return False
+        s = min(x[5], y[5])
+        return not (s > 1 and max(x[5], y[5]) % s == 0 and (x[3] - y[3]) % s != 0)
+
+    seen, group = {}, {}
+    for o in ops:
+        if o["dma"]:
+            group.setdefault(o["sem"], []).append(o["id"])
+    for o in ops:
+        dep = set()
+        for f, wr in [(f, False) for f in o["r"]] + [(f, True) for f in o["w"]]:
+            for (h, hw, q) in seen.get(f[0], []):
+                if (wr or hw) and meet(f, h):
+                    dep.update(group[ops[q]["sem"]] if ops[q]["dma"] else [q])
+        o["dep"] = dep
+        o["pre"] = dep | set(arrive[o["ext"]] if o["ext"] else [])
+        for f in o["r"]:
+            seen.setdefault(f[0], []).append((f, False, o["id"]))
+        for f in o["w"]:
+            seen.setdefault(f[0], []).append((f, True, o["id"]))
+    HOP = 0.08
+    for o in ops:
+        o["tail"], o["succ"], o["left"], o["est"] = 0.0, [], len(o["pre"]), 0.0
+    for o in ops:
+        for q in o["pre"]:
+            ops[q]["succ"].append(o["id"])
+    for o in reversed(ops):
+        o["tail"] = o["cost"] + o["lat"] + o["early"] + max([HOP + ops[s]["tail"] for s in o["succ"]] + [0.0])
+    free = {e: 0.0 for e in "vapts"}
+    ready = [o for o in ops if o["left"] == 0]
+    order = []
+    while ready:
+        best = min(ready, key=lambda o: (max(o["est"], free[o["eng"]]), -o["tail"], o["id"]))
+        while True:
+            t0 = max(best["est"], free[best["eng"]])
+            better = [o for o in ready if o["eng"] == best["eng"] and o["tail"] > best["tail"] + 0.05 and o["est"] < t0 + best["cost"] - 0.03]
+            if not better:
+                break
+            best = max(better, key=lambda o: o["tail"])
+        ready.remove(best)
+        order.append(best)
+        t0 = max(best["est"], free[best["eng"]])
+        free[best["eng"]] = t0 + best["cost"]
+        for s in best["succ"]:
+            ops[s]["est"] = max(ops[s]["est"], t0 + best["cost"] + best["lat"] + HOP)
+            ops[s]["left"] -= 1
+            if ops[s]["left"] == 0:
+                ready.append(ops[s])
+
+    queue = {"v": g.vector, "a": g.scalar, "p": g, "t": g.tensor, "s": g.sync}
+    total = {}
+    for o in order:
+        total[o["sem"]] = total.get(o["sem"], 0) + abs(o["inc"])
+        o["n"] = total[o["sem"]]
+    known = {e: {} for e in queue}
+    for o in order:
+        need = {}
+        for q in o["dep"]:
+            q = ops[q]
+            cnt = total[q["sem"]] if q["dma"] else q["n"]
+            if cnt > need.get(q["sem"], (0, None))[0]:
+                need[q["sem"]] = (cnt, q)
+        if o["ext"]:
+            need[o["ext"]] = (count[o["ext"]], None)
+        kn = known[o["eng"]]
+        for s in sorted(need):
+            cnt, q = need[s]
+            if any(s2 != s and q2 is not None and q2["kn"].get(s, 0) >= cnt for s2, (c2, q2) in need.items()):
+                continue
+            if kn.get(s, 0) < cnt:
+                queue[o["eng"]].wait_ge(T.sem[s], cnt)
+        for s, (cnt, q) in need.items():
+            kn[s] = max(kn.get(s, 0), cnt)
+            if q is not None:
+                for s2, c2 in q["kn"].items():
+                    kn[s2] = max(kn.get(s2, 0), c2)
+        o["kn"] = dict(kn)
+        ins = o["fn"]()
+        if o["inc"] > 0:
+            ins.then_inc(T.sem[o["sem"]], o["inc"])
+    total.update(count)
+    for s in sorted(total):
+        g.wait_ge(T.sem[s], total[s])

@@ -30,12 +30,12 @@ SCRATCH = {
     "kt": _sb(512, BF), "kq": _sb(128, MX), "ks": _sb(128, U8), "ht": _sb(512, BF),
     "kb": _sb(128, BF), "kbt": _sb(128, BF), "rows": _sb(512, BF), "op": _sb(256, BF), "opt": _sb(256, BF),
     "sm": _sb(64, F32), "m4": _sb(32, F32), "ix0": _sb(32, F32), "ixu": _sb(32, U16),
-    "xe": _sb(128, F32), "eqv": _sb(128, F32), "eq6": _sb(136, F32), "pa": _sb(128, F32), "tab": _sb(128, F32),
-    "ac0": _sb(128, F32), "ac1": _sb(128, F32),
-    "ci": _sb(64, I32), "yi": _sb(256, I32), "y2": _sb(128, F32), "y1": _sb(64, F32), "yt": _sb(64, F32),
+    "xe": _sb(128, F32), "eqv": _sb(136, F32), "pa": _sb(128, F32), "tab": _sb(128, F32),
+    "ac": _sb(576, F32),
+    "ci": _sb(64, I32), "yi": _sb(320, I32), "y2": _sb(128, F32), "y1": _sb(64, F32), "yt": _sb(64, F32),
     "sc": _sb(64, F32), "ku": _sb(4, U16), "fw": _sb(64, F32), "fw9": _sb(576, F32), "fg": _sb(64, F32), "ft": _sb(64, F32),
     "d0": _sb(32, F32), "d1": _sb(32, F32), "d2": _sb(32, F32), "d3": _sb(32, F32), "d4": _sb(32, F32), "d5": _sb(32, F32),
-    "yo": _sb(512, F32),
+    "d6": _sb(32, F32), "yo": _sb(512, F32),
     "ps": ("psum", [128, 4096], F32),
 }
 for _r in range(3):
@@ -50,7 +50,7 @@ SEMAPHORES = (["sv", "sa", "sp", "st", "l_par", "l_fl", "l_u", "l_x", "l_w", "l_
 ENG_SEM = {"v": "sv", "a": "sa", "p": "sp", "t": "st"}
 
 L_PJ, L_FJ, L_SEL, L_UREP, L_OWN, L_FSEL, L_FIN, L_KEY, L_REO, L_EXP, L_PS, L_PM, L_FIN2, L_REP = 0, 2, 4, 6, 14, 22, 26, 30, 32, 34, 42, 50, 58, 60
-CYC = 0.001
+CYC, HOP = 0.001, 0.22
 
 
 def rank_program(g, core, T, topo):
@@ -185,16 +185,15 @@ def rank_program(g, core, T, topo):
     dma("s", V("vt"), T.v[:, :], "l_v", 6.5)
 
     iota(V("pi", 0, 1), [[0, 1]], 0, 1, False)
-    iota(V("row", 0, 16), [[0, 2], [1, 8]], 0, 0)
     iota(V("jp"), [[32, 4], [0, 8]], 0, 1)
+    iota(V("row", 0, 16), [[3, 2], [0, 1], [1, 8]], 0, 0)
     iota(V("row", 16, 24), [[16, 8]], 0, 0)
     iota(V("row", 24, 32), [[0, 4], [64, 2]], 0, 0)
     iota(V("row", 48, 84), [[0, 9], [-16, 4]], 63, 0)
     RC, R16, R64, RREP = V("row", 0, 8), V("row", 16, 24), V("row", 24, 32), V("row", 48, 84)
-    RC2 = V("row", 0, 2)
+    RC2, R4 = V("row", 0, 2), V("row", 0, 8, 4)
     P = V("pi", 0, 1)
     ms(V("in0"), 0.0)
-    ms(V("lf", 0, 6), 0.0)
     fields = [(0, 7), (2, 3), (0, 1), (3, 1), (4, 1), (5, 3), None, None, (0, 15), (0, 3), (1, 1), (2, 1), (5, 1), (6, 1), (0, 31)]
     FQ7, FPH, FB0, FB3, FH, FA, FRHO, FT, FP, FP3, FB1, FB2, FA0, FA1, F31 = range(15)
     ts(V("fi", 15, 16), P, 4, A.logical_shift_right)
@@ -203,7 +202,7 @@ def rank_program(g, core, T, topo):
     for i, sm_ in enumerate(fields):
         if sm_ is not None:
             ts(V("fi", i, i + 1), P, sm_[0], A.logical_shift_right, sm_[1], A.bitwise_and)
-    cp(V("ff", 0, 8), V("fi", 0, 8))
+    cp(V("ff", 0, 6), V("fi", 0, 6))
     cp(V("ff", 8, 16), V("fi", 8, 16))
     for nm in ("va", "vb", "vc"):
         ms(V(nm, 0, 16), 0.0)
@@ -217,12 +216,9 @@ def rank_program(g, core, T, topo):
             ts(o, x, s, A.mult, b, A.add)
         return o
 
-    lin("v", fcol(FPH), 2.0, fcol(FH), LF(L_PJ))
-    c = lin("v", fcol(FA), 8.0, fcol(FH))
-    c = lin("v", fcol(FB3), 2.0, c)
-    c = lin("v", fcol(FRHO), 32.0, c)
-    lin("v", RC2, 4.0, c, LF(L_FJ, 2))
-    cp(V("lu", 0, 4), V("lf", 0, 4))
+    lin("v", fcol(FPH), 2.0, fcol(FH), L(L_PJ, 1))
+    c = lin("v", fcol(FB3), 2.0, lin("v", fcol(FA), 8.0, fcol(FH)))
+    ts(L(L_FJ, 2), R4, c, A.add, lin("v", V("fi", FRHO, FRHO + 1), 32.0, 0.0), A.add)
     c = lin("a", fcol(FA), 98400.0, 1024.0)
     lin("a", V("jp"), 1025.0, c, V("jfull"))
     CB0 = lin("a", fcol(FA), -128.0, 8.0)
@@ -231,7 +227,7 @@ def rank_program(g, core, T, topo):
     c = lin("a", fcol(FH), -16.0, 1.0)
     c = lin("a", fcol(FQ7), 16.0, c)
     SEL = lin("a", CX, 144.0, c, LF(L_SEL))
-    cp(V("lu", 4, 6), V("lf", 4, 6))
+    cp(V("lu", 4, 5), V("lf", 4, 5))
     ms(V("lf", 6, 100), 0.0)
     c = lin("a", fcol(FA), 98304.0, 1024.0)
     lin("a", V("jp"), 1024.0, c, V("jcode"))
@@ -250,12 +246,14 @@ def rank_program(g, core, T, topo):
     c = lin("a", lin("a", fcol(FB3), -1.0, fcol(FA0), func=F.Abs), 64.0, fcol(FQ7))
     lin("a", fcol(FA1), 32.0, lin("a", c, 1.0, 32.0), LF(L_FIN))
     lin("a", fcol(FA1), -32.0, lin("a", c, 1.0, 64.0), LF(L_FIN + 1))
-    c = lin("a", lin("a", fcol(FB0), -1.0, fcol(FB2), func=F.Abs), -1.0, fcol(FA0), func=F.Abs)
+    c = lin("a", fcol(FB0), -1.0, fcol(FA0), func=F.Abs)
     lin("a", c, 64.0, lin("a", lin("a", fcol(FB1), -1.0, fcol(FA1), func=F.Abs), 32.0, 40.0), LF(L_FIN + 2))
     lin("a", RC2, 0.0, lin("a", fcol(FP), 8.0, 0.0), LF(L_KEY, 2))
     cp(V("lu", 6, 32), V("lf", 6, 32))
     lin("a", RC2, 4.0, lin("a", fcol(FP3), 8.0, fcol(FPH)), LF(L_REO, 2))
-    lin("a", RC, 1.0, lin("a", CX, 16.0, lin("a", fcol(FB1), 8.0, 0.0)), LF(L_EXP, 8))
+    c = lin("a", fcol(FB0), -8.0, lin("a", fcol(FH), 8.0, 0.0), func=F.Relu)
+    c = lin("a", c, -1.0, lin("a", fcol(FB1), 8.0, 0.0), func=F.Abs)
+    lin("a", RC, 1.0, lin("a", CX, 16.0, c), LF(L_EXP, 8))
     lin("a", R16, 1.0, lin("a", fcol(FPH), 4.0, 3.0), LF(L_PS, 8))
     lin("a", R16, 1.0, lin("a", fcol(FP3), 4.0, -125.0), V("row", 32, 40))
     c = lin("a", lin("a", fcol(FP3), -1.0, fcol(FPH), func=F.Abs), 1.0, 0.0, func=F.Sign)
@@ -266,13 +264,15 @@ def rank_program(g, core, T, topo):
     early(2.0)
     iota(V("w8"), [[0, 136]], 0, 0)
     iota(V("w9"), [[0, 264]], 0, 0)
+    iota(V("kt", 320, 512), [[0, 192]], 0, 0)
     iota(V("ht", 256, 512), [[0, 256]], 0, 0)
     iota(V("vcon"), [[0, 8], [4, 4], [0, 4]], 0, 0)
     iota(V("horn"), [[0, 128]], 64, 0)
     iota(V("horn", 0, 128, 4), [[0, 32]], 0, 0)
+    iota(V("eqv", 128, 136), [[0, 8]], 0, 0)
     iota(V("lane"), [[0, 64]], 1, 0)
     iota(V("lane", 15, 64, 16), [[0, 4]], -1024, 0)
-    iota(V("eq6", 128, 136), [[0, 8]], 0, 0)
+    act(V("lane"), V("lane"), scale=0.0625)
     iota(V("in1"), [[0, 128]], 0, 0)
     for r in range(3):
         iota(V("fin%d" % r, 1, 64, 2), [[32, 2], [0, 16]], C + K * r, 0)
@@ -369,13 +369,14 @@ def rank_program(g, core, T, topo):
     def symbols(r):
         dst = T.cores[(rank - DIST[r]) % n_ranks]
         for t in range(4):
-            plane("v" if t < 2 else "a", r, "kt", t, 0, 128, 32)
+            plane("v" if t < 2 else "a", r, "kt", t, 0, 80, 32)
         quant(V("kq"), V("ks"), V("kt"))
         mm(V("ps", 1536, 1664), V("urq"), V("urs"), V("kq"), V("ks"))
         for b in range(4):
             mm(V("ps", 2048 + 512 * b, 2176 + 512 * b), V("wq", 128 * b, 128 * b + 128), V("wsc", 128 * b, 128 * b + 128), V("kq"), V("ks"))
-        ts(V("kb"), V("ps", 1536, 1664), 0.0, A.is_gt, CW4, A.mult)
-        tr(V("kbt"), V("kb"), 0.5)
+        ts(V("kb", 0, 80), V("ps", 1536, 1616), 0.0, A.is_gt, CW4, A.mult)
+        tr(V("kbt", 0, 64), V("kb", 0, 64), 0.5)
+        tr(V("kbt", 64, 128), V("kb", 16, 80), 0.5)
         tt(V("fs%d" % r), V("kbt", 0, 128, 4), V("kbt", 1, 128, 4), A.add)
         send(dst, V("fl%d" % r), V("fs%d" % r), "af%d" % r, 2.5)
         pieces(r, PIECES, "urq", "urs")
@@ -399,12 +400,11 @@ def rank_program(g, core, T, topo):
         fl, fin = "fl%d" % r, "fin%d" % r
         tt(V("xe"), IND(V(fl), L(L_EXP, 8)), V("vcon"), A.is_equal, ext="af%d" % r)
         act(V(fin, 0, 64, 2), IND(V(fl), L(L_FIN2, 2)), ext="af%d" % r)
-        scan(V("eqv"), V("horn"), V("xe"), 0.0, A.mult, A.add)
-        act(V("eq6", 0, 128), V("eqv"), scale=64.0)
-        act(V("pa"), IND(V("eqv"), L(L_PS, 8)), scale=64.0)
+        scan(V("eqv", 0, 128), V("horn"), V("xe"), 0.0, A.mult, A.add)
+        act(V("pa"), IND(V("eqv"), L(L_PS, 8)))
         tr(V("fw"), V(fin))
         early(1.0)
-        tt(V("tab"), IND(V("eq6"), L(L_PM, 8)), V("pa"), A.add)
+        tt(V("tab"), IND(V("eqv"), L(L_PM, 8)), V("pa"), A.add)
         act(V("fw9"), IND(V("fw"), L(L_REP, 36)))
         hq, hs = "hq%d" % r, "hs%d" % r
         for b in range(4):
@@ -413,36 +413,39 @@ def rank_program(g, core, T, topo):
         for b in range(4):
             act(V("pool", PW * b + C + K * r, PW * b + C + K * r + K), V("ps", 2048 + 512 * b, 2048 + 512 * b + K))
             early(1.5)
-        half = float(sum((3 - t) * 8 * 64 ** (3 - t) for t in range(4)))
-        for i in range(4):
-            for c in range(2):
-                k = 2 * i + c
-                w = IND(V("tab", 16 * k, 16 * k + 16), V("ixu", 4 * k, 4 * k + 4))
-                o = V("ac%d" % (i % 2), 64 * c, 64 * c + 64)
-                if i == 0:
-                    ts(o, w, half, A.add)
-                else:
-                    tt(o, w, V("ac%d" % (1 - i % 2), 64 * c, 64 * c + 64), A.add)
-        tt(V("ci"), V("ac1", 0, 64), V("ac1", 64, 128), A.add)
-        for t in range(4):
-            ts(V("yi", 64 * t, 64 * t + 64), V("ci"), 6 * (3 - t), A.logical_shift_right, 63 * 16, A.bitwise_and)
+        for k in range(8):
+            w = IND(V("tab", 16 * k, 16 * k + 16), V("ixu", 4 * k, 4 * k + 4))
+            o = V("ac", 64 * k, 64 * k + 64)
+            if k == 0:
+                ts(o, w, float(sum((3 - t) * 16 * 64 ** (2 - t) for t in range(3))), A.add)
+            elif k < 3:
+                cp(o, w)
+            else:
+                tt(o, w, V("ac", 64 * k - 192, 64 * k - 128), A.add)
+        tt(V("ac", 512, 576), V("ac", 320, 384), V("ac", 384, 448), A.add)
+        tt(V("ci"), V("ac", 512, 576), V("ac", 448, 512), A.add)
+        ts(V("yi", 256, 320), V("ci"), 15, A.bitwise_and)
+        for t in range(3):
+            ts(V("yi", 64 * t, 64 * t + 64), V("ci"), 6 * (3 - t) - 2, A.logical_shift_right, 63, A.bitwise_and)
+        ts(V("yi", 192, 256), V("yi", 256, 320), 4.0, A.mult)
         for c in range(2):
             tt(V("y2", 64 * c, 64 * c + 64), V("yi", 128 * c, 128 * c + 64), V("yi", 128 * c + 64, 128 * c + 128), A.max)
         tt(V("y1"), V("y2", 0, 64), V("y2", 64, 128), A.max)
         tr(V("yt"), V("y1"))
         scan(V("sc"), V("yt"), V("lane"), 0.0, A.max, A.add)
-        ts(V("ku"), V("sc", 15, 64, 16), 1024.0, A.add)
+        ts(V("ku"), V("sc", 15, 64, 16), 64.0, A.add, 16.0, A.mult)
         cp(V("fg"), IND(V("fw9"), V("ku")))
         tr(V("ft"), V("fg"))
         f4, kc = V("ft", 0, 64, 2), V("ft", 1, 64, 2)
         old, new = V("in%d" % (r % 2), 0, 128, 4), V("in%d" % (1 - r % 2), 0, 128, 4)
         tt(V("d0"), f4, V("m4"), A.not_equal)
         tt(V("d1"), kc, V("jcode"), A.add)
+        tt(V("d4"), f4, V("sm", 0, 32), A.not_equal)
         tt(V("d2"), f4, V("sm", 0, 32), A.is_equal)
         tt(V("d3"), V("d0"), V("d1"), A.mult)
-        tt(V("d4"), old, V("d3"), A.subtract)
-        tt(V("d5"), V("d4"), V("d2"), A.mult)
-        tt(new, V("d5"), V("d3"), A.add)
+        tt(V("d5"), V("d2"), old, A.mult)
+        tt(V("d6"), V("d3"), V("d4"), A.mult)
+        tt(new, V("d5"), V("d6"), A.add)
 
     for r in range(3):
         inherit(r)
@@ -479,7 +482,6 @@ def rank_program(g, core, T, topo):
             seen.setdefault(f[0], []).append((f, False, o["id"]))
         for f in o["w"]:
             seen.setdefault(f[0], []).append((f, True, o["id"]))
-    HOP = 0.08
     for o in ops:
         o["tail"], o["succ"], o["left"], o["est"] = 0.0, [], len(o["pre"]), 0.0
     for o in ops:

@@ -1,3 +1,4 @@
+import numpy as np
 from concourse.mybir import dt, AluOpType, ActivationFunctionType
 
 A = AluOpType
@@ -6,8 +7,12 @@ DIST = [1, 2, 4]
 C, K = 512, 64
 PW = C + 3 * K
 F32, BF, I32, U16, U8, MX = "float32", "bfloat16", "int32", "uint16", "uint8", "float8_e4m3fn_x4"
-PIECES = [(0, 256, "vaaa"), (256, 384, "vvaa"), (384, 512, "vvaa")]
-PIECES_LAST = [(0, 256, "vvaa"), (256, 384, "vaaa"), (384, 512, "vvaa")]
+GATH = [(0, 14, "vaaa"), (18, 26, "vvaa"), (26, 32, "vvaa")]
+PIECES = [(0, 288), (288, 512)]
+GATH_LAST = [(0, 16, "vvaa"), (16, 24, "vaaa"), (24, 32, "vvaa")]
+PIECES_LAST = [(0, 256), (256, 384), (384, 512)]
+LOOK = [(0, 12, "v"), (12, 32, "a")]
+U16T = True
 
 
 def _sb(n, d):
@@ -15,42 +20,96 @@ def _sb(n, d):
 
 
 SCRATCH = {
-    "parL": _sb(8, I32), "flr": _sb(256, I32), "xin": _sb(2048, BF), "ut": _sb(512, BF), "vt": _sb(512, BF),
+    "par2": _sb(32, I32), "parq": _sb(8, I32), "raw": _sb(128, I32), "xin": _sb(2048, BF), "ut": _sb(512, BF), "vt": _sb(512, BF),
     "wq": _sb(512, MX), "wsc": _sb(512, U8), "uq": _sb(128, MX), "us": _sb(128, U8), "urq": _sb(128, MX), "urs": _sb(128, U8),
+    "ukq": _sb(128, MX), "uks": _sb(128, U8),
     "vq": _sb(128, MX), "vs": _sb(128, U8), "one": _sb(516, BF), "eb": _sb(516, BF), "ebq": _sb(512, MX), "ebs": _sb(512, U8),
-    "pi": _sb(2, I32), "fi": _sb(16, I32), "ff": _sb(16, F32), "col": _sb(64, F32), "row": _sb(96, F32),
-    "lf": _sb(100, F32), "lu": _sb(100, U16), "jp": _sb(32, F32), "jfull": _sb(32, F32), "jcode": _sb(32, F32),
-    "vcon": _sb(128, F32), "horn": _sb(128, F32), "lane": _sb(64, F32),
-    "ptr": _sb(160, U16), "paru": _sb(8, U16),
-    "va": _sb(160, F32), "vb": _sb(160, F32), "vc": _sb(160, F32), "w8": _sb(136, F32), "w9": _sb(264, F32),
-    "tb": _sb(320, F32), "tc": _sb(288, F32), "kin": _sb(32, F32),
-    "yy": _sb(144, F32), "ei": _sb(48, I32), "ej": _sb(48, I32), "el": _sb(48, U16),
-    "in0": _sb(128, F32), "in1": _sb(128, F32), "flg": _sb(128, F32),
-    "pool": _sb(4 * PW, BF), "et": _sb(2048, BF), "eq": _sb(512, MX), "es": _sb(512, U8),
-    "kt": _sb(512, BF), "kq": _sb(128, MX), "ks": _sb(128, U8), "ht": _sb(512, BF),
-    "kb": _sb(128, BF), "kbt": _sb(128, BF), "rows": _sb(512, BF), "op": _sb(256, BF), "opt": _sb(256, BF),
-    "sm": _sb(64, F32), "m4": _sb(32, F32), "ix0": _sb(32, F32), "ixu": _sb(32, U16),
-    "xe": _sb(128, F32), "eqv": _sb(136, F32), "pa": _sb(128, F32), "tab": _sb(128, F32),
-    "ac": _sb(576, F32),
-    "ci": _sb(64, I32), "yi": _sb(320, I32), "y2": _sb(128, F32), "y1": _sb(64, F32), "yt": _sb(64, F32),
-    "sc": _sb(64, F32), "ku": _sb(4, U16), "fw": _sb(64, F32), "fw9": _sb(576, F32), "fg": _sb(64, F32), "ft": _sb(64, F32),
-    "d0": _sb(32, F32), "d1": _sb(32, F32), "d2": _sb(32, F32), "d3": _sb(32, F32), "d4": _sb(32, F32), "d5": _sb(32, F32),
-    "d6": _sb(32, F32), "yo": _sb(512, F32),
+    "pi": _sb(2, I32), "fi": _sb(24, I32), "ff": _sb(24, F32), "col": _sb(128, F32), "row": _sb(128, F32), "cnt": _sb(128, F32),
+    "lf": _sb(80, F32), "lu": _sb(80, U16), "cj": _sb(128, F32), "jc": _sb(96, F32),
+    "vcon": _sb(128, F32), "horn": _sb(128, F32), "lane": _sb(256, F32), "seg4": _sb(128, BF), "seg8": _sb(512, F32),
+    "ptr": _sb(176, U16), "paru": _sb(8, U16), "nt": _sb(640, F32), "r2": _sb(256, F32), "r3": _sb(256, F32), "ol": _sb(16, U16),
+    "va": _sb(160, F32), "vb": _sb(160, F32), "vc": _sb(160, F32), "w8": _sb(136, F32), "w9": _sb(264, F32), "prm": _sb(160, F32),
+    "vi": _sb(160, I32), "ti": _sb(288, I32), "tb": _sb(288, F32), "tc": _sb(288, F32),
+    "yy": _sb(48, I32), "el": _sb(32, U16), "nw": _sb(128, F32), "flg": _sb(128, F32),
+    "pool": _sb(4 * PW, BF), "et": _sb(2304, BF), "eq": _sb(512, MX), "es": _sb(512, U8),
+    "kq": _sb(128, MX), "ks": _sb(128, U8), "ht": _sb(512, BF),
+    "kb": _sb(80, BF), "kbt": _sb(128, BF), "rows": _sb(512, BF), "op": _sb(128, BF), "op2": _sb(128, BF), "opt": _sb(128, BF),
+    "x0": _sb(128, BF), "xs": _sb(128, U16 if U16T else BF), "xt": _sb(32, BF), "sm": _sb(64, BF), "ixu": _sb(32, U16),
+    "xe": _sb(128, F32), "tab": _sb(264, F32), "ac": _sb(512, F32), "ci": _sb(512, I32), "yt": _sb(64, I32), "yi": _sb(256, I32),
+    "sc": _sb(256, F32), "ku": _sb(4, U16), "fin": _sb(64, BF), "fw": _sb(576, BF), "fg": _sb(64, BF), "ft": _sb(64, BF),
+    "d0": _sb(128, F32), "d1": _sb(128, F32), "yo": _sb(512, F32),
     "ps": ("psum", [128, 4096], F32),
 }
 for _r in range(3):
     SCRATCH["fs%d" % _r] = _sb(32, BF)
     SCRATCH["fl%d" % _r] = _sb(32, BF)
-    SCRATCH["fin%d" % _r] = _sb(64, F32)
     SCRATCH["hq%d" % _r] = _sb(192, MX)
     SCRATCH["hs%d" % _r] = _sb(192, U8)
 
 SEMAPHORES = (["sv", "sa", "sp", "st", "l_par", "l_fl", "l_u", "l_x", "l_w", "l_v", "out", "sent"]
               + ["af%d" % r for r in range(3)] + ["ah%d" % r for r in range(3)])
 ENG_SEM = {"v": "sv", "a": "sa", "p": "sp", "t": "st"}
+CYC, HOP = 0.001, 0.2
+VAL, PTR = 2, 1
 
-L_PJ, L_FJ, L_SEL, L_UREP, L_OWN, L_FSEL, L_FIN, L_KEY, L_REO, L_EXP, L_PS, L_PM, L_FIN2, L_REP = 0, 2, 4, 6, 14, 22, 26, 30, 32, 34, 42, 50, 58, 60
-CYC, HOP = 0.001, 0.22
+
+def seen(h, c, lane):
+    return 32 * (c // 2) + lane if c % 2 == h else 128 + 32 * (c // 2 + 1 - h) + lane
+
+
+def slot(h, t):
+    return t if h == 0 else (3, 2, 0, 1)[t]
+
+
+def parents(m, e, p):
+    if m < 4:
+        return 32 * (2 * (m % 2) + p // 8) + 16 * (m // 2) + 2 * (p % 8) + e
+    return 32 * (2 * ((m - 4) // 2) + e) + 16 * (m % 2) + p
+
+
+LISTS = [
+    ("RAW", 8, lambda a, h, p, c: 8 * p + c),
+    ("SEL", 2, lambda a, h, p, c: seen(h, p % 8, PTR)),
+    ("PERM", 8, lambda a, h, p, c: 8 * p + (c + 1 - a % 2) % 8),
+    ("FS", 4, lambda a, h, p, c: seen(h, p // 2, 4 * (2 * (2 * (p % 2) + (a % 2 if c < 2 else 1 - a % 2)) + h) + VAL)),
+    ("UR", 8, lambda a, h, p, c: 16 * (p // 2) + p % 2),
+    ("UK", 8, lambda a, h, p, c: 64 * (c % 2) + 16 * (p // 4) + p % 4),
+    ("R2", 16, lambda a, h, p, c: parents(c // 2, c % 2, p) + h * (128 + 128 * a)),
+    ("XE", 8, lambda a, h, p, c: 8 * slot(h, p % 4) + c),
+    ("FIN", 2, lambda a, h, p, c: 8 * slot(h, 2 * c + h) + p % 8),
+]
+
+
+def table(n, f):
+    return np.array([[f(P // 32, P // 16 % 2, P % 16, c) for c in range(n)] for P in range(128)], dtype=np.int64)
+
+
+def terms(vec):
+    c = [int(z) for z in vec]
+    for b in range(7):
+        for P in range(128):
+            if P >> b & 1:
+                c[P] -= c[P ^ (1 << b)]
+    out, b = [], 0
+    while b < 7:
+        k, e = c[1 << b], b + 1
+        while k and e < 7 and c[1 << e] == k << (e - b):
+            e += 1
+        if k:
+            out.append(((b, (1 << (e - b)) - 1), k))
+        b = e
+    return c[0], out + [(m, c[m]) for m in range(1, 128) if m & (m - 1) and c[m]]
+
+
+def pattern(r):
+    n = len(r)
+    for n2 in range(n, 0, -1):
+        for n1 in range(n // n2, 0, -1):
+            if n % (n1 * n2) == 0:
+                s = [int(r[k] - r[0]) if k < n else 0 for k in (n1 * n2, n2, 1)]
+                if all(r[i] == r[0] + s[0] * (i // (n1 * n2)) + s[1] * (i // n2 % n1) + s[2] * (i % n2) for i in range(n)):
+                    return [[s[0], n // (n1 * n2)], [s[1], n1], [s[2], n2]]
+    return None
 
 
 def rank_program(g, core, T, topo):
@@ -70,31 +129,18 @@ def rank_program(g, core, T, topo):
             return (ap, [("ps", 0, 128, c0 // 512 * 512, c0 // 512 * 512 + 512, 1)], n, False)
         return (ap, [(name, p0, p1, c0, c1, st)], n, False)
 
+    def Q(name, a, c0, c1, st=1, n=1):
+        return V(name, c0, c1, st, 32 * a, 32 * (a + n))
+
     def IND(w, o):
         return (w[0].indirect(o[0]), w[1] + o[1], 16 * o[2], True)
-
-    def L(c, n):
-        return V("lu", c, c + n)
-
-    def LF(c, n=1):
-        return V("lf", c, c + n)
-
-    ncol = [0]
-
-    def newcol():
-        ncol[0] += 1
-        return V("col", ncol[0] - 1, ncol[0])
-
-    def fcol(c):
-        return V("ff", c, c + 1)
 
     def op(eng, fn, outs, ins, cost, lat=0.0, sem=None, inc=1, ext=None, gives=None):
         w = [f for v in outs for f in v[1]]
         r = []
         for v in ins:
             if isinstance(v, tuple):
-                for f in v[1]:
-                    (w if f[0] == "ps" else r).append(f)
+                r += v[1]
         ops.append({"eng": eng, "fn": fn, "r": r, "w": w, "sem": sem or ENG_SEM[eng], "inc": inc, "dma": sem is not None,
                     "ext": ext, "cost": cost, "lat": lat, "early": 0.0, "id": len(ops)})
         if gives is not None:
@@ -107,7 +153,7 @@ def rank_program(g, core, T, topo):
         return v[0] if isinstance(v, tuple) else v
 
     def cc(v, k=1.0):
-        return 0.05 + 1.5 * CYC * v[2] if v[3] else max(64, k * v[2]) * CYC
+        return 0.05 + 1.6 * CYC * v[2] if v[3] else max(64, k * v[2]) * CYC
 
     def cp(o, i):
         op("v", lambda: g.vector.tensor_copy(o[0], i[0]), [o], [i], cc(i))
@@ -127,8 +173,8 @@ def rank_program(g, core, T, topo):
     def ms(o, c):
         op("v", lambda: g.vector.memset(o[0], c), [o], [], cc(o))
 
-    def scan(o, d0, d1, init, o0, o1):
-        op("v", lambda: g.vector.tensor_tensor_scan(o[0], d0[0], d1[0], init, o0, o1), [o], [d0, d1], cc(d0))
+    def scan(o, d0, d1, init, o0, o1, k=1.0):
+        op("v", lambda: g.vector.tensor_tensor_scan(o[0], d0[0], d1[0], init, o0, o1), [o], [d0, d1], cc(d0, k))
 
     def act(o, i, func=None, scale=None, bias=None, ext=None):
         kw = {}
@@ -147,15 +193,18 @@ def rank_program(g, core, T, topo):
         else:
             op("p", lambda: g.iota(o[0], pat, base, cm), [o, POOL], [], 0.13 + 2 * CYC * o[2])
 
+    def fill(o, c, flt=True):
+        iota(o, [[0, o[2]]], c, 0, flt)
+
     def quant(q, s, i):
-        op("v", lambda: g.vector.quantize_mx(q[0], s[0], i[0]), [q, s], [i], 0.015 + 0.26 * CYC * i[2])
+        op("v", lambda: g.vector.quantize_mx(q[0], s[0], i[0]), [q, s], [i], 0.015 + 0.27 * CYC * i[2])
 
     def mm(o, lq, ls, rq, rs, ext=None):
-        op("t", lambda: g.tensor.matmul_mx(o[0], lq[0], ls[0], rq[0], rs[0], True, True), [o], [lq, ls, rq, rs], 0.7 * CYC * (rq[2] + 16), 0.05, ext=ext)
+        op("t", lambda: g.tensor.matmul_mx(o[0], lq[0], ls[0], rq[0], rs[0], True, True), [o], [lq, ls, rq, rs], 0.6 * CYC * (rq[2] + 16), ext=ext)
 
-    def dma(eng, o, i, sem, lat=1.8):
+    def dma(eng, o, i, sem, lat=1.8, after=None):
         q = {"s": g.sync, "a": g.scalar, "p": g}[eng]
-        op(eng, lambda: q.dma_start(ap(o), ap(i)), [o] if isinstance(o, tuple) else [], [i], 0.06, lat, sem=sem, inc=16)
+        op(eng, lambda: q.dma_start(ap(o), ap(i)), [o] if isinstance(o, tuple) else [], [i, after], 0.06, lat, sem=sem, inc=16)
 
     def u8(v):
         return (v[0].bitcast(dt.uint8), v[1], v[2], False)
@@ -167,156 +216,188 @@ def rank_program(g, core, T, topo):
         m = topo.mask(core, dst_core)
         n = len(topo.engines(core, dst_core))
         count[rsem] = count.get(rsem, 0) + n
-        op("p", lambda: g.remote_dma(o[0], i[0], T.sem[rsem], T.sem["sent"], pid, rid, m), [], [i], 0.1, lat, sem="sent", inc=-n, gives=rsem)
+        op("p", lambda: g.remote_dma(o[0], i[0], T.sem[rsem], T.sem["sent"], pid, rid, m), [], [i], 0.15, lat, sem="sent", inc=-n, gives=rsem)
 
-    for G in range(8):
-        a = G // 2
-        dma("s", V("parL", 0, 8, 1, 16 * G, 16 * G + 16), T.par[:, 8 * a:8 * a + 8], "l_par")
-    n = 0
-    for r in range(8):
-        for (d0, d1, s0) in ((0, 128 - 16 * r, 16 * r), (128 - 16 * r, 128, 0)):
-            if d1 > d0:
-                dma("a" if n < 11 else "s", V("flr", 32 * r, 32 * r + 32, 1, d0, d1), T.fl[s0:s0 + d1 - d0, :], "l_fl")
-                n += 1
-    dma("s", V("xin"), T.x[:, :], "l_x", 5.0)
-    dma("s", V("ut"), T.u[:, :], "l_u", 4.5)
-    dma("s", u8(V("wq")), T.wc[:, :], "l_w", 6.0)
-    dma("s", V("wsc"), T.ws[:, :], "l_w", 6.0)
-    dma("s", V("vt"), T.v[:, :], "l_v", 6.5)
+    GATE = (None, [("gate", 0, 128, 0, 1, 1)])
+    op("v", lambda: g.vector.memset(T.raw[:, :], 0), [V("raw"), GATE], [], 0.13)
+    dma("s", V("par2", 0, 32, 1, 0, 16), T.par[:, :], "l_par")
+    dma("a", V("par2", 0, 32, 1, 16, 32), T.par[:, :], "l_par")
+    for a in range(4):
+        dma("s" if a % 2 else "a", (T.raw[32 * a + VAL:32 * a + 32:4, :], [("raw", 32 * a + VAL, 32 * a + 32, 0, 128, 1)]), T.fl[:, 8 * a:8 * a + 8], "l_fl", 2.5)
+    for a in range(4):
+        dma("s" if a % 2 else "a", V("raw", 0, 128, 1, 32 * a + PTR, 32 * a + PTR + 1), T.par[:, 8 * a:8 * a + 8], "l_fl", 2.5)
+    dma("s", V("xin"), T.x[:, :], "l_x", 5.0, GATE)
+    dma("s", V("ut"), T.u[:, :], "l_u", 4.5, GATE)
+    dma("s", u8(V("wq")), T.wc[:, :], "l_w", 6.0, GATE)
+    dma("s", V("wsc"), T.ws[:, :], "l_w", 6.0, GATE)
+    dma("s", V("vt"), T.v[:, :], "l_v", 6.5, GATE)
 
     iota(V("pi", 0, 1), [[0, 1]], 0, 1, False)
-    iota(V("jp"), [[32, 4], [0, 8]], 0, 1)
-    iota(V("row", 0, 16), [[3, 2], [0, 1], [1, 8]], 0, 0)
-    iota(V("row", 16, 24), [[16, 8]], 0, 0)
-    iota(V("row", 24, 32), [[0, 4], [64, 2]], 0, 0)
-    iota(V("row", 48, 84), [[0, 9], [-16, 4]], 63, 0)
-    RC, R16, R64, RREP = V("row", 0, 8), V("row", 16, 24), V("row", 24, 32), V("row", 48, 84)
-    RC2, R4 = V("row", 0, 2), V("row", 0, 8, 4)
-    P = V("pi", 0, 1)
-    ms(V("in0"), 0.0)
-    fields = [(0, 7), (2, 3), (0, 1), (3, 1), (4, 1), (5, 3), None, None, (0, 15), (0, 3), (1, 1), (2, 1), (5, 1), (6, 1), (0, 31)]
-    FQ7, FPH, FB0, FB3, FH, FA, FRHO, FT, FP, FP3, FB1, FB2, FA0, FA1, F31 = range(15)
-    ts(V("fi", 15, 16), P, 4, A.logical_shift_right)
-    tt(V("fi", FT, FT + 1), P, V("fi", 15, 16), A.subtract)
-    ts(V("fi", FRHO, FRHO + 1), V("fi", FT, FT + 1), 7, A.bitwise_and)
-    for i, sm_ in enumerate(fields):
-        if sm_ is not None:
-            ts(V("fi", i, i + 1), P, sm_[0], A.logical_shift_right, sm_[1], A.bitwise_and)
-    cp(V("ff", 0, 6), V("fi", 0, 6))
-    cp(V("ff", 8, 16), V("fi", 8, 16))
-    for nm in ("va", "vb", "vc"):
-        ms(V(nm, 0, 16), 0.0)
+    iota(V("cnt"), [[1, 128]], 0, 0)
+    made, used = {}, {"ff": 0, "col": 0, "row": 0}
+
+    def new(name, n=1):
+        used[name] += n
+        return V(name, used[name] - n, used[name])
+
+    def feature(k):
+        if k not in made:
+            if isinstance(k, tuple):
+                o = made[k] = new("ff")
+                i = V("fi", used["ff"] - 1, used["ff"])
+                ts(i, V("pi", 0, 1), k[0], A.logical_shift_right, k[1], A.bitwise_and)
+                cp(o, i)
+            else:
+                low = k & -k
+                rest = k ^ low
+                o = made[k] = new("col")
+                act(o, feature(rest if rest & (rest - 1) else (rest.bit_length() - 1, 1)), scale=feature((low.bit_length() - 1, 1)))
+        return made[k]
+
+    def column(vec):
+        c0, tm = terms(vec)
+        prev, key = float(c0), ("c", c0)
+        for (k, coef) in tm or [((0, 1), 0)]:
+            key = key + (k, coef)
+            if key not in made:
+                made[key] = new("col")
+                act(made[key], feature(k), scale=float(coef), bias=prev)
+            prev = made[key]
+        return prev
+
+    def const(o, tb):
+        c = 0
+        while c < tb.shape[1]:
+            e = c + 1
+            while e < tb.shape[1] and (tb[:, e] - tb[0, e] == tb[:, c] - tb[0, c]).all():
+                e += 1
+            while pattern(tb[0, c:e]) is None:
+                e -= 1
+            r = tb[0, c:e] - tb[0, c]
+            pat = pattern(r)
+            if pat[0][1] * pat[1][1] == 1:
+                act(o(c, e), V("cnt", 0, e - c), scale=float(pat[2][0]), bias=column(tb[:, c]))
+            else:
+                unit = int(np.gcd.reduce(r))
+                key = ("r",) + tuple(int(z) // unit for z in r)
+                if key not in made:
+                    made[key] = new("row", e - c)
+                    iota(made[key], pattern(r // unit), 0, 0)
+                act(o(c, e), made[key], scale=float(unit), bias=column(tb[:, c]))
+            c = e
+
+    def colf(f):
+        return column(table(1, f)[:, 0])
+
+    at, c0 = {}, 0
+    for (name, n, f) in LISTS:
+        at[name] = (c0, n)
+        const(lambda c, e: V("lf", c0 + c, c0 + e), table(n, f))
+        cp(V("lu", c0, c0 + n), V("lf", c0, c0 + n))
+        c0 += n
+
+    def L(name, n=None):
+        return V("lu", at[name][0], at[name][0] + (n or at[name][1]))
+
+    act(V("cj"), V("cnt"), scale=colf(lambda a, h, p, c: 1025 * (p // 2 % 2)),
+        bias=colf(lambda a, h, p, c: 1025 * (128 * a + 1) * (p // 2 % 2) - 1))
+    PAD = colf(lambda a, h, p, c: -1000 * (p % 2))
+    for nm in ("va", "vb", "vc", "prm"):
+        act(V(nm, 0, 16), V("cnt", 0, 16), scale=0.0, bias=PAD)
         ms(V(nm, 144, 160), 0.0)
-
-    def lin(eng, x, s, b, out=None, func=None):
-        o = out if out is not None else newcol()
-        if eng == "a":
-            act(o, x, func, scale=s, bias=b)
-        else:
-            ts(o, x, s, A.mult, b, A.add)
-        return o
-
-    lin("v", fcol(FPH), 2.0, fcol(FH), L(L_PJ, 1))
-    c = lin("v", fcol(FB3), 2.0, lin("v", fcol(FA), 8.0, fcol(FH)))
-    ts(L(L_FJ, 2), R4, c, A.add, lin("v", V("fi", FRHO, FRHO + 1), 32.0, 0.0), A.add)
-    c = lin("a", fcol(FA), 98400.0, 1024.0)
-    lin("a", V("jp"), 1025.0, c, V("jfull"))
-    CB0 = lin("a", fcol(FA), -128.0, 8.0)
-    CB = lin("a", fcol(FA), -128.0, 519.0)
-    CX = lin("a", fcol(FB0), -1.0, fcol(FH), func=F.Abs)
-    c = lin("a", fcol(FH), -16.0, 1.0)
-    c = lin("a", fcol(FQ7), 16.0, c)
-    SEL = lin("a", CX, 144.0, c, LF(L_SEL))
-    cp(V("lu", 4, 5), V("lf", 4, 5))
-    ms(V("lf", 6, 100), 0.0)
-    c = lin("a", fcol(FA), 98304.0, 1024.0)
-    lin("a", V("jp"), 1024.0, c, V("jcode"))
-    lin("a", R16, 1.0, lin("a", fcol(FA), 128.0, fcol(FP)), LF(L_OWN, 8))
-    lin("a", R64, 1.0, lin("a", fcol(FPH), 16.0, fcol(FP3)), LF(L_UREP, 8))
-    CW = lin("a", fcol(FB0), -1.0, 2.0)
-    CW4 = lin("a", fcol(FB0), -4.0, 8.0)
-    C8 = lin("a", fcol(FA0), 100000.0, lin("a", fcol(FA), -128.0, 647.0 - 100000.0))
-    C9 = lin("a", fcol(FA1), 100000.0, 519.0 - 100000.0)
-    c = lin("a", lin("a", SEL, -1.0, 289.0), fcol(FB3), SEL)
-    c = lin("a", fcol(FH), 4.0, c)
-    s0 = lin("a", fcol(FA), 8.0, lin("a", c, 1.0, -1.0), LF(L_FSEL + 2))
-    lin("a", fcol(FA0), -16.0, lin("a", s0, 1.0, 8.0), LF(L_FSEL + 3))
-    lin("a", fcol(FA1), -32.0, lin("a", s0, 1.0, 16.0), LF(L_FSEL))
-    lin("a", fcol(FA), -8.0, lin("a", c, 1.0, 23.0), LF(L_FSEL + 1))
-    c = lin("a", lin("a", fcol(FB3), -1.0, fcol(FA0), func=F.Abs), 64.0, fcol(FQ7))
-    lin("a", fcol(FA1), 32.0, lin("a", c, 1.0, 32.0), LF(L_FIN))
-    lin("a", fcol(FA1), -32.0, lin("a", c, 1.0, 64.0), LF(L_FIN + 1))
-    c = lin("a", fcol(FB0), -1.0, fcol(FA0), func=F.Abs)
-    lin("a", c, 64.0, lin("a", lin("a", fcol(FB1), -1.0, fcol(FA1), func=F.Abs), 32.0, 40.0), LF(L_FIN + 2))
-    lin("a", RC2, 0.0, lin("a", fcol(FP), 8.0, 0.0), LF(L_KEY, 2))
-    cp(V("lu", 6, 32), V("lf", 6, 32))
-    lin("a", RC2, 4.0, lin("a", fcol(FP3), 8.0, fcol(FPH)), LF(L_REO, 2))
-    c = lin("a", fcol(FB0), -8.0, lin("a", fcol(FH), 8.0, 0.0), func=F.Relu)
-    c = lin("a", c, -1.0, lin("a", fcol(FB1), 8.0, 0.0), func=F.Abs)
-    lin("a", RC, 1.0, lin("a", CX, 16.0, c), LF(L_EXP, 8))
-    lin("a", R16, 1.0, lin("a", fcol(FPH), 4.0, 3.0), LF(L_PS, 8))
-    lin("a", R16, 1.0, lin("a", fcol(FP3), 4.0, -125.0), V("row", 32, 40))
-    c = lin("a", lin("a", fcol(FP3), -1.0, fcol(FPH), func=F.Abs), 1.0, 0.0, func=F.Sign)
-    lin("a", V("row", 32, 40), c, 128.0, LF(L_PM, 8))
-    lin("a", RC2, 8.0, fcol(FQ7), LF(L_FIN2, 2))
-    lin("a", RREP, 1.0, lin("a", fcol(FP), -1.0, 0.0), LF(L_REP, 36))
-    cp(V("lu", 32, 100), V("lf", 32, 100))
-    early(2.0)
-    iota(V("w8"), [[0, 136]], 0, 0)
-    iota(V("w9"), [[0, 264]], 0, 0)
-    iota(V("kt", 320, 512), [[0, 192]], 0, 0)
-    iota(V("ht", 256, 512), [[0, 256]], 0, 0)
-    iota(V("vcon"), [[0, 8], [4, 4], [0, 4]], 0, 0)
-    iota(V("horn"), [[0, 128]], 64, 0)
-    iota(V("horn", 0, 128, 4), [[0, 32]], 0, 0)
-    iota(V("eqv", 128, 136), [[0, 8]], 0, 0)
-    iota(V("lane"), [[0, 64]], 1, 0)
-    iota(V("lane", 15, 64, 16), [[0, 4]], -1024, 0)
-    act(V("lane"), V("lane"), scale=0.0625)
-    iota(V("in1"), [[0, 128]], 0, 0)
+    CB = colf(lambda a, h, p, c: 8 - 128 * a)
+    C8 = colf(lambda a, h, p, c: 136 - 128 * a if a % 2 else -1000)
+    C9 = colf(lambda a, h, p, c: 8 if a >= 2 else -1000)
+    CW = colf(lambda a, h, p, c: 2 - p % 2)
+    CG = colf(lambda a, h, p, c: 16 * (p // 2) + 3)
     for r in range(3):
-        iota(V("fin%d" % r, 1, 64, 2), [[32, 2], [0, 16]], C + K * r, 0)
-        act(V("fin%d" % r, 1, 64, 2), V("fin%d" % r, 1, 64, 2), bias=fcol(F31))
-    iota(V("one"), [[0, 516]], 1, 0)
+        const(lambda c, e: V("jc", 32 * r + c, 32 * r + e), table(32, lambda a, h, p, c: 1024 * (128 * a + 32 * (c // 8) + 16 * h + p + 1) + C + K * r))
+    const(lambda c, e: V("fin", 2 * c + 1, 2 * e, 2), table(32, lambda a, h, p, c: 16 * (0, 2, 1, 3)[2 * (c // 16) + h] + p))
+    for nm in ("w8", "w9"):
+        act(V(nm, 0, 8), V("cnt", 0, 8), scale=0.0, bias=PAD)
+        fill(V(nm, 8), 0)
+    for a1 in range(2):
+        iota(V("nt", 128 + 256 * a1, 384 + 256 * a1), [[224, 2], [1, 16], [32, 8]], 32 + 16 * a1, 0)
+    iota(V("nt", 128, 640, 8), [[16, 2], [32, 2], [1, 16]], 0, 0)
+    fill(V("vi", 0, 16), 0, False)
+    fill(V("vi", 144, 160), 0, False)
+    def afill(name, c0, c1, c, st=1):
+        for b in range(c0, c1, 128 * st):
+            o = V(name, b, min(c1, b + 128 * st), st)
+            act(o, V("cnt", 0, o[2]), scale=0.0, bias=float(c))
+
+    afill("et", 0, 256, 0)
+    afill("ht", 256, 512, 0)
+    afill("seg4", 0, 128, 1)
+    afill("seg4", 0, 128, 0, 4)
+    iota(V("vcon"), [[0, 8], [1, 4], [0, 4]], 0, 0)
+    afill("horn", 0, 128, 64)
+    afill("horn", 0, 128, 0, 4)
+    afill("tab", 0, 264, 0)
+    afill("seg8", 0, 512, 1)
+    afill("seg8", 0, 512, 0, 8)
+    afill("lane", 0, 256, 0)
+    afill("lane", 3, 256, 0.0625, 4)
+    afill("lane", 63, 256, -64, 64)
+    afill("d0", 0, 128, 0)
+    afill("d1", 3, 128, 0, 4)
+    afill("one", 0, 516, 1)
     op("p", lambda: g.affine_select(T.eb[:, :], T.one[:, :], [[-1, 516]], A.is_equal, 0.0, 3, 4), [V("eb"), POOL], [V("one")], 1.2)
     for b in range(4):
         quant(V("ebq", 128 * b, 128 * b + 128), V("ebs", 128 * b, 128 * b + 128), V("eb", 3 - b, 515 - b))
-        early(6.0)
+        early(4.0)
     for t in range(4):
         act(V("pool", PW * t, PW * t + C), V("xin", t, 2048, 4))
     quant(V("uq"), V("us"), V("ut"))
-    op("v", lambda: g.vector.tensor_copy(T.urq[:, :].bitcast(dt.uint32), T.uq[:, :].bitcast(dt.uint32).indirect(T.lu[:, L_UREP:L_UREP + 8])),
-       [V("urq")], [V("uq"), L(L_UREP, 8)], 0.25)
-    op("a", lambda: g.scalar.activation(T.urs[:, :], T.us[:, :].indirect(T.lu[:, L_UREP:L_UREP + 8]), F.Copy), [V("urs")], [V("us"), L(L_UREP, 8)], 0.25)
+
+    def pick(q, s, lst):
+        op("v", lambda: g.vector.tensor_copy(T[q][:, :].bitcast(dt.uint32), T.uq[:, :].bitcast(dt.uint32).indirect(lst[0])), [V(q)], [V("uq"), lst], 0.25)
+        op("a", lambda: g.scalar.activation(T[s][:, :], T.us[:, :].indirect(lst[0]), F.Copy), [V(s)], [V("us"), lst], 0.27)
+
+    pick("ukq", "uks", L("UK"))
+    pick("urq", "urs", L("UR"))
     quant(V("vq"), V("vs"), V("vt"))
     early(6.0)
 
-    ts(V("in0", 1, 128, 8), IND(V("parL"), L(L_PJ, 1)), -1.0, A.mult, 511.0, A.add)
-    tt(V("in0", 0, 128, 4), IND(V("flr"), L(L_FJ, 2)), V("jfull"), A.mult)
-    ts(V("ptr", 0, 8), V("parL"), CB0, A.add)
-    cp(V("paru"), V("parL"))
+    for a in range(4):
+        cp(Q("parq", a, 0, 8), Q("par2", 0, 8 * a, 8 * a + 8))
+    ts(V("ptr", 0, 8), V("parq"), CB, A.add)
+    cp(V("paru"), V("parq"))
+    for nm in ("va", "vb"):
+        tt(V(nm, 16, 144), IND(V("raw"), L("RAW")), V("cj"), A.mult)
+    tr(V("nw"), V("va", 16, 144))
+    act(V("nt", 0, 128), IND(V("nt", 128, 640), V("paru")))
+    act(V("r2"), IND(V("nt"), L("R2")))
+    for c in range(2):
+        tr(V("r3", 128 * c, 128 * c + 128), V("r2", 128 * c, 128 * c + 128))
+    cp(V("ol", 0, 8), V("r3", 0, 256, 32))
+    cp(V("ol", 8, 12), V("r3", 144, 256, 32))
+    cp(V("ol", 12, 16), V("r3", 16, 128, 32))
 
-    def both(src, tb="tb"):
+    def both(src, tb):
         tr(V(tb, 0, 128), V(src, 16, 144))
         tr(V(tb, 128, 288), V(src, 0, 160))
 
     def pointer(src, k, bias):
         tb = "tc" if k % 2 else "tb"
         both(src, tb)
-        ts(V("ptr", 16 * k, 16 * k + 16), IND(V(tb, 0, 288), L(L_SEL, 1)), -1.0, A.mult, bias, A.add)
+        ts(V("ptr", 16 * k, 16 * k + 16), IND(V(tb), L("SEL", 1)), -1.0, A.mult, bias, A.add)
 
     def step(o, w, own, lst, c0, c1, end):
         tt(V(o, 16 + c0, 16 + c1), IND(V(w, 8, 16 + end), V("ptr", 16 * lst + c0 // 16, 16 * lst + c1 // 16)), V(own, 16 + c0, 16 + c1), A.max)
 
     def inherit(r):
         first, last = r == 0, r == 3
-        src = V("in%d" % (r % 2))
-        tr(V("va", 16, 144), src)
-        tr(V("vb", 16, 144), src)
+        if not first:
+            tr(V("va", 16, 144), V("nw"))
+            tr(V("vb", 16, 144), V("nw"))
         if last:
             act(V("flg"), V("vb", 16, 144), F.Sign)
             for a in range(4):
-                dma("s", T.ofl[:, 128 * a:128 * a + 128], (T.flg[32 * a:32 * a + 32:4, :], V("flg")[1]), "out")
+                dma("s", T.ofl[:, 128 * a:128 * a + 128], (T.flg[32 * a + VAL:32 * a + 32:4, :], V("flg")[1]), "out")
+        else:
+            act(V("d1", 1, 128, 4), V("nw", VAL, 128, 4), scale=-1.0)
+            act(V("d1", 2, 128, 4), V("nw", VAL, 128, 4))
         old, cur, nxt = "va", "vb", "vc"
         for k in range(7):
             for (c0, c1) in (((0, 128),) if first else ((0, 64), (64, 128))):
@@ -326,86 +407,93 @@ def rank_program(g, core, T, topo):
                 pointer(cur, min(k + 1, 6), CB)
         for c0 in (32, 64, 96):
             step(cur, cur, cur, 6, c0, c0 + 32, c0)
-        (act if first else cp)(V("w8", 8, 136, 1, 32, 64), V(cur, 16, 144, 1, 0, 32))
-        act(V("w8", 8, 136, 1, 96, 128), V(cur, 16, 144, 1, 64, 96))
-        act(V("w9", 8, 136, 1, 64, 96), V(cur, 16, 144, 1, 0, 32))
-        act(V("w9", 8, 136, 1, 96, 128), V(cur, 16, 144, 1, 0, 32))
+        (act if first else cp)(Q("w8", 1, 8, 136), Q(cur, 0, 16, 144))
+        act(Q("w8", 3, 8, 136), Q(cur, 2, 16, 144))
+        act(Q("w9", 2, 8, 136), Q(cur, 0, 16, 144))
+        act(Q("w9", 3, 8, 136), Q(cur, 0, 16, 144))
         if first:
             pointer(cur, 8, C8)
         tt(V(old, 16, 144), IND(V("w8"), V("ptr", 128, 136)), V(cur, 16, 144), A.max)
         old, cur = cur, old
-        (act if first else cp)(V("w9", 136, 264, 1, 64, 96), V(cur, 16, 144, 1, 32, 64))
-        act(V("w9", 136, 264, 1, 96, 128), V(cur, 16, 144, 1, 32, 64))
+        cp(Q("w9", 2, 136, 264), Q(cur, 1, 16, 144))
+        (act if last else cp)(Q("w9", 3, 136, 264), Q(cur, 1, 16, 144))
+        if not last:
+            act(V("prm", 16, 144), IND(V(cur, 16, 144), L("PERM")))
         if first:
-            pointer(cur, 9, C9)
-        tt(V(old, 16, 144), IND(V("w9"), V("ptr", 144, 152)), V(cur, 16, 144), A.max)
-        old, cur = cur, old
-        if not last:
-            act(V("kin"), IND(V(cur, 16, 144), L(L_KEY, 2)))
-        both(cur)
-        if not last:
-            tr(V("tb", 288, 320), V("kin"))
-        cp(V("yy", 0, 64), IND(V("tb"), L(L_FSEL, 4)))
-        cp(V("yy", 64, 96, 1, 64, 128), V("yy", 0, 32, 1, 0, 64))
-        act(V("yy", 64, 96, 1, 0, 64), V("yy", 0, 32, 1, 64, 128))
+            pointer("prm", 9, C9)
+            pointer(cur, 10, C9)
+            early(30.0)
+        lst = 160 if last else 144
+        tt(V("vi", 16, 144), IND(V("w9"), V("ptr", lst, lst + 8)), V(cur if last else "prm", 16, 144), A.max)
+        both("vi", "ti")
+        ts(V("yy"), IND(V("ti"), L("FS", 3)), 1023, A.bitwise_and)
         for a in range(4):
-            b = a ^ 1
-            (cp if a >= 2 else act)(V("yy", 96, 144, 1, 32 * b, 32 * b + 32), V("yy", 48, 96, 1, 32 * a, 32 * a + 32))
-        cp(V("ei"), IND(V("yy"), L(L_FIN, 3)))
-        ts(V("ej"), V("ei"), 1023, A.bitwise_and)
-        cp(V("el"), V("ej"))
+            cp(Q("yy", a ^ 1, 16 * (a % 2), 16 * (a % 2) + 16), Q("yy", a, 32, 48))
+        for b in range(2):
+            for a in range(2):
+                cp(Q("el", 2 * b, 16 * a, 16 * a + 16, 1, 2) if last else Q("el", 2 * b, a, 32, 2, 2), Q("yy", 2 * a, b, 32, 2, 2))
 
-    def plane(eng, r, dst, t, c0, c1, l0):
-        w = IND(V("pool", PW * t, PW * t + C + K * r), V("el", l0, l0 + (c1 - c0) // 16))
-        (cp if eng == "v" else act)(V(dst, 4 * c0 + t, 4 * c1, 4), w)
+    def plane(eng, r, t, l0, l1, n0):
+        w = IND(V("pool", PW * t, PW * t + C + K * r), V("el", l0, l1))
+        (cp if eng == "v" else act)(V("et", 4 * (K + n0) + t, 4 * (K + n0 + 16 * (l1 - l0)), 4), w)
 
-    def pieces(r, parts, sq, ss):
-        for i, (c0, c1, engs) in enumerate(parts):
+    def pieces(r, gath, parts, sq, ss):
+        for (l0, l1, engs) in gath:
             for t in range(4):
-                plane(engs[t], r, "et", t, c0, c1, c0 // 16)
-            quant(V("eq", c0, c1), V("es", c0, c1), V("et", 4 * c0, 4 * c1))
+                plane(engs[t], r, t, l0, l1, 16 * l0 + (K if r < 3 and l0 < 14 else 0))
+        for i, (c0, c1) in enumerate(parts):
+            quant(V("eq", c0, c1), V("es", c0, c1), V("et", 4 * (K + c0), 4 * (K + c1)))
             mm(V("ps", 512 * i, 512 * i + c1 - c0), V(sq), V(ss), V("eq", c0, c1), V("es", c0, c1))
 
     def symbols(r):
         dst = T.cores[(rank - DIST[r]) % n_ranks]
         for t in range(4):
-            plane("v" if t < 2 else "a", r, "kt", t, 0, 80, 32)
-        quant(V("kq"), V("ks"), V("kt"))
-        mm(V("ps", 1536, 1664), V("urq"), V("urs"), V("kq"), V("ks"))
+            plane("v" if t < 2 else "a", r, t, 14, 18, 0)
+        quant(V("kq"), V("ks"), V("et", 0, 512))
+        mm(V("ps", 1536, 1664), V("ukq"), V("uks"), V("kq"), V("ks"))
         for b in range(4):
             mm(V("ps", 2048 + 512 * b, 2176 + 512 * b), V("wq", 128 * b, 128 * b + 128), V("wsc", 128 * b, 128 * b + 128), V("kq"), V("ks"))
-        ts(V("kb", 0, 80), V("ps", 1536, 1616), 0.0, A.is_gt, CW4, A.mult)
+        ts(V("kb", 0, 64), V("ps", 1600, 1664), 0.0, A.is_gt, CW, A.mult)
+        ts(V("kb", 64, 80), V("ps", 1600, 1616), 0.0, A.is_gt, CW, A.mult)
         tr(V("kbt", 0, 64), V("kb", 0, 64), 0.5)
         tr(V("kbt", 64, 128), V("kb", 16, 80), 0.5)
         tt(V("fs%d" % r), V("kbt", 0, 128, 4), V("kbt", 1, 128, 4), A.add)
-        send(dst, V("fl%d" % r), V("fs%d" % r), "af%d" % r, 2.5)
-        pieces(r, PIECES, "urq", "urs")
-        for i, (c0, c1, engs) in enumerate(PIECES):
+        send(dst, V("fl%d" % r), V("fs%d" % r), "af%d" % r, 2.3)
+        pieces(r, GATH, PIECES, "urq", "urs")
+        for i, (c0, c1) in enumerate(PIECES):
             ts(V("rows", c0, c1), V("ps", 512 * i, 512 * i + c1 - c0), 0.0, A.is_gt, CW, A.mult)
         for b in range(4):
-            act(V("ht", b, 256, 4), V("ps", 2048 + 512 * b, 2048 + 512 * b + K), scale=0.03125)
-        act(V("op", 0, 128), IND(V("rows"), L(L_OWN, 8)), scale=4.0)
-        cp(V("op", 128, 256), IND(V("rows"), V("paru")))
+            act(V("ht", b, 256, 4), V("ps", 2048 + 512 * b + K, 2048 + 512 * b + 2 * K), scale=0.03125)
         hq, hs = "hq%d" % r, "hs%d" % r
         quant(V(hq, 64, 192), V(hs, 64, 192), V("ht"))
-        send(dst, u8(V(hq, 0, 64)), u8(V(hq, 64, 128)), "ah%d" % r, 7.0)
-        send(dst, V(hs, 0, 64), V(hs, 64, 128), "ah%d" % r, 7.0)
-        tr(V("opt"), V("op"), 0.5)
-        tt(V("sm"), V("opt", 0, 256, 4), V("opt", 1, 256, 4), A.add)
-        act(V("m4"), V("sm", 32, 64), scale=4.0)
-        tt(V("ix0"), V("sm", 0, 32), V("sm", 32, 64), A.add)
-        cp(V("ixu"), IND(V("ix0"), L(L_REO, 2)))
+        send(dst, u8(V(hq, 0, 64)), u8(V(hq, 64, 128)), "ah%d" % r, 6.0)
+        send(dst, V(hs, 0, 64), V(hs, 64, 128), "ah%d" % r, 6.0)
+        act(V("op", 0, 64), IND(V("rows"), V("ol", 12, 16)), scale=7.0, bias=CG)
+        cp(V("op", 64, 128), IND(V("rows"), V("ol", 0, 4)))
+        tr(V("x0", 0, 128, 2), V("op", 0, 64), 0.5)
+        tr(V("x0", 1, 128, 2), V("op", 64, 128), 0.5)
+        scan(V("xs"), V("seg4"), V("x0"), 0.0, A.mult, A.add, 0.5)
+        if U16T:
+            tr(V("ixu"), V("xs", 3, 128, 4))
+        else:
+            tr(V("xt"), V("xs", 3, 128, 4))
+            cp(V("ixu"), V("xt"))
+        act(V("op2"), IND(V("rows"), V("ol", 4, 12)))
+        tr(V("opt"), V("op2"), 0.5)
+        tt(V("sm"), V("opt", 0, 128, 2), V("opt", 1, 128, 2), A.add)
+        early(1.0)
 
     def choose(r):
-        fl, fin = "fl%d" % r, "fin%d" % r
-        tt(V("xe"), IND(V(fl), L(L_EXP, 8)), V("vcon"), A.is_equal, ext="af%d" % r)
-        act(V(fin, 0, 64, 2), IND(V(fl), L(L_FIN2, 2)), ext="af%d" % r)
-        scan(V("eqv", 0, 128), V("horn"), V("xe"), 0.0, A.mult, A.add)
-        act(V("pa"), IND(V("eqv"), L(L_PS, 8)))
-        tr(V("fw"), V(fin))
-        early(1.0)
-        tt(V("tab"), IND(V("eqv"), L(L_PM, 8)), V("pa"), A.add)
-        act(V("fw9"), IND(V("fw"), L(L_REP, 36)))
+        fl = "fl%d" % r
+        tt(V("xe"), IND(V(fl), L("XE")), V("vcon"), A.is_equal, ext="af%d" % r)
+        scan(V("tab", 0, 256, 2), V("horn"), V("xe"), 0.0, A.mult, A.add)
+        for d in (1, -1, 2, -2, 3, -3):
+            e0, e1 = max(0, -d), 32 - max(0, d)
+            tt(V("tab", 8 * e0 + 6 + d, 8 * e1 + d, 8), V("tab", 8 * e0 + 6, 8 * e1, 8), V("tab", 8 * (e0 + d) + 6, 8 * (e1 + d), 8), A.add)
+        act(V("fin", 0, 64, 2), IND(V(fl), L("FIN")), ext="af%d" % r)
+        tr(V("fw", 0, 64), V("fin"), 0.5)
+        for k in range(1, 9):
+            act(V("fw", 64 * k, 64 * k + 64), V("fw", 0, 64))
         hq, hs = "hq%d" % r, "hs%d" % r
         for b in range(4):
             mm(V("ps", 2048 + 512 * b, 2176 + 512 * b), V("ebq", 128 * b, 128 * b + 128), V("ebs", 128 * b, 128 * b + 128),
@@ -413,47 +501,34 @@ def rank_program(g, core, T, topo):
         for b in range(4):
             act(V("pool", PW * b + C + K * r, PW * b + C + K * r + K), V("ps", 2048 + 512 * b, 2048 + 512 * b + K))
             early(1.5)
-        for k in range(8):
-            w = IND(V("tab", 16 * k, 16 * k + 16), V("ixu", 4 * k, 4 * k + 4))
-            o = V("ac", 64 * k, 64 * k + 64)
-            if k == 0:
-                ts(o, w, float(sum((3 - t) * 16 * 64 ** (2 - t) for t in range(3))), A.add)
-            elif k < 3:
-                cp(o, w)
+        tie = sum((3 - t) * 64 ** (3 - t) for t in range(4)) / 8.0
+        for (c0, c1, eng) in LOOK:
+            w, o = IND(V("tab"), V("ixu", c0, c1)), V("ac", 16 * c0, 16 * c1)
+            if eng == "v":
+                ts(o, w, 4.0, A.mult, tie, A.add)
             else:
-                tt(o, w, V("ac", 64 * k - 192, 64 * k - 128), A.add)
-        tt(V("ac", 512, 576), V("ac", 320, 384), V("ac", 384, 448), A.add)
-        tt(V("ci"), V("ac", 512, 576), V("ac", 448, 512), A.add)
-        ts(V("yi", 256, 320), V("ci"), 15, A.bitwise_and)
-        for t in range(3):
-            ts(V("yi", 64 * t, 64 * t + 64), V("ci"), 6 * (3 - t) - 2, A.logical_shift_right, 63, A.bitwise_and)
-        ts(V("yi", 192, 256), V("yi", 256, 320), 4.0, A.mult)
-        for c in range(2):
-            tt(V("y2", 64 * c, 64 * c + 64), V("yi", 128 * c, 128 * c + 64), V("yi", 128 * c + 64, 128 * c + 128), A.max)
-        tt(V("y1"), V("y2", 0, 64), V("y2", 64, 128), A.max)
-        tr(V("yt"), V("y1"))
-        scan(V("sc"), V("yt"), V("lane"), 0.0, A.max, A.add)
-        ts(V("ku"), V("sc", 15, 64, 16), 64.0, A.add, 16.0, A.mult)
-        cp(V("fg"), IND(V("fw9"), V("ku")))
-        tr(V("ft"), V("fg"))
-        f4, kc = V("ft", 0, 64, 2), V("ft", 1, 64, 2)
-        old, new = V("in%d" % (r % 2), 0, 128, 4), V("in%d" % (1 - r % 2), 0, 128, 4)
-        tt(V("d0"), f4, V("m4"), A.not_equal)
-        tt(V("d1"), kc, V("jcode"), A.add)
-        tt(V("d4"), f4, V("sm", 0, 32), A.not_equal)
-        tt(V("d2"), f4, V("sm", 0, 32), A.is_equal)
-        tt(V("d3"), V("d0"), V("d1"), A.mult)
-        tt(V("d5"), V("d2"), old, A.mult)
-        tt(V("d6"), V("d3"), V("d4"), A.mult)
-        tt(new, V("d5"), V("d6"), A.add)
+                act(o, w, scale=4.0, bias=tie)
+            scan(V("ci", 16 * c0, 16 * c1), V("seg8", 16 * c0, 16 * c1), o, 0.0, A.mult, A.add)
+        tr(V("yt"), V("ci", 7, 512, 8))
+        for t in range(4):
+            ts(V("yi", t, 256, 4), V("yt"), 6 * (3 - t), A.logical_shift_right, 63, A.bitwise_and)
+        scan(V("sc"), V("yi"), V("lane"), 0.0, A.max, A.add)
+        ts(V("ku"), V("sc", 63, 256, 64), -16.0, A.mult, -449.0, A.add)
+        cp(V("fg"), IND(V("fw"), V("ku")))
+        tr(V("ft"), V("fg"), 0.5)
+        f, kc = V("ft", 0, 64, 2), V("ft", 1, 64, 2)
+        tt(V("d1", 0, 128, 4), kc, V("jc", 32 * r, 32 * r + 32), A.add)
+        tt(V("d0", 1, 128, 4), f, V("sm", 0, 32), A.not_equal)
+        tt(V("d0", 2, 128, 4), f, V("sm", 32, 64), A.not_equal)
+        scan(V("nw"), V("d0"), V("d1"), 0.0, A.mult, A.add)
 
     for r in range(3):
         inherit(r)
         symbols(r)
         choose(r)
     inherit(3)
-    pieces(3, PIECES_LAST, "vq", "vs")
-    for i, (c0, c1, engs) in enumerate(PIECES_LAST):
+    pieces(3, GATH_LAST, PIECES_LAST, "vq", "vs")
+    for i, (c0, c1) in enumerate(PIECES_LAST):
         dma("s", T.oc[:, 4 * c0:4 * c1], u8(V("eq", c0, c1)), "out", 2.2)
         (act if i == 0 else cp)(V("yo", c0, c1), V("ps", 512 * i, 512 * i + c1 - c0))
         dma("a" if i == 1 else "s", T.y[:, c0:c1], V("yo", c0, c1), "out", 2.2)
@@ -466,22 +541,22 @@ def rank_program(g, core, T, topo):
         s = min(x[5], y[5])
         return not (s > 1 and max(x[5], y[5]) % s == 0 and (x[3] - y[3]) % s != 0)
 
-    seen, group = {}, {}
+    met, group = {}, {}
     for o in ops:
         if o["dma"]:
             group.setdefault(o["sem"], []).append(o["id"])
     for o in ops:
         dep = set()
         for f, wr in [(f, False) for f in o["r"]] + [(f, True) for f in o["w"]]:
-            for (h, hw, q) in seen.get(f[0], []):
-                if (wr or hw) and meet(f, h):
+            for (h, hw, q) in met.get(f[0], []):
+                if (wr or hw or (f[0] == "ps" and ops[q]["eng"] != o["eng"])) and meet(f, h):
                     dep.update(group[ops[q]["sem"]] if ops[q]["dma"] else [q])
         o["dep"] = dep
         o["pre"] = dep | set(arrive[o["ext"]] if o["ext"] else [])
         for f in o["r"]:
-            seen.setdefault(f[0], []).append((f, False, o["id"]))
+            met.setdefault(f[0], []).append((f, False, o["id"]))
         for f in o["w"]:
-            seen.setdefault(f[0], []).append((f, True, o["id"]))
+            met.setdefault(f[0], []).append((f, True, o["id"]))
     for o in ops:
         o["tail"], o["succ"], o["left"], o["est"] = 0.0, [], len(o["pre"]), 0.0
     for o in ops:

@@ -7,10 +7,10 @@ DIST = [1, 2, 4]
 C, K = 512, 64
 PW = C + 3 * K
 F32, BF, I32, U16, U8, MX = "float32", "bfloat16", "int32", "uint16", "uint8", "float8_e4m3fn_x4"
-GATH = [(0, 14, "vaaa"), (18, 26, "vvaa"), (26, 32, "vvaa")]
-PIECES = [(0, 288), (288, 512)]
-GATH_LAST = [(0, 16, "vvaa"), (16, 24, "vaaa"), (24, 32, "vvaa")]
-PIECES_LAST = [(0, 256), (256, 384), (384, 512)]
+GATH = [(0, 8, "xxxx"), (8, 14, "xxxx"), (18, 24, "xxxx"), (24, 32, "xxxx")]
+PIECES = [(0, 192), (192, 384), (384, 512)]
+GATH_LAST = [(0, 16, "vvaa"), (16, 32, "vvaa")]
+PIECES_LAST = [(0, 256), (256, 512)]
 LOOK = [(0, 12, "v"), (12, 32, "a")]
 U16T = True
 
@@ -23,12 +23,16 @@ SCRATCH = {
     "par2": _sb(32, I32), "parq": _sb(8, I32), "raw": _sb(128, I32), "xin": _sb(2048, BF), "ut": _sb(512, BF), "vt": _sb(512, BF),
     "wq": _sb(512, MX), "wsc": _sb(512, U8), "uq": _sb(128, MX), "us": _sb(128, U8), "urq": _sb(128, MX), "urs": _sb(128, U8),
     "ukq": _sb(128, MX), "uks": _sb(128, U8),
-    "vq": _sb(128, MX), "vs": _sb(128, U8), "one": _sb(516, BF), "eb": _sb(516, BF), "ebq": _sb(512, MX), "ebs": _sb(512, U8),
-    "pi": _sb(2, I32), "fi": _sb(24, I32), "ff": _sb(24, F32), "col": _sb(128, F32), "row": _sb(128, F32), "cnt": _sb(128, F32),
-    "lf": _sb(80, F32), "lu": _sb(80, U16), "cj": _sb(128, F32), "jc": _sb(96, F32),
-    "vcon": _sb(128, F32), "horn": _sb(128, F32), "lane": _sb(256, F32), "seg4": _sb(128, BF), "seg8": _sb(512, F32),
+    "vq": _sb(128, MX), "vs": _sb(128, U8), "eb": _sb(516, BF), "ebq": _sb(512, MX), "ebs": _sb(512, U8),
+    "pi": _sb(2, I32), "fi": _sb(24, I32), "ff": _sb(24, F32), "col": _sb(192, F32), "row": _sb(160, F32), "cnt": _sb(128, F32),
+    "lu": _sb(112, U16), "cj": _sb(128, F32), "jc": _sb(96, F32),
+    "vcon": _sb(128, F32), "horn": _sb(128, F32), "lane": _sb(256, F32), "seg4": _sb(128, BF), "seg8": _sb(520, F32),
     "ptr": _sb(176, U16), "paru": _sb(8, U16), "nt": _sb(640, F32), "r2": _sb(256, F32), "r3": _sb(256, F32), "ol": _sb(16, U16),
-    "va": _sb(160, F32), "vb": _sb(160, F32), "vc": _sb(160, F32), "w8": _sb(136, F32), "w9": _sb(264, F32), "prm": _sb(160, F32),
+    "va": _sb(160, F32), "vb": _sb(160, F32), "vc": _sb(160, F32), "vd": _sb(160, F32), "w8": _sb(136, F32), "w9": _sb(264, F32),
+    "prm": _sb(160, F32), "sa": _sb(136, F32), "sb": _sb(136, F32), "pr": _sb(480, BF), "pt": _sb(576, BF),
+    "wt": _sb(112, F32), "gt": _sb(512, F32), "th": _sb(384, F32), "bf": _sb(256, F32), "ba": _sb(160, F32), "bb": _sb(160, F32),
+    "bc": _sb(160, F32), "b8": _sb(136, F32), "bi": _sb(256, I32), "xb": _sb(896, BF), "xg": _sb(832, BF), "xh": _sb(832, BF),
+    "sh": _sb(56, U16),
     "vi": _sb(160, I32), "ti": _sb(288, I32), "tb": _sb(288, F32), "tc": _sb(288, F32),
     "yy": _sb(48, I32), "el": _sb(32, U16), "nw": _sb(128, F32), "flg": _sb(128, F32),
     "pool": _sb(4 * PW, BF), "et": _sb(2304, BF), "eq": _sb(512, MX), "es": _sb(512, U8),
@@ -49,7 +53,7 @@ for _r in range(3):
 SEMAPHORES = (["sv", "sa", "sp", "st", "l_par", "l_fl", "l_u", "l_x", "l_w", "l_v", "out", "sent"]
               + ["af%d" % r for r in range(3)] + ["ah%d" % r for r in range(3)])
 ENG_SEM = {"v": "sv", "a": "sa", "p": "sp", "t": "st"}
-CYC, HOP = 0.001, 0.2
+CYC, HOP = 0.00104, 0.2
 VAL, PTR = 2, 1
 
 
@@ -61,16 +65,25 @@ def slot(h, t):
     return t if h == 0 else (3, 2, 0, 1)[t]
 
 
+def rev(x):
+    return sum((x >> b & 1) << (6 - b) for b in range(7))
+
+
 def parents(m, e, p):
     if m < 4:
-        return 32 * (2 * (m % 2) + p // 8) + 16 * (m // 2) + 2 * (p % 8) + e
-    return 32 * (2 * ((m - 4) // 2) + e) + 16 * (m % 2) + p
+        return rev(32 * (2 * (m % 2) + p // 8) + 16 * (m // 2) + 2 * (p % 8) + e)
+    return rev(32 * (2 * ((m - 4) // 2) + e) + 16 * (m % 2) + p)
 
 
 LISTS = [
     ("RAW", 8, lambda a, h, p, c: 8 * p + c),
     ("SEL", 2, lambda a, h, p, c: seen(h, p % 8, PTR)),
-    ("PERM", 8, lambda a, h, p, c: 8 * p + (c + 1 - a % 2) % 8),
+    ("PERM", 8, lambda a, h, p, c: 8 * p + (c if a % 2 else 7 - c)),
+    ("REV", 8, lambda a, h, p, c: rev(16 * c + p)),
+    ("PERMR", 8, lambda a, h, p, c: rev(8 * p + (c if a % 2 else 7 - c))),
+    ("TWICE", 8, lambda a, h, p, c: 32 * (c // 2) + 16 * h + p),
+    ("PERM2", 8, lambda a, h, p, c: 8 * p + (2 * (c // 2) + h if a % 2 else 7 - 2 * (c // 2) - h)),
+    ("SA", 2, lambda a, h, p, c: 16 * (16 * c + p) + 4 * c + p // 4),
     ("FS", 4, lambda a, h, p, c: seen(h, p // 2, 4 * (2 * (2 * (p % 2) + (a % 2 if c < 2 else 1 - a % 2)) + h) + VAL)),
     ("UR", 8, lambda a, h, p, c: 16 * (p // 2) + p % 2),
     ("UK", 8, lambda a, h, p, c: 64 * (c % 2) + 16 * (p // 4) + p % 4),
@@ -95,7 +108,13 @@ def terms(vec):
         k, e = c[1 << b], b + 1
         while k and e < 7 and c[1 << e] == k << (e - b):
             e += 1
-        if k:
+        f = b + 1
+        while k and e == b + 1 and f < 7 and c[1 << f] << (f - b) == k:
+            f += 1
+        if f > b + 2:
+            out.append(((b, f, "backwards"), c[1 << (f - 1)]))
+            e = f
+        elif k:
             out.append(((b, (1 << (e - b)) - 1), k))
         b = e
     return c[0], out + [(m, c[m]) for m in range(1, 128) if m & (m - 1) and c[m]]
@@ -110,6 +129,23 @@ def pattern(r):
                 if all(r[i] == r[0] + s[0] * (i // (n1 * n2)) + s[1] * (i // n2 % n1) + s[2] * (i % n2) for i in range(n)):
                     return [[s[0], n // (n1 * n2)], [s[1], n1], [s[2], n2]]
     return None
+
+
+def product(d):
+    rows = [r for r in d if r.any()]
+    if not rows:
+        return d[:, 0], d[0]
+    r = rows[0] // np.gcd.reduce(rows[0])
+    k = int(np.nonzero(r)[0][0])
+    r = r if r[k] > 0 else -r
+    sc = d[:, k] // r[k]
+    return (sc, r) if (sc[:, None] * r[None, :] == d).all() and pattern(r) is not None else None
+
+
+FIELDS = [(0, 15), (0, 1), (1, 1), (4, 1), (5, 1), (6, 1), (5, 3), (1, 3), (2, 1), (3, 1), (2, 3), (1, 7), (0, 3), (0, 7), (0, 31)]
+FIRST = 8
+PLAN = {}
+TUNE = {"bb": 0.0, "bs": 0.0, "parts": ((0, 128),), "out": 0.8, "yo": "aaaa", "lat": 1.7, "bias": 0.1, "it": 6}
 
 
 def rank_program(g, core, T, topo):
@@ -153,10 +189,13 @@ def rank_program(g, core, T, topo):
         return v[0] if isinstance(v, tuple) else v
 
     def cc(v, k=1.0):
-        return 0.05 + 1.6 * CYC * v[2] if v[3] else max(64, k * v[2]) * CYC
+        return 0.05 + 1.56 * CYC * v[2] if v[3] else max(64, k * v[2]) * CYC
+
+    def rate(*vs):
+        return 0.5 if all(SCRATCH[v[1][0][0]][2] in (BF, U16) for v in vs) else 1.0
 
     def cp(o, i):
-        op("v", lambda: g.vector.tensor_copy(o[0], i[0]), [o], [i], cc(i))
+        op("v", lambda: g.vector.tensor_copy(o[0], i[0]), [o], [i], cc(i, rate(o, i)))
 
     def tt(o, a, b, alu, ext=None):
         op("v", lambda: g.vector.tensor_tensor(o[0], a[0], b[0], alu), [o], [a, b], cc(a, 2), ext=ext)
@@ -171,7 +210,7 @@ def rank_program(g, core, T, topo):
         op("v", lambda: g.vector.transpose(o[0], i[0]), [o], [i], cc(i, k))
 
     def ms(o, c):
-        op("v", lambda: g.vector.memset(o[0], c), [o], [], cc(o))
+        op("v", lambda: g.vector.memset(o[0], c), [o], [], cc(o, rate(o)))
 
     def scan(o, d0, d1, init, o0, o1, k=1.0):
         op("v", lambda: g.vector.tensor_tensor_scan(o[0], d0[0], d1[0], init, o0, o1), [o], [d0, d1], cc(d0, k))
@@ -183,21 +222,25 @@ def rank_program(g, core, T, topo):
         if bias is not None:
             kw["bias"] = ap(bias)
         fn = func if func is not None else (F.Identity if bias is not None else F.Copy)
-        op("a", lambda: g.scalar.activation(o[0], i[0], fn, **kw), [o], [i, scale, bias], cc(i) + 0.015, ext=ext)
-
-    POOL = (None, [("gpsimd", 0, 128, 0, 1, 1)])
+        op("a", lambda: g.scalar.activation(o[0], i[0], fn, **kw), [o], [i, scale, bias], cc(i) + (0.015 if i[3] else 0.0), ext=ext)
+        if func is None and i[1][0][0] != "ps":
+            if scale is None and bias is None:
+                alt = lambda: g.vector.tensor_copy(o[0], i[0])
+            else:
+                alt = lambda: g.vector.tensor_scalar(o[0], i[0], kw.get("scale", 1.0), kw.get("bias", 0.0), A.mult, A.add)
+            ops[-1]["ways"] = {"a": (ops[-1]["fn"], ops[-1]["cost"]), "v": (alt, cc(i, rate(o, i)))}
 
     def iota(o, pat, base, cm, flt=True):
         if flt:
-            op("p", lambda: g.iota(o[0], pat, base, cm, allow_small_or_imprecise_dtypes=True), [o, POOL], [], 0.13 + 2 * CYC * o[2])
+            op("p", lambda: g.iota(o[0], pat, base, cm, allow_small_or_imprecise_dtypes=True), [o], [], 0.13 + 2 * CYC * o[2])
         else:
-            op("p", lambda: g.iota(o[0], pat, base, cm), [o, POOL], [], 0.13 + 2 * CYC * o[2])
+            op("p", lambda: g.iota(o[0], pat, base, cm), [o], [], 0.13 + 2 * CYC * o[2])
 
     def fill(o, c, flt=True):
         iota(o, [[0, o[2]]], c, 0, flt)
 
     def quant(q, s, i):
-        op("v", lambda: g.vector.quantize_mx(q[0], s[0], i[0]), [q, s], [i], 0.015 + 0.27 * CYC * i[2])
+        op("v", lambda: g.vector.quantize_mx(q[0], s[0], i[0]), [q, s], [i], 0.012 + 0.265 * CYC * i[2])
 
     def mm(o, lq, ls, rq, rs, ext=None):
         op("t", lambda: g.tensor.matmul_mx(o[0], lq[0], ls[0], rq[0], rs[0], True, True), [o], [lq, ls, rq, rs], 0.6 * CYC * (rq[2] + 16), ext=ext)
@@ -234,7 +277,13 @@ def rank_program(g, core, T, topo):
 
     iota(V("pi", 0, 1), [[0, 1]], 0, 1, False)
     iota(V("cnt"), [[1, 128]], 0, 0)
-    made, used = {}, {"ff": 0, "col": 0, "row": 0}
+    made, used = {}, {"col": 0, "row": 0}
+    for (c0, c1) in ((0, FIRST), (FIRST, len(FIELDS))):
+        for c in range(c0, c1):
+            ts(V("fi", c, c + 1), V("pi", 0, 1), FIELDS[c][0], A.logical_shift_right, FIELDS[c][1], A.bitwise_and)
+            made[FIELDS[c]] = V("ff", c, c + 1)
+        cp(V("ff", c0, c1), V("fi", c0, c1))
+        early(20.0 if c0 else 0.0)
 
     def new(name, n=1):
         used[name] += n
@@ -243,10 +292,9 @@ def rank_program(g, core, T, topo):
     def feature(k):
         if k not in made:
             if isinstance(k, tuple):
-                o = made[k] = new("ff")
-                i = V("fi", used["ff"] - 1, used["ff"])
-                ts(i, V("pi", 0, 1), k[0], A.logical_shift_right, k[1], A.bitwise_and)
-                cp(o, i)
+                less = feature((k[0], k[1] - 1, k[2]) if k[1] - k[0] > 2 else (k[0], 1))
+                made[k] = new("col")
+                act(made[k], less, scale=2.0, bias=feature((k[1] - 1, 1)))
             else:
                 low = k & -k
                 rest = k ^ low
@@ -254,36 +302,49 @@ def rank_program(g, core, T, topo):
                 act(o, feature(rest if rest & (rest - 1) else (rest.bit_length() - 1, 1)), scale=feature((low.bit_length() - 1, 1)))
         return made[k]
 
-    def column(vec):
-        c0, tm = terms(vec)
+    def chain(tm, c0):
         prev, key = float(c0), ("c", c0)
-        for (k, coef) in tm or [((0, 1), 0)]:
+        if c0 == 0 and len(tm) == 1 and tm[0][1] == 1:
+            return feature(tm[0][0])
+        for (k, coef) in tm:
             key = key + (k, coef)
             if key not in made:
+                f = feature(k)
                 made[key] = new("col")
-                act(made[key], feature(k), scale=float(coef), bias=prev)
+                act(made[key], f, scale=float(coef), bias=prev)
             prev = made[key]
         return prev
 
-    def const(o, tb):
+    def column(vec):
+        c0, tm = terms(vec)
+        if len(tm) < 3 or c0 == 0:
+            return chain(tm, c0)
+        o = new("col")
+        act(o, chain(tm, 0), bias=float(c0))
+        return o
+
+    def const(o, tb, eng="a"):
         c = 0
         while c < tb.shape[1]:
-            e = c + 1
-            while e < tb.shape[1] and (tb[:, e] - tb[0, e] == tb[:, c] - tb[0, c]).all():
-                e += 1
-            while pattern(tb[0, c:e]) is None:
+            e = tb.shape[1]
+            while product(tb[:, c:e] - tb[:, c:c + 1]) is None:
                 e -= 1
-            r = tb[0, c:e] - tb[0, c]
-            pat = pattern(r)
-            if pat[0][1] * pat[1][1] == 1:
-                act(o(c, e), V("cnt", 0, e - c), scale=float(pat[2][0]), bias=column(tb[:, c]))
+            sc, r = product(tb[:, c:e] - tb[:, c:c + 1])
+            bias = tb[:, c]
+            if e == c + 1:
+                row, sc, bias = V("cnt", 1, 2), sc * 0 + tb[0, c], bias - tb[0, c]
+            elif (r == np.arange(e - c)).all() or not sc.any():
+                row = V("cnt", 0, e - c)
             else:
-                unit = int(np.gcd.reduce(r))
-                key = ("r",) + tuple(int(z) // unit for z in r)
+                key = ("r",) + tuple(int(z) for z in r)
                 if key not in made:
                     made[key] = new("row", e - c)
-                    iota(made[key], pattern(r // unit), 0, 0)
-                act(o(c, e), made[key], scale=float(unit), bias=column(tb[:, c]))
+                    iota(made[key], pattern(r), 0, 0)
+                row = made[key]
+            if eng == "a":
+                act(o(c, e), row, scale=column(sc), bias=column(bias))
+            else:
+                ts(o(c, e), row, column(sc), A.mult, column(bias), A.add)
             c = e
 
     def colf(f):
@@ -292,8 +353,7 @@ def rank_program(g, core, T, topo):
     at, c0 = {}, 0
     for (name, n, f) in LISTS:
         at[name] = (c0, n)
-        const(lambda c, e: V("lf", c0 + c, c0 + e), table(n, f))
-        cp(V("lu", c0, c0 + n), V("lf", c0, c0 + n))
+        const(lambda c, e: V("lu", c0 + c, c0 + e), table(n, f), "v")
         c0 += n
 
     def L(name, n=None):
@@ -302,52 +362,51 @@ def rank_program(g, core, T, topo):
     act(V("cj"), V("cnt"), scale=colf(lambda a, h, p, c: 1025 * (p // 2 % 2)),
         bias=colf(lambda a, h, p, c: 1025 * (128 * a + 1) * (p // 2 % 2) - 1))
     PAD = colf(lambda a, h, p, c: -1000 * (p % 2))
-    for nm in ("va", "vb", "vc", "prm"):
+    for nm in ("vb", "vc", "vd", "prm"):
         act(V(nm, 0, 16), V("cnt", 0, 16), scale=0.0, bias=PAD)
-        ms(V(nm, 144, 160), 0.0)
-    CB = colf(lambda a, h, p, c: 8 - 128 * a)
+    ms(V("pr"), 0.0)
+    CB = colf(lambda a, h, p, c: 16 - 128 * a)
     C8 = colf(lambda a, h, p, c: 136 - 128 * a if a % 2 else -1000)
     C9 = colf(lambda a, h, p, c: 8 if a >= 2 else -1000)
     CW = colf(lambda a, h, p, c: 2 - p % 2)
     CG = colf(lambda a, h, p, c: 16 * (p // 2) + 3)
-    for r in range(3):
-        const(lambda c, e: V("jc", 32 * r + c, 32 * r + e), table(32, lambda a, h, p, c: 1024 * (128 * a + 32 * (c // 8) + 16 * h + p + 1) + C + K * r))
+    const(lambda c, e: V("jc", c, e), table(32, lambda a, h, p, c: 1024 * (128 * a + rev(32 * (c // 8) + 16 * h + p) + 1) + C))
+    for r in (1, 2):
+        act(V("jc", 32 * r, 32 * r + 32), V("jc", 0, 32), bias=float(K * r))
     const(lambda c, e: V("fin", 2 * c + 1, 2 * e, 2), table(32, lambda a, h, p, c: 16 * (0, 2, 1, 3)[2 * (c // 16) + h] + p))
+    for nm in ("vc", "prm"):
+        fill(V(nm, 144, 160), 0)
     for nm in ("w8", "w9"):
         act(V(nm, 0, 8), V("cnt", 0, 8), scale=0.0, bias=PAD)
         fill(V(nm, 8), 0)
-    for a1 in range(2):
-        iota(V("nt", 128 + 256 * a1, 384 + 256 * a1), [[224, 2], [1, 16], [32, 8]], 32 + 16 * a1, 0)
+    for a in range(4):
+        iota(V("nt", 128 + 128 * a, 256 + 128 * a), [[1, 16], [32 if a % 2 else -32, 8]], (256 if a % 2 else 288) + 16 * (a // 2), 0)
     iota(V("nt", 128, 640, 8), [[16, 2], [32, 2], [1, 16]], 0, 0)
     fill(V("vi", 0, 16), 0, False)
     fill(V("vi", 144, 160), 0, False)
-    def afill(name, c0, c1, c, st=1):
-        for b in range(c0, c1, 128 * st):
-            o = V(name, b, min(c1, b + 128 * st), st)
-            act(o, V("cnt", 0, o[2]), scale=0.0, bias=float(c))
-
-    afill("et", 0, 256, 0)
-    afill("ht", 256, 512, 0)
-    afill("seg4", 0, 128, 1)
-    afill("seg4", 0, 128, 0, 4)
+    for nm in ("sa", "sb"):
+        fill(V(nm, 0, 8), 0)
+    fill(V("et", 0, 256), 0)
+    fill(V("ht", 256, 512), 0)
     iota(V("vcon"), [[0, 8], [1, 4], [0, 4]], 0, 0)
-    afill("horn", 0, 128, 64)
-    afill("horn", 0, 128, 0, 4)
-    afill("tab", 0, 264, 0)
-    afill("seg8", 0, 512, 1)
-    afill("seg8", 0, 512, 0, 8)
-    afill("lane", 0, 256, 0)
-    afill("lane", 3, 256, 0.0625, 4)
-    afill("lane", 63, 256, -64, 64)
-    afill("d0", 0, 128, 0)
-    afill("d1", 3, 128, 0, 4)
-    afill("one", 0, 516, 1)
-    op("p", lambda: g.affine_select(T.eb[:, :], T.one[:, :], [[-1, 516]], A.is_equal, 0.0, 3, 4), [V("eb"), POOL], [V("one")], 1.2)
+    fill(V("tab"), 0)
+    fill(V("d0"), 0)
+    fill(V("d1", 3, 128, 4), 0)
+    fill(V("seg4"), 1)
+    fill(V("seg4", 0, 128, 4), 0)
+    fill(V("horn"), 64)
+    fill(V("horn", 0, 128, 4), 0)
+    fill(V("lane"), 0)
+    ms(V("lane", 3, 256, 4), 0.0625)
+    fill(V("lane", 63, 256, 64), -64)
+    fill(V("seg8"), 1)
+    op("p", lambda: g.affine_select(T.eb[:, :], T.seg8[:, 0:516], [[-1, 516]], A.is_equal, 0.0, 3, 4), [V("eb")], [V("seg8")], 1.2)
+    fill(V("seg8", 0, 512, 8), 0)
     for b in range(4):
         quant(V("ebq", 128 * b, 128 * b + 128), V("ebs", 128 * b, 128 * b + 128), V("eb", 3 - b, 515 - b))
-        early(4.0)
     for t in range(4):
-        act(V("pool", PW * t, PW * t + C), V("xin", t, 2048, 4))
+        for c in range(2):
+            act(V("pool", PW * t + 256 * c, PW * t + 256 * c + 256), V("xin", 1024 * c + t, 1024 * c + 1024, 4))
     quant(V("uq"), V("us"), V("ut"))
 
     def pick(q, s, lst):
@@ -363,9 +422,18 @@ def rank_program(g, core, T, topo):
         cp(Q("parq", a, 0, 8), Q("par2", 0, 8 * a, 8 * a + 8))
     ts(V("ptr", 0, 8), V("parq"), CB, A.add)
     cp(V("paru"), V("parq"))
+    ts(V("pr", 16, 144), IND(V("raw"), L("RAW")), CB, A.add, 0.0, A.max)
     for nm in ("va", "vb"):
         tt(V(nm, 16, 144), IND(V("raw"), L("RAW")), V("cj"), A.mult)
-    tr(V("nw"), V("va", 16, 144))
+    act(V("flg"), IND(V("va", 16, 144), L("REV")))
+    tr(V("nw"), V("flg"))
+    for k in range(7):
+        b0, b1, t0 = 160 * (k % 3), 160 * ((k + 1) % 3), 288 * (k % 2)
+        act(V("pr", b1 + 16, b1 + 144), IND(V("pr", b0, b0 + 144), V("ptr", 16 * max(k - 1, 0), 16 * max(k - 1, 0) + 8)))
+        if k != 5:
+            tr(V("pt", t0, t0 + 128), V("pr", b1 + 16, b1 + 144), 0.5)
+            tr(V("pt", t0 + 128, t0 + 288), V("pr", b1, b1 + 160), 0.5)
+            cp(V("ptr", 16 * min(k + 1, 6), 16 * min(k + 1, 6) + 16), IND(V("pt", t0, t0 + 288), L("SEL", 1)))
     act(V("nt", 0, 128), IND(V("nt", 128, 640), V("paru")))
     act(V("r2"), IND(V("nt"), L("R2")))
     for c in range(2):
@@ -384,47 +452,119 @@ def rank_program(g, core, T, topo):
         ts(V("ptr", 16 * k, 16 * k + 16), IND(V(tb), L("SEL", 1)), -1.0, A.mult, bias, A.add)
 
     def step(o, w, own, lst, c0, c1, end):
-        tt(V(o, 16 + c0, 16 + c1), IND(V(w, 8, 16 + end), V("ptr", 16 * lst + c0 // 16, 16 * lst + c1 // 16)), V(own, 16 + c0, 16 + c1), A.max)
+        tt(V(o, 16 + c0, 16 + c1), IND(V(w, 0, 16 + end), V("ptr", 16 * lst + c0 // 16, 16 * lst + c1 // 16)), V(own, 16 + c0, 16 + c1), A.max)
+
+    def by_steps(old, cur, nxt, again, parts):
+        for k in range(7):
+            for (c0, c1) in parts:
+                step(nxt, cur, old, max(k - 1, 0), c0, c1, c1)
+            old, cur, nxt = cur, nxt, (old if k else again)
+        for c0 in (32, 64, 96):
+            step(cur, cur, cur, 6, c0, c0 + 32, c0)
+        return cur, old
+
+    def later_lists():
+        p = feature((0, 15))
+        top, big, far = new("col"), new("col"), new("col")
+        ts(top, p, 6.0, A.min)
+        ts(big, p, 6.5, A.is_gt, 32.0, A.mult)
+        act(big, big, bias=32.0)
+        ts(far, p, 8.0, A.is_equal, 128.0, A.mult)
+        cyc = new("row", 21)
+        iota(cyc, [[0, 3], [1, 7]], 0, 0)
+        cyc = V("row", used["row"] - 15, used["row"] - 1)
+        W = lambda k, c0=0, c1=9: V("wt", 16 * k + c0, 16 * k + c1)
+        ts(W(0, 0, 14), cyc, top, A.not_equal, 0.5, A.mult)
+        ts(W(1, 0, 14), cyc, top, A.is_equal, big, A.mult)
+        scan(W(2, 0, 14), W(0, 0, 14), W(1, 0, 14), 0.0, A.mult, A.add)
+        ms(W(0), 2.0)
+        ts(W(1), V("cnt", 0, 9), p, A.is_equal, 1024.0, A.mult)
+        scan(W(3), W(0), W(1), 0.0, A.mult, A.add)
+        ms(W(6), 0.0)
+        scan(W(4), W(0), W(6), -512.0, A.mult, A.add)
+        tt(W(5), W(3), W(1), A.subtract)
+        tt(W(5), W(5), W(4), A.add)
+        tt(W(6, 0, 7), W(3, 0, 7), W(2, 7, 14), A.add)
+        tt(W(6, 7, 8), W(3, 7, 8), far, A.add)
+        cp(W(6, 8, 9), W(3, 8, 9))
+        act(V("gt", 0, 1), V("cnt", 0, 1), bias=8.0)
+        for b in range(9):
+            act(V("gt", 1 << b, 2 << b), V("gt", 0, 1 << b), bias=W(6, b, b + 1))
+        for (k, c0, first) in ((3, 0, 0.0), (5, 128, -1024.0)):
+            o = new("col")
+            act(o, W(k, 7, 8), scale=feature((5, 1)), bias=first)
+            act(V("th", c0, c0 + 1), W(k, 8, 9), scale=feature((6, 1)), bias=o)
+            for b in range(7):
+                act(V("th", c0 + (1 << b), c0 + (2 << b)), V("th", c0, c0 + (1 << b)), bias=W(k, b, b + 1))
+        act(V("th", 256, 384), V("cnt"), scale=1024.0, bias=colf(lambda a, h, p, c: 1024 * (128 * a + 1)))
+        for nm in ("ba", "bb", "bc"):
+            fill(V(nm, 0, 16), 0)
+        fill(V("b8"), 0)
+        for c in (0, 64):
+            tt(V("bf", c, c + 64), IND(V("gt"), V("paru", c // 16, c // 16 + 4)), V("th", c, c + 64), A.is_lt)
+            tt(V("bf", c + 128, c + 192), IND(V("gt"), V("paru", c // 16, c // 16 + 4)), V("th", c + 128, c + 192), A.subtract)
+            tt(V("bf", c + 128, c + 192), V("bf", c + 128, c + 192), V("th", c + 256, c + 320), A.max)
+            tt(V("ba", c + 16, c + 80), V("bf", c, c + 64), V("bf", c + 128, c + 192), A.mult)
+        act(V("bb", 16, 144), V("ba", 16, 144))
+        early(TUNE["bb"])
+        cur, old = by_steps("ba", "bb", "bc", "ba", TUNE["parts"])
+        early(TUNE["bs"])
+        act(Q("b8", 1, 8, 136), Q(cur, 0, 16, 144))
+        act(Q("b8", 3, 8, 136), Q(cur, 2, 16, 144))
+        for c in (0, 64):
+            tt(V("bi", c, c + 64), IND(V("b8"), V("ptr", 128 + c // 16, 132 + c // 16)), V(cur, c + 16, c + 80), A.max)
+        ts(V("bi", 128, 256), V("bi", 0, 128), 1023, A.bitwise_and)
+        cp(V("bf", 0, 128), V("bi", 128, 256))
+        act(V("xb", 0, 128), IND(V("bf", 0, 128), L("REV")), bias=-8.0)
+        for k in range(6):
+            act(V("xb", 128 * k + 128, 128 * k + 256, 2), V("xb", 128 * k, 128 * k + 64))
+            act(V("xb", 128 * k + 129, 128 * k + 256, 2), V("xb", 128 * k + 64, 128 * k + 128))
+        for k in range(7):
+            act(V("xg", 64 * k, 64 * k + 64), IND(V("xb", 128 * k + 64, 128 * k + 128), L("TWICE", 4)))
+        act(V("xg", 448, 576), IND(V("xb", 0, 128), L("TWICE")))
+        act(V("xg", 576, 704), IND(V("bf", 0, 128), L("PERM2")), bias=-8.0)
+        act(V("xg", 704, 832), IND(V("bf", 0, 128), L("TWICE")), bias=-8.0)
+        for c in range(0, 832, 128):
+            tr(V("xh", c, min(c + 128, 832)), V("xg", c, min(c + 128, 832)), 0.5)
+        ts(V("sh", 0, 32), IND(V("xh", 0, 512), L("SA")), 8.0, A.add)
+        ts(V("sh", 32, 40), V("xh", 448 + 7, 576, 16), 8.0, A.add)
+        ts(V("sh", 40, 56), V("xh", 576 + 8, 832, 16), 8.0, A.add)
 
     def inherit(r):
         first, last = r == 0, r == 3
-        if not first:
-            tr(V("va", 16, 144), V("nw"))
-            tr(V("vb", 16, 144), V("nw"))
-        if last:
-            act(V("flg"), V("vb", 16, 144), F.Sign)
-            for a in range(4):
-                dma("s", T.ofl[:, 128 * a:128 * a + 128], (T.flg[32 * a + VAL:32 * a + 32:4, :], V("flg")[1]), "out")
-        else:
+        if not last:
             act(V("d1", 1, 128, 4), V("nw", VAL, 128, 4), scale=-1.0)
             act(V("d1", 2, 128, 4), V("nw", VAL, 128, 4))
-        old, cur, nxt = "va", "vb", "vc"
-        for k in range(7):
-            for (c0, c1) in (((0, 128),) if first else ((0, 64), (64, 128))):
-                step(nxt, cur, old, max(k - 1, 0), c0, c1, c1)
-            old, cur, nxt = cur, nxt, old
-            if first and (k < 5 or k == 6):
-                pointer(cur, min(k + 1, 6), CB)
-        for c0 in (32, 64, 96):
-            step(cur, cur, cur, 6, c0, c0 + 32, c0)
-        (act if first else cp)(Q("w8", 1, 8, 136), Q(cur, 0, 16, 144))
-        act(Q("w8", 3, 8, 136), Q(cur, 2, 16, 144))
-        act(Q("w9", 2, 8, 136), Q(cur, 0, 16, 144))
-        act(Q("w9", 3, 8, 136), Q(cur, 0, 16, 144))
+        if first:
+            cur, old = by_steps("va", "vb", "vc", "vd", ((0, 128),))
+            c0 = 16
+        else:
+            cur, old, c0 = "sa", "sb", 8
+            tr(V(cur, 8, 136), V("nw"))
+            for k in range(7):
+                tt(V(old, 9, 136, 2), IND(V(cur, 0, 72), V("sh", 4 * k, 4 * k + 4)), V(cur, 72, 136), A.max)
+                act(V(old, 8, 136, 2), V(cur, 8, 72))
+                cur, old = old, cur
+        if last:
+            tr(V("va", 16, 144), V("nw"))
+            act(V("flg"), IND(V("va", 16, 144), L("REV")), F.Sign)
+            for a in range(4):
+                dma("s", T.ofl[:, 128 * a:128 * a + 128], (T.flg[32 * a + VAL:32 * a + 32:4, :], V("flg")[1]), "out")
+        (act if first else cp)(Q("w8", 1, 8, 136), Q(cur, 0, c0, c0 + 128))
+        act(Q("w8", 3, 8, 136), Q(cur, 2, c0, c0 + 128))
+        act(Q("w9", 2, 8, 136), Q(cur, 0, c0, c0 + 128))
+        act(Q("w9", 3, 8, 136), Q(cur, 0, c0, c0 + 128))
         if first:
             pointer(cur, 8, C8)
-        tt(V(old, 16, 144), IND(V("w8"), V("ptr", 128, 136)), V(cur, 16, 144), A.max)
+        tt(V(old, c0, c0 + 128), IND(V("w8"), V("ptr", 128, 136) if first else V("sh", 32, 40)), V(cur, c0, c0 + 128), A.max)
         old, cur = cur, old
-        cp(Q("w9", 2, 136, 264), Q(cur, 1, 16, 144))
-        (act if last else cp)(Q("w9", 3, 136, 264), Q(cur, 1, 16, 144))
-        if not last:
-            act(V("prm", 16, 144), IND(V(cur, 16, 144), L("PERM")))
+        cp(Q("w9", 2, 136, 264), Q(cur, 1, c0, c0 + 128))
+        cp(Q("w9", 3, 136, 264), Q(cur, 1, c0, c0 + 128))
+        act(V("prm", 16, 144), IND(V(cur, c0, c0 + 128), L("PERM" if first else "REV" if last else "PERMR")))
         if first:
             pointer("prm", 9, C9)
-            pointer(cur, 10, C9)
-            early(30.0)
-        lst = 160 if last else 144
-        tt(V("vi", 16, 144), IND(V("w9"), V("ptr", lst, lst + 8)), V(cur if last else "prm", 16, 144), A.max)
+            later_lists()
+        tt(V("vi", 16, 144), IND(V("w9"), V("ptr", 144, 152) if first else V("sh", 48, 56) if last else V("sh", 40, 48)), V("prm", 16, 144), A.max)
         both("vi", "ti")
         ts(V("yy"), IND(V("ti"), L("FS", 3)), 1023, A.bitwise_and)
         for a in range(4):
@@ -436,6 +576,8 @@ def rank_program(g, core, T, topo):
     def plane(eng, r, t, l0, l1, n0):
         w = IND(V("pool", PW * t, PW * t + C + K * r), V("el", l0, l1))
         (cp if eng == "v" else act)(V("et", 4 * (K + n0) + t, 4 * (K + n0 + 16 * (l1 - l0)), 4), w)
+        if eng == "a":
+            del ops[-1]["ways"]
 
     def pieces(r, gath, parts, sq, ss):
         for (l0, l1, engs) in gath:
@@ -458,7 +600,7 @@ def rank_program(g, core, T, topo):
         tr(V("kbt", 0, 64), V("kb", 0, 64), 0.5)
         tr(V("kbt", 64, 128), V("kb", 16, 80), 0.5)
         tt(V("fs%d" % r), V("kbt", 0, 128, 4), V("kbt", 1, 128, 4), A.add)
-        send(dst, V("fl%d" % r), V("fs%d" % r), "af%d" % r, 2.3)
+        send(dst, V("fl%d" % r), V("fs%d" % r), "af%d" % r, TUNE["lat"] + (0.0 if r else 0.8))
         pieces(r, GATH, PIECES, "urq", "urs")
         for i, (c0, c1) in enumerate(PIECES):
             ts(V("rows", c0, c1), V("ps", 512 * i, 512 * i + c1 - c0), 0.0, A.is_gt, CW, A.mult)
@@ -466,8 +608,8 @@ def rank_program(g, core, T, topo):
             act(V("ht", b, 256, 4), V("ps", 2048 + 512 * b + K, 2048 + 512 * b + 2 * K), scale=0.03125)
         hq, hs = "hq%d" % r, "hs%d" % r
         quant(V(hq, 64, 192), V(hs, 64, 192), V("ht"))
-        send(dst, u8(V(hq, 0, 64)), u8(V(hq, 64, 128)), "ah%d" % r, 6.0)
-        send(dst, V(hs, 0, 64), V(hs, 64, 128), "ah%d" % r, 6.0)
+        send(dst, u8(V(hq, 0, 64)), u8(V(hq, 64, 128)), "ah%d" % r, 4.0)
+        send(dst, V(hs, 0, 64), V(hs, 64, 128), "ah%d" % r, 4.0)
         act(V("op", 0, 64), IND(V("rows"), V("ol", 12, 16)), scale=7.0, bias=CG)
         cp(V("op", 64, 128), IND(V("rows"), V("ol", 0, 4)))
         tr(V("x0", 0, 128, 2), V("op", 0, 64), 0.5)
@@ -529,9 +671,12 @@ def rank_program(g, core, T, topo):
     inherit(3)
     pieces(3, GATH_LAST, PIECES_LAST, "vq", "vs")
     for i, (c0, c1) in enumerate(PIECES_LAST):
+        ahead = TUNE["out"] * (len(PIECES_LAST) - 1 - i)
         dma("s", T.oc[:, 4 * c0:4 * c1], u8(V("eq", c0, c1)), "out", 2.2)
-        (act if i == 0 else cp)(V("yo", c0, c1), V("ps", 512 * i, 512 * i + c1 - c0))
-        dma("a" if i == 1 else "s", T.y[:, c0:c1], V("yo", c0, c1), "out", 2.2)
+        early(ahead + TUNE["out"] / 2)
+        (act if TUNE["yo"][i] == "a" else cp)(V("yo", c0, c1), V("ps", 512 * i, 512 * i + c1 - c0))
+        dma("s", T.y[:, c0:c1], V("yo", c0, c1), "out", 2.2)
+        early(ahead)
     for k in range(4):
         dma("a" if k % 2 else "s", T.osc[4 * k:4 * k + 4, :], V("es", 0, 512, 1, 32 * k, 32 * k + 4), "out")
 
@@ -558,32 +703,57 @@ def rank_program(g, core, T, topo):
         for f in o["w"]:
             met.setdefault(f[0], []).append((f, True, o["id"]))
     for o in ops:
-        o["tail"], o["succ"], o["left"], o["est"] = 0.0, [], len(o["pre"]), 0.0
+        o["succ"] = []
     for o in ops:
         for q in o["pre"]:
             ops[q]["succ"].append(o["id"])
-    for o in reversed(ops):
-        o["tail"] = o["cost"] + o["lat"] + o["early"] + max([HOP + ops[s]["tail"] for s in o["succ"]] + [0.0])
-    free = {e: 0.0 for e in "vapts"}
-    ready = [o for o in ops if o["left"] == 0]
+
+    def place(rank_, back):
+        start, left = {}, {o["id"]: len(o["succ" if back else "pre"]) for o in ops}
+        taken = {e: [] for e in "vapts"}
+        ready = [o["id"] for o in ops if left[o["id"]] == 0]
+        while ready:
+            i = min(ready, key=lambda q: (rank_[q], q))
+            ready.remove(i)
+            o = ops[i]
+            if back:
+                t = max([start[q] + ops[q]["cost"] + HOP for q in o["succ"]] + [0.0]) + o["lat"] + o["early"]
+            else:
+                t = max([start[q] + ops[q]["cost"] + ops[q]["lat"] + HOP for q in o["pre"]] + [0.0])
+            found = []
+            for (e, c) in ([(e, w[1]) for e, w in o["ways"].items()] if "ways" in o and not back else [(o["eng"], o["cost"])]):
+                tk, k, s = taken[e], 0, t
+                while k < len(tk) and tk[k][0] < s + c - 1e-9:
+                    s = max(s, tk[k][1])
+                    k += 1
+                found.append((s + c + (TUNE["bias"] if e == "v" else 0.0), e, c, s, k))
+            _, o["eng"], o["cost"], s, k = min(found)
+            taken[o["eng"]].insert(k, (s, s + o["cost"]))
+            start[i] = s
+            for q in o["pre" if back else "succ"]:
+                left[q] -= 1
+                if left[q] == 0:
+                    ready.append(q)
+        return start
+
+    if "order" not in PLAN:
+        tail = {}
+        for o in reversed(ops):
+            tail[o["id"]] = o["cost"] + o["lat"] + o["early"] + max([HOP + tail[s] for s in o["succ"]] + [0.0])
+        urgent, best = {q: -tail[q] for q in tail}, None
+        for _ in range(TUNE["it"]):
+            start = place(urgent, False)
+            end = {q: start[q] + ops[q]["cost"] + ops[q]["lat"] for q in start}
+            if best is None or max(end.values()) < best:
+                best, PLAN["order"] = max(end.values()), [(q, ops[q]["eng"]) for q in sorted(start, key=lambda q: (start[q], q))]
+            late = place({q: -end[q] for q in end}, True)
+            urgent = {q: -late[q] - ops[q]["cost"] for q in late}
+        PLAN["time"] = best
     order = []
-    while ready:
-        best = min(ready, key=lambda o: (max(o["est"], free[o["eng"]]), -o["tail"], o["id"]))
-        while True:
-            t0 = max(best["est"], free[best["eng"]])
-            better = [o for o in ready if o["eng"] == best["eng"] and o["tail"] > best["tail"] + 0.05 and o["est"] < t0 + best["cost"] - 0.03]
-            if not better:
-                break
-            best = max(better, key=lambda o: o["tail"])
-        ready.remove(best)
-        order.append(best)
-        t0 = max(best["est"], free[best["eng"]])
-        free[best["eng"]] = t0 + best["cost"]
-        for s in best["succ"]:
-            ops[s]["est"] = max(ops[s]["est"], t0 + best["cost"] + best["lat"] + HOP)
-            ops[s]["left"] -= 1
-            if ops[s]["left"] == 0:
-                ready.append(ops[s])
+    for (q, e) in PLAN["order"]:
+        order.append(ops[q])
+        if "ways" in ops[q]:
+            ops[q].update(eng=e, sem=ENG_SEM[e], fn=ops[q]["ways"][e][0])
 
     queue = {"v": g.vector, "a": g.scalar, "p": g, "t": g.tensor, "s": g.sync}
     total = {}

@@ -5,13 +5,14 @@ A = AluOpType
 F = ActivationFunctionType
 DIST = [1, 2, 4]
 C, K = 512, 64
-PW = C + 3 * K
+D0 = 4 * C - 3
+PW = 2256
 F32, BF, I32, U16, U8, MX = "float32", "bfloat16", "int32", "uint16", "uint8", "float8_e4m3fn_x4"
-GATH = [(0, 8, "xxxx"), (8, 14, "xxxx"), (18, 24, "xxxx"), (24, 32, "xxxx")]
-PIECES = [(0, 192), (192, 384), (384, 512)]
-GATH_LAST = [(0, 16, "vvaa"), (16, 32, "vvaa")]
+GATH = [(14, 22, "vvaa"), (22, 32, "xxxx"), (0, 6, "xxxx"), (6, 14, "xxxx")]
+PIECES = [(0, 128), (128, 384), (384, 512)]
+GATH_LAST = [(0, 16, "vvaa"), (16, 32, "xxxx")]
 PIECES_LAST = [(0, 256), (256, 512)]
-LOOK = [(0, 12, "v"), (12, 32, "a")]
+LOOK = [(0, 12, "v"), (12, 22, "a"), (22, 32, "a")]
 U16T = True
 
 
@@ -20,7 +21,7 @@ def _sb(n, d):
 
 
 SCRATCH = {
-    "par2": _sb(32, I32), "parq": _sb(8, I32), "raw": _sb(128, I32), "xin": _sb(2048, BF), "ut": _sb(512, BF), "vt": _sb(512, BF),
+    "par2": _sb(32, I32), "parq": _sb(8, I32), "raw": _sb(128, I32), "ut": _sb(512, BF), "vt": _sb(512, BF),
     "wq": _sb(512, MX), "wsc": _sb(512, U8), "uq": _sb(128, MX), "us": _sb(128, U8), "urq": _sb(128, MX), "urs": _sb(128, U8),
     "ukq": _sb(128, MX), "uks": _sb(128, U8),
     "vq": _sb(128, MX), "vs": _sb(128, U8), "eb": _sb(516, BF), "ebq": _sb(512, MX), "ebs": _sb(512, U8),
@@ -35,8 +36,8 @@ SCRATCH = {
     "sh": _sb(56, U16),
     "vi": _sb(160, I32), "ti": _sb(288, I32), "tb": _sb(288, F32), "tc": _sb(288, F32),
     "yy": _sb(48, I32), "el": _sb(32, U16), "nw": _sb(128, F32), "flg": _sb(128, F32),
-    "pool": _sb(4 * PW, BF), "et": _sb(2304, BF), "eq": _sb(512, MX), "es": _sb(512, U8),
-    "kq": _sb(128, MX), "ks": _sb(128, U8), "ht": _sb(512, BF),
+    "pool": _sb(4 * PW, BF), "et": _sb(2048, BF), "eq": _sb(512, MX), "es": _sb(512, U8),
+    "ht": _sb(512, BF),
     "kb": _sb(80, BF), "kbt": _sb(128, BF), "rows": _sb(512, BF), "op": _sb(128, BF), "op2": _sb(128, BF), "opt": _sb(128, BF),
     "x0": _sb(128, BF), "xs": _sb(128, U16 if U16T else BF), "xt": _sb(32, BF), "sm": _sb(64, BF), "ixu": _sb(32, U16),
     "xe": _sb(128, F32), "tab": _sb(264, F32), "ac": _sb(512, F32), "ci": _sb(512, I32), "yt": _sb(64, I32), "yi": _sb(256, I32),
@@ -79,17 +80,17 @@ LISTS = [
     ("RAW", 8, lambda a, h, p, c: 8 * p + c),
     ("SEL", 2, lambda a, h, p, c: seen(h, p % 8, PTR)),
     ("PERM", 8, lambda a, h, p, c: 8 * p + (c if a % 2 else 7 - c)),
+    ("FS", 4, lambda a, h, p, c: seen(h, p // 2, 4 * (2 * (2 * (p % 2) + (a % 2 if c < 2 else 1 - a % 2)) + h) + VAL)),
+    ("UK", 8, lambda a, h, p, c: 64 * (c % 2) + 16 * (p // 4) + p % 4),
+    ("UR", 8, lambda a, h, p, c: 16 * (p // 2) + p % 2),
+    ("R2", 16, lambda a, h, p, c: parents(c // 2, c % 2, p) + h * (128 + 128 * a)),
     ("REV", 8, lambda a, h, p, c: rev(16 * c + p)),
+    ("XE", 8, lambda a, h, p, c: 8 * slot(h, p % 4) + c),
+    ("FIN", 2, lambda a, h, p, c: 8 * slot(h, 2 * c + h) + p % 8),
     ("PERMR", 8, lambda a, h, p, c: rev(8 * p + (c if a % 2 else 7 - c))),
     ("TWICE", 8, lambda a, h, p, c: 32 * (c // 2) + 16 * h + p),
     ("PERM2", 8, lambda a, h, p, c: 8 * p + (2 * (c // 2) + h if a % 2 else 7 - 2 * (c // 2) - h)),
     ("SA", 2, lambda a, h, p, c: 16 * (16 * c + p) + 4 * c + p // 4),
-    ("FS", 4, lambda a, h, p, c: seen(h, p // 2, 4 * (2 * (2 * (p % 2) + (a % 2 if c < 2 else 1 - a % 2)) + h) + VAL)),
-    ("UR", 8, lambda a, h, p, c: 16 * (p // 2) + p % 2),
-    ("UK", 8, lambda a, h, p, c: 64 * (c % 2) + 16 * (p // 4) + p % 4),
-    ("R2", 16, lambda a, h, p, c: parents(c // 2, c % 2, p) + h * (128 + 128 * a)),
-    ("XE", 8, lambda a, h, p, c: 8 * slot(h, p % 4) + c),
-    ("FIN", 2, lambda a, h, p, c: 8 * slot(h, 2 * c + h) + p % 8),
 ]
 
 
@@ -145,7 +146,7 @@ def product(d):
 FIELDS = [(0, 15), (0, 1), (1, 1), (4, 1), (5, 1), (6, 1), (5, 3), (1, 3), (2, 1), (3, 1), (2, 3), (1, 7), (0, 3), (0, 7), (0, 31)]
 FIRST = 8
 PLAN = {}
-TUNE = {"bb": 0.0, "bs": 0.0, "parts": ((0, 128),), "out": 0.8, "yo": "aaaa", "lat": 1.7, "bias": 0.1, "it": 6}
+TUNE = {"bb": 0.0, "bs": 0.0, "parts": ((0, 128),), "out": 1.0, "yo": "avav", "lat": 1.1, "fl": 1.8, "bias": 0.03, "it": 6, "tries": 600, "sd": 0.5, "span": 2.5}
 
 
 def rank_program(g, core, T, topo):
@@ -223,7 +224,7 @@ def rank_program(g, core, T, topo):
             kw["bias"] = ap(bias)
         fn = func if func is not None else (F.Identity if bias is not None else F.Copy)
         op("a", lambda: g.scalar.activation(o[0], i[0], fn, **kw), [o], [i, scale, bias], cc(i) + (0.015 if i[3] else 0.0), ext=ext)
-        if func is None and i[1][0][0] != "ps":
+        if (func is None or (func == F.Relu and SCRATCH[o[1][0][0]][2] == U16)) and i[1][0][0] != "ps":
             if scale is None and bias is None:
                 alt = lambda: g.vector.tensor_copy(o[0], i[0])
             else:
@@ -245,7 +246,7 @@ def rank_program(g, core, T, topo):
     def mm(o, lq, ls, rq, rs, ext=None):
         op("t", lambda: g.tensor.matmul_mx(o[0], lq[0], ls[0], rq[0], rs[0], True, True), [o], [lq, ls, rq, rs], 0.6 * CYC * (rq[2] + 16), ext=ext)
 
-    def dma(eng, o, i, sem, lat=1.8, after=None):
+    def dma(eng, o, i, sem, lat=1.3, after=None):
         q = {"s": g.sync, "a": g.scalar, "p": g}[eng]
         op(eng, lambda: q.dma_start(ap(o), ap(i)), [o] if isinstance(o, tuple) else [], [i, after], 0.06, lat, sem=sem, inc=16)
 
@@ -266,14 +267,16 @@ def rank_program(g, core, T, topo):
     dma("s", V("par2", 0, 32, 1, 0, 16), T.par[:, :], "l_par")
     dma("a", V("par2", 0, 32, 1, 16, 32), T.par[:, :], "l_par")
     for a in range(4):
-        dma("s" if a % 2 else "a", (T.raw[32 * a + VAL:32 * a + 32:4, :], [("raw", 32 * a + VAL, 32 * a + 32, 0, 128, 1)]), T.fl[:, 8 * a:8 * a + 8], "l_fl", 2.5)
+        dma("s" if a % 2 else "a", (T.raw[32 * a + VAL:32 * a + 32:4, :], [("raw", 32 * a + VAL, 32 * a + 32, 0, 128, 1)]), T.fl[:, 8 * a:8 * a + 8], "l_fl", TUNE["fl"])
     for a in range(4):
-        dma("s" if a % 2 else "a", V("raw", 0, 128, 1, 32 * a + PTR, 32 * a + PTR + 1), T.par[:, 8 * a:8 * a + 8], "l_fl", 2.5)
-    dma("s", V("xin"), T.x[:, :], "l_x", 5.0, GATE)
-    dma("s", V("ut"), T.u[:, :], "l_u", 4.5, GATE)
-    dma("s", u8(V("wq")), T.wc[:, :], "l_w", 6.0, GATE)
-    dma("s", V("wsc"), T.ws[:, :], "l_w", 6.0, GATE)
-    dma("s", V("vt"), T.v[:, :], "l_v", 6.5, GATE)
+        dma("s" if a % 2 else "a", V("raw", 0, 128, 1, 32 * a + PTR, 32 * a + PTR + 1), T.par[:, 8 * a:8 * a + 8], "l_fl", TUNE["fl"])
+    dma("s", V("ut"), T.u[:, :], "l_u", 3.0, GATE)
+    early(9.0)
+    for t in range(4):
+        dma("s", V("pool", PW * t + 16 - t, PW * t + 16 - t + 4 * C), T.x[:, :], "l_x", 9.0, GATE)
+    dma("s", u8(V("wq")), T.wc[:, :], "l_w", 9.5, GATE)
+    dma("s", V("wsc"), T.ws[:, :], "l_w", 9.5, GATE)
+    dma("s", V("vt"), T.v[:, :], "l_v", 10.0, GATE)
 
     iota(V("pi", 0, 1), [[0, 1]], 0, 1, False)
     iota(V("cnt"), [[1, 128]], 0, 0)
@@ -282,7 +285,7 @@ def rank_program(g, core, T, topo):
         for c in range(c0, c1):
             ts(V("fi", c, c + 1), V("pi", 0, 1), FIELDS[c][0], A.logical_shift_right, FIELDS[c][1], A.bitwise_and)
             made[FIELDS[c]] = V("ff", c, c + 1)
-        cp(V("ff", c0, c1), V("fi", c0, c1))
+        act(V("ff", c0, c1), V("fi", c0, c1))
         early(20.0 if c0 else 0.0)
 
     def new(name, n=1):
@@ -309,7 +312,7 @@ def rank_program(g, core, T, topo):
         for (k, coef) in tm:
             key = key + (k, coef)
             if key not in made:
-                f = feature(k)
+                f = V("fi", FIELDS.index(k), FIELDS.index(k) + 1) if k in FIELDS else feature(k)
                 made[key] = new("col")
                 act(made[key], f, scale=float(coef), bias=prev)
             prev = made[key]
@@ -323,7 +326,7 @@ def rank_program(g, core, T, topo):
         act(o, chain(tm, 0), bias=float(c0))
         return o
 
-    def const(o, tb, eng="a"):
+    def const(o, tb):
         c = 0
         while c < tb.shape[1]:
             e = tb.shape[1]
@@ -341,10 +344,7 @@ def rank_program(g, core, T, topo):
                     made[key] = new("row", e - c)
                     iota(made[key], pattern(r), 0, 0)
                 row = made[key]
-            if eng == "a":
-                act(o(c, e), row, scale=column(sc), bias=column(bias))
-            else:
-                ts(o(c, e), row, column(sc), A.mult, column(bias), A.add)
+            act(o(c, e), row, scale=column(sc), bias=column(bias))
             c = e
 
     def colf(f):
@@ -353,24 +353,26 @@ def rank_program(g, core, T, topo):
     at, c0 = {}, 0
     for (name, n, f) in LISTS:
         at[name] = (c0, n)
-        const(lambda c, e: V("lu", c0 + c, c0 + e), table(n, f), "v")
+        const(lambda c, e: V("lu", c0 + c, c0 + e), table(n, f))
         c0 += n
 
     def L(name, n=None):
         return V("lu", at[name][0], at[name][0] + (n or at[name][1]))
 
-    act(V("cj"), V("cnt"), scale=colf(lambda a, h, p, c: 1025 * (p // 2 % 2)),
-        bias=colf(lambda a, h, p, c: 1025 * (128 * a + 1) * (p // 2 % 2) - 1))
+    act(V("cj"), V("cnt"), scale=4100.0, bias=colf(lambda a, h, p, c: 4100 * 128 * a + 4097))
+    act(V("cj"), V("cj"), scale=feature((1, 1)), bias=-1.0)
     PAD = colf(lambda a, h, p, c: -1000 * (p % 2))
     for nm in ("vb", "vc", "vd", "prm"):
         act(V(nm, 0, 16), V("cnt", 0, 16), scale=0.0, bias=PAD)
-    ms(V("pr"), 0.0)
+    for k in range(3):
+        fill(V("pr", 160 * k, 160 * k + 16), 0)
+        fill(V("pr", 160 * k + 144, 160 * k + 160), 0)
     CB = colf(lambda a, h, p, c: 16 - 128 * a)
     C8 = colf(lambda a, h, p, c: 136 - 128 * a if a % 2 else -1000)
     C9 = colf(lambda a, h, p, c: 8 if a >= 2 else -1000)
     CW = colf(lambda a, h, p, c: 2 - p % 2)
     CG = colf(lambda a, h, p, c: 16 * (p // 2) + 3)
-    const(lambda c, e: V("jc", c, e), table(32, lambda a, h, p, c: 1024 * (128 * a + rev(32 * (c // 8) + 16 * h + p) + 1) + C))
+    const(lambda c, e: V("jc", c, e), table(32, lambda a, h, p, c: 4096 * (128 * a + rev(32 * (c // 8) + 16 * h + p) + 1) + D0))
     for r in (1, 2):
         act(V("jc", 32 * r, 32 * r + 32), V("jc", 0, 32), bias=float(K * r))
     const(lambda c, e: V("fin", 2 * c + 1, 2 * e, 2), table(32, lambda a, h, p, c: 16 * (0, 2, 1, 3)[2 * (c // 16) + h] + p))
@@ -380,13 +382,12 @@ def rank_program(g, core, T, topo):
         act(V(nm, 0, 8), V("cnt", 0, 8), scale=0.0, bias=PAD)
         fill(V(nm, 8), 0)
     for a in range(4):
-        iota(V("nt", 128 + 128 * a, 256 + 128 * a), [[1, 16], [32 if a % 2 else -32, 8]], (256 if a % 2 else 288) + 16 * (a // 2), 0)
+        iota(V("nt", 128 + 128 * a, 256 + 128 * a), [[1, 16], [32 if a % 2 else -32, 8]], (32 if a % 2 else 512) + 16 * (a // 2), 0)
     iota(V("nt", 128, 640, 8), [[16, 2], [32, 2], [1, 16]], 0, 0)
     fill(V("vi", 0, 16), 0, False)
     fill(V("vi", 144, 160), 0, False)
     for nm in ("sa", "sb"):
         fill(V(nm, 0, 8), 0)
-    fill(V("et", 0, 256), 0)
     fill(V("ht", 256, 512), 0)
     iota(V("vcon"), [[0, 8], [1, 4], [0, 4]], 0, 0)
     fill(V("tab"), 0)
@@ -404,9 +405,6 @@ def rank_program(g, core, T, topo):
     fill(V("seg8", 0, 512, 8), 0)
     for b in range(4):
         quant(V("ebq", 128 * b, 128 * b + 128), V("ebs", 128 * b, 128 * b + 128), V("eb", 3 - b, 515 - b))
-    for t in range(4):
-        for c in range(2):
-            act(V("pool", PW * t + 256 * c, PW * t + 256 * c + 256), V("xin", 1024 * c + t, 1024 * c + 1024, 4))
     quant(V("uq"), V("us"), V("ut"))
 
     def pick(q, s, lst):
@@ -419,10 +417,10 @@ def rank_program(g, core, T, topo):
     early(6.0)
 
     for a in range(4):
-        cp(Q("parq", a, 0, 8), Q("par2", 0, 8 * a, 8 * a + 8))
-    ts(V("ptr", 0, 8), V("parq"), CB, A.add)
-    cp(V("paru"), V("parq"))
-    ts(V("pr", 16, 144), IND(V("raw"), L("RAW")), CB, A.add, 0.0, A.max)
+        act(Q("parq", a, 0, 8), Q("par2", 0, 8 * a, 8 * a + 8))
+    act(V("ptr", 0, 8), V("parq"), F.Relu, bias=CB)
+    act(V("paru"), V("parq"))
+    act(V("pr", 16, 144), IND(V("raw"), L("RAW")), F.Relu, bias=CB)
     for nm in ("va", "vb"):
         tt(V(nm, 16, 144), IND(V("raw"), L("RAW")), V("cj"), A.mult)
     act(V("flg"), IND(V("va", 16, 144), L("REV")))
@@ -433,14 +431,14 @@ def rank_program(g, core, T, topo):
         if k != 5:
             tr(V("pt", t0, t0 + 128), V("pr", b1 + 16, b1 + 144), 0.5)
             tr(V("pt", t0 + 128, t0 + 288), V("pr", b1, b1 + 160), 0.5)
-            cp(V("ptr", 16 * min(k + 1, 6), 16 * min(k + 1, 6) + 16), IND(V("pt", t0, t0 + 288), L("SEL", 1)))
+            act(V("ptr", 16 * min(k + 1, 6), 16 * min(k + 1, 6) + 16), IND(V("pt", t0, t0 + 288), L("SEL", 1)))
     act(V("nt", 0, 128), IND(V("nt", 128, 640), V("paru")))
     act(V("r2"), IND(V("nt"), L("R2")))
     for c in range(2):
         tr(V("r3", 128 * c, 128 * c + 128), V("r2", 128 * c, 128 * c + 128))
-    cp(V("ol", 0, 8), V("r3", 0, 256, 32))
-    cp(V("ol", 8, 12), V("r3", 144, 256, 32))
-    cp(V("ol", 12, 16), V("r3", 16, 128, 32))
+    act(V("ol", 0, 8), V("r3", 0, 256, 32))
+    act(V("ol", 8, 12), V("r3", 144, 256, 32))
+    act(V("ol", 12, 16), V("r3", 16, 128, 32))
 
     def both(src, tb):
         tr(V(tb, 0, 128), V(src, 16, 144))
@@ -449,7 +447,7 @@ def rank_program(g, core, T, topo):
     def pointer(src, k, bias):
         tb = "tc" if k % 2 else "tb"
         both(src, tb)
-        ts(V("ptr", 16 * k, 16 * k + 16), IND(V(tb), L("SEL", 1)), -1.0, A.mult, bias, A.add)
+        act(V("ptr", 16 * k, 16 * k + 16), IND(V(tb), L("SEL", 1)), F.Relu, -1.0, bias)
 
     def step(o, w, own, lst, c0, c1, end):
         tt(V(o, 16 + c0, 16 + c1), IND(V(w, 0, 16 + end), V("ptr", 16 * lst + c0 // 16, 16 * lst + c1 // 16)), V(own, 16 + c0, 16 + c1), A.max)
@@ -477,34 +475,30 @@ def rank_program(g, core, T, topo):
         ts(W(0, 0, 14), cyc, top, A.not_equal, 0.5, A.mult)
         ts(W(1, 0, 14), cyc, top, A.is_equal, big, A.mult)
         scan(W(2, 0, 14), W(0, 0, 14), W(1, 0, 14), 0.0, A.mult, A.add)
-        ms(W(0), 2.0)
-        ts(W(1), V("cnt", 0, 9), p, A.is_equal, 1024.0, A.mult)
-        scan(W(3), W(0), W(1), 0.0, A.mult, A.add)
-        ms(W(6), 0.0)
-        scan(W(4), W(0), W(6), -512.0, A.mult, A.add)
-        tt(W(5), W(3), W(1), A.subtract)
-        tt(W(5), W(5), W(4), A.add)
+        fill(W(4), 2)
+        ts(W(5), V("cnt", 0, 9), p, A.is_equal, 1024.0, A.mult)
+        scan(W(3), W(4), W(5), 0.0, A.mult, A.add)
         tt(W(6, 0, 7), W(3, 0, 7), W(2, 7, 14), A.add)
-        tt(W(6, 7, 8), W(3, 7, 8), far, A.add)
-        cp(W(6, 8, 9), W(3, 8, 9))
+        act(W(6, 7, 8), W(3, 7, 8), bias=far)
         act(V("gt", 0, 1), V("cnt", 0, 1), bias=8.0)
         for b in range(9):
-            act(V("gt", 1 << b, 2 << b), V("gt", 0, 1 << b), bias=W(6, b, b + 1))
-        for (k, c0, first) in ((3, 0, 0.0), (5, 128, -1024.0)):
-            o = new("col")
-            act(o, W(k, 7, 8), scale=feature((5, 1)), bias=first)
-            act(V("th", c0, c0 + 1), W(k, 8, 9), scale=feature((6, 1)), bias=o)
-            for b in range(7):
-                act(V("th", c0 + (1 << b), c0 + (2 << b)), V("th", c0, c0 + (1 << b)), bias=W(k, b, b + 1))
-        act(V("th", 256, 384), V("cnt"), scale=1024.0, bias=colf(lambda a, h, p, c: 1024 * (128 * a + 1)))
+            act(V("gt", 1 << b, 2 << b), V("gt", 0, 1 << b), bias=W(6 if b < 8 else 3, b, b + 1))
+        o = new("col")
+        act(o, W(3, 7, 8), scale=feature((5, 1)), bias=-1024.0)
+        act(V("th", 0, 1), W(3, 8, 9), scale=feature((6, 1)), bias=o)
+        for b in range(7):
+            act(V("th", 1 << b, 2 << b), V("th", 0, 1 << b), bias=W(3, b, b + 1))
+        act(V("th", 128, 256), V("cnt"), scale=1024.0, bias=colf(lambda a, h, p, c: 1024 * (128 * a + 1)))
         for nm in ("ba", "bb", "bc"):
             fill(V(nm, 0, 16), 0)
         fill(V("b8"), 0)
         for c in (0, 64):
-            tt(V("bf", c, c + 64), IND(V("gt"), V("paru", c // 16, c // 16 + 4)), V("th", c, c + 64), A.is_lt)
-            tt(V("bf", c + 128, c + 192), IND(V("gt"), V("paru", c // 16, c // 16 + 4)), V("th", c + 128, c + 192), A.subtract)
-            tt(V("bf", c + 128, c + 192), V("bf", c + 128, c + 192), V("th", c + 256, c + 320), A.max)
-            tt(V("ba", c + 16, c + 80), V("bf", c, c + 64), V("bf", c + 128, c + 192), A.mult)
+            tt(V("bf", c, c + 64), IND(V("gt"), V("paru", c // 16, c // 16 + 4)), V("th", c, c + 64), A.subtract)
+        act(V("bf", 128, 256), V("bf", 0, 128), F.Relu)
+        ts(V("th", 256, 384), V("bf", 0, 128), 1024.0, A.is_lt)
+        for c in (0, 64):
+            tt(V("bf", c + 128, c + 192), V("bf", c + 128, c + 192), V("th", c + 128, c + 192), A.add)
+            tt(V("ba", c + 16, c + 80), V("bf", c + 128, c + 192), V("th", c + 256, c + 320), A.mult)
         act(V("bb", 16, 144), V("ba", 16, 144))
         early(TUNE["bb"])
         cur, old = by_steps("ba", "bb", "bc", "ba", TUNE["parts"])
@@ -514,21 +508,20 @@ def rank_program(g, core, T, topo):
         for c in (0, 64):
             tt(V("bi", c, c + 64), IND(V("b8"), V("ptr", 128 + c // 16, 132 + c // 16)), V(cur, c + 16, c + 80), A.max)
         ts(V("bi", 128, 256), V("bi", 0, 128), 1023, A.bitwise_and)
-        cp(V("bf", 0, 128), V("bi", 128, 256))
-        act(V("xb", 0, 128), IND(V("bf", 0, 128), L("REV")), bias=-8.0)
+        act(V("xb", 0, 128), IND(V("bi", 128, 256), L("REV")), bias=-8.0)
         for k in range(6):
             act(V("xb", 128 * k + 128, 128 * k + 256, 2), V("xb", 128 * k, 128 * k + 64))
             act(V("xb", 128 * k + 129, 128 * k + 256, 2), V("xb", 128 * k + 64, 128 * k + 128))
         for k in range(7):
             act(V("xg", 64 * k, 64 * k + 64), IND(V("xb", 128 * k + 64, 128 * k + 128), L("TWICE", 4)))
         act(V("xg", 448, 576), IND(V("xb", 0, 128), L("TWICE")))
-        act(V("xg", 576, 704), IND(V("bf", 0, 128), L("PERM2")), bias=-8.0)
-        act(V("xg", 704, 832), IND(V("bf", 0, 128), L("TWICE")), bias=-8.0)
+        act(V("xg", 576, 704), IND(V("bi", 128, 256), L("PERM2")), bias=-8.0)
+        act(V("xg", 704, 832), IND(V("bi", 128, 256), L("TWICE")), bias=-8.0)
         for c in range(0, 832, 128):
             tr(V("xh", c, min(c + 128, 832)), V("xg", c, min(c + 128, 832)), 0.5)
-        ts(V("sh", 0, 32), IND(V("xh", 0, 512), L("SA")), 8.0, A.add)
-        ts(V("sh", 32, 40), V("xh", 448 + 7, 576, 16), 8.0, A.add)
-        ts(V("sh", 40, 56), V("xh", 576 + 8, 832, 16), 8.0, A.add)
+        act(V("sh", 0, 32), IND(V("xh", 0, 512), L("SA")), bias=8.0)
+        act(V("sh", 32, 40), V("xh", 448 + 7, 576, 16), bias=8.0)
+        act(V("sh", 40, 56), V("xh", 576 + 8, 832, 16), bias=8.0)
 
     def inherit(r):
         first, last = r == 0, r == 3
@@ -550,68 +543,70 @@ def rank_program(g, core, T, topo):
             act(V("flg"), IND(V("va", 16, 144), L("REV")), F.Sign)
             for a in range(4):
                 dma("s", T.ofl[:, 128 * a:128 * a + 128], (T.flg[32 * a + VAL:32 * a + 32:4, :], V("flg")[1]), "out")
-        (act if first else cp)(Q("w8", 1, 8, 136), Q(cur, 0, c0, c0 + 128))
-        act(Q("w8", 3, 8, 136), Q(cur, 2, c0, c0 + 128))
+        for a in (0, 2):
+            if first:
+                act(Q("w8", a + 1, 8, 136), Q(cur, a, c0, c0 + 128))
+            else:
+                act(Q("w8", a + 1, 8, 136, 2), Q(old, a, 8, 72))
+                act(Q("w8", a + 1, 9, 136, 2), Q(cur, a, 9, 136, 2))
         act(Q("w9", 2, 8, 136), Q(cur, 0, c0, c0 + 128))
         act(Q("w9", 3, 8, 136), Q(cur, 0, c0, c0 + 128))
         if first:
             pointer(cur, 8, C8)
         tt(V(old, c0, c0 + 128), IND(V("w8"), V("ptr", 128, 136) if first else V("sh", 32, 40)), V(cur, c0, c0 + 128), A.max)
         old, cur = cur, old
-        cp(Q("w9", 2, 136, 264), Q(cur, 1, c0, c0 + 128))
-        cp(Q("w9", 3, 136, 264), Q(cur, 1, c0, c0 + 128))
+        act(Q("w9", 2, 136, 264), Q(cur, 1, c0, c0 + 128))
+        act(Q("w9", 3, 136, 264), Q(cur, 1, c0, c0 + 128))
         act(V("prm", 16, 144), IND(V(cur, c0, c0 + 128), L("PERM" if first else "REV" if last else "PERMR")))
         if first:
             pointer("prm", 9, C9)
             later_lists()
         tt(V("vi", 16, 144), IND(V("w9"), V("ptr", 144, 152) if first else V("sh", 48, 56) if last else V("sh", 40, 48)), V("prm", 16, 144), A.max)
         both("vi", "ti")
-        ts(V("yy"), IND(V("ti"), L("FS", 3)), 1023, A.bitwise_and)
+        ts(V("yy"), IND(V("ti"), L("FS", 3)), 4095, A.bitwise_and)
         for a in range(4):
-            cp(Q("yy", a ^ 1, 16 * (a % 2), 16 * (a % 2) + 16), Q("yy", a, 32, 48))
+            act(Q("yy", a ^ 1, 16 * (a % 2), 16 * (a % 2) + 16), Q("yy", a, 32, 48))
         for b in range(2):
             for a in range(2):
-                cp(Q("el", 2 * b, 16 * a, 16 * a + 16, 1, 2) if last else Q("el", 2 * b, a, 32, 2, 2), Q("yy", 2 * a, b, 32, 2, 2))
+                act(Q("el", 2 * b, 16 * a, 16 * a + 16, 1, 2) if last else Q("el", 2 * b, a, 32, 2, 2), Q("yy", 2 * a, b, 32, 2, 2))
 
     def plane(eng, r, t, l0, l1, n0):
-        w = IND(V("pool", PW * t, PW * t + C + K * r), V("el", l0, l1))
-        (cp if eng == "v" else act)(V("et", 4 * (K + n0) + t, 4 * (K + n0 + 16 * (l1 - l0)), 4), w)
+        w = IND(V("pool", PW * t + 16, PW * t + 16 + D0 + K * r), V("el", l0, l1))
+        (cp if eng == "v" else act)(V("et", 4 * n0 + t, 4 * (n0 + 16 * (l1 - l0)), 4), w)
         if eng == "a":
             del ops[-1]["ways"]
 
     def pieces(r, gath, parts, sq, ss):
         for (l0, l1, engs) in gath:
             for t in range(4):
-                plane(engs[t], r, t, l0, l1, 16 * l0 + (K if r < 3 and l0 < 14 else 0))
+                plane(engs[t], r, t, l0, l1, 16 * ((l0 - 14) % 32 if r < 3 else l0))
         for i, (c0, c1) in enumerate(parts):
-            quant(V("eq", c0, c1), V("es", c0, c1), V("et", 4 * (K + c0), 4 * (K + c1)))
+            quant(V("eq", c0, c1), V("es", c0, c1), V("et", 4 * c0, 4 * c1))
+            if i == 0 and r < 3:
+                mm(V("ps", 1536, 1664), V("ukq"), V("uks"), V("eq", 0, 128), V("es", 0, 128))
             mm(V("ps", 512 * i, 512 * i + c1 - c0), V(sq), V(ss), V("eq", c0, c1), V("es", c0, c1))
 
     def symbols(r):
         dst = T.cores[(rank - DIST[r]) % n_ranks]
-        for t in range(4):
-            plane("v" if t < 2 else "a", r, t, 14, 18, 0)
-        quant(V("kq"), V("ks"), V("et", 0, 512))
-        mm(V("ps", 1536, 1664), V("ukq"), V("uks"), V("kq"), V("ks"))
+        pieces(r, GATH, PIECES, "urq", "urs")
         for b in range(4):
-            mm(V("ps", 2048 + 512 * b, 2176 + 512 * b), V("wq", 128 * b, 128 * b + 128), V("wsc", 128 * b, 128 * b + 128), V("kq"), V("ks"))
-        ts(V("kb", 0, 64), V("ps", 1600, 1664), 0.0, A.is_gt, CW, A.mult)
-        ts(V("kb", 64, 80), V("ps", 1600, 1616), 0.0, A.is_gt, CW, A.mult)
+            mm(V("ps", 2048 + 512 * b, 2176 + 512 * b), V("wq", 128 * b, 128 * b + 128), V("wsc", 128 * b, 128 * b + 128), V("eq", 0, 128), V("es", 0, 128))
+        ts(V("kb", 0, 64), V("ps", 1536, 1600), 0.0, A.is_gt, CW, A.mult)
+        ts(V("kb", 64, 80), V("ps", 1536, 1552), 0.0, A.is_gt, CW, A.mult)
         tr(V("kbt", 0, 64), V("kb", 0, 64), 0.5)
         tr(V("kbt", 64, 128), V("kb", 16, 80), 0.5)
         tt(V("fs%d" % r), V("kbt", 0, 128, 4), V("kbt", 1, 128, 4), A.add)
         send(dst, V("fl%d" % r), V("fs%d" % r), "af%d" % r, TUNE["lat"] + (0.0 if r else 0.8))
-        pieces(r, GATH, PIECES, "urq", "urs")
         for i, (c0, c1) in enumerate(PIECES):
             ts(V("rows", c0, c1), V("ps", 512 * i, 512 * i + c1 - c0), 0.0, A.is_gt, CW, A.mult)
         for b in range(4):
-            act(V("ht", b, 256, 4), V("ps", 2048 + 512 * b + K, 2048 + 512 * b + 2 * K), scale=0.03125)
+            act(V("ht", b, 256, 4), V("ps", 2048 + 512 * b, 2048 + 512 * b + K), scale=0.03125)
         hq, hs = "hq%d" % r, "hs%d" % r
         quant(V(hq, 64, 192), V(hs, 64, 192), V("ht"))
         send(dst, u8(V(hq, 0, 64)), u8(V(hq, 64, 128)), "ah%d" % r, 4.0)
         send(dst, V(hs, 0, 64), V(hs, 64, 128), "ah%d" % r, 4.0)
         act(V("op", 0, 64), IND(V("rows"), V("ol", 12, 16)), scale=7.0, bias=CG)
-        cp(V("op", 64, 128), IND(V("rows"), V("ol", 0, 4)))
+        act(V("op", 64, 128), IND(V("rows"), V("ol", 0, 4)))
         tr(V("x0", 0, 128, 2), V("op", 0, 64), 0.5)
         tr(V("x0", 1, 128, 2), V("op", 64, 128), 0.5)
         scan(V("xs"), V("seg4"), V("x0"), 0.0, A.mult, A.add, 0.5)
@@ -641,7 +636,7 @@ def rank_program(g, core, T, topo):
             mm(V("ps", 2048 + 512 * b, 2176 + 512 * b), V("ebq", 128 * b, 128 * b + 128), V("ebs", 128 * b, 128 * b + 128),
                V(hq, 0, 128), V(hs, 0, 128), ext="ah%d" % r)
         for b in range(4):
-            act(V("pool", PW * b + C + K * r, PW * b + C + K * r + K), V("ps", 2048 + 512 * b, 2048 + 512 * b + K))
+            act(V("pool", PW * b + 16 + D0 + K * r, PW * b + 16 + D0 + K * r + K), V("ps", 2048 + 512 * b, 2048 + 512 * b + K))
             early(1.5)
         tie = sum((3 - t) * 64 ** (3 - t) for t in range(4)) / 8.0
         for (c0, c1, eng) in LOOK:
@@ -652,7 +647,8 @@ def rank_program(g, core, T, topo):
                 act(o, w, scale=4.0, bias=tie)
             scan(V("ci", 16 * c0, 16 * c1), V("seg8", 16 * c0, 16 * c1), o, 0.0, A.mult, A.add)
         tr(V("yt"), V("ci", 7, 512, 8))
-        for t in range(4):
+        act(V("yi", 0, 256, 4), V("yt"), scale=64.0 ** -3, bias=-0.28)
+        for t in range(1, 4):
             ts(V("yi", t, 256, 4), V("yt"), 6 * (3 - t), A.logical_shift_right, 63, A.bitwise_and)
         scan(V("sc"), V("yi"), V("lane"), 0.0, A.max, A.add)
         ts(V("ku"), V("sc", 63, 256, 64), -16.0, A.mult, -449.0, A.add)
@@ -672,11 +668,11 @@ def rank_program(g, core, T, topo):
     pieces(3, GATH_LAST, PIECES_LAST, "vq", "vs")
     for i, (c0, c1) in enumerate(PIECES_LAST):
         ahead = TUNE["out"] * (len(PIECES_LAST) - 1 - i)
-        dma("s", T.oc[:, 4 * c0:4 * c1], u8(V("eq", c0, c1)), "out", 2.2)
-        early(ahead + TUNE["out"] / 2)
+        dma("s", T.oc[:, 4 * c0:4 * c1], u8(V("eq", c0, c1)), "out", 1.1)
+        ops[-1].update(early=ahead + TUNE["out"] / 2, move=0.16 + 0.0013 * (c1 - c0))
         (act if TUNE["yo"][i] == "a" else cp)(V("yo", c0, c1), V("ps", 512 * i, 512 * i + c1 - c0))
-        dma("s", T.y[:, c0:c1], V("yo", c0, c1), "out", 2.2)
-        early(ahead)
+        dma("s", T.y[:, c0:c1], V("yo", c0, c1), "out", 1.1)
+        ops[-1].update(early=ahead, move=0.16 + 0.0013 * (c1 - c0))
     for k in range(4):
         dma("a" if k % 2 else "s", T.osc[4 * k:4 * k + 4, :], V("es", 0, 512, 1, 32 * k, 32 * k + 4), "out")
 
@@ -736,6 +732,12 @@ def rank_program(g, core, T, topo):
                     ready.append(q)
         return start
 
+    def ends(start):
+        end, free = {q: start[q] + ops[q]["cost"] + ops[q]["lat"] for q in start}, 0.0
+        for q in sorted(group["out"], key=lambda q: start[q]):
+            free = end[q] = max(end[q], free) + ops[q].get("move", 0.05)
+        return end
+
     if "order" not in PLAN:
         tail = {}
         for o in reversed(ops):
@@ -743,11 +745,21 @@ def rank_program(g, core, T, topo):
         urgent, best = {q: -tail[q] for q in tail}, None
         for _ in range(TUNE["it"]):
             start = place(urgent, False)
-            end = {q: start[q] + ops[q]["cost"] + ops[q]["lat"] for q in start}
+            end = ends(start)
             if best is None or max(end.values()) < best:
                 best, PLAN["order"] = max(end.values()), [(q, ops[q]["eng"]) for q in sorted(start, key=lambda q: (start[q], q))]
             late = place({q: -end[q] for q in end}, True)
+            if best == max(end.values()):
+                kept = urgent
             urgent = {q: -late[q] - ops[q]["cost"] for q in late}
+        rng = np.random.default_rng(1)
+        for _ in range(TUNE["tries"]):
+            lo = min(kept.values()) + rng.random() * best
+            urgent = {q: kept[q] + (float(rng.normal()) * TUNE["sd"] if lo <= kept[q] < lo + TUNE["span"] else 0.0) for q in kept}
+            start = place(urgent, False)
+            end = max(ends(start).values())
+            if end <= best:
+                best, kept, PLAN["order"] = end, urgent, [(q, ops[q]["eng"]) for q in sorted(start, key=lambda q: (start[q], q))]
         PLAN["time"] = best
     order = []
     for (q, e) in PLAN["order"]:

@@ -10,9 +10,10 @@ PW = 2256
 F32, BF, I32, U16, U8, MX = "float32", "bfloat16", "int32", "uint16", "uint8", "float8_e4m3fn_x4"
 GATH = [(14, 22, "vvaa"), (22, 32, "xxxx"), (0, 6, "xxxx"), (6, 14, "xxxx")]
 PIECES = [(0, 128), (128, 384), (384, 512)]
-GATH_LAST = [(0, 16, "vvaa"), (16, 32, "xxxx")]
-PIECES_LAST = [(0, 256), (256, 512)]
-LOOK = [(0, 12, "v"), (12, 22, "a"), (22, 32, "a")]
+GATH_LAST = [(0, 16, "vvaa"), (16, 24, "xxxx"), (24, 32, "xxxx")]
+PIECES_LAST = [(0, 256), (256, 384), (384, 512)]
+STORES = [(0, 256), (256, 512)]
+LOOK = [(0, 14, "v"), (14, 24, "a"), (24, 32, "a")]
 U16T = True
 
 
@@ -21,18 +22,18 @@ def _sb(n, d):
 
 
 SCRATCH = {
-    "par2": _sb(32, I32), "parq": _sb(8, I32), "raw": _sb(128, I32), "ut": _sb(512, BF), "vt": _sb(512, BF),
+    "parq": _sb(8, I32), "raw": _sb(128, I32), "ut": _sb(512, BF), "vt": _sb(512, BF),
     "wq": _sb(512, MX), "wsc": _sb(512, U8), "uq": _sb(128, MX), "us": _sb(128, U8), "urq": _sb(128, MX), "urs": _sb(128, U8),
     "ukq": _sb(128, MX), "uks": _sb(128, U8),
     "vq": _sb(128, MX), "vs": _sb(128, U8), "eb": _sb(516, BF), "ebq": _sb(512, MX), "ebs": _sb(512, U8),
     "pi": _sb(2, I32), "fi": _sb(24, I32), "ff": _sb(24, F32), "col": _sb(192, F32), "row": _sb(160, F32), "cnt": _sb(128, F32),
-    "lu": _sb(112, U16), "cj": _sb(128, F32), "jc": _sb(96, F32),
-    "vcon": _sb(128, F32), "horn": _sb(128, F32), "lane": _sb(256, F32), "seg4": _sb(128, BF), "seg8": _sb(520, F32),
+    "lu": _sb(112, U16), "cj": _sb(128, F32), "jc": _sb(256, F32),
+    "vcon": _sb(128, F32), "horn": _sb(128, F32), "lane": _sb(64, F32), "seg4": _sb(128, BF), "seg8": _sb(520, F32),
     "ptr": _sb(176, U16), "paru": _sb(8, U16), "nt": _sb(640, F32), "r2": _sb(256, F32), "r3": _sb(256, F32), "ol": _sb(16, U16),
-    "va": _sb(160, F32), "vb": _sb(160, F32), "vc": _sb(160, F32), "vd": _sb(160, F32), "w8": _sb(136, F32), "w9": _sb(264, F32),
-    "prm": _sb(160, F32), "sa": _sb(136, F32), "sb": _sb(136, F32), "pr": _sb(480, BF), "pt": _sb(576, BF),
+    "va": _sb(160, F32), "vb": _sb(160, F32), "vc": _sb(160, F32), "vd": _sb(160, F32), "w8": _sb(144, F32), "w9": _sb(264, F32),
+    "prm": _sb(160, F32), "sa": _sb(136, F32), "sb": _sb(136, F32), "pj": _sb(128, BF), "pr": _sb(480, BF), "pt": _sb(576, BF),
     "wt": _sb(112, F32), "gt": _sb(512, F32), "th": _sb(384, F32), "bf": _sb(256, F32), "ba": _sb(160, F32), "bb": _sb(160, F32),
-    "bc": _sb(160, F32), "b8": _sb(136, F32), "bi": _sb(256, I32), "xb": _sb(896, BF), "xg": _sb(832, BF), "xh": _sb(832, BF),
+    "bc": _sb(160, F32), "b8": _sb(144, F32), "bi": _sb(256, I32), "bj": _sb(256, I32), "xb": _sb(896, BF), "xg": _sb(832, BF), "xh": _sb(832, BF),
     "sh": _sb(56, U16),
     "vi": _sb(160, I32), "ti": _sb(288, I32), "tb": _sb(288, F32), "tc": _sb(288, F32),
     "yy": _sb(48, I32), "el": _sb(32, U16), "nw": _sb(128, F32), "flg": _sb(128, F32),
@@ -41,8 +42,8 @@ SCRATCH = {
     "kb": _sb(80, BF), "kbt": _sb(128, BF), "rows": _sb(512, BF), "op": _sb(128, BF), "op2": _sb(128, BF), "opt": _sb(128, BF),
     "x0": _sb(128, BF), "xs": _sb(128, U16 if U16T else BF), "xt": _sb(32, BF), "sm": _sb(64, BF), "ixu": _sb(32, U16),
     "xe": _sb(128, F32), "tab": _sb(264, F32), "ac": _sb(512, F32), "ci": _sb(512, I32), "yt": _sb(64, I32), "yi": _sb(256, I32),
-    "sc": _sb(256, F32), "ku": _sb(4, U16), "fin": _sb(64, BF), "fw": _sb(576, BF), "fg": _sb(64, BF), "ft": _sb(64, BF),
-    "d0": _sb(128, F32), "d1": _sb(128, F32), "yo": _sb(512, F32),
+    "sc": _sb(256, U16), "fin": _sb(64, BF), "fw": _sb(576, BF), "fk": _sb(576, BF), "fg": _sb(64, F32), "ne": _sb(64, BF), "smr": _sb(64, BF),
+    "d0": _sb(128, BF), "d1": _sb(128, F32), "yo": _sb(512, F32),
     "ps": ("psum", [128, 4096], F32),
 }
 for _r in range(3):
@@ -54,8 +55,8 @@ for _r in range(3):
 SEMAPHORES = (["sv", "sa", "sp", "st", "l_par", "l_fl", "l_u", "l_x", "l_w", "l_v", "out", "sent"]
               + ["af%d" % r for r in range(3)] + ["ah%d" % r for r in range(3)])
 ENG_SEM = {"v": "sv", "a": "sa", "p": "sp", "t": "st"}
-CYC, HOP = 0.00104, 0.2
-VAL, PTR = 2, 1
+CYC, HOP = 0.00105, 0.22
+VAL, PTR = 3, 1
 
 
 def seen(h, c, lane):
@@ -77,8 +78,9 @@ def parents(m, e, p):
 
 
 LISTS = [
+    ("PJ", 1, lambda a, h, p, c: 2 * (p // 4) + h),
     ("RAW", 8, lambda a, h, p, c: 8 * p + c),
-    ("SEL", 2, lambda a, h, p, c: seen(h, p % 8, PTR)),
+    ("SEL", 1, lambda a, h, p, c: seen(h, p % 8, PTR)),
     ("PERM", 8, lambda a, h, p, c: 8 * p + (c if a % 2 else 7 - c)),
     ("FS", 4, lambda a, h, p, c: seen(h, p // 2, 4 * (2 * (2 * (p % 2) + (a % 2 if c < 2 else 1 - a % 2)) + h) + VAL)),
     ("UK", 8, lambda a, h, p, c: 64 * (c % 2) + 16 * (p // 4) + p % 4),
@@ -86,11 +88,10 @@ LISTS = [
     ("R2", 16, lambda a, h, p, c: parents(c // 2, c % 2, p) + h * (128 + 128 * a)),
     ("REV", 8, lambda a, h, p, c: rev(16 * c + p)),
     ("XE", 8, lambda a, h, p, c: 8 * slot(h, p % 4) + c),
-    ("FIN", 2, lambda a, h, p, c: 8 * slot(h, 2 * c + h) + p % 8),
+    ("FIN", 4, lambda a, h, p, c: 8 * slot(h, 2 * (c // 2) + h) + p // 2),
     ("PERMR", 8, lambda a, h, p, c: rev(8 * p + (c if a % 2 else 7 - c))),
     ("TWICE", 8, lambda a, h, p, c: 32 * (c // 2) + 16 * h + p),
     ("PERM2", 8, lambda a, h, p, c: 8 * p + (2 * (c // 2) + h if a % 2 else 7 - 2 * (c // 2) - h)),
-    ("SA", 2, lambda a, h, p, c: 16 * (16 * c + p) + 4 * c + p // 4),
 ]
 
 
@@ -143,10 +144,10 @@ def product(d):
     return (sc, r) if (sc[:, None] * r[None, :] == d).all() and pattern(r) is not None else None
 
 
-FIELDS = [(0, 15), (0, 1), (1, 1), (4, 1), (5, 1), (6, 1), (5, 3), (1, 3), (2, 1), (3, 1), (2, 3), (1, 7), (0, 3), (0, 7), (0, 31)]
+FIELDS = [(2, 3), (4, 1), (5, 3), (0, 15), (0, 1), (1, 1), (1, 3), (5, 1), (6, 1), (2, 1), (3, 1), (1, 7), (0, 3), (0, 7), (0, 31)]
 FIRST = 8
 PLAN = {}
-TUNE = {"bb": 0.0, "bs": 0.0, "parts": ((0, 128),), "out": 1.0, "yo": "avav", "lat": 1.1, "fl": 1.8, "bias": 0.03, "it": 6, "tries": 600, "sd": 0.5, "span": 2.5}
+TUNE = {"bb": 0.0, "bs": 1.0, "parts": ((0, 128),), "out": 1.0, "yo": "aav", "lat": 0.9, "fl": 1.8, "bias": 0.03, "it": 10, "first": ((0, 128),), "tie": False, "xh": ((0, 64), (64, 192), (192, 320), (320, 448), (448, 576), (576, 704), (704, 832)), "cases": ((0.81, 1.0, 0.22), (1.05, 1.0, 0.2), (1.16, 1.15, 0.24), (1.18, 1.2, 0.24)), "act": 0.02, "tries": 2400, "sd": (0.2, 0.4, 0.8), "span": (1.0, 2.0, 3.0)}
 
 
 def rank_program(g, core, T, topo):
@@ -179,7 +180,8 @@ def rank_program(g, core, T, topo):
             if isinstance(v, tuple):
                 r += v[1]
         ops.append({"eng": eng, "fn": fn, "r": r, "w": w, "sem": sem or ENG_SEM[eng], "inc": inc, "dma": sem is not None,
-                    "ext": ext, "cost": cost, "lat": lat, "early": 0.0, "id": len(ops)})
+                    "ext": ext, "cost": cost, "lat": lat, "early": 0.0, "id": len(ops),
+                    "picks": any(isinstance(v, tuple) and len(v) > 3 and v[3] for v in ins)})
         if gives is not None:
             arrive.setdefault(gives, []).append(len(ops) - 1)
 
@@ -190,7 +192,7 @@ def rank_program(g, core, T, topo):
         return v[0] if isinstance(v, tuple) else v
 
     def cc(v, k=1.0):
-        return 0.05 + 1.56 * CYC * v[2] if v[3] else max(64, k * v[2]) * CYC
+        return 0.055 + 1.56 * CYC * v[2] if v[3] else 0.005 + max(64, k * v[2]) * CYC
 
     def rate(*vs):
         return 0.5 if all(SCRATCH[v[1][0][0]][2] in (BF, U16) for v in vs) else 1.0
@@ -223,7 +225,7 @@ def rank_program(g, core, T, topo):
         if bias is not None:
             kw["bias"] = ap(bias)
         fn = func if func is not None else (F.Identity if bias is not None else F.Copy)
-        op("a", lambda: g.scalar.activation(o[0], i[0], fn, **kw), [o], [i, scale, bias], cc(i) + (0.015 if i[3] else 0.0), ext=ext)
+        op("a", lambda: g.scalar.activation(o[0], i[0], fn, **kw), [o], [i, scale, bias], cc(i) + 0.015, ext=ext)
         if (func is None or (func == F.Relu and SCRATCH[o[1][0][0]][2] == U16)) and i[1][0][0] != "ps":
             if scale is None and bias is None:
                 alt = lambda: g.vector.tensor_copy(o[0], i[0])
@@ -255,28 +257,26 @@ def rank_program(g, core, T, topo):
 
     count = {}
 
-    def send(dst_core, o, i, rsem, lat):
+    def send(dst_core, o, i, rsem, lat, every=1):
         rid, pid = topo.addr(dst_core)[:2]
-        m = topo.mask(core, dst_core)
-        n = len(topo.engines(core, dst_core))
+        use = topo.engines(core, dst_core)[::every]
+        m, n = sum(1 << e for e in use), len(use)
         count[rsem] = count.get(rsem, 0) + n
         op("p", lambda: g.remote_dma(o[0], i[0], T.sem[rsem], T.sem["sent"], pid, rid, m), [], [i], 0.15, lat, sem="sent", inc=-n, gives=rsem)
 
-    GATE = (None, [("gate", 0, 128, 0, 1, 1)])
-    op("v", lambda: g.vector.memset(T.raw[:, :], 0), [V("raw"), GATE], [], 0.13)
-    dma("s", V("par2", 0, 32, 1, 0, 16), T.par[:, :], "l_par")
-    dma("a", V("par2", 0, 32, 1, 16, 32), T.par[:, :], "l_par")
+    op("v", lambda: g.vector.memset(T.raw[:, :], 0), [V("raw")], [], 0.13)
+    for G in range(8):
+        dma("s" if G % 2 else "a", V("parq", 0, 8, 1, 16 * G, 16 * G + 16), T.par[:, 8 * (G // 2):8 * (G // 2) + 8], "l_par")
+        early(5.0)
     for a in range(4):
         dma("s" if a % 2 else "a", (T.raw[32 * a + VAL:32 * a + 32:4, :], [("raw", 32 * a + VAL, 32 * a + 32, 0, 128, 1)]), T.fl[:, 8 * a:8 * a + 8], "l_fl", TUNE["fl"])
     for a in range(4):
         dma("s" if a % 2 else "a", V("raw", 0, 128, 1, 32 * a + PTR, 32 * a + PTR + 1), T.par[:, 8 * a:8 * a + 8], "l_fl", TUNE["fl"])
-    dma("s", V("ut"), T.u[:, :], "l_u", 3.0, GATE)
-    early(9.0)
-    for t in range(4):
-        dma("s", V("pool", PW * t + 16 - t, PW * t + 16 - t + 4 * C), T.x[:, :], "l_x", 9.0, GATE)
-    dma("s", u8(V("wq")), T.wc[:, :], "l_w", 9.5, GATE)
-    dma("s", V("wsc"), T.ws[:, :], "l_w", 9.5, GATE)
-    dma("s", V("vt"), T.v[:, :], "l_v", 10.0, GATE)
+    loads = ([(V("ut"), T.u[:, :], "l_u", 5.0)] + [(V("pool", PW * t + 16 - t, PW * t + 16 - t + 4 * C), T.x[:, :], "l_x", 10.0) for t in range(4)]
+             + [(u8(V("wq")), T.wc[:, :], "l_w", 11.0), (V("wsc"), T.ws[:, :], "l_w", 11.0), (V("vt"), T.v[:, :], "l_v", 14.0)])
+    for (o, i, sem, lat) in loads:
+        dma("s", o, i, sem, lat)
+        ops[-1]["behind"] = [q["id"] for q in ops[:-1] if q["eng"] == "s"]
 
     iota(V("pi", 0, 1), [[0, 1]], 0, 1, False)
     iota(V("cnt"), [[1, 128]], 0, 0)
@@ -305,14 +305,17 @@ def rank_program(g, core, T, topo):
                 act(o, feature(rest if rest & (rest - 1) else (rest.bit_length() - 1, 1)), scale=feature((low.bit_length() - 1, 1)))
         return made[k]
 
-    def chain(tm, c0):
+    def whole(k):
+        return V("fi", FIELDS.index(k), FIELDS.index(k) + 1) if k in FIELDS else feature(k)
+
+    def chain(tm, c0, anew=False):
         prev, key = float(c0), ("c", c0)
-        if c0 == 0 and len(tm) == 1 and tm[0][1] == 1:
+        if c0 == 0 and len(tm) == 1 and tm[0][1] == 1 and not anew:
             return feature(tm[0][0])
         for (k, coef) in tm:
             key = key + (k, coef)
             if key not in made:
-                f = V("fi", FIELDS.index(k), FIELDS.index(k) + 1) if k in FIELDS else feature(k)
+                f = whole(k)
                 made[key] = new("col")
                 act(made[key], f, scale=float(coef), bias=prev)
             prev = made[key]
@@ -353,34 +356,42 @@ def rank_program(g, core, T, topo):
     at, c0 = {}, 0
     for (name, n, f) in LISTS:
         at[name] = (c0, n)
-        const(lambda c, e: V("lu", c0 + c, c0 + e), table(n, f))
-        c0 += n
+        if n == 1:
+            k0, tm = terms(table(1, f)[:, 0])
+            act(V("lu", c0, c0 + 1), whole(tm[0][0]), scale=float(tm[0][1]), bias=chain(tm[1:], k0, True))
+        else:
+            const(lambda c, e: V("lu", c0 + c, c0 + e), table(n, f))
+        c0 += n + n % 2
 
     def L(name, n=None):
         return V("lu", at[name][0], at[name][0] + (n or at[name][1]))
 
     act(V("cj"), V("cnt"), scale=4100.0, bias=colf(lambda a, h, p, c: 4100 * 128 * a + 4097))
     act(V("cj"), V("cj"), scale=feature((1, 1)), bias=-1.0)
-    PAD = colf(lambda a, h, p, c: -1000 * (p % 2))
     for nm in ("vb", "vc", "vd", "prm"):
-        act(V(nm, 0, 16), V("cnt", 0, 16), scale=0.0, bias=PAD)
+        fill(V(nm, 0, 16), -1000)
+    ms(V("pj"), 0.0)
     for k in range(3):
         fill(V("pr", 160 * k, 160 * k + 16), 0)
         fill(V("pr", 160 * k + 144, 160 * k + 160), 0)
     CB = colf(lambda a, h, p, c: 16 - 128 * a)
-    C8 = colf(lambda a, h, p, c: 136 - 128 * a if a % 2 else -1000)
-    C9 = colf(lambda a, h, p, c: 8 if a >= 2 else -1000)
+    C8, C9 = colf(lambda a, h, p, c: 136 - 128 * a), 8.0
     CW = colf(lambda a, h, p, c: 2 - p % 2)
     CG = colf(lambda a, h, p, c: 16 * (p // 2) + 3)
-    const(lambda c, e: V("jc", c, e), table(32, lambda a, h, p, c: 4096 * (128 * a + rev(32 * (c // 8) + 16 * h + p) + 1) + D0))
+    const(lambda c, e: V("jc", 2 * c, 2 * e, 2), table(32, lambda a, h, p, c: 4096 * (128 * a + rev(32 * (c // 8) + 16 * h + p) + 1) + D0))
+    fill(V("jc", 1, 64, 2), 0)
+    tr(V("jc", 64, 128), V("jc", 0, 64))
+    even = colf(lambda a, h, p, c: 1 - p % 2)
     for r in (1, 2):
-        act(V("jc", 32 * r, 32 * r + 32), V("jc", 0, 32), bias=float(K * r))
-    const(lambda c, e: V("fin", 2 * c + 1, 2 * e, 2), table(32, lambda a, h, p, c: 16 * (0, 2, 1, 3)[2 * (c // 16) + h] + p))
+        act(V("jc", 64 * r + 64, 64 * r + 128), V("jc", 64, 128), bias=colf(lambda a, h, p, c: K * r * (1 - p % 2)))
+    iota(V("fin"), [[16, 2], [32, 2], [1, 16]], 0, 0)
+    act(V("fk", 0, 64), V("fin"), scale=even)
+    for (c0, c1) in ((64, 128), (128, 256), (256, 512), (512, 576)):
+        act(V("fk", c0, c1), V("fk", 0, c1 - c0))
     for nm in ("vc", "prm"):
         fill(V(nm, 144, 160), 0)
     for nm in ("w8", "w9"):
-        act(V(nm, 0, 8), V("cnt", 0, 8), scale=0.0, bias=PAD)
-        fill(V(nm, 8), 0)
+        fill(V(nm), -1000)
     for a in range(4):
         iota(V("nt", 128 + 128 * a, 256 + 128 * a), [[1, 16], [32 if a % 2 else -32, 8]], (32 if a % 2 else 512) + 16 * (a // 2), 0)
     iota(V("nt", 128, 640, 8), [[16, 2], [32, 2], [1, 16]], 0, 0)
@@ -391,15 +402,14 @@ def rank_program(g, core, T, topo):
     fill(V("ht", 256, 512), 0)
     iota(V("vcon"), [[0, 8], [1, 4], [0, 4]], 0, 0)
     fill(V("tab"), 0)
-    fill(V("d0"), 0)
-    fill(V("d1", 3, 128, 4), 0)
+    iota(V("d0", 0, 128, 2), [[0, 32], [1, 2]], 0, 0)
     fill(V("seg4"), 1)
     fill(V("seg4", 0, 128, 4), 0)
-    fill(V("horn"), 64)
+    fill(V("horn"), 16)
     fill(V("horn", 0, 128, 4), 0)
-    fill(V("lane"), 0)
-    ms(V("lane", 3, 256, 4), 0.0625)
-    fill(V("lane", 63, 256, 64), -64)
+    fill(V("lane"), -16)
+    fill(V("lane", 3, 64, 4), 47)
+    fill(V("lane", 63, 64), 63)
     fill(V("seg8"), 1)
     op("p", lambda: g.affine_select(T.eb[:, :], T.seg8[:, 0:516], [[-1, 516]], A.is_equal, 0.0, 3, 4), [V("eb")], [V("seg8")], 1.2)
     fill(V("seg8", 0, 512, 8), 0)
@@ -416,11 +426,10 @@ def rank_program(g, core, T, topo):
     quant(V("vq"), V("vs"), V("vt"))
     early(6.0)
 
-    for a in range(4):
-        act(Q("parq", a, 0, 8), Q("par2", 0, 8 * a, 8 * a + 8))
     act(V("ptr", 0, 8), V("parq"), F.Relu, bias=CB)
     act(V("paru"), V("parq"))
-    act(V("pr", 16, 144), IND(V("raw"), L("RAW")), F.Relu, bias=CB)
+    act(V("pj", PTR, 128, 8), IND(V("parq"), L("PJ", 1)), F.Relu, bias=CB)
+    tr(V("pr", 16, 144), V("pj"), 0.5)
     for nm in ("va", "vb"):
         tt(V(nm, 16, 144), IND(V("raw"), L("RAW")), V("cj"), A.mult)
     act(V("flg"), IND(V("va", 16, 144), L("REV")))
@@ -508,18 +517,21 @@ def rank_program(g, core, T, topo):
         for c in (0, 64):
             tt(V("bi", c, c + 64), IND(V("b8"), V("ptr", 128 + c // 16, 132 + c // 16)), V(cur, c + 16, c + 80), A.max)
         ts(V("bi", 128, 256), V("bi", 0, 128), 1023, A.bitwise_and)
-        act(V("xb", 0, 128), IND(V("bi", 128, 256), L("REV")), bias=-8.0)
+        act(V("bj", 0, 128), IND(V(cur, 16, 144), L("REV")))
+        ts(V("bj", 128, 256), V("bj", 0, 128), 1023, A.bitwise_and)
+        X = lambda k, c0, c1, st=1: V("xb" if k else "bj", 128 * max(k, 1) + c0, 128 * max(k, 1) + c1, st)
         for k in range(6):
-            act(V("xb", 128 * k + 128, 128 * k + 256, 2), V("xb", 128 * k, 128 * k + 64))
-            act(V("xb", 128 * k + 129, 128 * k + 256, 2), V("xb", 128 * k + 64, 128 * k + 128))
+            act(X(k + 1, 0, 128, 2), X(k, 0, 64), bias=None if k else -8.0)
+            act(X(k + 1, 1, 128, 2), X(k, 64, 128), bias=None if k else -8.0)
         for k in range(7):
-            act(V("xg", 64 * k, 64 * k + 64), IND(V("xb", 128 * k + 64, 128 * k + 128), L("TWICE", 4)))
-        act(V("xg", 448, 576), IND(V("xb", 0, 128), L("TWICE")))
+            act(V("xg", 64 * k, 64 * k + 64), IND(X(k, 64, 128), L("TWICE", 4)), bias=None if k else -8.0)
+        act(V("xg", 448, 576), IND(X(0, 0, 128), L("TWICE")), bias=-8.0)
         act(V("xg", 576, 704), IND(V("bi", 128, 256), L("PERM2")), bias=-8.0)
         act(V("xg", 704, 832), IND(V("bi", 128, 256), L("TWICE")), bias=-8.0)
-        for c in range(0, 832, 128):
-            tr(V("xh", c, min(c + 128, 832)), V("xg", c, min(c + 128, 832)), 0.5)
-        act(V("sh", 0, 32), IND(V("xh", 0, 512), L("SA")), bias=8.0)
+        for (c0, c1) in TUNE["xh"]:
+            tr(V("xh", c0, c1), V("xg", c0, c1), 0.5)
+        for k in range(7):
+            act(V("sh", 4 * k, 4 * k + 4), V("xh", 65 * k, 64 * k + 64, 16), bias=8.0)
         act(V("sh", 32, 40), V("xh", 448 + 7, 576, 16), bias=8.0)
         act(V("sh", 40, 56), V("xh", 576 + 8, 832, 16), bias=8.0)
 
@@ -527,9 +539,9 @@ def rank_program(g, core, T, topo):
         first, last = r == 0, r == 3
         if not last:
             act(V("d1", 1, 128, 4), V("nw", VAL, 128, 4), scale=-1.0)
-            act(V("d1", 2, 128, 4), V("nw", VAL, 128, 4))
+            act(V("d1", 3, 128, 4), V("nw", VAL, 128, 4))
         if first:
-            cur, old = by_steps("va", "vb", "vc", "vd", ((0, 128),))
+            cur, old = by_steps("va", "vb", "vc", "vd", TUNE["first"])
             c0 = 16
         else:
             cur, old, c0 = "sa", "sb", 8
@@ -561,7 +573,8 @@ def rank_program(g, core, T, topo):
         if first:
             pointer("prm", 9, C9)
             later_lists()
-        tt(V("vi", 16, 144), IND(V("w9"), V("ptr", 144, 152) if first else V("sh", 48, 56) if last else V("sh", 40, 48)), V("prm", 16, 144), A.max)
+        lst, l0 = ("ptr", 144) if first else ("sh", 48 if last else 40)
+        tt(V("vi", 16, 144), IND(V("w9"), V(lst, l0, l0 + 8)), V("prm", 16, 144), A.max)
         both("vi", "ti")
         ts(V("yy"), IND(V("ti"), L("FS", 3)), 4095, A.bitwise_and)
         for a in range(4):
@@ -596,7 +609,7 @@ def rank_program(g, core, T, topo):
         tr(V("kbt", 0, 64), V("kb", 0, 64), 0.5)
         tr(V("kbt", 64, 128), V("kb", 16, 80), 0.5)
         tt(V("fs%d" % r), V("kbt", 0, 128, 4), V("kbt", 1, 128, 4), A.add)
-        send(dst, V("fl%d" % r), V("fs%d" % r), "af%d" % r, TUNE["lat"] + (0.0 if r else 0.8))
+        send(dst, V("fl%d" % r), V("fs%d" % r), "af%d" % r, TUNE["lat"] + (0.0 if r else 1.2), 1 if r else 2)
         for i, (c0, c1) in enumerate(PIECES):
             ts(V("rows", c0, c1), V("ps", 512 * i, 512 * i + c1 - c0), 0.0, A.is_gt, CW, A.mult)
         for b in range(4):
@@ -617,7 +630,9 @@ def rank_program(g, core, T, topo):
             cp(V("ixu"), V("xt"))
         act(V("op2"), IND(V("rows"), V("ol", 4, 12)))
         tr(V("opt"), V("op2"), 0.5)
-        tt(V("sm"), V("opt", 0, 128, 2), V("opt", 1, 128, 2), A.add)
+        for c in range(2):
+            tt(V("sm", c, 64, 2), V("opt", 64 * c, 64 * c + 64, 2), V("opt", 64 * c + 1, 64 * c + 64, 2), A.add)
+        tr(V("smr"), V("sm"), 0.5)
         early(1.0)
 
     def choose(r):
@@ -627,10 +642,10 @@ def rank_program(g, core, T, topo):
         for d in (1, -1, 2, -2, 3, -3):
             e0, e1 = max(0, -d), 32 - max(0, d)
             tt(V("tab", 8 * e0 + 6 + d, 8 * e1 + d, 8), V("tab", 8 * e0 + 6, 8 * e1, 8), V("tab", 8 * (e0 + d) + 6, 8 * (e1 + d), 8), A.add)
-        act(V("fin", 0, 64, 2), IND(V(fl), L("FIN")), ext="af%d" % r)
+        act(V("fin"), IND(V(fl), L("FIN")), ext="af%d" % r)
         tr(V("fw", 0, 64), V("fin"), 0.5)
-        for k in range(1, 9):
-            act(V("fw", 64 * k, 64 * k + 64), V("fw", 0, 64))
+        for (c0, c1) in ((64, 128), (128, 256), (256, 512), (512, 576)):
+            act(V("fw", c0, c1), V("fw", 0, c1 - c0))
         hq, hs = "hq%d" % r, "hs%d" % r
         for b in range(4):
             mm(V("ps", 2048 + 512 * b, 2176 + 512 * b), V("ebq", 128 * b, 128 * b + 128), V("ebs", 128 * b, 128 * b + 128),
@@ -638,26 +653,24 @@ def rank_program(g, core, T, topo):
         for b in range(4):
             act(V("pool", PW * b + 16 + D0 + K * r, PW * b + 16 + D0 + K * r + K), V("ps", 2048 + 512 * b, 2048 + 512 * b + K))
             early(1.5)
-        tie = sum((3 - t) * 64 ** (3 - t) for t in range(4)) / 8.0
+        ones = 64.0 * 0x1111
         for (c0, c1, eng) in LOOK:
             w, o = IND(V("tab"), V("ixu", c0, c1)), V("ac", 16 * c0, 16 * c1)
             if eng == "v":
-                ts(o, w, 4.0, A.mult, tie, A.add)
+                ts(o, w, -64.0, A.mult, ones, A.add)
             else:
-                act(o, w, scale=4.0, bias=tie)
+                act(o, w, scale=-64.0, bias=ones)
             scan(V("ci", 16 * c0, 16 * c1), V("seg8", 16 * c0, 16 * c1), o, 0.0, A.mult, A.add)
         tr(V("yt"), V("ci", 7, 512, 8))
-        act(V("yi", 0, 256, 4), V("yt"), scale=64.0 ** -3, bias=-0.28)
-        for t in range(1, 4):
-            ts(V("yi", t, 256, 4), V("yt"), 6 * (3 - t), A.logical_shift_right, 63, A.bitwise_and)
-        scan(V("sc"), V("yi"), V("lane"), 0.0, A.max, A.add)
-        ts(V("ku"), V("sc", 63, 256, 64), -16.0, A.mult, -449.0, A.add)
-        cp(V("fg"), IND(V("fw"), V("ku")))
-        tr(V("ft"), V("fg"), 0.5)
-        f, kc = V("ft", 0, 64, 2), V("ft", 1, 64, 2)
-        tt(V("d1", 0, 128, 4), kc, V("jc", 32 * r, 32 * r + 32), A.add)
-        tt(V("d0", 1, 128, 4), f, V("sm", 0, 32), A.not_equal)
-        tt(V("d0", 2, 128, 4), f, V("sm", 32, 64), A.not_equal)
+        for t in range(4):
+            ts(V("yi", t, 256, 4), V("yt"), 4 * (3 - t), A.logical_shift_right, 15 << 6, A.bitwise_and)
+        for c in range(4):
+            scan(V("sc", c, 256, 4), V("yi", 64 * c, 64 * c + 64), V("lane"), 1000.0, A.min, A.add)
+        ku = V("sc", 252, 256)
+        tt(V("fg"), IND(V("fk"), ku), V("jc", 64 * r + 64, 64 * r + 128), A.add)
+        tt(V("ne"), IND(V("fw"), ku), V("smr"), A.not_equal)
+        tr(V("d1", 0, 128, 2), V("fg"))
+        tr(V("d0", 1, 128, 2), V("ne"), 0.5)
         scan(V("nw"), V("d0"), V("d1"), 0.0, A.mult, A.add)
 
     for r in range(3):
@@ -667,10 +680,11 @@ def rank_program(g, core, T, topo):
     inherit(3)
     pieces(3, GATH_LAST, PIECES_LAST, "vq", "vs")
     for i, (c0, c1) in enumerate(PIECES_LAST):
-        ahead = TUNE["out"] * (len(PIECES_LAST) - 1 - i)
+        (act if TUNE["yo"][i] == "a" else cp)(V("yo", c0, c1), V("ps", 512 * i, 512 * i + c1 - c0))
+    for i, (c0, c1) in enumerate(STORES):
+        ahead = TUNE["out"] * (len(STORES) - 1 - i)
         dma("s", T.oc[:, 4 * c0:4 * c1], u8(V("eq", c0, c1)), "out", 1.1)
         ops[-1].update(early=ahead + TUNE["out"] / 2, move=0.16 + 0.0013 * (c1 - c0))
-        (act if TUNE["yo"][i] == "a" else cp)(V("yo", c0, c1), V("ps", 512 * i, 512 * i + c1 - c0))
         dma("s", T.y[:, c0:c1], V("yo", c0, c1), "out", 1.1)
         ops[-1].update(early=ahead, move=0.16 + 0.0013 * (c1 - c0))
     for k in range(4):
@@ -694,6 +708,7 @@ def rank_program(g, core, T, topo):
                     dep.update(group[ops[q]["sem"]] if ops[q]["dma"] else [q])
         o["dep"] = dep
         o["pre"] = dep | set(arrive[o["ext"]] if o["ext"] else [])
+        o["behind"] = o.get("behind", [])
         for f in o["r"]:
             met.setdefault(f[0], []).append((f, False, o["id"]))
         for f in o["w"]:
@@ -715,10 +730,12 @@ def rank_program(g, core, T, topo):
             if back:
                 t = max([start[q] + ops[q]["cost"] + HOP for q in o["succ"]] + [0.0]) + o["lat"] + o["early"]
             else:
-                t = max([start[q] + ops[q]["cost"] + ops[q]["lat"] + HOP for q in o["pre"]] + [0.0])
+                t = max([start[q] + ops[q]["cost"] + ops[q]["lat"] + HOP for q in o["pre"]] + [0.4 + 0.061 * len(o["behind"]) if o["behind"] else 0.0])
             found = []
             for (e, c) in ([(e, w[1]) for e, w in o["ways"].items()] if "ways" in o and not back else [(o["eng"], o["cost"])]):
-                tk, k, s = taken[e], 0, t
+                tk, k, s = taken[e], len(taken[e]), t
+                while k and tk[k - 1][1] > t:
+                    k -= 1
                 while k < len(tk) and tk[k][0] < s + c - 1e-9:
                     s = max(s, tk[k][1])
                     k += 1
@@ -752,14 +769,24 @@ def rank_program(g, core, T, topo):
             if best == max(end.values()):
                 kept = urgent
             urgent = {q: -late[q] - ops[q]["cost"] for q in late}
-        rng = np.random.default_rng(1)
-        for _ in range(TUNE["tries"]):
-            lo = min(kept.values()) + rng.random() * best
-            urgent = {q: kept[q] + (float(rng.normal()) * TUNE["sd"] if lo <= kept[q] < lo + TUNE["span"] else 0.0) for q in kept}
+        def replay(order, k, picks, hop):
+            free, start, done = {e: 0.0 for e in "vapts"}, {}, {}
+            for q in order:
+                o = ops[q]
+                start[q] = max([done[z] + hop for z in o["pre"]] + [free[o["eng"]]])
+                free[o["eng"]] = start[q] + o["cost"] * (1.0 if o["dma"] else k * picks if o["picks"] else k)
+                done[q] = free[o["eng"]] + o["lat"]
+            return max(ends(start).values()) / (k + 2)
+
+        rng, whole, best = np.random.default_rng(1), best, None
+        for i in range(TUNE["tries"] + 1):
+            lo, sd, span = min(kept.values()) + rng.random() * whole, TUNE["sd"][i % 3], TUNE["span"][i // 3 % 3]
+            urgent = {q: kept[q] + (float(rng.normal()) * sd if i and lo <= kept[q] < lo + span else 0.0) for q in kept}
             start = place(urgent, False)
-            end = max(ends(start).values())
-            if end <= best:
-                best, kept, PLAN["order"] = end, urgent, [(q, ops[q]["eng"]) for q in sorted(start, key=lambda q: (start[q], q))]
+            order = sorted(start, key=lambda q: (start[q], q))
+            end = sum(replay(order, *case) for case in TUNE["cases"])
+            if best is None or end <= best:
+                best, kept, PLAN["order"] = end, urgent, [(q, ops[q]["eng"]) for q in order]
         PLAN["time"] = best
     order = []
     for (q, e) in PLAN["order"]:

@@ -5,16 +5,17 @@ A = AluOpType
 F = ActivationFunctionType
 DIST = [1, 2, 4]
 C, K = 512, 64
-D0 = 4 * C - 3
-PW = 2256
+X0 = 3 * K
+DB = X0 + C
+PW = DB + 3 * K
 F32, BF, I32, U16, U8, MX = "float32", "bfloat16", "int32", "uint16", "uint8", "float8_e4m3fn_x4"
-GATH = [(14, 22, "vvaa"), (22, 32, "xxxx"), (0, 6, "xxxx"), (6, 14, "xxxx")]
-PIECES = [(0, 128), (128, 384), (384, 512)]
-GATH_LAST = [(0, 16, "vvaa"), (16, 24, "xxxx"), (24, 32, "xxxx")]
+GATH = [(0, 4, 0, "vvaa"), (4, 14, 64, "xxxx"), (14, 24, 224, "xxxx"), (24, 32, 384, "xxxx")]
+PIECES = [(-64, 64), (64, 384), (384, 512)]
+GATH_LAST = [(0, 8, 0, "vvaa"), (16, 24, 128, "xxxx"), (8, 16, 256, "xxxx"), (24, 32, 384, "xxxx")]
 PIECES_LAST = [(0, 256), (256, 384), (384, 512)]
 STORES = [(0, 256), (256, 512)]
 LOOK = [(0, 14, "v"), (14, 24, "a"), (24, 32, "a")]
-U16T = True
+FLW = 4
 
 
 def _sb(n, d):
@@ -22,28 +23,28 @@ def _sb(n, d):
 
 
 SCRATCH = {
-    "parq": _sb(8, I32), "raw": _sb(128, I32), "ut": _sb(512, BF), "vt": _sb(512, BF),
+    "parq": _sb(32, I32), "raw": _sb(16 * FLW, I32), "ut": _sb(512, BF), "vt": _sb(512, BF),
     "wq": _sb(512, MX), "wsc": _sb(512, U8), "uq": _sb(128, MX), "us": _sb(128, U8), "urq": _sb(128, MX), "urs": _sb(128, U8),
     "ukq": _sb(128, MX), "uks": _sb(128, U8),
     "vq": _sb(128, MX), "vs": _sb(128, U8), "eb": _sb(516, BF), "ebq": _sb(512, MX), "ebs": _sb(512, U8),
-    "pi": _sb(2, I32), "fi": _sb(24, I32), "ff": _sb(24, F32), "col": _sb(192, F32), "row": _sb(160, F32), "cnt": _sb(128, F32),
-    "lu": _sb(112, U16), "cj": _sb(128, F32), "jc": _sb(256, F32),
-    "vcon": _sb(128, F32), "horn": _sb(128, F32), "lane": _sb(64, F32), "seg4": _sb(128, BF), "seg8": _sb(520, F32),
-    "ptr": _sb(176, U16), "paru": _sb(8, U16), "nt": _sb(640, F32), "r2": _sb(256, F32), "r3": _sb(256, F32), "ol": _sb(16, U16),
-    "va": _sb(160, F32), "vb": _sb(160, F32), "vc": _sb(160, F32), "vd": _sb(160, F32), "w8": _sb(144, F32), "w9": _sb(264, F32),
-    "prm": _sb(160, F32), "sa": _sb(136, F32), "sb": _sb(136, F32), "pj": _sb(128, BF), "pr": _sb(480, BF), "pt": _sb(576, BF),
-    "wt": _sb(112, F32), "gt": _sb(512, F32), "th": _sb(384, F32), "bf": _sb(256, F32), "ba": _sb(160, F32), "bb": _sb(160, F32),
-    "bc": _sb(160, F32), "b8": _sb(144, F32), "bi": _sb(256, I32), "bj": _sb(256, I32), "xb": _sb(896, BF), "xg": _sb(832, BF), "xh": _sb(832, BF),
-    "sh": _sb(56, U16),
+    "pi": _sb(2, I32), "fi": _sb(48, I32), "col": _sb(128, F32), "row": _sb(256, F32), "cnt": _sb(128, F32),
+    "lu": _sb(128, U16), "cj": _sb(128, F32), "jc": _sb(128, F32), "pjc": _sb(16, F32), "plw": _sb(264, F32),
+    "vcon": _sb(128, F32), "horn": _sb(128, F32), "lane": _sb(128, F32), "seg4": _sb(128, BF), "seg8": _sb(520, F32),
+    "ptr": _sb(176, U16), "paru": _sb(16, U16), "nt": _sb(768, F32), "r2": _sb(256, F32), "r3": _sb(256, F32), "ol": _sb(16, U16),
+    "va": _sb(96, F32), "vb": _sb(96, F32), "vc": _sb(96, F32), "vd": _sb(96, F32), "v7": _sb(96, F32), "v8": _sb(208, F32),
+    "w7": _sb(72, F32), "ww": _sb(264, F32), "tq": _sb(128, F32),
+    "prm": _sb(160, F32), "sa": _sb(72, F32), "sb": _sb(72, F32), "pj": _sb(64, F32), "pr": _sb(288, F32), "pt": _sb(320, F32),
+    "wt": _sb(176, F32), "gt": _sb(80, F32), "th": _sb(256, F32), "ba": _sb(80, F32), "bb": _sb(80, F32), "bc": _sb(80, F32),
+    "r7": _sb(128, F32), "w2": _sb(264, F32), "xg": _sb(896, BF), "xh": _sb(1728, BF), "sh": _sb(64, U16),
     "vi": _sb(160, I32), "ti": _sb(288, I32), "tb": _sb(288, F32), "tc": _sb(288, F32),
-    "yy": _sb(48, I32), "el": _sb(32, U16), "nw": _sb(128, F32), "flg": _sb(128, F32),
-    "pool": _sb(4 * PW, BF), "et": _sb(2048, BF), "eq": _sb(512, MX), "es": _sb(512, U8),
+    "yy": _sb(96, I32), "el": _sb(32, U16), "nw": _sb(264, F32), "flg": _sb(64, F32),
+    "xt": _sb(4 * C, BF), "pool": _sb(4 * PW, BF), "et": _sb(4 * 576, BF), "eq": _sb(576, MX), "es": _sb(576, U8),
     "ht": _sb(512, BF),
     "kb": _sb(80, BF), "kbt": _sb(128, BF), "rows": _sb(512, BF), "op": _sb(128, BF), "op2": _sb(128, BF), "opt": _sb(128, BF),
-    "x0": _sb(128, BF), "xs": _sb(128, U16 if U16T else BF), "xt": _sb(32, BF), "sm": _sb(64, BF), "ixu": _sb(32, U16),
+    "x0": _sb(128, BF), "xs": _sb(128, U16), "sm": _sb(128, BF), "ixu": _sb(32, U16),
     "xe": _sb(128, F32), "tab": _sb(264, F32), "ac": _sb(512, F32), "ci": _sb(512, I32), "yt": _sb(64, I32), "yi": _sb(256, I32),
-    "sc": _sb(256, U16), "fin": _sb(64, BF), "fw": _sb(576, BF), "fk": _sb(576, BF), "fg": _sb(64, F32), "ne": _sb(64, BF), "smr": _sb(64, BF),
-    "d0": _sb(128, BF), "d1": _sb(128, F32), "yo": _sb(512, F32),
+    "sc": _sb(256, U16), "fin": _sb(64, BF), "fwt": _sb(64, BF), "fw": _sb(576, BF), "fk": _sb(576, BF), "smr": _sb(128, BF),
+    "d0": _sb(256, BF), "d1": _sb(256, F32), "yo": _sb(512, F32),
     "ps": ("psum", [128, 4096], F32),
 }
 for _r in range(3):
@@ -56,11 +57,11 @@ SEMAPHORES = (["sv", "sa", "sp", "st", "l_par", "l_fl", "l_u", "l_x", "l_w", "l_
               + ["af%d" % r for r in range(3)] + ["ah%d" % r for r in range(3)])
 ENG_SEM = {"v": "sv", "a": "sa", "p": "sp", "t": "st"}
 CYC, HOP = 0.00105, 0.22
-VAL, PTR = 3, 1
+PTR = 1
 
 
-def seen(h, c, lane):
-    return 32 * (c // 2) + lane if c % 2 == h else 128 + 32 * (c // 2 + 1 - h) + lane
+def seen(h, c, lane, n):
+    return 32 * (c // 2) + lane if c % 2 == h else n + 32 * (c // 2 + 1 - h) + lane
 
 
 def slot(h, t):
@@ -68,30 +69,45 @@ def slot(h, t):
 
 
 def rev(x):
-    return sum((x >> b & 1) << (6 - b) for b in range(7))
+    return sum((x >> b & 1) << (5 - b) for b in range(6))
 
 
 def parents(m, e, p):
     if m < 4:
-        return rev(32 * (2 * (m % 2) + p // 8) + 16 * (m // 2) + 2 * (p % 8) + e)
-    return rev(32 * (2 * ((m - 4) // 2) + e) + 16 * (m % 2) + p)
+        return 64 * (p // 8) + rev(16 * (2 * (m % 2) + m // 2) + 2 * (p % 8) + e)
+    return 64 * e + rev(16 * (m - 4) + p)
+
+
+def spread(a, h, p, c, last):
+    if last:
+        bm, run = p % 4, 4 * (c // 2 if c < 4 else c - 4) + p // 4
+    else:
+        bm, run = (c, p // 2) if c < 4 else (2 * (c - 4) + p // 8, p % 8)
+    return seen(h, run, 16 * (bm % 2) + 2 * (2 * (2 * (bm // 2) + (a % 2 if c < 4 else 1 - a % 2)) + h), 128)
 
 
 LISTS = [
-    ("PJ", 1, lambda a, h, p, c: 2 * (p // 4) + h),
-    ("RAW", 8, lambda a, h, p, c: 8 * p + c),
-    ("SEL", 1, lambda a, h, p, c: seen(h, p % 8, PTR)),
-    ("PERM", 8, lambda a, h, p, c: 8 * p + (c if a % 2 else 7 - c)),
-    ("FS", 4, lambda a, h, p, c: seen(h, p // 2, 4 * (2 * (2 * (p % 2) + (a % 2 if c < 2 else 1 - a % 2)) + h) + VAL)),
+    ("PB", 1, lambda a, h, p, c: 16 * h + 4 * a + p % 4),
+    ("PJ", 1, lambda a, h, p, c: 16 * (p // 4 % 2) + 4 * a + 2 * (p // 8) + h),
+    ("RAW", 4, lambda a, h, p, c: FLW * p + (16 * h + 4 * a) % FLW + c),
+    ("SEL", 1, lambda a, h, p, c: seen(h, p % 4, 16 * h + PTR, 64)),
+    ("PERM", 8, lambda a, h, p, c: 16 + 64 * (1 + (1 - h) - p // 8) + 8 * (p % 8) + c),
+    ("SELX", 1, lambda a, h, p, c: seen(h, p % 8, 16 * (1 - h) + PTR, 128)),
+    ("FS", 6, lambda a, h, p, c: spread(a, h, p, c, False)),
     ("UK", 8, lambda a, h, p, c: 64 * (c % 2) + 16 * (p // 4) + p % 4),
     ("UR", 8, lambda a, h, p, c: 16 * (p // 2) + p % 2),
-    ("R2", 16, lambda a, h, p, c: parents(c // 2, c % 2, p) + h * (128 + 128 * a)),
-    ("REV", 8, lambda a, h, p, c: rev(16 * c + p)),
-    ("XE", 8, lambda a, h, p, c: 8 * slot(h, p % 4) + c),
+    ("PU", 1, lambda a, h, p, c: 16 * (p // 4 % 2) + 4 * a + p % 4),
+    ("R2", 16, lambda a, h, p, c: parents(c // 2, c % 2, p) + 128 * h),
+    ("REV", 4, lambda a, h, p, c: rev(16 * c + p)),
+    ("XE", 8, lambda a, h, p, c: 8 * (p % 4) + c),
     ("FIN", 4, lambda a, h, p, c: 8 * slot(h, 2 * (c // 2) + h) + p // 2),
-    ("PERMR", 8, lambda a, h, p, c: rev(8 * p + (c if a % 2 else 7 - c))),
-    ("TWICE", 8, lambda a, h, p, c: 32 * (c // 2) + 16 * h + p),
-    ("PERM2", 8, lambda a, h, p, c: 8 * p + (2 * (c // 2) + h if a % 2 else 7 - 2 * (c // 2) - h)),
+    ("KP", 4, lambda a, h, p, c: 32 * (c % 2) + 16 * (p // 8) + 8 * (c // 2) + p % 8),
+    ("LV", 12, None),
+    ("SELV", 1, lambda a, h, p, c: seen(h, p, 16 * h + p // 2, 192)),
+    ("SELW", 1, lambda a, h, p, c: seen(h, p, 16 * h, 256)),
+    ("NK", 8, lambda a, h, p, c: 16 * (p % 8) + 8 * (c // 4) + 2 * (c % 4) + p // 8),
+    ("FSL", 6, lambda a, h, p, c: spread(a, h, p, c, True)),
+    ("REVF", 4, lambda a, h, p, c: 11 + 4 * rev(16 * c + p)),
 ]
 
 
@@ -99,27 +115,62 @@ def table(n, f):
     return np.array([[f(P // 32, P // 16 % 2, P % 16, c) for c in range(n)] for P in range(128)], dtype=np.int64)
 
 
-def terms(vec):
-    c = [int(z) for z in vec]
+_P = np.arange(128.0)
+FEATURES = {"P": _P}
+for _s in range(7):
+    for _w in range(1, 6):
+        if _s + _w <= (7 if _s > 4 else 5) and (_s + _w <= 4 or _s in (0, 4, 5, 6)):
+            FEATURES[(_s, (1 << _w) - 1)] = _P // (1 << _s) % (1 << _w)
+for _s in range(3):
+    FEATURES[("x", _s)] = (_P // 16 + _P // (1 << _s)) % 2
+
+
+def bits(vec):
+    c = [float(z) for z in vec]
     for b in range(7):
         for P in range(128):
             if P >> b & 1:
                 c[P] -= c[P ^ (1 << b)]
-    out, b = [], 0
-    while b < 7:
-        k, e = c[1 << b], b + 1
-        while k and e < 7 and c[1 << e] == k << (e - b):
-            e += 1
-        f = b + 1
-        while k and e == b + 1 and f < 7 and c[1 << f] << (f - b) == k:
-            f += 1
-        if f > b + 2:
-            out.append(((b, f, "backwards"), c[1 << (f - 1)]))
-            e = f
-        elif k:
-            out.append(((b, (1 << (e - b)) - 1), k))
-        b = e
-    return c[0], out + [(m, c[m]) for m in range(1, 128) if m & (m - 1) and c[m]]
+    return {m: c[m] for m in range(1, 128) if c[m]}
+
+
+def terms(vec, known, have, reuse, free):
+    form = {k: bits(v) for k, v in known.items()}
+    found = []
+
+    def search(t, tm, depth):
+        if not t:
+            found.append(tm)
+        elif depth:
+            for m in {min(t), max(t)} if len(tm) < 2 else (max(t),):
+                for k, f in form.items():
+                    if m in f and (16 * t[m] / f[m]) % 1 == 0 and all(k != z[0] for z in tm):
+                        q, u = t[m] / f[m], dict(t)
+                        for j in f:
+                            u[j] = u.get(j, 0.0) - q * f[j]
+                            if not u[j]:
+                                del u[j]
+                        if len(u) < len(t) + (0 if tm else 1) and len(u) <= 5 * (depth - 1):
+                            search(u, tm + [(k, q)], depth - 1)
+
+    depth = 0
+    while not found:
+        search(bits(vec), [], depth)
+        depth += 1
+    if depth < 4:
+        search(bits(vec), [], depth)
+    best = None
+    for tm in found:
+        c0 = vec[0] - sum(q * known[k][0] for k, q in tm)
+        more = set(k for k, q in tm if k not in have) | set(z for k, q in tm if k[0] == "x" and k not in have for z in ((4, 1), (k[1], 1)) if z not in have)
+        ways = [(len(tm), c0, None, tm)]
+        for k, q in tm:
+            if q == 1 and k[0] in ("col", "x") and k in have and (c0 == 0 or free) and (reuse or len(tm) > 1):
+                ways.append((len(tm) - 1, 0, k, [z for z in tm if z[0] != k]))
+        for w in ways:
+            if best is None or w[0] + len(more) < best[0]:
+                best = (w[0] + len(more),) + w[1:]
+    return best[1:]
 
 
 def pattern(r):
@@ -144,10 +195,11 @@ def product(d):
     return (sc, r) if (sc[:, None] * r[None, :] == d).all() and pattern(r) is not None else None
 
 
-FIELDS = [(2, 3), (4, 1), (5, 3), (0, 15), (0, 1), (1, 1), (1, 3), (5, 1), (6, 1), (2, 1), (3, 1), (1, 7), (0, 3), (0, 7), (0, 31)]
-FIRST = 8
 PLAN = {}
-TUNE = {"bb": 0.0, "bs": 1.0, "parts": ((0, 128),), "out": 1.0, "yo": "aav", "lat": 0.9, "fl": 1.8, "bias": 0.03, "it": 10, "first": ((0, 128),), "tie": False, "xh": ((0, 64), (64, 192), (192, 320), (320, 448), (448, 576), (576, 704), (704, 832)), "cases": ((0.81, 1.0, 0.22), (1.05, 1.0, 0.2), (1.16, 1.15, 0.24), (1.18, 1.2, 0.24)), "act": 0.02, "tries": 2400, "sd": (0.2, 0.4, 0.8), "span": (1.0, 2.0, 3.0)}
+TUNE = {"xp": 256, "far": 7, "steps": 7, "runs": ((32, 64),), "gath": GATH, "pieces": PIECES, "gath3": GATH_LAST, "pieces3": PIECES_LAST,
+        "look": LOOK, "bb": 0.0, "bs": 1.0, "out": 1.0, "yo": "aav", "lat": 0.9, "fl": 2.2, "bias": 0.03, "it": 10,
+        "cases": ((0.81, 1.0, 0.22), (1.05, 1.0, 0.2), (1.16, 1.15, 0.24), (1.18, 1.2, 0.24)), "tries": 2400, "sd": (0.2, 0.4, 0.8),
+        "span": (1.0, 2.0, 3.0)}
 
 
 def rank_program(g, core, T, topo):
@@ -241,6 +293,7 @@ def rank_program(g, core, T, topo):
 
     def fill(o, c, flt=True):
         iota(o, [[0, o[2]]], c, 0, flt)
+        ops[-1]["ways"] = {"p": (ops[-1]["fn"], ops[-1]["cost"]), "v": (lambda: g.vector.memset(o[0], float(c) if flt else c), cc(o, rate(o)))}
 
     def quant(q, s, i):
         op("v", lambda: g.vector.quantize_mx(q[0], s[0], i[0]), [q, s], [i], 0.012 + 0.265 * CYC * i[2])
@@ -264,70 +317,58 @@ def rank_program(g, core, T, topo):
         count[rsem] = count.get(rsem, 0) + n
         op("p", lambda: g.remote_dma(o[0], i[0], T.sem[rsem], T.sem["sent"], pid, rid, m), [], [i], 0.15, lat, sem="sent", inc=-n, gives=rsem)
 
-    op("v", lambda: g.vector.memset(T.raw[:, :], 0), [V("raw")], [], 0.13)
-    for G in range(8):
-        dma("s" if G % 2 else "a", V("parq", 0, 8, 1, 16 * G, 16 * G + 16), T.par[:, 8 * (G // 2):8 * (G // 2) + 8], "l_par")
+    op("v", lambda: g.vector.memset(T.raw[:, :], 1), [V("raw")], [], cc(V("raw")))
+    for H in range(8):
+        dma("s" if H % 2 else "a", V("parq", 0, 32, 1, 16 * H, 16 * H + 16), T.par[:, :], "l_par")
         early(5.0)
-    for a in range(4):
-        dma("s" if a % 2 else "a", (T.raw[32 * a + VAL:32 * a + 32:4, :], [("raw", 32 * a + VAL, 32 * a + 32, 0, 128, 1)]), T.fl[:, 8 * a:8 * a + 8], "l_fl", TUNE["fl"])
-    for a in range(4):
-        dma("s" if a % 2 else "a", V("raw", 0, 128, 1, 32 * a + PTR, 32 * a + PTR + 1), T.par[:, 8 * a:8 * a + 8], "l_fl", TUNE["fl"])
-    loads = ([(V("ut"), T.u[:, :], "l_u", 5.0)] + [(V("pool", PW * t + 16 - t, PW * t + 16 - t + 4 * C), T.x[:, :], "l_x", 10.0) for t in range(4)]
-             + [(u8(V("wq")), T.wc[:, :], "l_w", 11.0), (V("wsc"), T.ws[:, :], "l_w", 11.0), (V("vt"), T.v[:, :], "l_v", 14.0)])
+    for H in range(8):
+        c0 = (16 * (H % 2) + 4 * (H // 2)) // FLW * FLW
+        dma("s" if H % 2 else "a", (T.raw[16 * H:16 * H + 16:2, :], [("raw", 16 * H, 16 * H + 16, 0, 16 * FLW, 1)]), T.fl[:, c0:c0 + FLW], "l_fl", TUNE["fl"])
+    loads = [(V("xt"), T.x[:, :], "l_x", 4.0), (V("ut"), T.u[:, :], "l_u", 5.0), (u8(V("wq")), T.wc[:, :], "l_w", 7.0),
+             (V("wsc"), T.ws[:, :], "l_w", 7.0), (V("vt"), T.v[:, :], "l_v", 8.0)]
     for (o, i, sem, lat) in loads:
-        dma("s", o, i, sem, lat)
+        dma("s", o, i, sem, lat, V("parq"))
         ops[-1]["behind"] = [q["id"] for q in ops[:-1] if q["eng"] == "s"]
 
     iota(V("pi", 0, 1), [[0, 1]], 0, 1, False)
     iota(V("cnt"), [[1, 128]], 0, 0)
-    made, used = {}, {"col": 0, "row": 0}
-    for (c0, c1) in ((0, FIRST), (FIRST, len(FIELDS))):
-        for c in range(c0, c1):
-            ts(V("fi", c, c + 1), V("pi", 0, 1), FIELDS[c][0], A.logical_shift_right, FIELDS[c][1], A.bitwise_and)
-            made[FIELDS[c]] = V("ff", c, c + 1)
-        act(V("ff", c0, c1), V("fi", c0, c1))
-        early(20.0 if c0 else 0.0)
+    used, rows = {"col": 0, "row": 0, "fi": 0}, {}
+    have = {"P": V("pi", 0, 1)}
+    known_ = dict(FEATURES)
 
     def new(name, n=1):
         used[name] += n
         return V(name, used[name] - n, used[name])
 
     def feature(k):
-        if k not in made:
-            if isinstance(k, tuple):
-                less = feature((k[0], k[1] - 1, k[2]) if k[1] - k[0] > 2 else (k[0], 1))
-                made[k] = new("col")
-                act(made[k], less, scale=2.0, bias=feature((k[1] - 1, 1)))
+        if k not in have:
+            if k[0] == "x":
+                x, y = feature((4, 1)), feature((k[1], 1))
+                have[k] = new("col")
+                tt(have[k], x, y, A.not_equal)
             else:
-                low = k & -k
-                rest = k ^ low
-                o = made[k] = new("col")
-                act(o, feature(rest if rest & (rest - 1) else (rest.bit_length() - 1, 1)), scale=feature((low.bit_length() - 1, 1)))
-        return made[k]
+                have[k] = new("fi")
+                ts(have[k], have["P"], k[0], A.logical_shift_right, k[1], A.bitwise_and)
+        return have[k]
 
-    def whole(k):
-        return V("fi", FIELDS.index(k), FIELDS.index(k) + 1) if k in FIELDS else feature(k)
-
-    def chain(tm, c0, anew=False):
-        prev, key = float(c0), ("c", c0)
-        if c0 == 0 and len(tm) == 1 and tm[0][1] == 1 and not anew:
-            return feature(tm[0][0])
-        for (k, coef) in tm:
-            key = key + (k, coef)
-            if key not in made:
-                f = whole(k)
-                made[key] = new("col")
-                act(made[key], f, scale=float(coef), bias=prev)
-            prev = made[key]
-        return prev
+    def summed(vec, o=None, free=False):
+        key = ("sum", tuple(int(z) for z in vec), o is None, free)
+        if key not in PLAN:
+            PLAN[key] = terms(vec, known_, have, o is None, free)
+        c0, start, tm = PLAN[key]
+        prev, acc = (have[start], known_[start].copy()) if start else (float(c0), np.full(128, float(c0)))
+        for i, (k, coef) in enumerate(tm):
+            f, acc = feature(k), acc + coef * known_[k]
+            out = o if o is not None and i == len(tm) - 1 else new("col")
+            act(out, f, scale=float(coef), bias=prev)
+            if out is not o:
+                name = ("col", used["col"])
+                have[name], known_[name] = out, acc
+            prev = out
+        return prev, int(vec[0] - acc[0])
 
     def column(vec):
-        c0, tm = terms(vec)
-        if len(tm) < 3 or c0 == 0:
-            return chain(tm, c0)
-        o = new("col")
-        act(o, chain(tm, 0), bias=float(c0))
-        return o
+        return summed(vec)[0]
 
     def const(o, tb):
         c = 0
@@ -336,18 +377,19 @@ def rank_program(g, core, T, topo):
             while product(tb[:, c:e] - tb[:, c:c + 1]) is None:
                 e -= 1
             sc, r = product(tb[:, c:e] - tb[:, c:c + 1])
-            bias = tb[:, c]
             if e == c + 1:
-                row, sc, bias = V("cnt", 1, 2), sc * 0 + tb[0, c], bias - tb[0, c]
+                summed(tb[:, c], o(c, e))
             elif (r == np.arange(e - c)).all() or not sc.any():
-                row = V("cnt", 0, e - c)
+                act(o(c, e), V("cnt", 0, e - c), scale=column(sc), bias=column(tb[:, c]))
             else:
-                key = ("r",) + tuple(int(z) for z in r)
-                if key not in made:
-                    made[key] = new("row", e - c)
-                    iota(made[key], pattern(r), 0, 0)
-                row = made[key]
-            act(o(c, e), row, scale=column(sc), bias=column(bias))
+                same = (sc == sc[0]).all()
+                bias, c0 = summed(tb[:, c], None, True) if same else (column(tb[:, c]), 0)
+                r = r * sc[0] + c0 if same else r
+                key = tuple(int(z) for z in r)
+                if key not in rows:
+                    rows[key] = new("row", e - c)
+                    iota(rows[key], pattern(r), int(r[0]), 0)
+                act(o(c, e), rows[key], scale=1.0 if same else column(sc), bias=bias)
             c = e
 
     def colf(f):
@@ -356,60 +398,71 @@ def rank_program(g, core, T, topo):
     at, c0 = {}, 0
     for (name, n, f) in LISTS:
         at[name] = (c0, n)
-        if n == 1:
-            k0, tm = terms(table(1, f)[:, 0])
-            act(V("lu", c0, c0 + 1), whole(tm[0][0]), scale=float(tm[0][1]), bias=chain(tm[1:], k0, True))
-        else:
+        if f is not None:
             const(lambda c, e: V("lu", c0 + c, c0 + e), table(n, f))
         c0 += n + n % 2
 
     def L(name, n=None):
         return V("lu", at[name][0], at[name][0] + (n or at[name][1]))
 
-    act(V("cj"), V("cnt"), scale=4100.0, bias=colf(lambda a, h, p, c: 4100 * 128 * a + 4097))
-    act(V("cj"), V("cj"), scale=feature((1, 1)), bias=-1.0)
-    for nm in ("vb", "vc", "vd", "prm"):
-        fill(V(nm, 0, 16), -1000)
+    const(lambda c, e: V("pjc", c, e), table(16, lambda a, h, p, c: 16 - 64 * (4 * (c // 4 % 2) + a)))
+    CB = colf(lambda a, h, p, c: 16 - 64 * (4 * h + a))
+    cb = new("col")
+    act(cb, colf(lambda a, h, p, c: 4098 * 64 * (4 * h + a) + 4096 + X0 - 16), scale=colf(lambda a, h, p, c: 1 - p % 2), bias=CB)
+    act(V("cj", 0, 64), V("cnt", 0, 64), scale=colf(lambda a, h, p, c: 4097 * (1 - p % 2)), bias=cb)
+    for t in range(4):
+        fill(V("pool", PW * t, PW * t + X0), 0)
+        for c in range(0, C, TUNE["xp"]):
+            act(V("pool", PW * t + X0 + c, PW * t + X0 + c + TUNE["xp"]), V("xt", 4 * c + t, 4 * (c + TUNE["xp"]), 4))
     ms(V("pj"), 0.0)
+    pad = colf(lambda a, h, p, c: -1000 * (p % 2))
+    for (nm, n) in (("vb", 16), ("vc", 16), ("vd", 16), ("w7", 72), ("ww", 8)):
+        act(V(nm, 0, n), V("cnt", 0, n), scale=0.0, bias=pad)
     for k in range(3):
-        fill(V("pr", 160 * k, 160 * k + 16), 0)
-        fill(V("pr", 160 * k + 144, 160 * k + 160), 0)
-    CB = colf(lambda a, h, p, c: 16 - 128 * a)
-    C8, C9 = colf(lambda a, h, p, c: 136 - 128 * a), 8.0
+        fill(V("pr", 96 * k, 96 * k + 16), 0)
+        fill(V("pr", 96 * k + 80, 96 * k + 96), 0)
+    for nm in ("vb", "vc", "vd", "v7"):
+        fill(V(nm, 80, 96), 0)
+    for nm in ("v7", "v8", "prm"):
+        fill(V(nm, 0, 16), 0)
+    fill(V("prm", 144, 160), 0)
+    fill(V("v8", 144, 208), 8)
+    act(V("v8", 80, 144), V("cnt", 0, 64), scale=-1.0, bias=colf(lambda a, h, p, c: -64 * a))
+    C7, C8 = colf(lambda a, h, p, c: 72 - 64 * (4 * h + a) - 512 * (1 - a % 2)), colf(lambda a, h, p, c: 8 - 256 * h)
     CW = colf(lambda a, h, p, c: 2 - p % 2)
     CG = colf(lambda a, h, p, c: 16 * (p // 2) + 3)
-    const(lambda c, e: V("jc", 2 * c, 2 * e, 2), table(32, lambda a, h, p, c: 4096 * (128 * a + rev(32 * (c // 8) + 16 * h + p) + 1) + D0))
-    fill(V("jc", 1, 64, 2), 0)
-    tr(V("jc", 64, 128), V("jc", 0, 64))
-    even = colf(lambda a, h, p, c: 1 - p % 2)
-    for r in (1, 2):
-        act(V("jc", 64 * r + 64, 64 * r + 128), V("jc", 64, 128), bias=colf(lambda a, h, p, c: K * r * (1 - p % 2)))
-    iota(V("fin"), [[16, 2], [32, 2], [1, 16]], 0, 0)
-    act(V("fk", 0, 64), V("fin"), scale=even)
+    act(V("jc", 0, 64), IND(V("cnt", 0, 64), L("REV")))
+    act(V("jc", 64, 128), V("jc", 0, 64), scale=4096.0, bias=colf(lambda a, h, p, c: 4096 * (64 * (4 * h + a) + 1) + DB * h))
+    for u in range(2):
+        iota(V("fk", 32 * u, 32 * u + 32), [[16, 2], [32, 2], [1, 8]], 8 * u, 0)
     for (c0, c1) in ((64, 128), (128, 256), (256, 512), (512, 576)):
         act(V("fk", c0, c1), V("fk", 0, c1 - c0))
-    for nm in ("vc", "prm"):
-        fill(V(nm, 144, 160), 0)
-    for nm in ("w8", "w9"):
-        fill(V(nm), -1000)
-    for a in range(4):
-        iota(V("nt", 128 + 128 * a, 256 + 128 * a), [[1, 16], [32 if a % 2 else -32, 8]], (32 if a % 2 else 512) + 16 * (a // 2), 0)
-    iota(V("nt", 128, 640, 8), [[16, 2], [32, 2], [1, 16]], 0, 0)
+    for k in range(4):
+        iota(V("nt", 256 + 128 * k, 384 + 128 * k), [[32, 2], [1, 8], [64, 8]], 16 * (k % 2) + 8 * (k // 2), 0)
+    const(lambda c, e: V("nt", 128 + c, 128 + e), table(128, lambda a, h, p, c: 64 * (c % 8) + 32 * (a % 2) + 16 * (a // 2) + c // 8))
     fill(V("vi", 0, 16), 0, False)
     fill(V("vi", 144, 160), 0, False)
-    for nm in ("sa", "sb"):
+    for nm in ("sa", "sb", "nw"):
         fill(V(nm, 0, 8), 0)
     fill(V("ht", 256, 512), 0)
+    fill(V("et", 0, 256), 0)
+    fill(V("sm", 1, 128, 2), 0)
     iota(V("vcon"), [[0, 8], [1, 4], [0, 4]], 0, 0)
     fill(V("tab"), 0)
-    iota(V("d0", 0, 128, 2), [[0, 32], [1, 2]], 0, 0)
+    fill(V("d0", 0, 256, 4), 0)
+    fill(V("d0", 1, 256, 4), 1)
     fill(V("seg4"), 1)
     fill(V("seg4", 0, 128, 4), 0)
     fill(V("horn"), 16)
     fill(V("horn", 0, 128, 4), 0)
-    fill(V("lane"), -16)
-    fill(V("lane", 3, 64, 4), 47)
-    fill(V("lane", 63, 64), 63)
+    fill(V("lane"), -8)
+    for h in range(2):
+        key = [32 * (e // 32) + e // 4 % 8 + 8 * [slot(h, t) for t in range(4)].index(e % 4) for e in range(64)] + [0]
+        for s in range(4):
+            if key[s] - key[s + 1] != -8:
+                fill(V("lane", 64 * h + s, 64 * h + 64, 4), key[s] - key[s + 1])
+        for e in (31, 63):
+            fill(V("lane", 64 * h + e, 64 * h + e + 1), key[e] - key[e + 1])
     fill(V("seg8"), 1)
     op("p", lambda: g.affine_select(T.eb[:, :], T.seg8[:, 0:516], [[-1, 516]], A.is_equal, 0.0, 3, 4), [V("eb")], [V("seg8")], 1.2)
     fill(V("seg8", 0, 512, 8), 0)
@@ -426,194 +479,215 @@ def rank_program(g, core, T, topo):
     quant(V("vq"), V("vs"), V("vt"))
     early(6.0)
 
-    act(V("ptr", 0, 8), V("parq"), F.Relu, bias=CB)
-    act(V("paru"), V("parq"))
-    act(V("pj", PTR, 128, 8), IND(V("parq"), L("PJ", 1)), F.Relu, bias=CB)
-    tr(V("pr", 16, 144), V("pj"), 0.5)
+    act(V("ptr", 0, 16), IND(V("parq"), L("PB")), F.Relu, bias=CB)
+    act(V("paru"), IND(V("parq"), L("PU")))
+    tt(V("pj", PTR, 64, 4), IND(V("parq"), L("PJ")), V("pjc"), A.add)
+    tr(V("pr", 16, 80), V("pj"))
+    tt(V("cj", 64, 128), V("cj", 0, 64), V("pr", 16, 80), A.subtract)
     for nm in ("va", "vb"):
-        tt(V(nm, 16, 144), IND(V("raw"), L("RAW")), V("cj"), A.mult)
-    act(V("flg"), IND(V("va", 16, 144), L("REV")))
-    tr(V("nw"), V("flg"))
-    for k in range(7):
-        b0, b1, t0 = 160 * (k % 3), 160 * ((k + 1) % 3), 288 * (k % 2)
-        act(V("pr", b1 + 16, b1 + 144), IND(V("pr", b0, b0 + 144), V("ptr", 16 * max(k - 1, 0), 16 * max(k - 1, 0) + 8)))
-        if k != 5:
-            tr(V("pt", t0, t0 + 128), V("pr", b1 + 16, b1 + 144), 0.5)
-            tr(V("pt", t0 + 128, t0 + 288), V("pr", b1, b1 + 160), 0.5)
-            act(V("ptr", 16 * min(k + 1, 6), 16 * min(k + 1, 6) + 16), IND(V("pt", t0, t0 + 288), L("SEL", 1)))
-    act(V("nt", 0, 128), IND(V("nt", 128, 640), V("paru")))
-    act(V("r2"), IND(V("nt"), L("R2")))
+        tt(V(nm, 16, 80), IND(V("raw"), L("RAW")), V("cj", 64, 128), A.mult)
+    act(V("nw", 11, 264, 4), IND(V("va", 16, 80), L("REV")))
+    far = TUNE["far"]
+    for k in range(far):
+        b0, b1, t0 = 96 * (k % 3), 96 * ((k + 1) % 3), 160 * (k % 2)
+        act(V("pr", b1 + 16, b1 + 80), IND(V("pr", b0, b0 + 80), V("ptr", 16 * max(k - 1, 0), 16 * max(k - 1, 0) + 4)))
+        if k != 5 or far == 6:
+            tr(V("pt", t0, t0 + 64), V("pr", b1 + 16, b1 + 80))
+            tr(V("pt", t0 + 64, t0 + 160), V("pr", b1, b1 + 96))
+            act(V("ptr", 16 * min(k + 1, 6), 16 * min(k + 1, 6) + 16), IND(V("pt", t0, t0 + 160), L("SEL")), F.Relu)
+    act(V("nt", 0, 128), IND(V("nt", 256, 768), V("paru", 0, 8)))
+    act(V("r2"), IND(V("nt", 0, 256), L("R2")))
     for c in range(2):
         tr(V("r3", 128 * c, 128 * c + 128), V("r2", 128 * c, 128 * c + 128))
     act(V("ol", 0, 8), V("r3", 0, 256, 32))
     act(V("ol", 8, 12), V("r3", 144, 256, 32))
     act(V("ol", 12, 16), V("r3", 16, 128, 32))
 
-    def both(src, tb):
-        tr(V(tb, 0, 128), V(src, 16, 144))
-        tr(V(tb, 128, 288), V(src, 0, 160))
+    def both(src, tb, n, s0=0, t0=0, k=1.0):
+        tr(V(tb, t0, t0 + n), V(src, s0 + 16, s0 + 16 + n), k)
+        tr(V(tb, t0 + n, t0 + 2 * n + 32), V(src, s0, s0 + n + 32), k)
 
-    def pointer(src, k, bias):
+    def pointer(src, k, bias, n, sel):
         tb = "tc" if k % 2 else "tb"
-        both(src, tb)
-        act(V("ptr", 16 * k, 16 * k + 16), IND(V(tb), L("SEL", 1)), F.Relu, -1.0, bias)
+        both(src, tb, n)
+        act(V("ptr", 16 * k, 16 * k + 16), IND(V(tb, 0, 2 * n + 32), L(sel)), F.Relu, -1.0, bias)
 
     def step(o, w, own, lst, c0, c1, end):
         tt(V(o, 16 + c0, 16 + c1), IND(V(w, 0, 16 + end), V("ptr", 16 * lst + c0 // 16, 16 * lst + c1 // 16)), V(own, 16 + c0, 16 + c1), A.max)
 
-    def by_steps(old, cur, nxt, again, parts):
-        for k in range(7):
-            for (c0, c1) in parts:
-                step(nxt, cur, old, max(k - 1, 0), c0, c1, c1)
+    def by_steps(old, cur, nxt, again, runs):
+        for k in range(TUNE["steps"]):
+            step(nxt, cur, old, max(k - 1, 0), 0, 64, 64)
             old, cur, nxt = cur, nxt, (old if k else again)
-        for c0 in (32, 64, 96):
-            step(cur, cur, cur, 6, c0, c0 + 32, c0)
-        return cur, old
+        for (c0, c1) in runs:
+            step(cur, cur, cur, 6, c0, c1, c0)
+        return cur
+
+    def share(src, c0, a, dst="ww"):
+        for b in range(4):
+            act(Q(dst, b, 8 + 64 * a, 72 + 64 * a), Q(src, a, c0, c0 + 64))
 
     def later_lists():
-        p = feature((0, 15))
-        top, big, far = new("col"), new("col"), new("col")
-        ts(top, p, 6.0, A.min)
-        ts(big, p, 6.5, A.is_gt, 32.0, A.mult)
-        act(big, big, bias=32.0)
-        ts(far, p, 8.0, A.is_equal, 128.0, A.mult)
-        cyc = new("row", 21)
-        iota(cyc, [[0, 3], [1, 7]], 0, 0)
-        cyc = V("row", used["row"] - 15, used["row"] - 1)
-        W = lambda k, c0=0, c1=9: V("wt", 16 * k + c0, 16 * k + c1)
-        ts(W(0, 0, 14), cyc, top, A.not_equal, 0.5, A.mult)
-        ts(W(1, 0, 14), cyc, top, A.is_equal, big, A.mult)
-        scan(W(2, 0, 14), W(0, 0, 14), W(1, 0, 14), 0.0, A.mult, A.add)
-        fill(W(4), 2)
-        ts(W(5), V("cnt", 0, 9), p, A.is_equal, 1024.0, A.mult)
+        p = colf(lambda a, h, p, c: p)
+        fill(V("wt", 64, 70), 2)
+        scan(V("wt", 112, 118), V("wt", 64, 70), V("wt", 64, 70), 1.0, A.mult, A.max)
+        half = colf(lambda a, h, p, c: rev(32 + p))
+        act(V("wt", 128, 140, 2), V("wt", 112, 118), scale=half)
+        act(V("wt", 144, 150), V("wt", 112, 118), scale=2.0)
+        tt(V("wt", 129, 140, 2), V("wt", 128, 140, 2), V("wt", 144, 150), A.add)
+        act(V("fi", 32, 44), V("wt", 128, 140), scale=0.5 / 63, bias=-0.501)
+        act(V("wt", 144, 156), V("fi", 32, 44), scale=-126.0)
+        tt(V("wt", 160, 172), V("wt", 128, 140), V("wt", 144, 156), A.add)
+        act(L("LV"), V("wt", 160, 172), scale=0.5)
+        cyc = new("row", 12)
+        iota(cyc, [[0, 2], [1, 6]], 0, 0)
+        W = lambda k, c0=0, c1=6: V("wt", 16 * k + c0, 16 * k + c1)
+        ts(W(0, 0, 12), cyc, p, A.not_equal, 0.5, A.mult)
+        ts(W(1, 0, 12), cyc, p, A.is_equal, 32.0, A.mult)
+        scan(W(2, 0, 12), W(0, 0, 12), W(1, 0, 12), 0.0, A.mult, A.add)
+        ts(W(5), V("cnt", 0, 6), p, A.is_equal)
         scan(W(3), W(4), W(5), 0.0, A.mult, A.add)
-        tt(W(6, 0, 7), W(3, 0, 7), W(2, 7, 14), A.add)
-        act(W(6, 7, 8), W(3, 7, 8), bias=far)
-        act(V("gt", 0, 1), V("cnt", 0, 1), bias=8.0)
-        for b in range(9):
-            act(V("gt", 1 << b, 2 << b), V("gt", 0, 1 << b), bias=W(6 if b < 8 else 3, b, b + 1))
-        o = new("col")
-        act(o, W(3, 7, 8), scale=feature((5, 1)), bias=-1024.0)
-        act(V("th", 0, 1), W(3, 8, 9), scale=feature((6, 1)), bias=o)
-        for b in range(7):
+        act(W(5), W(3), scale=-64.0)
+        tt(W(6), W(5), W(2, 6, 12), A.subtract)
+        fill(V("gt", 0, 16), 128)
+        fill(V("gt", 16, 17), 0)
+        fill(V("th", 0, 1), 0)
+        for b in range(6):
+            act(V("gt", 16 + (1 << b), 16 + (2 << b)), V("gt", 16, 16 + (1 << b)), bias=W(6, b, b + 1))
             act(V("th", 1 << b, 2 << b), V("th", 0, 1 << b), bias=W(3, b, b + 1))
-        act(V("th", 128, 256), V("cnt"), scale=1024.0, bias=colf(lambda a, h, p, c: 1024 * (128 * a + 1)))
+        act(V("th", 64, 128), V("th", 0, 64), scale=8192.0)
+        act(V("th", 128, 192), V("th", 0, 64), scale=8128.0, bias=72.0)
         for nm in ("ba", "bb", "bc"):
-            fill(V(nm, 0, 16), 0)
-        fill(V("b8"), 0)
-        for c in (0, 64):
-            tt(V("bf", c, c + 64), IND(V("gt"), V("paru", c // 16, c // 16 + 4)), V("th", c, c + 64), A.subtract)
-        act(V("bf", 128, 256), V("bf", 0, 128), F.Relu)
-        ts(V("th", 256, 384), V("bf", 0, 128), 1024.0, A.is_lt)
-        for c in (0, 64):
-            tt(V("bf", c + 128, c + 192), V("bf", c + 128, c + 192), V("th", c + 128, c + 192), A.add)
-            tt(V("ba", c + 16, c + 80), V("bf", c + 128, c + 192), V("th", c + 256, c + 320), A.mult)
-        act(V("bb", 16, 144), V("ba", 16, 144))
+            fill(V(nm, 0, 16), -10000)
+        for nm in ("ba", "bb"):
+            tt(V(nm, 16, 80), IND(V("gt"), V("ptr", 0, 4)), V("th", 64, 128), A.add)
         early(TUNE["bb"])
-        cur, old = by_steps("ba", "bb", "bc", "ba", TUNE["parts"])
+        cur = by_steps("ba", "bb", "bc", "ba", TUNE["runs"] if TUNE["steps"] < 7 else ())
         early(TUNE["bs"])
-        act(Q("b8", 1, 8, 136), Q(cur, 0, 16, 144))
-        act(Q("b8", 3, 8, 136), Q(cur, 2, 16, 144))
-        for c in (0, 64):
-            tt(V("bi", c, c + 64), IND(V("b8"), V("ptr", 128 + c // 16, 132 + c // 16)), V(cur, c + 16, c + 80), A.max)
-        ts(V("bi", 128, 256), V("bi", 0, 128), 1023, A.bitwise_and)
-        act(V("bj", 0, 128), IND(V(cur, 16, 144), L("REV")))
-        ts(V("bj", 128, 256), V("bj", 0, 128), 1023, A.bitwise_and)
-        X = lambda k, c0, c1, st=1: V("xb" if k else "bj", 128 * max(k, 1) + c0, 128 * max(k, 1) + c1, st)
-        for k in range(6):
-            act(X(k + 1, 0, 128, 2), X(k, 0, 64), bias=None if k else -8.0)
-            act(X(k + 1, 1, 128, 2), X(k, 64, 128), bias=None if k else -8.0)
-        for k in range(7):
-            act(V("xg", 64 * k, 64 * k + 64), IND(X(k, 64, 128), L("TWICE", 4)), bias=None if k else -8.0)
-        act(V("xg", 448, 576), IND(X(0, 0, 128), L("TWICE")), bias=-8.0)
-        act(V("xg", 576, 704), IND(V("bi", 128, 256), L("PERM2")), bias=-8.0)
-        act(V("xg", 704, 832), IND(V("bi", 128, 256), L("TWICE")), bias=-8.0)
-        for (c0, c1) in TUNE["xh"]:
-            tr(V("xh", c0, c1), V("xg", c0, c1), 0.5)
-        for k in range(7):
-            act(V("sh", 4 * k, 4 * k + 4), V("xh", 65 * k, 64 * k + 64, 16), bias=8.0)
-        act(V("sh", 32, 40), V("xh", 448 + 7, 576, 16), bias=8.0)
-        act(V("sh", 40, 56), V("xh", 576 + 8, 832, 16), bias=8.0)
+        tt(V("th", 192, 256), V("th", 128, 192), V(cur, 16, 80), A.subtract)
+        for (c0, c1) in ((0, 16), (208, 240), (304, 336), (592, 624), (880, 896)):
+            fill(V("xg", c0, c1), 0)
+        fill(V("xh", 416, 480), 0)
+        first = new("col")
+        ts(first, p, 0.0, A.is_equal)
+        sc, bi = new("col"), new("col")
+        act(sc, first, scale=3.0, bias=1.0)
+        act(bi, first, scale=-21.0)
+        for c in (0, 6):
+            act(V("xg", 16 + 16 * c, 112 + 16 * c), IND(V("th", 192, 256), V("lu", at["LV"][0] + c, at["LV"][0] + c + 6)), scale=sc, bias=bi)
+        both("xg", "xh", 192, 0, 0, 0.5)
+        act(V("sh", 0, 16), IND(V("xh", 0, 480), L("SELV")), F.Relu)
+        fill(V("plw", 0, 8), -8)
+        for s in range(4):
+            act(V("plw", 8 + 64 * s, 72 + 64 * s), V("jc", 0, 64), bias=64.0 * s)
+        act(V("r7", 0, 64), IND(V("plw", 0, 72), V("ptr", 112, 116)))
+        act(V("xg", 240, 304), IND(V("r7", 0, 64), L("REV")))
+        both("xg", "xh", 64, 224, 480, 0.5)
+        act(V("sh", 16, 32), IND(V("xh", 480, 640), L("SEL")), F.Relu, bias=8.0)
+        fill(V("w2", 0, 136), -8)
+        act(V("r7", 64, 128), IND(V("plw", 0, 136), V("ptr", 128, 132)))
+        for a in (2, 3):
+            share("r7", 64, a, "w2")
+        act(V("xg", 336, 464), IND(V("plw"), V("ptr", 144, 152)))
+        act(V("xg", 464, 592), IND(V("w2"), V("ptr", 144, 152)))
+        for k in range(2):
+            act(V("xg", 624 + 128 * k, 752 + 128 * k), IND(V("xg", 336 + 128 * k, 464 + 128 * k), L("NK")))
+        for k in range(2):
+            both("xg", "xh", 256, 320 + 288 * k, 640 + 544 * k, 0.5)
+            act(V("sh", 32 + 16 * k, 48 + 16 * k), IND(V("xh", 640 + 544 * k, 1184 + 544 * k), L("SELW")), F.Relu, bias=8.0)
 
     def inherit(r):
         first, last = r == 0, r == 3
         if not last:
-            act(V("d1", 1, 128, 4), V("nw", VAL, 128, 4), scale=-1.0)
-            act(V("d1", 3, 128, 4), V("nw", VAL, 128, 4))
+            act(V("d1", 0, 256, 4), V("jc", 64, 128), bias=float(K * r))
+            act(V("d1", 2, 256, 4), V("nw", 11, 264, 4), scale=-1.0)
+            act(V("d1", 3, 256, 4), V("nw", 11, 264, 4))
         if first:
-            cur, old = by_steps("va", "vb", "vc", "vd", TUNE["first"])
-            c0 = 16
+            cur, c0 = by_steps("va", "vb", "vc", "vd", TUNE["runs"]), 16
+            pointer(cur, 7, C7, 64, "SEL")
         else:
-            cur, old, c0 = "sa", "sb", 8
-            tr(V(cur, 8, 136), V("nw"))
-            for k in range(7):
-                tt(V(old, 9, 136, 2), IND(V(cur, 0, 72), V("sh", 4 * k, 4 * k + 4)), V(cur, 72, 136), A.max)
-                act(V(old, 8, 136, 2), V(cur, 8, 72))
+            tt(V("sb", 9, 72, 2), IND(V("nw", 0, 136), V("sh", 0, 2)), V("nw", 139, 264, 4), A.max)
+            act(V("sb", 8, 72, 2), V("nw", 11, 136, 4))
+            cur, old, c0 = "sb", "sa", 8
+            for k in range(1, 6):
+                tt(V(old, 9, 72, 2), IND(V(cur, 0, 40), V("sh", 2 * k, 2 * k + 2)), V(cur, 40, 72), A.max)
+                act(V(old, 8, 72, 2), V(cur, 8, 40))
                 cur, old = old, cur
         if last:
-            tr(V("va", 16, 144), V("nw"))
-            act(V("flg"), IND(V("va", 16, 144), L("REV")), F.Sign)
-            for a in range(4):
-                dma("s", T.ofl[:, 128 * a:128 * a + 128], (T.flg[32 * a + VAL:32 * a + 32:4, :], V("flg")[1]), "out")
+            act(V("flg"), IND(V("nw"), L("REVF")), F.Sign)
+            for H in range(8):
+                B = 4 * (H % 2) + H // 2
+                dma("s", T.ofl[:, 64 * B:64 * B + 64], (T.flg[16 * H:16 * H + 16:2, :], V("flg")[1]), "out")
         for a in (0, 2):
-            if first:
-                act(Q("w8", a + 1, 8, 136), Q(cur, a, c0, c0 + 128))
-            else:
-                act(Q("w8", a + 1, 8, 136, 2), Q(old, a, 8, 72))
-                act(Q("w8", a + 1, 9, 136, 2), Q(cur, a, 9, 136, 2))
-        act(Q("w9", 2, 8, 136), Q(cur, 0, c0, c0 + 128))
-        act(Q("w9", 3, 8, 136), Q(cur, 0, c0, c0 + 128))
+            act(Q("w7", a + 1, 8, 72), Q(cur, a, c0, c0 + 64))
+        for a in (0, 2)[:1 if first else 2]:
+            share(cur, c0, a)
+        nxt = "v7" if first else old
+        tt(V(nxt, c0, c0 + 64), IND(V("w7"), V("ptr", 112, 116) if first else V("sh", 16, 20)), V(cur, c0, c0 + 64), A.max)
         if first:
-            pointer(cur, 8, C8)
-        tt(V(old, c0, c0 + 128), IND(V("w8"), V("ptr", 128, 136) if first else V("sh", 32, 40)), V(cur, c0, c0 + 128), A.max)
-        old, cur = cur, old
-        act(Q("w9", 2, 136, 264), Q(cur, 1, c0, c0 + 128))
-        act(Q("w9", 3, 136, 264), Q(cur, 1, c0, c0 + 128))
-        act(V("prm", 16, 144), IND(V(cur, c0, c0 + 128), L("PERM" if first else "REV" if last else "PERMR")))
-        if first:
-            pointer("prm", 9, C9)
+            share(nxt, c0, 1)
+            pointer(nxt, 8, C8, 64, "SEL")
+            tt(V("v8", 16, 80), IND(V("ww", 0, 136), V("ptr", 128, 132)), V(nxt, 16, 80), A.max)
+            for a in (2, 3):
+                share("v8", 16, a)
+            act(V("prm", 16, 144), IND(V("v8"), L("PERM")))
+            pointer("prm", 9, 8.0, 128, "SELX")
+            for c in range(2):
+                act(V("vi", 16 + 64 * c, 80 + 64 * c), IND(V("ww"), V("ptr", 144 + 4 * c, 148 + 4 * c)))
             later_lists()
-        lst, l0 = ("ptr", 144) if first else ("sh", 48 if last else 40)
-        tt(V("vi", 16, 144), IND(V("w9"), V(lst, l0, l0 + 8)), V("prm", 16, 144), A.max)
-        both("vi", "ti")
-        ts(V("yy"), IND(V("ti"), L("FS", 3)), 4095, A.bitwise_and)
+        else:
+            for a in (1, 3):
+                share(nxt, c0, a)
+            l0 = 48 if last else 32
+            for c in range(2):
+                act(V("tq", 64 * c, 64 * c + 64), IND(V("ww", 0, 136), V("sh", l0 + 8 + 4 * c, l0 + 12 + 4 * c)))
+            tt(V("vi", 16, 144), IND(V("ww"), V("sh", l0, l0 + 8)), V("tq"), A.max)
+        both("vi", "ti", 128)
+        ts(V("yy"), IND(V("ti"), L("FSL" if last else "FS")), 4095, A.bitwise_and)
         for a in range(4):
-            act(Q("yy", a ^ 1, 16 * (a % 2), 16 * (a % 2) + 16), Q("yy", a, 32, 48))
+            if last:
+                for u in range(2):
+                    act(Q("yy", a ^ 1, 32 * u + 16 * (a % 2), 32 * u + 16 * (a % 2) + 16), Q("yy", a, 64 + 16 * u, 80 + 16 * u))
+            else:
+                act(Q("yy", a ^ 1, a % 2, 64, 2), Q("yy", a, 64, 96))
         for b in range(2):
-            for a in range(2):
-                act(Q("el", 2 * b, 16 * a, 16 * a + 16, 1, 2) if last else Q("el", 2 * b, a, 32, 2, 2), Q("yy", 2 * a, b, 32, 2, 2))
+            for s in range(2):
+                if last:
+                    tt(Q("el", 2 * b, 16 * s, 16 * s + 16, 1, 2), Q("yy", 2 * s, 2 * b, 64, 4, 2), Q("yy", 2 * s, 2 * b + 1, 64, 4, 2), A.max)
+                else:
+                    tt(Q("el", 2 * b, s, 32, 2, 2), Q("yy", 2 * s, 32 * b, 32 * b + 16, 1, 2), Q("yy", 2 * s, 32 * b + 16, 32 * b + 32, 1, 2), A.max)
 
     def plane(eng, r, t, l0, l1, n0):
-        w = IND(V("pool", PW * t + 16, PW * t + 16 + D0 + K * r), V("el", l0, l1))
-        (cp if eng == "v" else act)(V("et", 4 * n0 + t, 4 * (n0 + 16 * (l1 - l0)), 4), w)
+        w = IND(V("pool", PW * t, PW * t + DB + K * r), V("el", l0, l1))
+        (cp if eng == "v" else act)(V("et", 4 * (K + n0) + t, 4 * (K + n0 + 16 * (l1 - l0)), 4), w)
         if eng == "a":
             del ops[-1]["ways"]
 
     def pieces(r, gath, parts, sq, ss):
-        for (l0, l1, engs) in gath:
+        for (l0, l1, n0, engs) in gath:
             for t in range(4):
-                plane(engs[t], r, t, l0, l1, 16 * ((l0 - 14) % 32 if r < 3 else l0))
+                plane(engs[t], r, t, l0, l1, n0)
         for i, (c0, c1) in enumerate(parts):
-            quant(V("eq", c0, c1), V("es", c0, c1), V("et", 4 * c0, 4 * c1))
+            quant(V("eq", K + c0, K + c1), V("es", K + c0, K + c1), V("et", 4 * (K + c0), 4 * (K + c1)))
             if i == 0 and r < 3:
                 mm(V("ps", 1536, 1664), V("ukq"), V("uks"), V("eq", 0, 128), V("es", 0, 128))
-            mm(V("ps", 512 * i, 512 * i + c1 - c0), V(sq), V(ss), V("eq", c0, c1), V("es", c0, c1))
+            mm(V("ps", 512 * i, 512 * i + c1 - c0), V(sq), V(ss), V("eq", K + c0, K + c1), V("es", K + c0, K + c1))
 
     def symbols(r):
         dst = T.cores[(rank - DIST[r]) % n_ranks]
-        pieces(r, GATH, PIECES, "urq", "urs")
+        pieces(r, TUNE["gath"], TUNE["pieces"], "urq", "urs")
         for b in range(4):
             mm(V("ps", 2048 + 512 * b, 2176 + 512 * b), V("wq", 128 * b, 128 * b + 128), V("wsc", 128 * b, 128 * b + 128), V("eq", 0, 128), V("es", 0, 128))
-        ts(V("kb", 0, 64), V("ps", 1536, 1600), 0.0, A.is_gt, CW, A.mult)
-        ts(V("kb", 64, 80), V("ps", 1536, 1552), 0.0, A.is_gt, CW, A.mult)
+        ts(V("kb", 0, 64), V("ps", 1600, 1664), 0.0, A.is_gt, CW, A.mult)
+        ts(V("kb", 64, 80), V("ps", 1600, 1616), 0.0, A.is_gt, CW, A.mult)
         tr(V("kbt", 0, 64), V("kb", 0, 64), 0.5)
         tr(V("kbt", 64, 128), V("kb", 16, 80), 0.5)
         tt(V("fs%d" % r), V("kbt", 0, 128, 4), V("kbt", 1, 128, 4), A.add)
         send(dst, V("fl%d" % r), V("fs%d" % r), "af%d" % r, TUNE["lat"] + (0.0 if r else 1.2), 1 if r else 2)
-        for i, (c0, c1) in enumerate(PIECES):
-            ts(V("rows", c0, c1), V("ps", 512 * i, 512 * i + c1 - c0), 0.0, A.is_gt, CW, A.mult)
+        for i, (c0, c1) in enumerate(TUNE["pieces"]):
+            ts(V("rows", max(c0, 0), c1), V("ps", 512 * i + max(-c0, 0), 512 * i + c1 - c0), 0.0, A.is_gt, CW, A.mult)
         for b in range(4):
-            act(V("ht", b, 256, 4), V("ps", 2048 + 512 * b, 2048 + 512 * b + K), scale=0.03125)
+            act(V("ht", b, 256, 4), V("ps", 2112 + 512 * b, 2112 + 512 * b + K), scale=0.03125)
         hq, hs = "hq%d" % r, "hs%d" % r
         quant(V(hq, 64, 192), V(hs, 64, 192), V("ht"))
         send(dst, u8(V(hq, 0, 64)), u8(V(hq, 64, 128)), "ah%d" % r, 4.0)
@@ -623,15 +697,10 @@ def rank_program(g, core, T, topo):
         tr(V("x0", 0, 128, 2), V("op", 0, 64), 0.5)
         tr(V("x0", 1, 128, 2), V("op", 64, 128), 0.5)
         scan(V("xs"), V("seg4"), V("x0"), 0.0, A.mult, A.add, 0.5)
-        if U16T:
-            tr(V("ixu"), V("xs", 3, 128, 4))
-        else:
-            tr(V("xt"), V("xs", 3, 128, 4))
-            cp(V("ixu"), V("xt"))
+        tr(V("ixu"), V("xs", 3, 128, 4))
         act(V("op2"), IND(V("rows"), V("ol", 4, 12)))
         tr(V("opt"), V("op2"), 0.5)
-        for c in range(2):
-            tt(V("sm", c, 64, 2), V("opt", 64 * c, 64 * c + 64, 2), V("opt", 64 * c + 1, 64 * c + 64, 2), A.add)
+        tt(V("sm", 0, 128, 2), V("opt", 0, 128, 2), V("opt", 1, 128, 2), A.add)
         tr(V("smr"), V("sm"), 0.5)
         early(1.0)
 
@@ -643,7 +712,8 @@ def rank_program(g, core, T, topo):
             e0, e1 = max(0, -d), 32 - max(0, d)
             tt(V("tab", 8 * e0 + 6 + d, 8 * e1 + d, 8), V("tab", 8 * e0 + 6, 8 * e1, 8), V("tab", 8 * (e0 + d) + 6, 8 * (e1 + d), 8), A.add)
         act(V("fin"), IND(V(fl), L("FIN")), ext="af%d" % r)
-        tr(V("fw", 0, 64), V("fin"), 0.5)
+        tr(V("fwt"), V("fin"), 0.5)
+        act(V("fw", 0, 64), IND(V("fwt"), L("KP")))
         for (c0, c1) in ((64, 128), (128, 256), (256, 512), (512, 576)):
             act(V("fw", c0, c1), V("fw", 0, c1 - c0))
         hq, hs = "hq%d" % r, "hs%d" % r
@@ -651,10 +721,11 @@ def rank_program(g, core, T, topo):
             mm(V("ps", 2048 + 512 * b, 2176 + 512 * b), V("ebq", 128 * b, 128 * b + 128), V("ebs", 128 * b, 128 * b + 128),
                V(hq, 0, 128), V(hs, 0, 128), ext="ah%d" % r)
         for b in range(4):
-            act(V("pool", PW * b + 16 + D0 + K * r, PW * b + 16 + D0 + K * r + K), V("ps", 2048 + 512 * b, 2048 + 512 * b + K))
-            early(1.5)
+            for d0 in (0, DB):
+                act(V("pool", PW * b + d0 + K * r, PW * b + d0 + K * r + K), V("ps", 2048 + 512 * b, 2048 + 512 * b + K))
+                early(1.5)
         ones = 64.0 * 0x1111
-        for (c0, c1, eng) in LOOK:
+        for (c0, c1, eng) in TUNE["look"]:
             w, o = IND(V("tab"), V("ixu", c0, c1)), V("ac", 16 * c0, 16 * c1)
             if eng == "v":
                 ts(o, w, -64.0, A.mult, ones, A.add)
@@ -665,30 +736,29 @@ def rank_program(g, core, T, topo):
         for t in range(4):
             ts(V("yi", t, 256, 4), V("yt"), 4 * (3 - t), A.logical_shift_right, 15 << 6, A.bitwise_and)
         for c in range(4):
-            scan(V("sc", c, 256, 4), V("yi", 64 * c, 64 * c + 64), V("lane"), 1000.0, A.min, A.add)
+            scan(V("sc", c, 256, 4), V("yi", 64 * c, 64 * c + 64), V("lane", 64 * (c % 2), 64 * (c % 2) + 64), 1000.0, A.min, A.add)
         ku = V("sc", 252, 256)
-        tt(V("fg"), IND(V("fk"), ku), V("jc", 64 * r + 64, 64 * r + 128), A.add)
-        tt(V("ne"), IND(V("fw"), ku), V("smr"), A.not_equal)
-        tr(V("d1", 0, 128, 2), V("fg"))
-        tr(V("d0", 1, 128, 2), V("ne"), 0.5)
-        scan(V("nw"), V("d0"), V("d1"), 0.0, A.mult, A.add)
+        act(V("d1", 1, 256, 4), IND(V("fk"), ku))
+        tt(V("d0", 2, 256, 4), IND(V("fw"), ku), V("smr", 0, 64), A.not_equal)
+        tt(V("d0", 3, 256, 4), IND(V("fw"), ku), V("smr", 64, 128), A.not_equal)
+        scan(V("nw", 8, 264), V("d0"), V("d1"), 0.0, A.mult, A.add)
 
     for r in range(3):
         inherit(r)
         symbols(r)
         choose(r)
     inherit(3)
-    pieces(3, GATH_LAST, PIECES_LAST, "vq", "vs")
-    for i, (c0, c1) in enumerate(PIECES_LAST):
+    pieces(3, TUNE["gath3"], TUNE["pieces3"], "vq", "vs")
+    for i, (c0, c1) in enumerate(TUNE["pieces3"]):
         (act if TUNE["yo"][i] == "a" else cp)(V("yo", c0, c1), V("ps", 512 * i, 512 * i + c1 - c0))
     for i, (c0, c1) in enumerate(STORES):
         ahead = TUNE["out"] * (len(STORES) - 1 - i)
-        dma("s", T.oc[:, 4 * c0:4 * c1], u8(V("eq", c0, c1)), "out", 1.1)
+        dma("s", T.oc[:, 4 * c0:4 * c1], u8(V("eq", K + c0, K + c1)), "out", 1.1)
         ops[-1].update(early=ahead + TUNE["out"] / 2, move=0.16 + 0.0013 * (c1 - c0))
         dma("s", T.y[:, c0:c1], V("yo", c0, c1), "out", 1.1)
         ops[-1].update(early=ahead, move=0.16 + 0.0013 * (c1 - c0))
     for k in range(4):
-        dma("a" if k % 2 else "s", T.osc[4 * k:4 * k + 4, :], V("es", 0, 512, 1, 32 * k, 32 * k + 4), "out")
+        dma("a" if k % 2 else "s", T.osc[4 * k:4 * k + 4, :], V("es", K, K + 512, 1, 32 * k, 32 * k + 4), "out")
 
     def meet(x, y):
         if x[1] >= y[2] or y[1] >= x[2] or x[3] >= y[4] or y[3] >= x[4]:

@@ -1,4 +1,5 @@
 import numpy as np
+from concourse.bass import DstId, RemoteDMATransfer
 from concourse.mybir import dt, AluOpType, ActivationFunctionType
 
 A = AluOpType
@@ -6,16 +7,17 @@ F = ActivationFunctionType
 DIST = [1, 2, 4]
 C, K = 512, 64
 X0 = 3 * K
-DB = X0 + C
+DB = X0 + 4 * C
 PW = DB + 3 * K
+LOADS = 1
 F32, BF, I32, U16, U8, MX = "float32", "bfloat16", "int32", "uint16", "uint8", "float8_e4m3fn_x4"
-GATH = [(0, 4, 0, "vvaa"), (4, 14, 64, "xxxx"), (14, 24, 224, "xxxx"), (24, 32, 384, "xxxx")]
-PIECES = [(-64, 64), (64, 384), (384, 512)]
-GATH_LAST = [(0, 8, 0, "vvaa"), (16, 24, 128, "xxxx"), (8, 16, 256, "xxxx"), (24, 32, 384, "xxxx")]
+GATH = [(0, 4, 0, "vvaa"), (4, 16, 64, "hxxx"), (16, 32, 256, "hxxx")]
+PIECES = [(-64, 64), (64, 256), (256, 512)]
+GATH_LAST = [(32, 36, 0, "xxxx"), (36, 40, 64, "xxxx"), (16, 24, 128, "xxxx"), (8, 16, 256, "xxxx"), (24, 32, 384, "xxxx")]
 PIECES_LAST = [(0, 256), (256, 384), (384, 512)]
 STORES = [(0, 256), (256, 512)]
 LOOK = [(0, 14, "v"), (14, 24, "a"), (24, 32, "a")]
-FLW = 4
+FLW = 32
 
 
 def _sb(n, d):
@@ -28,35 +30,36 @@ SCRATCH = {
     "ukq": _sb(128, MX), "uks": _sb(128, U8),
     "vq": _sb(128, MX), "vs": _sb(128, U8), "eb": _sb(516, BF), "ebq": _sb(512, MX), "ebs": _sb(512, U8),
     "pi": _sb(2, I32), "fi": _sb(48, I32), "col": _sb(128, F32), "row": _sb(256, F32), "cnt": _sb(128, F32),
-    "lu": _sb(128, U16), "cj": _sb(128, F32), "jc": _sb(128, F32), "pjc": _sb(16, F32), "plw": _sb(264, F32),
-    "vcon": _sb(128, F32), "horn": _sb(128, F32), "lane": _sb(128, F32), "seg4": _sb(128, BF), "seg8": _sb(520, F32),
+    "lu": _sb(176, U16), "cj": _sb(128, F32), "jc": _sb(128, F32), "pjc": _sb(16, F32), "plw": _sb(264, F32),
+    "horn": _sb(128, F32), "lane": _sb(128, F32), "seg8": _sb(512, BF),
     "ptr": _sb(176, U16), "paru": _sb(16, U16), "nt": _sb(768, F32), "r2": _sb(256, F32), "r3": _sb(256, F32), "ol": _sb(16, U16),
-    "va": _sb(96, F32), "vb": _sb(96, F32), "vc": _sb(96, F32), "vd": _sb(96, F32), "v7": _sb(96, F32), "v8": _sb(208, F32),
+    "va": _sb(96, F32), "vb": _sb(96, F32), "vc": _sb(96, F32), "vd": _sb(96, F32), "v7": _sb(96, F32), "v8": _sb(320, F32),
     "w7": _sb(72, F32), "ww": _sb(264, F32), "tq": _sb(128, F32),
-    "prm": _sb(160, F32), "sa": _sb(72, F32), "sb": _sb(72, F32), "pj": _sb(64, F32), "pr": _sb(288, F32), "pt": _sb(320, F32),
-    "wt": _sb(176, F32), "gt": _sb(80, F32), "th": _sb(256, F32), "ba": _sb(80, F32), "bb": _sb(80, F32), "bc": _sb(80, F32),
+    "sa": _sb(72, F32), "sb": _sb(72, F32), "pj": _sb(64, F32), "pr": _sb(288, F32), "pt": _sb(320, F32),
+    "wt": _sb(176, F32), "gt": _sb(208, F32), "gi": _sb(128, I32), "th": _sb(256, F32), "ba": _sb(80, F32), "bb": _sb(80, F32), "bc": _sb(80, F32),
     "r7": _sb(128, F32), "w2": _sb(264, F32), "xg": _sb(896, BF), "xh": _sb(1728, BF), "sh": _sb(64, U16),
     "vi": _sb(160, I32), "ti": _sb(288, I32), "tb": _sb(288, F32), "tc": _sb(288, F32),
-    "yy": _sb(96, I32), "el": _sb(32, U16), "nw": _sb(264, F32), "flg": _sb(64, F32),
-    "xt": _sb(4 * C, BF), "pool": _sb(4 * PW, BF), "et": _sb(4 * 576, BF), "eq": _sb(576, MX), "es": _sb(576, U8),
+    "yy": _sb(96, I32), "el": _sb(40, U16), "ea": _sb(176, I32), "eb2": _sb(320, I32), "ec": _sb(32, I32), "nw": _sb(264, F32), "flg": _sb(64, F32),
+    "pool": _sb(4 * PW, BF), "et": _sb(4 * 576, BF), "eq": _sb(576, MX), "es": _sb(576, U8),
     "ht": _sb(512, BF),
-    "kb": _sb(80, BF), "kbt": _sb(128, BF), "rows": _sb(512, BF), "op": _sb(128, BF), "op2": _sb(128, BF), "opt": _sb(128, BF),
-    "x0": _sb(128, BF), "xs": _sb(128, U16), "sm": _sb(128, BF), "ixu": _sb(32, U16),
+    "kb": _sb(80, BF), "rows": _sb(512, BF), "op": _sb(128, BF), "op2": _sb(128, BF), "opt": _sb(128, BF),
+    "x0": _sb(192, BF), "xs": _sb(192, U16), "seg6": _sb(192, BF), "sm": _sb(128, BF), "ixu": _sb(32, U16),
     "xe": _sb(128, F32), "tab": _sb(264, F32), "ac": _sb(512, F32), "ci": _sb(512, I32), "yt": _sb(64, I32), "yi": _sb(256, I32),
     "sc": _sb(256, U16), "fin": _sb(64, BF), "fwt": _sb(64, BF), "fw": _sb(576, BF), "fk": _sb(576, BF), "smr": _sb(128, BF),
     "d0": _sb(256, BF), "d1": _sb(256, F32), "yo": _sb(512, F32),
     "ps": ("psum", [128, 4096], F32),
 }
 for _r in range(3):
-    SCRATCH["fs%d" % _r] = _sb(32, BF)
+    SCRATCH["fs%d" % _r] = _sb(128, BF)
     SCRATCH["fl%d" % _r] = _sb(32, BF)
     SCRATCH["hq%d" % _r] = _sb(192, MX)
     SCRATCH["hs%d" % _r] = _sb(192, U8)
 
-SEMAPHORES = (["sv", "sa", "sp", "st", "l_par", "l_fl", "l_u", "l_x", "l_w", "l_v", "out", "sent"]
+SEMAPHORES = (["sv", "sa", "sp", "st", "l_par", "l_fl", "l_u", "l_x", "l_y", "l_w", "l_v", "out", "sent"]
               + ["af%d" % r for r in range(3)] + ["ah%d" % r for r in range(3)])
 ENG_SEM = {"v": "sv", "a": "sa", "p": "sp", "t": "st"}
 CYC, HOP = 0.00105, 0.22
+TOP = 512
 PTR = 1
 
 
@@ -87,25 +90,25 @@ def spread(a, h, p, c, last):
 
 
 LISTS = [
-    ("PB", 1, lambda a, h, p, c: 16 * h + 4 * a + p % 4),
-    ("PJ", 1, lambda a, h, p, c: 16 * (p // 4 % 2) + 4 * a + 2 * (p // 8) + h),
+    ("PB", 1, None),
+    ("PJ", 1, None),
     ("RAW", 4, lambda a, h, p, c: FLW * p + (16 * h + 4 * a) % FLW + c),
     ("SEL", 1, lambda a, h, p, c: seen(h, p % 4, 16 * h + PTR, 64)),
-    ("PERM", 8, lambda a, h, p, c: 16 + 64 * (1 + (1 - h) - p // 8) + 8 * (p % 8) + c),
-    ("SELX", 1, lambda a, h, p, c: seen(h, p % 8, 16 * (1 - h) + PTR, 128)),
+    ("SEL6", 1, lambda a, h, p, c: seen(h, 2 + p // 2 % 2, 16 * h + PTR, 64)),
+    ("SELX", 1, lambda a, h, p, c: 32 * (p % 8) + 16 * (1 - h) + PTR),
     ("FS", 6, lambda a, h, p, c: spread(a, h, p, c, False)),
-    ("UK", 8, lambda a, h, p, c: 64 * (c % 2) + 16 * (p // 4) + p % 4),
+    ("UK", 8, lambda a, h, p, c: 16 * (p % 8) + p // 8),
     ("UR", 8, lambda a, h, p, c: 16 * (p // 2) + p % 2),
     ("PU", 1, lambda a, h, p, c: 16 * (p // 4 % 2) + 4 * a + p % 4),
     ("R2", 16, lambda a, h, p, c: parents(c // 2, c % 2, p) + 128 * h),
     ("REV", 4, lambda a, h, p, c: rev(16 * c + p)),
-    ("XE", 8, lambda a, h, p, c: 8 * (p % 4) + c),
-    ("FIN", 4, lambda a, h, p, c: 8 * slot(h, 2 * (c // 2) + h) + p // 2),
+    ("FIN", 4, lambda a, h, p, c: slot(h, 2 * (c // 2) + h) + 4 * (p // 2)),
     ("KP", 4, lambda a, h, p, c: 32 * (c % 2) + 16 * (p // 8) + 8 * (c // 2) + p % 8),
     ("LV", 12, None),
-    ("SELV", 1, lambda a, h, p, c: seen(h, p, 16 * h + p // 2, 192)),
+    ("SELV", 1, lambda a, h, p, c: seen(h, p % 8 + 4 * (p // 8), 16 * h + p % 8 // 2 + 2 * (p // 8), 192)),
     ("SELW", 1, lambda a, h, p, c: seen(h, p, 16 * h, 256)),
     ("NK", 8, lambda a, h, p, c: 16 * (p % 8) + 8 * (c // 4) + 2 * (c % 4) + p // 8),
+    ("FE", 1, lambda a, h, p, c: seen(h, p % 4, 2 * (2 * (p // 4) + h), 64)),
     ("FSL", 6, lambda a, h, p, c: spread(a, h, p, c, True)),
     ("REVF", 4, lambda a, h, p, c: 11 + 4 * rev(16 * c + p)),
 ]
@@ -121,6 +124,8 @@ for _s in range(7):
     for _w in range(1, 6):
         if _s + _w <= (7 if _s > 4 else 5) and (_s + _w <= 4 or _s in (0, 4, 5, 6)):
             FEATURES[(_s, (1 << _w) - 1)] = _P // (1 << _s) % (1 << _w)
+for _s, _w in ((0, 19), (3, 12), (0, 4), (2, 2)):
+    FEATURES[(_s, _w)] = 1.0 * (np.arange(128) >> _s & _w)
 for _s in range(3):
     FEATURES[("x", _s)] = (_P // 16 + _P // (1 << _s)) % 2
 
@@ -196,9 +201,11 @@ def product(d):
 
 
 PLAN = {}
-TUNE = {"xp": 256, "far": 7, "steps": 7, "runs": ((32, 64),), "gath": GATH, "pieces": PIECES, "gath3": GATH_LAST, "pieces3": PIECES_LAST,
-        "look": LOOK, "bb": 0.0, "bs": 1.0, "out": 1.0, "yo": "aav", "lat": 0.9, "fl": 2.2, "bias": 0.03, "it": 10,
-        "cases": ((0.81, 1.0, 0.22), (1.05, 1.0, 0.2), (1.16, 1.15, 0.24), (1.18, 1.2, 0.24)), "tries": 2400, "sd": (0.2, 0.4, 0.8),
+TUNE = {"ccut": ((0, 2), (2, 4)), "bcut": ((0, 64), (64, 128)), "late": 1, "scat": 4.0, "past": ("eb", "lane", "xg", "w2", "plw", "fk", "sm", "sa", "sb", "nw", "ht"), "anew": 0.5, "run": 25,
+        "main": 0.5, "soon": 1.5, "marks": (("nw", 0), ("el", 0), ("nw", 30)), "last": 1000, "hot": 1.0, "moves": 110000, "heat": 0.04,
+        "guard": 1.0, "xp": 256, "steps": 7, "runs": ((32, 48), (48, 64)), "gath": GATH, "pieces": PIECES, "gath3": GATH_LAST,
+        "pieces3": PIECES_LAST, "look": LOOK, "bb": 1.0, "bs": 2.0, "out": 1.0, "yo": "aav", "lat": 0.9, "fl": 1.6, "bias": 0.06, "it": 10,
+        "cases": ((1.0, 1.0, 0.19, 1.1), (0.9, 0.85, 0.19, 1.35), (1.17, 1.2, 0.24, 0.9)), "tries": 20, "sd": (0.1, 0.25, 0.5),
         "span": (1.0, 2.0, 3.0)}
 
 
@@ -285,6 +292,22 @@ def rank_program(g, core, T, topo):
                 alt = lambda: g.vector.tensor_scalar(o[0], i[0], kw.get("scale", 1.0), kw.get("bias", 0.0), A.mult, A.add)
             ops[-1]["ways"] = {"a": (ops[-1]["fn"], ops[-1]["cost"]), "v": (alt, cc(i, rate(o, i)))}
 
+    def above(o, i):
+        act(o, i, F.Sign)
+        ops[-1]["ways"] = {"a": (ops[-1]["fn"], ops[-1]["cost"]), "v": (lambda: g.vector.tensor_scalar(o[0], i[0], 0.0, None, A.is_gt), cc(i))}
+
+    def equal(o, i, s, ext):
+        fn = lambda: g.vector.tensor_scalar(o[0], i[0], float(s), None, A.is_equal)
+        if s in (0, 3):
+            act(o, i, F.Relu, scale=1.0 if s else -1.0, bias=-2.0 if s else 1.0, ext=ext)
+            ops[-1]["ways"] = {"a": (ops[-1]["fn"], ops[-1]["cost"]), "v": (fn, cc(i))}
+        else:
+            op("v", fn, [o], [i], cc(i), ext=ext)
+
+    def weigh(o, i, w):
+        act(o, i, F.Relu, scale=w)
+        ops[-1]["ways"] = {"a": (ops[-1]["fn"], ops[-1]["cost"]), "v": (lambda: g.vector.tensor_scalar(o[0], i[0], 0.0, w[0], A.max, A.mult), cc(i))}
+
     def iota(o, pat, base, cm, flt=True):
         if flt:
             op("p", lambda: g.iota(o[0], pat, base, cm, allow_small_or_imprecise_dtypes=True), [o], [], 0.13 + 2 * CYC * o[2])
@@ -310,25 +333,35 @@ def rank_program(g, core, T, topo):
 
     count = {}
 
-    def send(dst_core, o, i, rsem, lat, every=1):
+    def send(dst_core, o, i, rsem, lat, every=1, plus=None):
         rid, pid = topo.addr(dst_core)[:2]
         use = topo.engines(core, dst_core)[::every]
         m, n = sum(1 << e for e in use), len(use)
         count[rsem] = count.get(rsem, 0) + n
-        op("p", lambda: g.remote_dma(o[0], i[0], T.sem[rsem], T.sem["sent"], pid, rid, m), [], [i], 0.15, lat, sem="sent", inc=-n, gives=rsem)
+        if plus is None:
+            fn = lambda: g.remote_dma(o[0], i[0], T.sem[rsem], T.sem["sent"], pid, rid, m)
+        else:
+            fn = lambda: g.remote_dma_fused([RemoteDMATransfer(dst_ids=[DstId(rid=rid, pnc=pid)], dma_engine_mask=m, remote_sem=T.sem[rsem],
+                                                               srcs=[v[0] for v in [i] + plus], dsts=[o[0]], alu_op=1)], local_sem=T.sem["sent"])
+        op("p", fn, [], [i] + (plus or []), 0.15, lat, sem="sent", inc=-n, gives=rsem)
 
-    op("v", lambda: g.vector.memset(T.raw[:, :], 1), [V("raw")], [], cc(V("raw")))
+    for c in range(0, 16 * FLW, 256):
+        ms(V("raw", c, min(c + 256, 16 * FLW)), 1)
     for H in range(8):
         dma("s" if H % 2 else "a", V("parq", 0, 32, 1, 16 * H, 16 * H + 16), T.par[:, :], "l_par")
         early(5.0)
     for H in range(8):
         c0 = (16 * (H % 2) + 4 * (H // 2)) // FLW * FLW
         dma("s" if H % 2 else "a", (T.raw[16 * H:16 * H + 16:2, :], [("raw", 16 * H, 16 * H + 16, 0, 16 * FLW, 1)]), T.fl[:, c0:c0 + FLW], "l_fl", TUNE["fl"])
-    loads = [(V("xt"), T.x[:, :], "l_x", 4.0), (V("ut"), T.u[:, :], "l_u", 5.0), (u8(V("wq")), T.wc[:, :], "l_w", 7.0),
-             (V("wsc"), T.ws[:, :], "l_w", 7.0), (V("vt"), T.v[:, :], "l_v", 8.0)]
+        ops[-1]["ahead"] = 5.0
+    xin = lambda t: (V("pool", PW * t + X0 - t, PW * t + DB - t), T.x[:, :], "l_x" if t == 0 else "l_y", 4.0 + 2.5 * (LOADS - 1 if t else 0) + (1.0 if t else 0.0))
+    more = 2.0 * (LOADS - 1)
+    loads = ([xin(0), (V("ut"), T.u[:, :], "l_u", 5.0)] + [xin(t) for t in range(1, LOADS)]
+             + [(u8(V("wq")), T.wc[:, :], "l_w", 7.0 + more), (V("wsc"), T.ws[:, :], "l_w", 7.0 + more), (V("vt"), T.v[:, :], "l_v", 8.0 + more)])
     for (o, i, sem, lat) in loads:
-        dma("s", o, i, sem, lat, V("parq"))
+        dma("s", o, i, sem, lat - 1.0, V("raw"))
         ops[-1]["behind"] = [q["id"] for q in ops[:-1] if q["eng"] == "s"]
+        ops[-1]["ahead"] = 100.0 - len(ops)
 
     iota(V("pi", 0, 1), [[0, 1]], 0, 1, False)
     iota(V("cnt"), [[1, 128]], 0, 0)
@@ -395,6 +428,11 @@ def rank_program(g, core, T, topo):
     def colf(f):
         return column(table(1, f)[:, 0])
 
+    tt(V("lu", 0, 1), feature((0, 19)), feature((3, 12)), A.add)
+    pj0, pj1 = new("col"), new("col")
+    tt(pj0, feature((0, 4)), feature((5, 3)), A.add)
+    tt(pj1, feature((2, 2)), feature((4, 1)), A.add)
+    act(V("lu", 2, 3), pj0, scale=4.0, bias=pj1)
     at, c0 = {}, 0
     for (name, n, f) in LISTS:
         at[name] = (c0, n)
@@ -407,30 +445,30 @@ def rank_program(g, core, T, topo):
 
     const(lambda c, e: V("pjc", c, e), table(16, lambda a, h, p, c: 16 - 64 * (4 * (c // 4 % 2) + a)))
     CB = colf(lambda a, h, p, c: 16 - 64 * (4 * h + a))
-    cb = new("col")
-    act(cb, colf(lambda a, h, p, c: 4098 * 64 * (4 * h + a) + 4096 + X0 - 16), scale=colf(lambda a, h, p, c: 1 - p % 2), bias=CB)
-    act(V("cj", 0, 64), V("cnt", 0, 64), scale=colf(lambda a, h, p, c: 4097 * (1 - p % 2)), bias=cb)
-    for t in range(4):
-        fill(V("pool", PW * t, PW * t + X0), 0)
+    act(V("cj", 0, 64), V("cnt", 0, 64), scale=4100.0, bias=colf(lambda a, h, p, c: 4101 * 64 * (4 * h + a) + 4096 + X0 - 16 - TOP))
+    act(V("cj", 0, 64), V("cj", 0, 64), scale=colf(lambda a, h, p, c: 1 - p % 2), bias=colf(lambda a, h, p, c: TOP + 16 - 64 * (4 * h + a)))
+    for t in range(LOADS, 4):
         for c in range(0, C, TUNE["xp"]):
-            act(V("pool", PW * t + X0 + c, PW * t + X0 + c + TUNE["xp"]), V("xt", 4 * c + t, 4 * (c + TUNE["xp"]), 4))
+            act(V("pool", PW * t + X0 + 4 * c, PW * t + X0 + 4 * (c + TUNE["xp"]), 4), V("pool", X0 + 4 * c + t, X0 + 4 * (c + TUNE["xp"]), 4))
     ms(V("pj"), 0.0)
-    pad = colf(lambda a, h, p, c: -1000 * (p % 2))
-    for (nm, n) in (("vb", 16), ("vc", 16), ("vd", 16), ("w7", 72), ("ww", 8)):
-        act(V(nm, 0, n), V("cnt", 0, n), scale=0.0, bias=pad)
-    for k in range(3):
-        fill(V("pr", 96 * k, 96 * k + 16), 0)
-        fill(V("pr", 96 * k + 80, 96 * k + 96), 0)
-    for nm in ("vb", "vc", "vd", "v7"):
+    for (nm, n) in (("vb", 16), ("vc", 16), ("vd", 16), ("w7", 8), ("ww", 8), ("v7", 16)):
+        fill(V(nm, 0, n), 0)
+    for k in range(4):
+        fill(V("pr", 80 * k, 80 * k + 16), 0)
+    for nm in ("vc", "v7"):
         fill(V(nm, 80, 96), 0)
-    for nm in ("v7", "v8", "prm"):
-        fill(V(nm, 0, 16), 0)
-    fill(V("prm", 144, 160), 0)
-    fill(V("v8", 144, 208), 8)
-    act(V("v8", 80, 144), V("cnt", 0, 64), scale=-1.0, bias=colf(lambda a, h, p, c: -64 * a))
-    C7, C8 = colf(lambda a, h, p, c: 72 - 64 * (4 * h + a) - 512 * (1 - a % 2)), colf(lambda a, h, p, c: 8 - 256 * h)
+    fill(V("v8", 192, 256), TOP + 8)
+    for c0 in (64, 256):
+        act(V("v8", c0, c0 + 64), V("cnt", 0, 64), scale=-1.0, bias=colf(lambda a, h, p, c: TOP - 64 * a))
+    C7 = colf(lambda a, h, p, c: TOP + 72 - 64 * (4 * h + a) - 512 * (1 - a % 2))
+    C8 = colf(lambda a, h, p, c: TOP + 8 - 256 * h)
     CW = colf(lambda a, h, p, c: 2 - p % 2)
-    CG = colf(lambda a, h, p, c: 16 * (p // 2) + 3)
+    CW7 = colf(lambda a, h, p, c: 126 - 63 * (p % 2))
+    CK = colf(lambda a, h, p, c: 2 - p // 8)
+    fill(V("seg6"), 1)
+    fill(V("seg6", 0, 192, 6), 0)
+    iota(V("x0", 2, 192, 3), [[0, 4], [8, 8], [-300, 2]], 6, 0)
+    act(V("x0", 2, 192, 3), V("x0", 2, 192, 3), F.Relu)
     act(V("jc", 0, 64), IND(V("cnt", 0, 64), L("REV")))
     act(V("jc", 64, 128), V("jc", 0, 64), scale=4096.0, bias=colf(lambda a, h, p, c: 4096 * (64 * (4 * h + a) + 1) + DB * h))
     for u in range(2):
@@ -440,6 +478,9 @@ def rank_program(g, core, T, topo):
     for k in range(4):
         iota(V("nt", 256 + 128 * k, 384 + 128 * k), [[32, 2], [1, 8], [64, 8]], 16 * (k % 2) + 8 * (k // 2), 0)
     const(lambda c, e: V("nt", 128 + c, 128 + e), table(128, lambda a, h, p, c: 64 * (c % 8) + 32 * (a % 2) + 16 * (a // 2) + c // 8))
+    fill(V("ea", 0, 16), 0, False)
+    fill(V("ea", 80, 96), 0, False)
+    fill(V("ea", 160, 176), 0, False)
     fill(V("vi", 0, 16), 0, False)
     fill(V("vi", 144, 160), 0, False)
     for nm in ("sa", "sb", "nw"):
@@ -447,14 +488,10 @@ def rank_program(g, core, T, topo):
     fill(V("ht", 256, 512), 0)
     fill(V("et", 0, 256), 0)
     fill(V("sm", 1, 128, 2), 0)
-    iota(V("vcon"), [[0, 8], [1, 4], [0, 4]], 0, 0)
-    fill(V("tab"), 0)
-    fill(V("d0", 0, 256, 4), 0)
-    fill(V("d0", 1, 256, 4), 1)
-    fill(V("seg4"), 1)
-    fill(V("seg4", 0, 128, 4), 0)
-    fill(V("horn"), 16)
-    fill(V("horn", 0, 128, 4), 0)
+    fill(V("seg8"), 1)
+    fill(V("seg8", 0, 512, 8), 0)
+    act(V("d0"), V("seg8", 0, 512, 2))
+    act(V("horn"), V("seg8", 0, 256, 2), scale=16.0)
     fill(V("lane"), -8)
     for h in range(2):
         key = [32 * (e // 32) + e // 4 % 8 + 8 * [slot(h, t) for t in range(4)].index(e % 4) for e in range(64)] + [0]
@@ -463,9 +500,8 @@ def rank_program(g, core, T, topo):
                 fill(V("lane", 64 * h + s, 64 * h + 64, 4), key[s] - key[s + 1])
         for e in (31, 63):
             fill(V("lane", 64 * h + e, 64 * h + e + 1), key[e] - key[e + 1])
-    fill(V("seg8"), 1)
-    op("p", lambda: g.affine_select(T.eb[:, :], T.seg8[:, 0:516], [[-1, 516]], A.is_equal, 0.0, 3, 4), [V("eb")], [V("seg8")], 1.2)
-    fill(V("seg8", 0, 512, 8), 0)
+    fill(V("eb"), 0)
+    ts(V("eb", 3, 515, 4), V("cnt"), colf(lambda a, h, p, c: 32 * a + 16 * h + p), A.is_equal)
     for b in range(4):
         quant(V("ebq", 128 * b, 128 * b + 128), V("ebs", 128 * b, 128 * b + 128), V("eb", 3 - b, 515 - b))
     quant(V("uq"), V("us"), V("ut"))
@@ -487,14 +523,12 @@ def rank_program(g, core, T, topo):
     for nm in ("va", "vb"):
         tt(V(nm, 16, 80), IND(V("raw"), L("RAW")), V("cj", 64, 128), A.mult)
     act(V("nw", 11, 264, 4), IND(V("va", 16, 80), L("REV")))
-    far = TUNE["far"]
-    for k in range(far):
-        b0, b1, t0 = 96 * (k % 3), 96 * ((k + 1) % 3), 160 * (k % 2)
+    for k in range(6):
+        b0, b1, t0 = 80 * (k % 3), 80 * ((k + 1) % 3), 160 * (k % 2)
         act(V("pr", b1 + 16, b1 + 80), IND(V("pr", b0, b0 + 80), V("ptr", 16 * max(k - 1, 0), 16 * max(k - 1, 0) + 4)))
-        if k != 5 or far == 6:
-            tr(V("pt", t0, t0 + 64), V("pr", b1 + 16, b1 + 80))
-            tr(V("pt", t0 + 64, t0 + 160), V("pr", b1, b1 + 96))
-            act(V("ptr", 16 * min(k + 1, 6), 16 * min(k + 1, 6) + 16), IND(V("pt", t0, t0 + 160), L("SEL")), F.Relu)
+        tr(V("pt", t0, t0 + 64), V("pr", b1 + 16, b1 + 80))
+        tr(V("pt", t0 + 64, t0 + 160), V("pr", b1, b1 + 96))
+        act(V("ptr", 16 * k + 16, 16 * k + 32), IND(V("pt", t0, t0 + 160), L("SEL" if k < 5 else "SEL6")), F.Relu)
     act(V("nt", 0, 128), IND(V("nt", 256, 768), V("paru", 0, 8)))
     act(V("r2"), IND(V("nt", 0, 256), L("R2")))
     for c in range(2):
@@ -513,7 +547,8 @@ def rank_program(g, core, T, topo):
         act(V("ptr", 16 * k, 16 * k + 16), IND(V(tb, 0, 2 * n + 32), L(sel)), F.Relu, -1.0, bias)
 
     def step(o, w, own, lst, c0, c1, end):
-        tt(V(o, 16 + c0, 16 + c1), IND(V(w, 0, 16 + end), V("ptr", 16 * lst + c0 // 16, 16 * lst + c1 // 16)), V(own, 16 + c0, 16 + c1), A.max)
+        l0 = 16 * lst + (c0 - 32) // 8 * (c0 > 0)
+        tt(V(o, 16 + c0, 16 + c1), IND(V(w, 0, 16 + end), V("ptr", l0, l0 + (c1 - c0) // 16)), V(own, 16 + c0, 16 + c1), A.max)
 
     def by_steps(old, cur, nxt, again, runs):
         for k in range(TUNE["steps"]):
@@ -539,35 +574,31 @@ def rank_program(g, core, T, topo):
         act(V("wt", 144, 156), V("fi", 32, 44), scale=-126.0)
         tt(V("wt", 160, 172), V("wt", 128, 140), V("wt", 144, 156), A.add)
         act(L("LV"), V("wt", 160, 172), scale=0.5)
-        cyc = new("row", 12)
-        iota(cyc, [[0, 2], [1, 6]], 0, 0)
         W = lambda k, c0=0, c1=6: V("wt", 16 * k + c0, 16 * k + c1)
-        ts(W(0, 0, 12), cyc, p, A.not_equal, 0.5, A.mult)
-        ts(W(1, 0, 12), cyc, p, A.is_equal, 32.0, A.mult)
-        scan(W(2, 0, 12), W(0, 0, 12), W(1, 0, 12), 0.0, A.mult, A.add)
-        ts(W(5), V("cnt", 0, 6), p, A.is_equal)
-        scan(W(3), W(4), W(5), 0.0, A.mult, A.add)
-        act(W(5), W(3), scale=-64.0)
-        tt(W(6), W(5), W(2, 6, 12), A.subtract)
+        ts(W(0), V("cnt", 0, 6), p, A.is_equal, 1.0 / 32, A.mult)
+        ts(W(1), V("cnt", 0, 6), p, A.add, 5.0, A.is_equal)
+        scan(W(2), W(4), W(0), 0.0, A.mult, A.add)
+        scan(W(3), W(4), W(1), 0.0, A.mult, A.add)
+        act(V("gi", 0, 64), V("cnt", 0, 64), scale=W(2, 5, 6), bias=-0.499)
+        act(V("th", 0, 64), V("jc", 0, 64), scale=W(3, 5, 6))
+        act(V("gi", 64, 128), V("th", 0, 64), scale=1.0 / 63, bias=-0.499)
+        act(V("gt", 80, 144), V("gi", 0, 64), scale=-64.0)
+        act(V("gt", 144, 208), V("gi", 64, 128), scale=63.0)
+        tt(V("gt", 80, 144), V("gt", 80, 144), V("th", 0, 64), A.subtract)
+        tt(V("gt", 16, 80), V("gt", 80, 144), V("gt", 144, 208), A.add)
         fill(V("gt", 0, 16), 128)
-        fill(V("gt", 16, 17), 0)
-        fill(V("th", 0, 1), 0)
-        for b in range(6):
-            act(V("gt", 16 + (1 << b), 16 + (2 << b)), V("gt", 16, 16 + (1 << b)), bias=W(6, b, b + 1))
-            act(V("th", 1 << b, 2 << b), V("th", 0, 1 << b), bias=W(3, b, b + 1))
-        act(V("th", 64, 128), V("th", 0, 64), scale=8192.0)
-        act(V("th", 128, 192), V("th", 0, 64), scale=8128.0, bias=72.0)
+        act(V("th", 64, 128), V("gi", 0, 64), scale=8192.0)
+        act(V("th", 128, 192), V("gi", 0, 64), scale=8128.0, bias=72.0)
         for nm in ("ba", "bb", "bc"):
             fill(V(nm, 0, 16), -10000)
         for nm in ("ba", "bb"):
-            tt(V(nm, 16, 80), IND(V("gt"), V("ptr", 0, 4)), V("th", 64, 128), A.add)
+            tt(V(nm, 16, 80), IND(V("gt", 0, 80), V("ptr", 0, 4)), V("th", 64, 128), A.add)
         early(TUNE["bb"])
         cur = by_steps("ba", "bb", "bc", "ba", TUNE["runs"] if TUNE["steps"] < 7 else ())
         early(TUNE["bs"])
         tt(V("th", 192, 256), V("th", 128, 192), V(cur, 16, 80), A.subtract)
         for (c0, c1) in ((0, 16), (208, 240), (304, 336), (592, 624), (880, 896)):
             fill(V("xg", c0, c1), 0)
-        fill(V("xh", 416, 480), 0)
         first = new("col")
         ts(first, p, 0.0, A.is_equal)
         sc, bi = new("col"), new("col")
@@ -576,7 +607,7 @@ def rank_program(g, core, T, topo):
         for c in (0, 6):
             act(V("xg", 16 + 16 * c, 112 + 16 * c), IND(V("th", 192, 256), V("lu", at["LV"][0] + c, at["LV"][0] + c + 6)), scale=sc, bias=bi)
         both("xg", "xh", 192, 0, 0, 0.5)
-        act(V("sh", 0, 16), IND(V("xh", 0, 480), L("SELV")), F.Relu)
+        act(V("sh", 0, 16), IND(V("xh", 0, 416), L("SELV")), F.Relu)
         fill(V("plw", 0, 8), -8)
         for s in range(4):
             act(V("plw", 8 + 64 * s, 72 + 64 * s), V("jc", 0, 64), bias=64.0 * s)
@@ -592,6 +623,7 @@ def rank_program(g, core, T, topo):
         act(V("xg", 464, 592), IND(V("w2"), V("ptr", 144, 152)))
         for k in range(2):
             act(V("xg", 624 + 128 * k, 752 + 128 * k), IND(V("xg", 336 + 128 * k, 464 + 128 * k), L("NK")))
+            early(TUNE["scat"])
         for k in range(2):
             both("xg", "xh", 256, 320 + 288 * k, 640 + 544 * k, 0.5)
             act(V("sh", 32 + 16 * k, 48 + 16 * k), IND(V("xh", 640 + 544 * k, 1184 + 544 * k), L("SELW")), F.Relu, bias=8.0)
@@ -610,7 +642,7 @@ def rank_program(g, core, T, topo):
             act(V("sb", 8, 72, 2), V("nw", 11, 136, 4))
             cur, old, c0 = "sb", "sa", 8
             for k in range(1, 6):
-                tt(V(old, 9, 72, 2), IND(V(cur, 0, 40), V("sh", 2 * k, 2 * k + 2)), V(cur, 40, 72), A.max)
+                tt(V(old, 9, 72, 2), IND(V(cur, 0, 40), V("sh", 2 * k + k // 4 * 4, 2 * k + k // 4 * 4 + 2)), V(cur, 40, 72), A.max)
                 act(V(old, 8, 72, 2), V(cur, 8, 40))
                 cur, old = old, cur
         if last:
@@ -624,14 +656,25 @@ def rank_program(g, core, T, topo):
             share(cur, c0, a)
         nxt = "v7" if first else old
         tt(V(nxt, c0, c0 + 64), IND(V("w7"), V("ptr", 112, 116) if first else V("sh", 16, 20)), V(cur, c0, c0 + 64), A.max)
+        n0 = len(ops)
+        for k, (src, quads) in enumerate(((cur, (0,)), (nxt, (1,))) if last else ()):
+            act(V("ea", 80 * k + 16, 80 * k + 80), IND(V(src, c0, c0 + 64), L("REV")))
+            both("ea", "eb2", 64, 80 * k, 160 * k)
+            ts(V("ec", 16 * k, 16 * k + 16), IND(V("eb2", 160 * k, 160 * k + 160), L("FE")), 4095, A.bitwise_and)
+            for a in quads:
+                for b in range(4):
+                    act(Q("el", b, 32 + 4 * a, 36 + 4 * a), Q("ec", a, 16 * k + 4 * b, 16 * k + 4 * b + 4))
+        for o in ops[n0:]:
+            o["ahead"] = TUNE["soon"]
         if first:
             share(nxt, c0, 1)
             pointer(nxt, 8, C8, 64, "SEL")
-            tt(V("v8", 16, 80), IND(V("ww", 0, 136), V("ptr", 128, 132)), V(nxt, 16, 80), A.max)
+            tt(V("v8", 128, 192), IND(V("ww", 0, 136), V("ptr", 128, 132)), V(nxt, 16, 80), A.max)
             for a in (2, 3):
-                share("v8", 16, a)
-            act(V("prm", 16, 144), IND(V("v8"), L("PERM")))
-            pointer("prm", 9, 8.0, 128, "SELX")
+                share("v8", 128, a)
+            for k in range(8):
+                tr(V("tc", 32 * k, 32 * k + 32), V("v8", 64 + k, 320, 8))
+            act(V("ptr", 144, 160), IND(V("tc", 0, 256), L("SELX")), F.Relu, -1.0, TOP + 8.0)
             for c in range(2):
                 act(V("vi", 16 + 64 * c, 80 + 64 * c), IND(V("ww"), V("ptr", 144 + 4 * c, 148 + 4 * c)))
             later_lists()
@@ -641,19 +684,25 @@ def rank_program(g, core, T, topo):
             l0 = 48 if last else 32
             for c in range(2):
                 act(V("tq", 64 * c, 64 * c + 64), IND(V("ww", 0, 136), V("sh", l0 + 8 + 4 * c, l0 + 12 + 4 * c)))
-            tt(V("vi", 16, 144), IND(V("ww"), V("sh", l0, l0 + 8)), V("tq"), A.max)
-        both("vi", "ti", 128)
+            for (e0, e1) in TUNE["bcut"]:
+                tt(V("vi", 16 + e0, 16 + e1), IND(V("ww"), V("sh", l0 + e0 // 16, l0 + e1 // 16)), V("tq", e0, e1), A.max)
+        for (e0, e1) in TUNE["bcut"]:
+            tr(V("ti", e0, e1), V("vi", 16 + e0, 16 + e1))
+            e1 += 32 * (e1 == 128)
+            tr(V("ti", 128 + e0, 128 + e1), V("vi", e0, e1))
         ts(V("yy"), IND(V("ti"), L("FSL" if last else "FS")), 4095, A.bitwise_and)
+        ops[-1]["mark"] = "el"
         for a in range(4):
             if last:
-                for u in range(2):
+                for u in range(1 - a // 2, 2):
                     act(Q("yy", a ^ 1, 32 * u + 16 * (a % 2), 32 * u + 16 * (a % 2) + 16), Q("yy", a, 64 + 16 * u, 80 + 16 * u))
             else:
                 act(Q("yy", a ^ 1, a % 2, 64, 2), Q("yy", a, 64, 96))
         for b in range(2):
             for s in range(2):
                 if last:
-                    tt(Q("el", 2 * b, 16 * s, 16 * s + 16, 1, 2), Q("yy", 2 * s, 2 * b, 64, 4, 2), Q("yy", 2 * s, 2 * b + 1, 64, 4, 2), A.max)
+                    u = 1 - s
+                    tt(Q("el", 2 * b, 16 * s + 8 * u, 16 * s + 16, 1, 2), Q("yy", 2 * s, 32 * u + 2 * b, 64, 4, 2), Q("yy", 2 * s, 32 * u + 2 * b + 1, 64, 4, 2), A.max)
                 else:
                     tt(Q("el", 2 * b, s, 32, 2, 2), Q("yy", 2 * s, 32 * b, 32 * b + 16, 1, 2), Q("yy", 2 * s, 32 * b + 16, 32 * b + 32, 1, 2), A.max)
 
@@ -666,7 +715,12 @@ def rank_program(g, core, T, topo):
     def pieces(r, gath, parts, sq, ss):
         for (l0, l1, n0, engs) in gath:
             for t in range(4):
-                plane(engs[t], r, t, l0, l1, n0)
+                if engs[t] == "h":
+                    m = (l0 + l1) // 4 * 2
+                    plane("x", r, t, l0, m, n0)
+                    plane("x", r, t, m, l1, n0 + 16 * (m - l0))
+                else:
+                    plane(engs[t], r, t, l0, l1, n0)
         for i, (c0, c1) in enumerate(parts):
             quant(V("eq", K + c0, K + c1), V("es", K + c0, K + c1), V("et", 4 * (K + c0), 4 * (K + c1)))
             if i == 0 and r < 3:
@@ -678,27 +732,27 @@ def rank_program(g, core, T, topo):
         pieces(r, TUNE["gath"], TUNE["pieces"], "urq", "urs")
         for b in range(4):
             mm(V("ps", 2048 + 512 * b, 2176 + 512 * b), V("wq", 128 * b, 128 * b + 128), V("wsc", 128 * b, 128 * b + 128), V("eq", 0, 128), V("es", 0, 128))
-        ts(V("kb", 0, 64), V("ps", 1600, 1664), 0.0, A.is_gt, CW, A.mult)
-        ts(V("kb", 64, 80), V("ps", 1600, 1616), 0.0, A.is_gt, CW, A.mult)
-        tr(V("kbt", 0, 64), V("kb", 0, 64), 0.5)
-        tr(V("kbt", 64, 128), V("kb", 16, 80), 0.5)
-        tt(V("fs%d" % r), V("kbt", 0, 128, 4), V("kbt", 1, 128, 4), A.add)
-        send(dst, V("fl%d" % r), V("fs%d" % r), "af%d" % r, TUNE["lat"] + (0.0 if r else 1.2), 1 if r else 2)
+        ts(V("kb", 0, 64), V("ps", 1600, 1664), 0.0, A.is_gt, CK, A.mult)
+        ts(V("kb", 64, 80), V("ps", 1600, 1616), 0.0, A.is_gt, CK, A.mult)
+        fs = "fs%d" % r
+        for t, c0 in enumerate((0, 32, 16, 48)):
+            tr(V(fs, t, 128, 4), V("kb", c0, c0 + 32), 0.5)
+        send(dst, V("fl%d" % r), V(fs, 0, 32), "af%d" % r, TUNE["lat"] + (0.0 if r else 1.2), 1 if r else 2, [V(fs, 32, 64)])
         for i, (c0, c1) in enumerate(TUNE["pieces"]):
-            ts(V("rows", max(c0, 0), c1), V("ps", 512 * i + max(-c0, 0), 512 * i + c1 - c0), 0.0, A.is_gt, CW, A.mult)
+            above(V("rows", max(c0, 0), c1), V("ps", 512 * i + max(-c0, 0), 512 * i + c1 - c0))
         for b in range(4):
             act(V("ht", b, 256, 4), V("ps", 2112 + 512 * b, 2112 + 512 * b + K), scale=0.03125)
         hq, hs = "hq%d" % r, "hs%d" % r
         quant(V(hq, 64, 192), V(hs, 64, 192), V("ht"))
         send(dst, u8(V(hq, 0, 64)), u8(V(hq, 64, 128)), "ah%d" % r, 4.0)
         send(dst, V(hs, 0, 64), V(hs, 64, 128), "ah%d" % r, 4.0)
-        act(V("op", 0, 64), IND(V("rows"), V("ol", 12, 16)), scale=7.0, bias=CG)
-        act(V("op", 64, 128), IND(V("rows"), V("ol", 0, 4)))
-        tr(V("x0", 0, 128, 2), V("op", 0, 64), 0.5)
-        tr(V("x0", 1, 128, 2), V("op", 64, 128), 0.5)
-        scan(V("xs"), V("seg4"), V("x0"), 0.0, A.mult, A.add, 0.5)
-        tr(V("ixu"), V("xs", 3, 128, 4))
-        act(V("op2"), IND(V("rows"), V("ol", 4, 12)))
+        weigh(V("op", 0, 64), IND(V("rows"), V("ol", 12, 16)), CW7)
+        weigh(V("op", 64, 128), IND(V("rows"), V("ol", 0, 4)), CW)
+        tr(V("x0", 0, 192, 3), V("op", 0, 64), 0.5)
+        tr(V("x0", 1, 192, 3), V("op", 64, 128), 0.5)
+        scan(V("xs"), V("seg6"), V("x0"), 0.0, A.mult, A.add, 0.5)
+        tr(V("ixu"), V("xs", 5, 192, 6))
+        weigh(V("op2"), IND(V("rows"), V("ol", 4, 12)), CW)
         tr(V("opt"), V("op2"), 0.5)
         tt(V("sm", 0, 128, 2), V("opt", 0, 128, 2), V("opt", 1, 128, 2), A.add)
         tr(V("smr"), V("sm"), 0.5)
@@ -706,11 +760,12 @@ def rank_program(g, core, T, topo):
 
     def choose(r):
         fl = "fl%d" % r
-        tt(V("xe"), IND(V(fl), L("XE")), V("vcon"), A.is_equal, ext="af%d" % r)
+        for s in range(4):
+            equal(V("xe", 32 * s, 32 * s + 32), V(fl), s, "af%d" % r)
         scan(V("tab", 0, 256, 2), V("horn"), V("xe"), 0.0, A.mult, A.add)
         for d in (1, -1, 2, -2, 3, -3):
-            e0, e1 = max(0, -d), 32 - max(0, d)
-            tt(V("tab", 8 * e0 + 6 + d, 8 * e1 + d, 8), V("tab", 8 * e0 + 6, 8 * e1, 8), V("tab", 8 * (e0 + d) + 6, 8 * (e1 + d), 8), A.add)
+            e0, e1 = max(0, -d), 4 - max(0, d)
+            tt(V("tab", 64 * e0 + 6 + d, 64 * e1 + d, 8), V("tab", 64 * e0 + 6, 64 * e1, 8), V("tab", 64 * (e0 + d) + 6, 64 * (e1 + d), 8), A.add)
         act(V("fin"), IND(V(fl), L("FIN")), ext="af%d" % r)
         tr(V("fwt"), V("fin"), 0.5)
         act(V("fw", 0, 64), IND(V("fwt"), L("KP")))
@@ -737,14 +792,18 @@ def rank_program(g, core, T, topo):
             ts(V("yi", t, 256, 4), V("yt"), 4 * (3 - t), A.logical_shift_right, 15 << 6, A.bitwise_and)
         for c in range(4):
             scan(V("sc", c, 256, 4), V("yi", 64 * c, 64 * c + 64), V("lane", 64 * (c % 2), 64 * (c % 2) + 64), 1000.0, A.min, A.add)
-        ku = V("sc", 252, 256)
-        act(V("d1", 1, 256, 4), IND(V("fk"), ku))
-        tt(V("d0", 2, 256, 4), IND(V("fw"), ku), V("smr", 0, 64), A.not_equal)
-        tt(V("d0", 3, 256, 4), IND(V("fw"), ku), V("smr", 64, 128), A.not_equal)
-        scan(V("nw", 8, 264), V("d0"), V("d1"), 0.0, A.mult, A.add)
+        for (c0, c1) in TUNE["ccut"]:
+            ku, e0, e1 = V("sc", 252 + c0, 252 + c1), 16 * c0, 16 * c1
+            act(V("d1", 4 * e0 + 1, 4 * e1, 4), IND(V("fk"), ku))
+            tt(V("d0", 4 * e0 + 2, 4 * e1, 4), IND(V("fw"), ku), V("smr", e0, e1), A.not_equal)
+            tt(V("d0", 4 * e0 + 3, 4 * e1, 4), IND(V("fw"), ku), V("smr", 64 + e0, 64 + e1), A.not_equal)
+            scan(V("nw", 8 + 4 * e0, 8 + 4 * e1), V("d0", 4 * e0, 4 * e1), V("d1", 4 * e0, 4 * e1), 0.0, A.mult, A.add)
+        ops[-1]["mark"] = "nw"
 
+    later = []
     for r in range(3):
         inherit(r)
+        later.append(len(ops))
         symbols(r)
         choose(r)
     inherit(3)
@@ -763,9 +822,17 @@ def rank_program(g, core, T, topo):
     def meet(x, y):
         if x[1] >= y[2] or y[1] >= x[2] or x[3] >= y[4] or y[3] >= x[4]:
             return False
+        if y[4] - y[3] <= 4 or x[4] - x[3] <= 4:
+            return bool(set(range(x[3], x[4], x[5])) & set(range(y[3], y[4], y[5])))
         s = min(x[5], y[5])
         return not (s > 1 and max(x[5], y[5]) % s == 0 and (x[3] - y[3]) % s != 0)
 
+    for o in ops:
+        if any(f[0] in ("kb", "xe", "tab") or f[0][:2] == "fs" and o["r"] or f[:5] in (("et", 0, 128, 256, 512), ("eq", 0, 128, 0, 128), ("ps", 0, 128, 1536, 2048))
+               or f[0] == "et" and 256 <= f[3] < 260 for f in o["w"]) or o["sem"] == "sent" and o["r"][0][0][:2] == "fs":
+            o["ahead"] = TUNE["hot"]
+        if o["id"] > later[0] and any(f[0] in ("sa", "sb", "w7", "ww", "tq", "vi", "ti", "yy") or f[0] == "el" and f[3] < 32 for f in o["w"]):
+            o["ahead"] = TUNE["main"]
     met, group = {}, {}
     for o in ops:
         if o["dma"]:
@@ -783,8 +850,30 @@ def rank_program(g, core, T, topo):
             met.setdefault(f[0], []).append((f, False, o["id"]))
         for f in o["w"]:
             met.setdefault(f[0], []).append((f, True, o["id"]))
+    need = [0.0] * len(ops)
+    for o in reversed(ops):
+        for q in o["pre"]:
+            if q < o["id"]:
+                need[q] = max(need[q], need[o["id"]] + o["cost"] + o["lat"] + HOP)
+    scans = [o["id"] for o in ops if o.get("mark") == "nw"]
+    for o in ops[:later[0]]:
+        if not o["dma"] and need[o["id"]] < need[scans[1]]:
+            o["pre"] = o["pre"] | {scans[TUNE["late"]]}
     for o in ops:
         o["succ"] = []
+        if o["w"] and o["w"][0][0] in TUNE["past"] and not o["r"]:
+            o["pre"] = o["pre"] | set(q for q in ops[arrive["af0"][0]]["dep"])
+    ops_ = sorted(ops, key=lambda o: o["id"])
+    seen_, topo_ = set(), []
+    while ops_:
+        rest = []
+        for o in ops_:
+            if o["pre"] <= seen_:
+                seen_.add(o["id"])
+                topo_.append(o)
+            else:
+                rest.append(o)
+        ops_ = rest
     for o in ops:
         for q in o["pre"]:
             ops[q]["succ"].append(o["id"])
@@ -792,15 +881,17 @@ def rank_program(g, core, T, topo):
     def place(rank_, back):
         start, left = {}, {o["id"]: len(o["succ" if back else "pre"]) for o in ops}
         taken = {e: [] for e in "vapts"}
-        ready = [o["id"] for o in ops if left[o["id"]] == 0]
+        rank_ = [rank_[o["id"]] - (0.0 if back else o.get("ahead", 0.0)) for o in ops]
+        ready = [(rank_[o["id"]], o["id"]) for o in ops if left[o["id"]] == 0]
         while ready:
-            i = min(ready, key=lambda q: (rank_[q], q))
+            i = min(ready)
             ready.remove(i)
+            i = i[1]
             o = ops[i]
             if back:
                 t = max([start[q] + ops[q]["cost"] + HOP for q in o["succ"]] + [0.0]) + o["lat"] + o["early"]
             else:
-                t = max([start[q] + ops[q]["cost"] + ops[q]["lat"] + HOP for q in o["pre"]] + [0.4 + 0.061 * len(o["behind"]) if o["behind"] else 0.0])
+                t = max([start[q] + ops[q]["cost"] + ops[q]["lat"] + HOP for q in o["pre"]] + [start[z] + 0.061 for z in o["behind"] if z in start] + [0.0])
             found = []
             for (e, c) in ([(e, w[1]) for e, w in o["ways"].items()] if "ways" in o and not back else [(o["eng"], o["cost"])]):
                 tk, k, s = taken[e], len(taken[e]), t
@@ -811,12 +902,13 @@ def rank_program(g, core, T, topo):
                     k += 1
                 found.append((s + c + (TUNE["bias"] if e == "v" else 0.0), e, c, s, k))
             _, o["eng"], o["cost"], s, k = min(found)
-            taken[o["eng"]].insert(k, (s, s + o["cost"]))
+            tk = taken[o["eng"]]
+            tk.insert(k, (max(s - TUNE["guard"], tk[k - 1][1] if k else 0.0) if o["sem"] == "sent" and not back else s, s + o["cost"]))
             start[i] = s
             for q in o["pre" if back else "succ"]:
                 left[q] -= 1
                 if left[q] == 0:
-                    ready.append(q)
+                    ready.append((rank_[q], q))
         return start
 
     def ends(start):
@@ -827,7 +919,7 @@ def rank_program(g, core, T, topo):
 
     if "order" not in PLAN:
         tail = {}
-        for o in reversed(ops):
+        for o in reversed(topo_):
             tail[o["id"]] = o["cost"] + o["lat"] + o["early"] + max([HOP + tail[s] for s in o["succ"]] + [0.0])
         urgent, best = {q: -tail[q] for q in tail}, None
         for _ in range(TUNE["it"]):
@@ -854,9 +946,151 @@ def rank_program(g, core, T, topo):
             urgent = {q: kept[q] + (float(rng.normal()) * sd if i and lo <= kept[q] < lo + span else 0.0) for q in kept}
             start = place(urgent, False)
             order = sorted(start, key=lambda q: (start[q], q))
-            end = sum(replay(order, *case) for case in TUNE["cases"])
+            end = sum(replay(order, *case[:3]) for case in TUNE["cases"])
             if best is None or end <= best:
                 best, kept, PLAN["order"] = end, urgent, [(q, ops[q]["eng"]) for q in order]
+        n, cases = len(ops), TUNE["cases"]
+        above, pre = [0] * n, [None] * n
+        for o in topo_:
+            far_ = 0
+            for q in o["pre"]:
+                far_ |= above[q]
+            pre[o["id"]] = [q for q in o["pre"] if not far_ >> q & 1]
+            above[o["id"]] = far_ | sum(1 << q for q in o["pre"])
+        succ = [[] for _ in ops]
+        for q in range(n):
+            for z in pre[q]:
+                succ[z].append(q)
+        ways = [{e: w[1] for e, w in o["ways"].items()} if "ways" in o else {o["eng"]: o["cost"]} for o in ops]
+        lats, move = [[o["lat"] * c[3] for o in ops] for c in cases], [o.get("move", 0.05) if o["sem"] == "out" else None for o in ops]
+        scale = [[1.0 if o["dma"] else c[0] * c[1] if o["picks"] else c[0] for o in ops] for c in cases]
+
+        def run(part, eng, c, state, whole):
+            hop, sc, lat = cases[c][2], scale[c], lats[c]
+            free, done, last, why, out, end, at_ = dict(state[0]), state[1], {}, {}, 0.0, 0.0, None
+            for q in part:
+                e = eng[q]
+                t, w = free[e], last.get(e)
+                for z in pre[q]:
+                    if done[z] > t:
+                        t, w = done[z], z
+                why[q], last[e] = w, q
+                free[e] = t = t + ways[q][e] * sc[q]
+                t += lat[q]
+                if move[q] is not None:
+                    t = out = max(t, out) + move[q]
+                done[q] = t + hop
+                if t > end and (whole or e in "va"):
+                    end, at_ = t, q
+            return end / (cases[c][0] + 2), at_, why, free
+
+        def fast(part, eng, c, state, whole):
+            lat, free, done, out, cost, end = lats[c], dict(state[0]), state[1], 0.0, costs[c], 0.0
+            hop = cases[c][2]
+            for q in part:
+                e = eng[q]
+                t = free[e]
+                for z in pre[q]:
+                    if done[z] > t:
+                        t = done[z]
+                free[e] = t = t + cost[e][q]
+                if slow[q]:
+                    t += lat[q]
+                    if move[q] is not None:
+                        t = out = max(t, out) + move[q]
+                    if whole and t > end:
+                        end = t
+                done[q] = t + hop
+            return max(end, free["v"], free["a"]) / (cases[c][0] + 2)
+
+        slow = [o["dma"] for o in ops]
+        costs = [{e: [ways[q].get(e, 0.0) * sc[q] for q in range(n)] for e in "vapts"} for sc in scale]
+
+        def improve(order, eng, i0, i1, moves, heat):
+            states = []
+            for c in range(len(cases)):
+                done = [0.0] * n
+                states.append((run(order[:i0], eng, c, ({e: 0.0 for e in "vapts"}, done), True)[3], done))
+            part, whole = order[i0:i1], i1 == n
+            each = [fast(part, eng, c, states[c], whole) for c in range(len(cases))]
+            best = now = sum(each)
+            kept_, helds = (part, eng), None
+            for i in range(moves):
+                if helds is None:
+                    helds = []
+                    for c in range(len(cases)):
+                        _, q, why, _ = run(part, eng, c, states[c], whole)
+                        while why.get(q) is not None:
+                            if why[q] not in pre[q] and not ops[q]["behind"]:
+                                helds.append((why[q], q))
+                            q = why[q]
+                    ends_ = list(states[0][1])
+                if not helds:
+                    break
+                p, q = helds[int(rng.integers(len(helds)))]
+                kind, trial, eng2 = rng.random(), list(part), eng
+                ip, iq = part.index(p), part.index(q)
+                if rng.random() < TUNE["anew"]:
+                    ip = max(0, ip - int(rng.integers(0, TUNE["run"])))
+                    iq = min(len(part), iq + 1 + int(rng.integers(0, TUNE["run"])))
+                    hop, free, done, eng2 = cases[0][2], dict(states[0][0]), list(ends_), dict(eng)
+                    for z in part[:ip]:
+                        free[eng[z]] = ends_[z] - hop - lats[0][z]
+                    sd, taken, starts = TUNE["sd"][i % 3], {e: [] for e in free}, {}
+                    rank_ = {z: ends_[z] - lats[0][z] - costs[0][eng[z]][z] + sd * float(rng.normal()) for z in part[ip:iq]}
+                    for z in part[iq - 1:ip - 1 if ip else None:-1]:
+                        for y in pre[z]:
+                            if y in rank_ and rank_[y] >= rank_[z]:
+                                rank_[y] = rank_[z] - 0.001
+                    for z in sorted(rank_, key=rank_.get):
+                        t, found = max([done[y] for y in pre[z]] + [0.0]), []
+                        for e in ways[z]:
+                            s, c = max(t, free[e]), costs[0][e][z]
+                            for (s0, s1) in taken[e]:
+                                if s0 >= s + c - 1e-9:
+                                    break
+                                s = max(s, s1)
+                            found.append((s + c + (TUNE["bias"] if e == "v" else 0.0), e, s, c))
+                        _, e, s, c = min(found)
+                        taken[e].append((s, s + c))
+                        taken[e].sort()
+                        eng2[z], starts[z], done[z] = e, s, s + c + lats[0][z] + hop
+                    trial[ip:iq] = sorted(starts, key=lambda z: (starts[z], rank_[z]))
+                    if any(ops[z]["behind"] for z in starts):
+                        continue
+                elif kind < 0.3:
+                    z = p if len(ways[p]) > 1 and (rng.random() < 0.6 or len(ways[q]) == 1) else q
+                    if len(ways[z]) == 1:
+                        continue
+                    eng2 = dict(eng)
+                    eng2[z] = [e for e in ways[z] if e != eng[z]][0]
+                elif kind < 0.65:
+                    iq = min(len(part) - 1, iq + int(rng.integers(0, 16)) * (rng.random() < 0.4))
+                    late = [z for z in part[ip:iq + 1] if z == p or above[z] >> p & 1]
+                    trial[ip:iq + 1] = [z for z in part[ip:iq + 1] if z not in late] + late
+                else:
+                    ip = max(0, ip - int(rng.integers(0, 16)) * (rng.random() < 0.4))
+                    soon = [z for z in part[ip:iq + 1] if z == q or above[q] >> z & 1]
+                    trial[ip:iq + 1] = soon + [z for z in part[ip:iq + 1] if z not in soon]
+                bar, new_ = heat * (1 - i / moves) * rng.random(), []
+                for c in range(len(cases)):
+                    new_.append(fast(trial, eng2, c, states[c], whole))
+                    if new_[0] > each[0] + bar + 0.03:
+                        break
+                end = sum(new_)
+                if len(new_) == len(cases) and end <= now + bar:
+                    part, eng, each, now, helds = trial, eng2, new_, end, None
+                    if end < best:
+                        best, kept_ = end, (part, eng)
+            return order[:i0] + kept_[0] + order[i1:], kept_[1], best
+
+        order, eng = [q for q, e in PLAN["order"]], {q: e for q, e in PLAN["order"]}
+        for mark, back in TUNE["marks"]:
+            cuts = [0] + [i + 1 for i, q in enumerate(order) if ops[q].get("mark") == mark] + [n]
+            for i0, i1 in zip(cuts, cuts[1:]):
+                order, eng, best = improve(order, eng, max(0, i0 - back), i1, TUNE["moves"] * (i1 - i0) // n, TUNE["heat"])
+        order, eng, best = improve(order, eng, 0, n, TUNE["last"], 0.0)
+        PLAN["order"] = [(z, eng[z]) for z in order]
         PLAN["time"] = best
     order = []
     for (q, e) in PLAN["order"]:

import numpy as np
from concourse.bass import DstId, RemoteDMATransfer
from concourse.mybir import dt, AluOpType, ActivationFunctionType

A = AluOpType
F = ActivationFunctionType
DIST = [1, 2, 4]
C, K = 512, 64
X0 = 3 * K
DB = X0 + 4 * C
PW = DB + 3 * K
LOADS = 1
F32, BF, I32, U16, U8, MX = "float32", "bfloat16", "int32", "uint16", "uint8", "float8_e4m3fn_x4"
GATH = [(0, 4, 0, "vvaa"), (4, 16, 64, "hxxx"), (16, 32, 256, "hxxx")]
PIECES = [(-64, 64), (64, 256), (256, 512)]
GATH_LAST = [(32, 36, 0, "xxxx"), (36, 40, 64, "xxxx"), (16, 24, 128, "xxxx"), (8, 16, 256, "xxxx"), (24, 32, 384, "xxxx")]
PIECES_LAST = [(0, 256), (256, 384), (384, 512)]
STORES = [(0, 256), (256, 512)]
LOOK = [(0, 14, "v"), (14, 24, "a"), (24, 32, "a")]
FLW = 32


def _sb(n, d):
    return ("sbuf", [128, n], d)


SCRATCH = {
    "parq": _sb(32, I32), "raw": _sb(16 * FLW, I32), "ut": _sb(512, BF), "vt": _sb(512, BF),
    "wq": _sb(512, MX), "wsc": _sb(512, U8), "uq": _sb(128, MX), "us": _sb(128, U8), "urq": _sb(128, MX), "urs": _sb(128, U8),
    "ukq": _sb(128, MX), "uks": _sb(128, U8),
    "vq": _sb(128, MX), "vs": _sb(128, U8), "eb": _sb(516, BF), "ebq": _sb(512, MX), "ebs": _sb(512, U8),
    "pi": _sb(2, I32), "fi": _sb(48, I32), "col": _sb(128, F32), "row": _sb(256, F32), "cnt": _sb(128, F32),
    "lu": _sb(176, U16), "cj": _sb(128, F32), "jc": _sb(128, F32), "pjc": _sb(16, F32), "plw": _sb(264, F32),
    "horn": _sb(128, F32), "lane": _sb(128, F32), "seg8": _sb(512, BF),
    "ptr": _sb(176, U16), "paru": _sb(16, U16), "nt": _sb(768, F32), "r2": _sb(256, F32), "r3": _sb(256, F32), "ol": _sb(16, U16),
    "va": _sb(96, F32), "vb": _sb(96, F32), "vc": _sb(96, F32), "vd": _sb(96, F32), "v7": _sb(96, F32), "v8": _sb(320, F32),
    "w7": _sb(72, F32), "ww": _sb(264, F32), "tq": _sb(128, F32),
    "sa": _sb(72, F32), "sb": _sb(72, F32), "pj": _sb(64, F32), "pr": _sb(288, F32), "pt": _sb(320, F32),
    "wt": _sb(176, F32), "gt": _sb(208, F32), "gi": _sb(128, I32), "th": _sb(256, F32), "ba": _sb(80, F32), "bb": _sb(80, F32), "bc": _sb(80, F32),
    "r7": _sb(128, F32), "w2": _sb(264, F32), "xg": _sb(896, BF), "xh": _sb(1728, BF), "sh": _sb(64, U16),
    "vi": _sb(160, I32), "ti": _sb(288, I32), "tb": _sb(288, F32), "tc": _sb(288, F32),
    "yy": _sb(96, I32), "el": _sb(40, U16), "ea": _sb(176, I32), "eb2": _sb(320, I32), "ec": _sb(32, I32), "nw": _sb(264, F32), "flg": _sb(64, F32),
    "pool": _sb(4 * PW, BF), "et": _sb(4 * 576, BF), "eq": _sb(576, MX), "es": _sb(576, U8),
    "ht": _sb(512, BF),
    "kb": _sb(80, BF), "rows": _sb(512, BF), "op": _sb(128, BF), "op2": _sb(128, BF), "opt": _sb(128, BF),
    "x0": _sb(192, BF), "xs": _sb(192, U16), "seg6": _sb(192, BF), "sm": _sb(128, BF), "ixu": _sb(32, U16),
    "xe": _sb(128, F32), "tab": _sb(264, F32), "ac": _sb(512, F32), "ci": _sb(512, I32), "yt": _sb(64, I32), "yi": _sb(256, I32),
    "sc": _sb(256, U16), "fin": _sb(64, BF), "fwt": _sb(64, BF), "fw": _sb(576, BF), "fk": _sb(576, BF), "smr": _sb(128, BF),
    "d0": _sb(256, BF), "d1": _sb(256, F32), "yo": _sb(512, F32),
    "ps": ("psum", [128, 4096], F32),
}
for _r in range(3):
    SCRATCH["fs%d" % _r] = _sb(128, BF)
    SCRATCH["fl%d" % _r] = _sb(32, BF)
    SCRATCH["hq%d" % _r] = _sb(192, MX)
    SCRATCH["hs%d" % _r] = _sb(192, U8)

SEMAPHORES = (["sv", "sa", "sp", "st", "l_par", "l_fl", "l_u", "l_x", "l_y", "l_w", "l_v", "out", "sent"]
              + ["af%d" % r for r in range(3)] + ["ah%d" % r for r in range(3)])
ENG_SEM = {"v": "sv", "a": "sa", "p": "sp", "t": "st"}
CYC, HOP = 0.00105, 0.22
TOP = 512
PTR = 1


def seen(h, c, lane, n):
    return 32 * (c // 2) + lane if c % 2 == h else n + 32 * (c // 2 + 1 - h) + lane


def slot(h, t):
    return t if h == 0 else (3, 2, 0, 1)[t]


def rev(x):
    return sum((x >> b & 1) << (5 - b) for b in range(6))


def parents(m, e, p):
    if m < 4:
        return 64 * (p // 8) + rev(16 * (2 * (m % 2) + m // 2) + 2 * (p % 8) + e)
    return 64 * e + rev(16 * (m - 4) + p)


def spread(a, h, p, c, last):
    if last:
        bm, run = p % 4, 4 * (c // 2 if c < 4 else c - 4) + p // 4
    else:
        bm, run = (c, p // 2) if c < 4 else (2 * (c - 4) + p // 8, p % 8)
    return seen(h, run, 16 * (bm % 2) + 2 * (2 * (2 * (bm // 2) + (a % 2 if c < 4 else 1 - a % 2)) + h), 128)


LISTS = [
    ("PB", 1, None),
    ("PJ", 1, None),
    ("RAW", 4, lambda a, h, p, c: FLW * p + (16 * h + 4 * a) % FLW + c),
    ("SEL", 1, lambda a, h, p, c: seen(h, p % 4, 16 * h + PTR, 64)),
    ("SEL6", 1, lambda a, h, p, c: seen(h, 2 + p // 2 % 2, 16 * h + PTR, 64)),
    ("SELX", 1, lambda a, h, p, c: 32 * (p % 8) + 16 * (1 - h) + PTR),
    ("FS", 6, lambda a, h, p, c: spread(a, h, p, c, False)),
    ("UK", 8, lambda a, h, p, c: 16 * (p % 8) + p // 8),
    ("UR", 8, lambda a, h, p, c: 16 * (p // 2) + p % 2),
    ("PU", 1, lambda a, h, p, c: 16 * (p // 4 % 2) + 4 * a + p % 4),
    ("R2", 16, lambda a, h, p, c: parents(c // 2, c % 2, p) + 128 * h),
    ("REV", 4, lambda a, h, p, c: rev(16 * c + p)),
    ("FIN", 4, lambda a, h, p, c: slot(h, 2 * (c // 2) + h) + 4 * (p // 2)),
    ("KP", 4, lambda a, h, p, c: 32 * (c % 2) + 16 * (p // 8) + 8 * (c // 2) + p % 8),
    ("LV", 12, None),
    ("SELV", 1, lambda a, h, p, c: seen(h, p % 8 + 4 * (p // 8), 16 * h + p % 8 // 2 + 2 * (p // 8), 192)),
    ("SELW", 1, lambda a, h, p, c: seen(h, p, 16 * h, 256)),
    ("NK", 8, lambda a, h, p, c: 16 * (p % 8) + 8 * (c // 4) + 2 * (c % 4) + p // 8),
    ("FE", 1, lambda a, h, p, c: seen(h, p % 4, 2 * (2 * (p // 4) + h), 64)),
    ("FSL", 6, lambda a, h, p, c: spread(a, h, p, c, True)),
    ("REVF", 4, lambda a, h, p, c: 11 + 4 * rev(16 * c + p)),
]


def table(n, f):
    return np.array([[f(P // 32, P // 16 % 2, P % 16, c) for c in range(n)] for P in range(128)], dtype=np.int64)


_P = np.arange(128.0)
FEATURES = {"P": _P}
for _s in range(7):
    for _w in range(1, 6):
        if _s + _w <= (7 if _s > 4 else 5) and (_s + _w <= 4 or _s in (0, 4, 5, 6)):
            FEATURES[(_s, (1 << _w) - 1)] = _P // (1 << _s) % (1 << _w)
for _s, _w in ((0, 19), (3, 12), (0, 4), (2, 2)):
    FEATURES[(_s, _w)] = 1.0 * (np.arange(128) >> _s & _w)
for _s in range(3):
    FEATURES[("x", _s)] = (_P // 16 + _P // (1 << _s)) % 2


def bits(vec):
    c = [float(z) for z in vec]
    for b in range(7):
        for P in range(128):
            if P >> b & 1:
                c[P] -= c[P ^ (1 << b)]
    return {m: c[m] for m in range(1, 128) if c[m]}


def terms(vec, known, have, reuse, free):
    form = {k: bits(v) for k, v in known.items()}
    found = []

    def search(t, tm, depth):
        if not t:
            found.append(tm)
        elif depth:
            for m in {min(t), max(t)} if len(tm) < 2 else (max(t),):
                for k, f in form.items():
                    if m in f and (16 * t[m] / f[m]) % 1 == 0 and all(k != z[0] for z in tm):
                        q, u = t[m] / f[m], dict(t)
                        for j in f:
                            u[j] = u.get(j, 0.0) - q * f[j]
                            if not u[j]:
                                del u[j]
                        if len(u) < len(t) + (0 if tm else 1) and len(u) <= 5 * (depth - 1):
                            search(u, tm + [(k, q)], depth - 1)

    depth = 0
    while not found:
        search(bits(vec), [], depth)
        depth += 1
    if depth < 4:
        search(bits(vec), [], depth)
    best = None
    for tm in found:
        c0 = vec[0] - sum(q * known[k][0] for k, q in tm)
        more = set(k for k, q in tm if k not in have) | set(z for k, q in tm if k[0] == "x" and k not in have for z in ((4, 1), (k[1], 1)) if z not in have)
        ways = [(len(tm), c0, None, tm)]
        for k, q in tm:
            if q == 1 and k[0] in ("col", "x") and k in have and (c0 == 0 or free) and (reuse or len(tm) > 1):
                ways.append((len(tm) - 1, 0, k, [z for z in tm if z[0] != k]))
        for w in ways:
            if best is None or w[0] + len(more) < best[0]:
                best = (w[0] + len(more),) + w[1:]
    return best[1:]


def pattern(r):
    n = len(r)
    for n2 in range(n, 0, -1):
        for n1 in range(n // n2, 0, -1):
            if n % (n1 * n2) == 0:
                s = [int(r[k] - r[0]) if k < n else 0 for k in (n1 * n2, n2, 1)]
                if all(r[i] == r[0] + s[0] * (i // (n1 * n2)) + s[1] * (i // n2 % n1) + s[2] * (i % n2) for i in range(n)):
                    return [[s[0], n // (n1 * n2)], [s[1], n1], [s[2], n2]]
    return None


def product(d):
    rows = [r for r in d if r.any()]
    if not rows:
        return d[:, 0], d[0]
    r = rows[0] // np.gcd.reduce(rows[0])
    k = int(np.nonzero(r)[0][0])
    r = r if r[k] > 0 else -r
    sc = d[:, k] // r[k]
    return (sc, r) if (sc[:, None] * r[None, :] == d).all() and pattern(r) is not None else None


PLAN = {}
TUNE = {"ccut": ((0, 2), (2, 4)), "bcut": ((0, 64), (64, 128)), "late": 1, "scat": 4.0, "past": ("eb", "lane", "xg", "w2", "plw", "fk", "sm", "sa", "sb", "nw", "ht"), "anew": 0.5, "run": 25,
        "main": 0.5, "soon": 1.5, "marks": (("nw", 0), ("el", 0), ("nw", 30)), "last": 1000, "hot": 1.0, "moves": 110000, "heat": 0.04,
        "guard": 1.0, "xp": 256, "steps": 7, "runs": ((32, 48), (48, 64)), "gath": GATH, "pieces": PIECES, "gath3": GATH_LAST,
        "pieces3": PIECES_LAST, "look": LOOK, "bb": 1.0, "bs": 2.0, "out": 1.0, "yo": "aav", "lat": 0.9, "fl": 1.6, "bias": 0.06, "it": 10,
        "cases": ((1.0, 1.0, 0.19, 1.1), (0.9, 0.85, 0.19, 1.35), (1.17, 1.2, 0.24, 0.9)), "tries": 20, "sd": (0.1, 0.25, 0.5),
        "span": (1.0, 2.0, 3.0)}


def rank_program(g, core, T, topo):
    rank = T.rank_of(core)
    if rank is None:
        return
    n_ranks = len(T.cores)
    ops = []
    arrive = {}

    def V(name, c0=0, c1=None, st=1, p0=0, p1=128):
        if c1 is None:
            c1 = T[name].shape[1]
        ap = T[name][p0:p1, c0:c1:st] if st > 1 else T[name][p0:p1, c0:c1]
        n = (c1 - c0 + st - 1) // st
        if name == "ps":
            return (ap, [("ps", 0, 128, c0 // 512 * 512, c0 // 512 * 512 + 512, 1)], n, False)
        return (ap, [(name, p0, p1, c0, c1, st)], n, False)

    def Q(name, a, c0, c1, st=1, n=1):
        return V(name, c0, c1, st, 32 * a, 32 * (a + n))

    def IND(w, o):
        return (w[0].indirect(o[0]), w[1] + o[1], 16 * o[2], True)

    def op(eng, fn, outs, ins, cost, lat=0.0, sem=None, inc=1, ext=None, gives=None):
        w = [f for v in outs for f in v[1]]
        r = []
        for v in ins:
            if isinstance(v, tuple):
                r += v[1]
        ops.append({"eng": eng, "fn": fn, "r": r, "w": w, "sem": sem or ENG_SEM[eng], "inc": inc, "dma": sem is not None,
                    "ext": ext, "cost": cost, "lat": lat, "early": 0.0, "id": len(ops),
                    "picks": any(isinstance(v, tuple) and len(v) > 3 and v[3] for v in ins)})
        if gives is not None:
            arrive.setdefault(gives, []).append(len(ops) - 1)

    def early(t):
        ops[-1]["early"] = t

    def ap(v):
        return v[0] if isinstance(v, tuple) else v

    def cc(v, k=1.0):
        return 0.055 + 1.56 * CYC * v[2] if v[3] else 0.005 + max(64, k * v[2]) * CYC

    def rate(*vs):
        return 0.5 if all(SCRATCH[v[1][0][0]][2] in (BF, U16) for v in vs) else 1.0

    def cp(o, i):
        op("v", lambda: g.vector.tensor_copy(o[0], i[0]), [o], [i], cc(i, rate(o, i)))

    def tt(o, a, b, alu, ext=None):
        op("v", lambda: g.vector.tensor_tensor(o[0], a[0], b[0], alu), [o], [a, b], cc(a, 2), ext=ext)

    def ts(o, a, s1, o0, s2=None, o1=None):
        if o1 is None:
            op("v", lambda: g.vector.tensor_scalar(o[0], a[0], ap(s1), None, o0), [o], [a, s1], cc(a))
        else:
            op("v", lambda: g.vector.tensor_scalar(o[0], a[0], ap(s1), ap(s2), o0, o1), [o], [a, s1, s2], cc(a))

    def tr(o, i, k=1.0):
        op("v", lambda: g.vector.transpose(o[0], i[0]), [o], [i], cc(i, k))

    def ms(o, c):
        op("v", lambda: g.vector.memset(o[0], c), [o], [], cc(o, rate(o)))

    def scan(o, d0, d1, init, o0, o1, k=1.0):
        op("v", lambda: g.vector.tensor_tensor_scan(o[0], d0[0], d1[0], init, o0, o1), [o], [d0, d1], cc(d0, k))

    def act(o, i, func=None, scale=None, bias=None, ext=None):
        kw = {}
        if scale is not None:
            kw["scale"] = ap(scale)
        if bias is not None:
            kw["bias"] = ap(bias)
        fn = func if func is not None else (F.Identity if bias is not None else F.Copy)
        op("a", lambda: g.scalar.activation(o[0], i[0], fn, **kw), [o], [i, scale, bias], cc(i) + 0.015, ext=ext)
        if (func is None or (func == F.Relu and SCRATCH[o[1][0][0]][2] == U16)) and i[1][0][0] != "ps":
            if scale is None and bias is None:
                alt = lambda: g.vector.tensor_copy(o[0], i[0])
            else:
                alt = lambda: g.vector.tensor_scalar(o[0], i[0], kw.get("scale", 1.0), kw.get("bias", 0.0), A.mult, A.add)
            ops[-1]["ways"] = {"a": (ops[-1]["fn"], ops[-1]["cost"]), "v": (alt, cc(i, rate(o, i)))}

    def above(o, i):
        act(o, i, F.Sign)
        ops[-1]["ways"] = {"a": (ops[-1]["fn"], ops[-1]["cost"]), "v": (lambda: g.vector.tensor_scalar(o[0], i[0], 0.0, None, A.is_gt), cc(i))}

    def equal(o, i, s, ext):
        fn = lambda: g.vector.tensor_scalar(o[0], i[0], float(s), None, A.is_equal)
        if s in (0, 3):
            act(o, i, F.Relu, scale=1.0 if s else -1.0, bias=-2.0 if s else 1.0, ext=ext)
            ops[-1]["ways"] = {"a": (ops[-1]["fn"], ops[-1]["cost"]), "v": (fn, cc(i))}
        else:
            op("v", fn, [o], [i], cc(i), ext=ext)

    def weigh(o, i, w):
        act(o, i, F.Relu, scale=w)
        ops[-1]["ways"] = {"a": (ops[-1]["fn"], ops[-1]["cost"]), "v": (lambda: g.vector.tensor_scalar(o[0], i[0], 0.0, w[0], A.max, A.mult), cc(i))}

    def iota(o, pat, base, cm, flt=True):
        if flt:
            op("p", lambda: g.iota(o[0], pat, base, cm, allow_small_or_imprecise_dtypes=True), [o], [], 0.13 + 2 * CYC * o[2])
        else:
            op("p", lambda: g.iota(o[0], pat, base, cm), [o], [], 0.13 + 2 * CYC * o[2])

    def fill(o, c, flt=True):
        iota(o, [[0, o[2]]], c, 0, flt)
        ops[-1]["ways"] = {"p": (ops[-1]["fn"], ops[-1]["cost"]), "v": (lambda: g.vector.memset(o[0], float(c) if flt else c), cc(o, rate(o)))}

    def quant(q, s, i):
        op("v", lambda: g.vector.quantize_mx(q[0], s[0], i[0]), [q, s], [i], 0.012 + 0.265 * CYC * i[2])

    def mm(o, lq, ls, rq, rs, ext=None):
        op("t", lambda: g.tensor.matmul_mx(o[0], lq[0], ls[0], rq[0], rs[0], True, True), [o], [lq, ls, rq, rs], 0.6 * CYC * (rq[2] + 16), ext=ext)

    def dma(eng, o, i, sem, lat=1.3, after=None):
        q = {"s": g.sync, "a": g.scalar, "p": g}[eng]
        op(eng, lambda: q.dma_start(ap(o), ap(i)), [o] if isinstance(o, tuple) else [], [i, after], 0.06, lat, sem=sem, inc=16)

    def u8(v):
        return (v[0].bitcast(dt.uint8), v[1], v[2], False)

    count = {}

    def send(dst_core, o, i, rsem, lat, every=1, plus=None):
        rid, pid = topo.addr(dst_core)[:2]
        use = topo.engines(core, dst_core)[::every]
        m, n = sum(1 << e for e in use), len(use)
        count[rsem] = count.get(rsem, 0) + n
        if plus is None:
            fn = lambda: g.remote_dma(o[0], i[0], T.sem[rsem], T.sem["sent"], pid, rid, m)
        else:
            fn = lambda: g.remote_dma_fused([RemoteDMATransfer(dst_ids=[DstId(rid=rid, pnc=pid)], dma_engine_mask=m, remote_sem=T.sem[rsem],
                                                               srcs=[v[0] for v in [i] + plus], dsts=[o[0]], alu_op=1)], local_sem=T.sem["sent"])
        op("p", fn, [], [i] + (plus or []), 0.15, lat, sem="sent", inc=-n, gives=rsem)

    for c in range(0, 16 * FLW, 256):
        ms(V("raw", c, min(c + 256, 16 * FLW)), 1)
    for H in range(8):
        dma("s" if H % 2 else "a", V("parq", 0, 32, 1, 16 * H, 16 * H + 16), T.par[:, :], "l_par")
        early(5.0)
    for H in range(8):
        c0 = (16 * (H % 2) + 4 * (H // 2)) // FLW * FLW
        dma("s" if H % 2 else "a", (T.raw[16 * H:16 * H + 16:2, :], [("raw", 16 * H, 16 * H + 16, 0, 16 * FLW, 1)]), T.fl[:, c0:c0 + FLW], "l_fl", TUNE["fl"])
        ops[-1]["ahead"] = 5.0
    xin = lambda t: (V("pool", PW * t + X0 - t, PW * t + DB - t), T.x[:, :], "l_x" if t == 0 else "l_y", 4.0 + 2.5 * (LOADS - 1 if t else 0) + (1.0 if t else 0.0))
    more = 2.0 * (LOADS - 1)
    loads = ([xin(0), (V("ut"), T.u[:, :], "l_u", 5.0)] + [xin(t) for t in range(1, LOADS)]
             + [(u8(V("wq")), T.wc[:, :], "l_w", 7.0 + more), (V("wsc"), T.ws[:, :], "l_w", 7.0 + more), (V("vt"), T.v[:, :], "l_v", 8.0 + more)])
    for (o, i, sem, lat) in loads:
        dma("s", o, i, sem, lat - 1.0, V("raw"))
        ops[-1]["behind"] = [q["id"] for q in ops[:-1] if q["eng"] == "s"]
        ops[-1]["ahead"] = 100.0 - len(ops)

    iota(V("pi", 0, 1), [[0, 1]], 0, 1, False)
    iota(V("cnt"), [[1, 128]], 0, 0)
    used, rows = {"col": 0, "row": 0, "fi": 0}, {}
    have = {"P": V("pi", 0, 1)}
    known_ = dict(FEATURES)

    def new(name, n=1):
        used[name] += n
        return V(name, used[name] - n, used[name])

    def feature(k):
        if k not in have:
            if k[0] == "x":
                x, y = feature((4, 1)), feature((k[1], 1))
                have[k] = new("col")
                tt(have[k], x, y, A.not_equal)
            else:
                have[k] = new("fi")
                ts(have[k], have["P"], k[0], A.logical_shift_right, k[1], A.bitwise_and)
        return have[k]

    def summed(vec, o=None, free=False):
        key = ("sum", tuple(int(z) for z in vec), o is None, free)
        if key not in PLAN:
            PLAN[key] = terms(vec, known_, have, o is None, free)
        c0, start, tm = PLAN[key]
        prev, acc = (have[start], known_[start].copy()) if start else (float(c0), np.full(128, float(c0)))
        for i, (k, coef) in enumerate(tm):
            f, acc = feature(k), acc + coef * known_[k]
            out = o if o is not None and i == len(tm) - 1 else new("col")
            act(out, f, scale=float(coef), bias=prev)
            if out is not o:
                name = ("col", used["col"])
                have[name], known_[name] = out, acc
            prev = out
        return prev, int(vec[0] - acc[0])

    def column(vec):
        return summed(vec)[0]

    def const(o, tb):
        c = 0
        while c < tb.shape[1]:
            e = tb.shape[1]
            while product(tb[:, c:e] - tb[:, c:c + 1]) is None:
                e -= 1
            sc, r = product(tb[:, c:e] - tb[:, c:c + 1])
            if e == c + 1:
                summed(tb[:, c], o(c, e))
            elif (r == np.arange(e - c)).all() or not sc.any():
                act(o(c, e), V("cnt", 0, e - c), scale=column(sc), bias=column(tb[:, c]))
            else:
                same = (sc == sc[0]).all()
                bias, c0 = summed(tb[:, c], None, True) if same else (column(tb[:, c]), 0)
                r = r * sc[0] + c0 if same else r
                key = tuple(int(z) for z in r)
                if key not in rows:
                    rows[key] = new("row", e - c)
                    iota(rows[key], pattern(r), int(r[0]), 0)
                act(o(c, e), rows[key], scale=1.0 if same else column(sc), bias=bias)
            c = e

    def colf(f):
        return column(table(1, f)[:, 0])

    tt(V("lu", 0, 1), feature((0, 19)), feature((3, 12)), A.add)
    pj0, pj1 = new("col"), new("col")
    tt(pj0, feature((0, 4)), feature((5, 3)), A.add)
    tt(pj1, feature((2, 2)), feature((4, 1)), A.add)
    act(V("lu", 2, 3), pj0, scale=4.0, bias=pj1)
    at, c0 = {}, 0
    for (name, n, f) in LISTS:
        at[name] = (c0, n)
        if f is not None:
            const(lambda c, e: V("lu", c0 + c, c0 + e), table(n, f))
        c0 += n + n % 2

    def L(name, n=None):
        return V("lu", at[name][0], at[name][0] + (n or at[name][1]))

    const(lambda c, e: V("pjc", c, e), table(16, lambda a, h, p, c: 16 - 64 * (4 * (c // 4 % 2) + a)))
    CB = colf(lambda a, h, p, c: 16 - 64 * (4 * h + a))
    act(V("cj", 0, 64), V("cnt", 0, 64), scale=4100.0, bias=colf(lambda a, h, p, c: 4101 * 64 * (4 * h + a) + 4096 + X0 - 16 - TOP))
    act(V("cj", 0, 64), V("cj", 0, 64), scale=colf(lambda a, h, p, c: 1 - p % 2), bias=colf(lambda a, h, p, c: TOP + 16 - 64 * (4 * h + a)))
    for t in range(LOADS, 4):
        for c in range(0, C, TUNE["xp"]):
            act(V("pool", PW * t + X0 + 4 * c, PW * t + X0 + 4 * (c + TUNE["xp"]), 4), V("pool", X0 + 4 * c + t, X0 + 4 * (c + TUNE["xp"]), 4))
    ms(V("pj"), 0.0)
    for (nm, n) in (("vb", 16), ("vc", 16), ("vd", 16), ("w7", 8), ("ww", 8), ("v7", 16)):
        fill(V(nm, 0, n), 0)
    for k in range(4):
        fill(V("pr", 80 * k, 80 * k + 16), 0)
    for nm in ("vc", "v7"):
        fill(V(nm, 80, 96), 0)
    fill(V("v8", 192, 256), TOP + 8)
    for c0 in (64, 256):
        act(V("v8", c0, c0 + 64), V("cnt", 0, 64), scale=-1.0, bias=colf(lambda a, h, p, c: TOP - 64 * a))
    C7 = colf(lambda a, h, p, c: TOP + 72 - 64 * (4 * h + a) - 512 * (1 - a % 2))
    C8 = colf(lambda a, h, p, c: TOP + 8 - 256 * h)
    CW = colf(lambda a, h, p, c: 2 - p % 2)
    CW7 = colf(lambda a, h, p, c: 126 - 63 * (p % 2))
    CK = colf(lambda a, h, p, c: 2 - p // 8)
    fill(V("seg6"), 1)
    fill(V("seg6", 0, 192, 6), 0)
    iota(V("x0", 2, 192, 3), [[0, 4], [8, 8], [-300, 2]], 6, 0)
    act(V("x0", 2, 192, 3), V("x0", 2, 192, 3), F.Relu)
    act(V("jc", 0, 64), IND(V("cnt", 0, 64), L("REV")))
    act(V("jc", 64, 128), V("jc", 0, 64), scale=4096.0, bias=colf(lambda a, h, p, c: 4096 * (64 * (4 * h + a) + 1) + DB * h))
    for u in range(2):
        iota(V("fk", 32 * u, 32 * u + 32), [[16, 2], [32, 2], [1, 8]], 8 * u, 0)
    for (c0, c1) in ((64, 128), (128, 256), (256, 512), (512, 576)):
        act(V("fk", c0, c1), V("fk", 0, c1 - c0))
    for k in range(4):
        iota(V("nt", 256 + 128 * k, 384 + 128 * k), [[32, 2], [1, 8], [64, 8]], 16 * (k % 2) + 8 * (k // 2), 0)
    const(lambda c, e: V("nt", 128 + c, 128 + e), table(128, lambda a, h, p, c: 64 * (c % 8) + 32 * (a % 2) + 16 * (a // 2) + c // 8))
    fill(V("ea", 0, 16), 0, False)
    fill(V("ea", 80, 96), 0, False)
    fill(V("ea", 160, 176), 0, False)
    fill(V("vi", 0, 16), 0, False)
    fill(V("vi", 144, 160), 0, False)
    for nm in ("sa", "sb", "nw"):
        fill(V(nm, 0, 8), 0)
    fill(V("ht", 256, 512), 0)
    fill(V("et", 0, 256), 0)
    fill(V("sm", 1, 128, 2), 0)
    fill(V("seg8"), 1)
    fill(V("seg8", 0, 512, 8), 0)
    act(V("d0"), V("seg8", 0, 512, 2))
    act(V("horn"), V("seg8", 0, 256, 2), scale=16.0)
    fill(V("lane"), -8)
    for h in range(2):
        key = [32 * (e // 32) + e // 4 % 8 + 8 * [slot(h, t) for t in range(4)].index(e % 4) for e in range(64)] + [0]
        for s in range(4):
            if key[s] - key[s + 1] != -8:
                fill(V("lane", 64 * h + s, 64 * h + 64, 4), key[s] - key[s + 1])
        for e in (31, 63):
            fill(V("lane", 64 * h + e, 64 * h + e + 1), key[e] - key[e + 1])
    fill(V("eb"), 0)
    ts(V("eb", 3, 515, 4), V("cnt"), colf(lambda a, h, p, c: 32 * a + 16 * h + p), A.is_equal)
    for b in range(4):
        quant(V("ebq", 128 * b, 128 * b + 128), V("ebs", 128 * b, 128 * b + 128), V("eb", 3 - b, 515 - b))
    quant(V("uq"), V("us"), V("ut"))

    def pick(q, s, lst):
        op("v", lambda: g.vector.tensor_copy(T[q][:, :].bitcast(dt.uint32), T.uq[:, :].bitcast(dt.uint32).indirect(lst[0])), [V(q)], [V("uq"), lst], 0.25)
        op("a", lambda: g.scalar.activation(T[s][:, :], T.us[:, :].indirect(lst[0]), F.Copy), [V(s)], [V("us"), lst], 0.27)

    pick("ukq", "uks", L("UK"))
    pick("urq", "urs", L("UR"))
    quant(V("vq"), V("vs"), V("vt"))
    early(6.0)

    act(V("ptr", 0, 16), IND(V("parq"), L("PB")), F.Relu, bias=CB)
    act(V("paru"), IND(V("parq"), L("PU")))
    tt(V("pj", PTR, 64, 4), IND(V("parq"), L("PJ")), V("pjc"), A.add)
    tr(V("pr", 16, 80), V("pj"))
    tt(V("cj", 64, 128), V("cj", 0, 64), V("pr", 16, 80), A.subtract)
    for nm in ("va", "vb"):
        tt(V(nm, 16, 80), IND(V("raw"), L("RAW")), V("cj", 64, 128), A.mult)
    act(V("nw", 11, 264, 4), IND(V("va", 16, 80), L("REV")))
    for k in range(6):
        b0, b1, t0 = 80 * (k % 3), 80 * ((k + 1) % 3), 160 * (k % 2)
        act(V("pr", b1 + 16, b1 + 80), IND(V("pr", b0, b0 + 80), V("ptr", 16 * max(k - 1, 0), 16 * max(k - 1, 0) + 4)))
        tr(V("pt", t0, t0 + 64), V("pr", b1 + 16, b1 + 80))
        tr(V("pt", t0 + 64, t0 + 160), V("pr", b1, b1 + 96))
        act(V("ptr", 16 * k + 16, 16 * k + 32), IND(V("pt", t0, t0 + 160), L("SEL" if k < 5 else "SEL6")), F.Relu)
    act(V("nt", 0, 128), IND(V("nt", 256, 768), V("paru", 0, 8)))
    act(V("r2"), IND(V("nt", 0, 256), L("R2")))
    for c in range(2):
        tr(V("r3", 128 * c, 128 * c + 128), V("r2", 128 * c, 128 * c + 128))
    act(V("ol", 0, 8), V("r3", 0, 256, 32))
    act(V("ol", 8, 12), V("r3", 144, 256, 32))
    act(V("ol", 12, 16), V("r3", 16, 128, 32))

    def both(src, tb, n, s0=0, t0=0, k=1.0):
        tr(V(tb, t0, t0 + n), V(src, s0 + 16, s0 + 16 + n), k)
        tr(V(tb, t0 + n, t0 + 2 * n + 32), V(src, s0, s0 + n + 32), k)

    def pointer(src, k, bias, n, sel):
        tb = "tc" if k % 2 else "tb"
        both(src, tb, n)
        act(V("ptr", 16 * k, 16 * k + 16), IND(V(tb, 0, 2 * n + 32), L(sel)), F.Relu, -1.0, bias)

    def step(o, w, own, lst, c0, c1, end):
        l0 = 16 * lst + (c0 - 32) // 8 * (c0 > 0)
        tt(V(o, 16 + c0, 16 + c1), IND(V(w, 0, 16 + end), V("ptr", l0, l0 + (c1 - c0) // 16)), V(own, 16 + c0, 16 + c1), A.max)

    def by_steps(old, cur, nxt, again, runs):
        for k in range(TUNE["steps"]):
            step(nxt, cur, old, max(k - 1, 0), 0, 64, 64)
            old, cur, nxt = cur, nxt, (old if k else again)
        for (c0, c1) in runs:
            step(cur, cur, cur, 6, c0, c1, c0)
        return cur

    def share(src, c0, a, dst="ww"):
        for b in range(4):
            act(Q(dst, b, 8 + 64 * a, 72 + 64 * a), Q(src, a, c0, c0 + 64))

    def later_lists():
        p = colf(lambda a, h, p, c: p)
        fill(V("wt", 64, 70), 2)
        scan(V("wt", 112, 118), V("wt", 64, 70), V("wt", 64, 70), 1.0, A.mult, A.max)
        half = colf(lambda a, h, p, c: rev(32 + p))
        act(V("wt", 128, 140, 2), V("wt", 112, 118), scale=half)
        act(V("wt", 144, 150), V("wt", 112, 118), scale=2.0)
        tt(V("wt", 129, 140, 2), V("wt", 128, 140, 2), V("wt", 144, 150), A.add)
        act(V("fi", 32, 44), V("wt", 128, 140), scale=0.5 / 63, bias=-0.501)
        act(V("wt", 144, 156), V("fi", 32, 44), scale=-126.0)
        tt(V("wt", 160, 172), V("wt", 128, 140), V("wt", 144, 156), A.add)
        act(L("LV"), V("wt", 160, 172), scale=0.5)
        W = lambda k, c0=0, c1=6: V("wt", 16 * k + c0, 16 * k + c1)
        ts(W(0), V("cnt", 0, 6), p, A.is_equal, 1.0 / 32, A.mult)
        ts(W(1), V("cnt", 0, 6), p, A.add, 5.0, A.is_equal)
        scan(W(2), W(4), W(0), 0.0, A.mult, A.add)
        scan(W(3), W(4), W(1), 0.0, A.mult, A.add)
        act(V("gi", 0, 64), V("cnt", 0, 64), scale=W(2, 5, 6), bias=-0.499)
        act(V("th", 0, 64), V("jc", 0, 64), scale=W(3, 5, 6))
        act(V("gi", 64, 128), V("th", 0, 64), scale=1.0 / 63, bias=-0.499)
        act(V("gt", 80, 144), V("gi", 0, 64), scale=-64.0)
        act(V("gt", 144, 208), V("gi", 64, 128), scale=63.0)
        tt(V("gt", 80, 144), V("gt", 80, 144), V("th", 0, 64), A.subtract)
        tt(V("gt", 16, 80), V("gt", 80, 144), V("gt", 144, 208), A.add)
        fill(V("gt", 0, 16), 128)
        act(V("th", 64, 128), V("gi", 0, 64), scale=8192.0)
        act(V("th", 128, 192), V("gi", 0, 64), scale=8128.0, bias=72.0)
        for nm in ("ba", "bb", "bc"):
            fill(V(nm, 0, 16), -10000)
        for nm in ("ba", "bb"):
            tt(V(nm, 16, 80), IND(V("gt", 0, 80), V("ptr", 0, 4)), V("th", 64, 128), A.add)
        early(TUNE["bb"])
        cur = by_steps("ba", "bb", "bc", "ba", TUNE["runs"] if TUNE["steps"] < 7 else ())
        early(TUNE["bs"])
        tt(V("th", 192, 256), V("th", 128, 192), V(cur, 16, 80), A.subtract)
        for (c0, c1) in ((0, 16), (208, 240), (304, 336), (592, 624), (880, 896)):
            fill(V("xg", c0, c1), 0)
        first = new("col")
        ts(first, p, 0.0, A.is_equal)
        sc, bi = new("col"), new("col")
        act(sc, first, scale=3.0, bias=1.0)
        act(bi, first, scale=-21.0)
        for c in (0, 6):
            act(V("xg", 16 + 16 * c, 112 + 16 * c), IND(V("th", 192, 256), V("lu", at["LV"][0] + c, at["LV"][0] + c + 6)), scale=sc, bias=bi)
        both("xg", "xh", 192, 0, 0, 0.5)
        act(V("sh", 0, 16), IND(V("xh", 0, 416), L("SELV")), F.Relu)
        fill(V("plw", 0, 8), -8)
        for s in range(4):
            act(V("plw", 8 + 64 * s, 72 + 64 * s), V("jc", 0, 64), bias=64.0 * s)
        act(V("r7", 0, 64), IND(V("plw", 0, 72), V("ptr", 112, 116)))
        act(V("xg", 240, 304), IND(V("r7", 0, 64), L("REV")))
        both("xg", "xh", 64, 224, 480, 0.5)
        act(V("sh", 16, 32), IND(V("xh", 480, 640), L("SEL")), F.Relu, bias=8.0)
        fill(V("w2", 0, 136), -8)
        act(V("r7", 64, 128), IND(V("plw", 0, 136), V("ptr", 128, 132)))
        for a in (2, 3):
            share("r7", 64, a, "w2")
        act(V("xg", 336, 464), IND(V("plw"), V("ptr", 144, 152)))
        act(V("xg", 464, 592), IND(V("w2"), V("ptr", 144, 152)))
        for k in range(2):
            act(V("xg", 624 + 128 * k, 752 + 128 * k), IND(V("xg", 336 + 128 * k, 464 + 128 * k), L("NK")))
            early(TUNE["scat"])
        for k in range(2):
            both("xg", "xh", 256, 320 + 288 * k, 640 + 544 * k, 0.5)
            act(V("sh", 32 + 16 * k, 48 + 16 * k), IND(V("xh", 640 + 544 * k, 1184 + 544 * k), L("SELW")), F.Relu, bias=8.0)

    def inherit(r):
        first, last = r == 0, r == 3
        if not last:
            act(V("d1", 0, 256, 4), V("jc", 64, 128), bias=float(K * r))
            act(V("d1", 2, 256, 4), V("nw", 11, 264, 4), scale=-1.0)
            act(V("d1", 3, 256, 4), V("nw", 11, 264, 4))
        if first:
            cur, c0 = by_steps("va", "vb", "vc", "vd", TUNE["runs"]), 16
            pointer(cur, 7, C7, 64, "SEL")
        else:
            tt(V("sb", 9, 72, 2), IND(V("nw", 0, 136), V("sh", 0, 2)), V("nw", 139, 264, 4), A.max)
            act(V("sb", 8, 72, 2), V("nw", 11, 136, 4))
            cur, old, c0 = "sb", "sa", 8
            for k in range(1, 6):
                tt(V(old, 9, 72, 2), IND(V(cur, 0, 40), V("sh", 2 * k + k // 4 * 4, 2 * k + k // 4 * 4 + 2)), V(cur, 40, 72), A.max)
                act(V(old, 8, 72, 2), V(cur, 8, 40))
                cur, old = old, cur
        if last:
            act(V("flg"), IND(V("nw"), L("REVF")), F.Sign)
            for H in range(8):
                B = 4 * (H % 2) + H // 2
                dma("s", T.ofl[:, 64 * B:64 * B + 64], (T.flg[16 * H:16 * H + 16:2, :], V("flg")[1]), "out")
        for a in (0, 2):
            act(Q("w7", a + 1, 8, 72), Q(cur, a, c0, c0 + 64))
        for a in (0, 2)[:1 if first else 2]:
            share(cur, c0, a)
        nxt = "v7" if first else old
        tt(V(nxt, c0, c0 + 64), IND(V("w7"), V("ptr", 112, 116) if first else V("sh", 16, 20)), V(cur, c0, c0 + 64), A.max)
        n0 = len(ops)
        for k, (src, quads) in enumerate(((cur, (0,)), (nxt, (1,))) if last else ()):
            act(V("ea", 80 * k + 16, 80 * k + 80), IND(V(src, c0, c0 + 64), L("REV")))
            both("ea", "eb2", 64, 80 * k, 160 * k)
            ts(V("ec", 16 * k, 16 * k + 16), IND(V("eb2", 160 * k, 160 * k + 160), L("FE")), 4095, A.bitwise_and)
            for a in quads:
                for b in range(4):
                    act(Q("el", b, 32 + 4 * a, 36 + 4 * a), Q("ec", a, 16 * k + 4 * b, 16 * k + 4 * b + 4))
        for o in ops[n0:]:
            o["ahead"] = TUNE["soon"]
        if first:
            share(nxt, c0, 1)
            pointer(nxt, 8, C8, 64, "SEL")
            tt(V("v8", 128, 192), IND(V("ww", 0, 136), V("ptr", 128, 132)), V(nxt, 16, 80), A.max)
            for a in (2, 3):
                share("v8", 128, a)
            for k in range(8):
                tr(V("tc", 32 * k, 32 * k + 32), V("v8", 64 + k, 320, 8))
            act(V("ptr", 144, 160), IND(V("tc", 0, 256), L("SELX")), F.Relu, -1.0, TOP + 8.0)
            for c in range(2):
                act(V("vi", 16 + 64 * c, 80 + 64 * c), IND(V("ww"), V("ptr", 144 + 4 * c, 148 + 4 * c)))
            later_lists()
        else:
            for a in (1, 3):
                share(nxt, c0, a)
            l0 = 48 if last else 32
            for c in range(2):
                act(V("tq", 64 * c, 64 * c + 64), IND(V("ww", 0, 136), V("sh", l0 + 8 + 4 * c, l0 + 12 + 4 * c)))
            for (e0, e1) in TUNE["bcut"]:
                tt(V("vi", 16 + e0, 16 + e1), IND(V("ww"), V("sh", l0 + e0 // 16, l0 + e1 // 16)), V("tq", e0, e1), A.max)
        for (e0, e1) in TUNE["bcut"]:
            tr(V("ti", e0, e1), V("vi", 16 + e0, 16 + e1))
            e1 += 32 * (e1 == 128)
            tr(V("ti", 128 + e0, 128 + e1), V("vi", e0, e1))
        ts(V("yy"), IND(V("ti"), L("FSL" if last else "FS")), 4095, A.bitwise_and)
        ops[-1]["mark"] = "el"
        for a in range(4):
            if last:
                for u in range(1 - a // 2, 2):
                    act(Q("yy", a ^ 1, 32 * u + 16 * (a % 2), 32 * u + 16 * (a % 2) + 16), Q("yy", a, 64 + 16 * u, 80 + 16 * u))
            else:
                act(Q("yy", a ^ 1, a % 2, 64, 2), Q("yy", a, 64, 96))
        for b in range(2):
            for s in range(2):
                if last:
                    u = 1 - s
                    tt(Q("el", 2 * b, 16 * s + 8 * u, 16 * s + 16, 1, 2), Q("yy", 2 * s, 32 * u + 2 * b, 64, 4, 2), Q("yy", 2 * s, 32 * u + 2 * b + 1, 64, 4, 2), A.max)
                else:
                    tt(Q("el", 2 * b, s, 32, 2, 2), Q("yy", 2 * s, 32 * b, 32 * b + 16, 1, 2), Q("yy", 2 * s, 32 * b + 16, 32 * b + 32, 1, 2), A.max)

    def plane(eng, r, t, l0, l1, n0):
        w = IND(V("pool", PW * t, PW * t + DB + K * r), V("el", l0, l1))
        (cp if eng == "v" else act)(V("et", 4 * (K + n0) + t, 4 * (K + n0 + 16 * (l1 - l0)), 4), w)
        if eng == "a":
            del ops[-1]["ways"]

    def pieces(r, gath, parts, sq, ss):
        for (l0, l1, n0, engs) in gath:
            for t in range(4):
                if engs[t] == "h":
                    m = (l0 + l1) // 4 * 2
                    plane("x", r, t, l0, m, n0)
                    plane("x", r, t, m, l1, n0 + 16 * (m - l0))
                else:
                    plane(engs[t], r, t, l0, l1, n0)
        for i, (c0, c1) in enumerate(parts):
            quant(V("eq", K + c0, K + c1), V("es", K + c0, K + c1), V("et", 4 * (K + c0), 4 * (K + c1)))
            if i == 0 and r < 3:
                mm(V("ps", 1536, 1664), V("ukq"), V("uks"), V("eq", 0, 128), V("es", 0, 128))
            mm(V("ps", 512 * i, 512 * i + c1 - c0), V(sq), V(ss), V("eq", K + c0, K + c1), V("es", K + c0, K + c1))

    def symbols(r):
        dst = T.cores[(rank - DIST[r]) % n_ranks]
        pieces(r, TUNE["gath"], TUNE["pieces"], "urq", "urs")
        for b in range(4):
            mm(V("ps", 2048 + 512 * b, 2176 + 512 * b), V("wq", 128 * b, 128 * b + 128), V("wsc", 128 * b, 128 * b + 128), V("eq", 0, 128), V("es", 0, 128))
        ts(V("kb", 0, 64), V("ps", 1600, 1664), 0.0, A.is_gt, CK, A.mult)
        ts(V("kb", 64, 80), V("ps", 1600, 1616), 0.0, A.is_gt, CK, A.mult)
        fs = "fs%d" % r
        for t, c0 in enumerate((0, 32, 16, 48)):
            tr(V(fs, t, 128, 4), V("kb", c0, c0 + 32), 0.5)
        send(dst, V("fl%d" % r), V(fs, 0, 32), "af%d" % r, TUNE["lat"] + (0.0 if r else 1.2), 1 if r else 2, [V(fs, 32, 64)])
        for i, (c0, c1) in enumerate(TUNE["pieces"]):
            above(V("rows", max(c0, 0), c1), V("ps", 512 * i + max(-c0, 0), 512 * i + c1 - c0))
        for b in range(4):
            act(V("ht", b, 256, 4), V("ps", 2112 + 512 * b, 2112 + 512 * b + K), scale=0.03125)
        hq, hs = "hq%d" % r, "hs%d" % r
        quant(V(hq, 64, 192), V(hs, 64, 192), V("ht"))
        send(dst, u8(V(hq, 0, 64)), u8(V(hq, 64, 128)), "ah%d" % r, 4.0)
        send(dst, V(hs, 0, 64), V(hs, 64, 128), "ah%d" % r, 4.0)
        weigh(V("op", 0, 64), IND(V("rows"), V("ol", 12, 16)), CW7)
        weigh(V("op", 64, 128), IND(V("rows"), V("ol", 0, 4)), CW)
        tr(V("x0", 0, 192, 3), V("op", 0, 64), 0.5)
        tr(V("x0", 1, 192, 3), V("op", 64, 128), 0.5)
        scan(V("xs"), V("seg6"), V("x0"), 0.0, A.mult, A.add, 0.5)
        tr(V("ixu"), V("xs", 5, 192, 6))
        weigh(V("op2"), IND(V("rows"), V("ol", 4, 12)), CW)
        tr(V("opt"), V("op2"), 0.5)
        tt(V("sm", 0, 128, 2), V("opt", 0, 128, 2), V("opt", 1, 128, 2), A.add)
        tr(V("smr"), V("sm"), 0.5)
        early(1.0)

    def choose(r):
        fl = "fl%d" % r
        for s in range(4):
            equal(V("xe", 32 * s, 32 * s + 32), V(fl), s, "af%d" % r)
        scan(V("tab", 0, 256, 2), V("horn"), V("xe"), 0.0, A.mult, A.add)
        for d in (1, -1, 2, -2, 3, -3):
            e0, e1 = max(0, -d), 4 - max(0, d)
            tt(V("tab", 64 * e0 + 6 + d, 64 * e1 + d, 8), V("tab", 64 * e0 + 6, 64 * e1, 8), V("tab", 64 * (e0 + d) + 6, 64 * (e1 + d), 8), A.add)
        act(V("fin"), IND(V(fl), L("FIN")), ext="af%d" % r)
        tr(V("fwt"), V("fin"), 0.5)
        act(V("fw", 0, 64), IND(V("fwt"), L("KP")))
        for (c0, c1) in ((64, 128), (128, 256), (256, 512), (512, 576)):
            act(V("fw", c0, c1), V("fw", 0, c1 - c0))
        hq, hs = "hq%d" % r, "hs%d" % r
        for b in range(4):
            mm(V("ps", 2048 + 512 * b, 2176 + 512 * b), V("ebq", 128 * b, 128 * b + 128), V("ebs", 128 * b, 128 * b + 128),
               V(hq, 0, 128), V(hs, 0, 128), ext="ah%d" % r)
        for b in range(4):
            for d0 in (0, DB):
                act(V("pool", PW * b + d0 + K * r, PW * b + d0 + K * r + K), V("ps", 2048 + 512 * b, 2048 + 512 * b + K))
                early(1.5)
        ones = 64.0 * 0x1111
        for (c0, c1, eng) in TUNE["look"]:
            w, o = IND(V("tab"), V("ixu", c0, c1)), V("ac", 16 * c0, 16 * c1)
            if eng == "v":
                ts(o, w, -64.0, A.mult, ones, A.add)
            else:
                act(o, w, scale=-64.0, bias=ones)
            scan(V("ci", 16 * c0, 16 * c1), V("seg8", 16 * c0, 16 * c1), o, 0.0, A.mult, A.add)
        tr(V("yt"), V("ci", 7, 512, 8))
        for t in range(4):
            ts(V("yi", t, 256, 4), V("yt"), 4 * (3 - t), A.logical_shift_right, 15 << 6, A.bitwise_and)
        for c in range(4):
            scan(V("sc", c, 256, 4), V("yi", 64 * c, 64 * c + 64), V("lane", 64 * (c % 2), 64 * (c % 2) + 64), 1000.0, A.min, A.add)
        for (c0, c1) in TUNE["ccut"]:
            ku, e0, e1 = V("sc", 252 + c0, 252 + c1), 16 * c0, 16 * c1
            act(V("d1", 4 * e0 + 1, 4 * e1, 4), IND(V("fk"), ku))
            tt(V("d0", 4 * e0 + 2, 4 * e1, 4), IND(V("fw"), ku), V("smr", e0, e1), A.not_equal)
            tt(V("d0", 4 * e0 + 3, 4 * e1, 4), IND(V("fw"), ku), V("smr", 64 + e0, 64 + e1), A.not_equal)
            scan(V("nw", 8 + 4 * e0, 8 + 4 * e1), V("d0", 4 * e0, 4 * e1), V("d1", 4 * e0, 4 * e1), 0.0, A.mult, A.add)
        ops[-1]["mark"] = "nw"

    later = []
    for r in range(3):
        inherit(r)
        later.append(len(ops))
        symbols(r)
        choose(r)
    inherit(3)
    pieces(3, TUNE["gath3"], TUNE["pieces3"], "vq", "vs")
    for i, (c0, c1) in enumerate(TUNE["pieces3"]):
        (act if TUNE["yo"][i] == "a" else cp)(V("yo", c0, c1), V("ps", 512 * i, 512 * i + c1 - c0))
    for i, (c0, c1) in enumerate(STORES):
        ahead = TUNE["out"] * (len(STORES) - 1 - i)
        dma("s", T.oc[:, 4 * c0:4 * c1], u8(V("eq", K + c0, K + c1)), "out", 1.1)
        ops[-1].update(early=ahead + TUNE["out"] / 2, move=0.16 + 0.0013 * (c1 - c0))
        dma("s", T.y[:, c0:c1], V("yo", c0, c1), "out", 1.1)
        ops[-1].update(early=ahead, move=0.16 + 0.0013 * (c1 - c0))
    for k in range(4):
        dma("a" if k % 2 else "s", T.osc[4 * k:4 * k + 4, :], V("es", K, K + 512, 1, 32 * k, 32 * k + 4), "out")

    def meet(x, y):
        if x[1] >= y[2] or y[1] >= x[2] or x[3] >= y[4] or y[3] >= x[4]:
            return False
        if y[4] - y[3] <= 4 or x[4] - x[3] <= 4:
            return bool(set(range(x[3], x[4], x[5])) & set(range(y[3], y[4], y[5])))
        s = min(x[5], y[5])
        return not (s > 1 and max(x[5], y[5]) % s == 0 and (x[3] - y[3]) % s != 0)

    for o in ops:
        if any(f[0] in ("kb", "xe", "tab") or f[0][:2] == "fs" and o["r"] or f[:5] in (("et", 0, 128, 256, 512), ("eq", 0, 128, 0, 128), ("ps", 0, 128, 1536, 2048))
               or f[0] == "et" and 256 <= f[3] < 260 for f in o["w"]) or o["sem"] == "sent" and o["r"][0][0][:2] == "fs":
            o["ahead"] = TUNE["hot"]
        if o["id"] > later[0] and any(f[0] in ("sa", "sb", "w7", "ww", "tq", "vi", "ti", "yy") or f[0] == "el" and f[3] < 32 for f in o["w"]):
            o["ahead"] = TUNE["main"]
    met, group = {}, {}
    for o in ops:
        if o["dma"]:
            group.setdefault(o["sem"], []).append(o["id"])
    for o in ops:
        dep = set()
        for f, wr in [(f, False) for f in o["r"]] + [(f, True) for f in o["w"]]:
            for (h, hw, q) in met.get(f[0], []):
                if (wr or hw or (f[0] == "ps" and ops[q]["eng"] != o["eng"])) and meet(f, h):
                    dep.update(group[ops[q]["sem"]] if ops[q]["dma"] else [q])
        o["dep"] = dep
        o["pre"] = dep | set(arrive[o["ext"]] if o["ext"] else [])
        o["behind"] = o.get("behind", [])
        for f in o["r"]:
            met.setdefault(f[0], []).append((f, False, o["id"]))
        for f in o["w"]:
            met.setdefault(f[0], []).append((f, True, o["id"]))
    need = [0.0] * len(ops)
    for o in reversed(ops):
        for q in o["pre"]:
            if q < o["id"]:
                need[q] = max(need[q], need[o["id"]] + o["cost"] + o["lat"] + HOP)
    scans = [o["id"] for o in ops if o.get("mark") == "nw"]
    for o in ops[:later[0]]:
        if not o["dma"] and need[o["id"]] < need[scans[1]]:
            o["pre"] = o["pre"] | {scans[TUNE["late"]]}
    for o in ops:
        o["succ"] = []
        if o["w"] and o["w"][0][0] in TUNE["past"] and not o["r"]:
            o["pre"] = o["pre"] | set(q for q in ops[arrive["af0"][0]]["dep"])
    ops_ = sorted(ops, key=lambda o: o["id"])
    seen_, topo_ = set(), []
    while ops_:
        rest = []
        for o in ops_:
            if o["pre"] <= seen_:
                seen_.add(o["id"])
                topo_.append(o)
            else:
                rest.append(o)
        ops_ = rest
    for o in ops:
        for q in o["pre"]:
            ops[q]["succ"].append(o["id"])

    def place(rank_, back):
        start, left = {}, {o["id"]: len(o["succ" if back else "pre"]) for o in ops}
        taken = {e: [] for e in "vapts"}
        rank_ = [rank_[o["id"]] - (0.0 if back else o.get("ahead", 0.0)) for o in ops]
        ready = [(rank_[o["id"]], o["id"]) for o in ops if left[o["id"]] == 0]
        while ready:
            i = min(ready)
            ready.remove(i)
            i = i[1]
            o = ops[i]
            if back:
                t = max([start[q] + ops[q]["cost"] + HOP for q in o["succ"]] + [0.0]) + o["lat"] + o["early"]
            else:
                t = max([start[q] + ops[q]["cost"] + ops[q]["lat"] + HOP for q in o["pre"]] + [start[z] + 0.061 for z in o["behind"] if z in start] + [0.0])
            found = []
            for (e, c) in ([(e, w[1]) for e, w in o["ways"].items()] if "ways" in o and not back else [(o["eng"], o["cost"])]):
                tk, k, s = taken[e], len(taken[e]), t
                while k and tk[k - 1][1] > t:
                    k -= 1
                while k < len(tk) and tk[k][0] < s + c - 1e-9:
                    s = max(s, tk[k][1])
                    k += 1
                found.append((s + c + (TUNE["bias"] if e == "v" else 0.0), e, c, s, k))
            _, o["eng"], o["cost"], s, k = min(found)
            tk = taken[o["eng"]]
            tk.insert(k, (max(s - TUNE["guard"], tk[k - 1][1] if k else 0.0) if o["sem"] == "sent" and not back else s, s + o["cost"]))
            start[i] = s
            for q in o["pre" if back else "succ"]:
                left[q] -= 1
                if left[q] == 0:
                    ready.append((rank_[q], q))
        return start

    def ends(start):
        end, free = {q: start[q] + ops[q]["cost"] + ops[q]["lat"] for q in start}, 0.0
        for q in sorted(group["out"], key=lambda q: start[q]):
            free = end[q] = max(end[q], free) + ops[q].get("move", 0.05)
        return end

    if "order" not in PLAN:
        tail = {}
        for o in reversed(topo_):
            tail[o["id"]] = o["cost"] + o["lat"] + o["early"] + max([HOP + tail[s] for s in o["succ"]] + [0.0])
        urgent, best = {q: -tail[q] for q in tail}, None
        for _ in range(TUNE["it"]):
            start = place(urgent, False)
            end = ends(start)
            if best is None or max(end.values()) < best:
                best, PLAN["order"] = max(end.values()), [(q, ops[q]["eng"]) for q in sorted(start, key=lambda q: (start[q], q))]
            late = place({q: -end[q] for q in end}, True)
            if best == max(end.values()):
                kept = urgent
            urgent = {q: -late[q] - ops[q]["cost"] for q in late}
        def replay(order, k, picks, hop):
            free, start, done = {e: 0.0 for e in "vapts"}, {}, {}
            for q in order:
                o = ops[q]
                start[q] = max([done[z] + hop for z in o["pre"]] + [free[o["eng"]]])
                free[o["eng"]] = start[q] + o["cost"] * (1.0 if o["dma"] else k * picks if o["picks"] else k)
                done[q] = free[o["eng"]] + o["lat"]
            return max(ends(start).values()) / (k + 2)

        rng, whole, best = np.random.default_rng(1), best, None
        for i in range(TUNE["tries"] + 1):
            lo, sd, span = min(kept.values()) + rng.random() * whole, TUNE["sd"][i % 3], TUNE["span"][i // 3 % 3]
            urgent = {q: kept[q] + (float(rng.normal()) * sd if i and lo <= kept[q] < lo + span else 0.0) for q in kept}
            start = place(urgent, False)
            order = sorted(start, key=lambda q: (start[q], q))
            end = sum(replay(order, *case[:3]) for case in TUNE["cases"])
            if best is None or end <= best:
                best, kept, PLAN["order"] = end, urgent, [(q, ops[q]["eng"]) for q in order]
        n, cases = len(ops), TUNE["cases"]
        above, pre = [0] * n, [None] * n
        for o in topo_:
            far_ = 0
            for q in o["pre"]:
                far_ |= above[q]
            pre[o["id"]] = [q for q in o["pre"] if not far_ >> q & 1]
            above[o["id"]] = far_ | sum(1 << q for q in o["pre"])
        succ = [[] for _ in ops]
        for q in range(n):
            for z in pre[q]:
                succ[z].append(q)
        ways = [{e: w[1] for e, w in o["ways"].items()} if "ways" in o else {o["eng"]: o["cost"]} for o in ops]
        lats, move = [[o["lat"] * c[3] for o in ops] for c in cases], [o.get("move", 0.05) if o["sem"] == "out" else None for o in ops]
        scale = [[1.0 if o["dma"] else c[0] * c[1] if o["picks"] else c[0] for o in ops] for c in cases]

        def run(part, eng, c, state, whole):
            hop, sc, lat = cases[c][2], scale[c], lats[c]
            free, done, last, why, out, end, at_ = dict(state[0]), state[1], {}, {}, 0.0, 0.0, None
            for q in part:
                e = eng[q]
                t, w = free[e], last.get(e)
                for z in pre[q]:
                    if done[z] > t:
                        t, w = done[z], z
                why[q], last[e] = w, q
                free[e] = t = t + ways[q][e] * sc[q]
                t += lat[q]
                if move[q] is not None:
                    t = out = max(t, out) + move[q]
                done[q] = t + hop
                if t > end and (whole or e in "va"):
                    end, at_ = t, q
            return end / (cases[c][0] + 2), at_, why, free

        def fast(part, eng, c, state, whole):
            lat, free, done, out, cost, end = lats[c], dict(state[0]), state[1], 0.0, costs[c], 0.0
            hop = cases[c][2]
            for q in part:
                e = eng[q]
                t = free[e]
                for z in pre[q]:
                    if done[z] > t:
                        t = done[z]
                free[e] = t = t + cost[e][q]
                if slow[q]:
                    t += lat[q]
                    if move[q] is not None:
                        t = out = max(t, out) + move[q]
                    if whole and t > end:
                        end = t
                done[q] = t + hop
            return max(end, free["v"], free["a"]) / (cases[c][0] + 2)

        slow = [o["dma"] for o in ops]
        costs = [{e: [ways[q].get(e, 0.0) * sc[q] for q in range(n)] for e in "vapts"} for sc in scale]

        def improve(order, eng, i0, i1, moves, heat):
            states = []
            for c in range(len(cases)):
                done = [0.0] * n
                states.append((run(order[:i0], eng, c, ({e: 0.0 for e in "vapts"}, done), True)[3], done))
            part, whole = order[i0:i1], i1 == n
            each = [fast(part, eng, c, states[c], whole) for c in range(len(cases))]
            best = now = sum(each)
            kept_, helds = (part, eng), None
            for i in range(moves):
                if helds is None:
                    helds = []
                    for c in range(len(cases)):
                        _, q, why, _ = run(part, eng, c, states[c], whole)
                        while why.get(q) is not None:
                            if why[q] not in pre[q] and not ops[q]["behind"]:
                                helds.append((why[q], q))
                            q = why[q]
                    ends_ = list(states[0][1])
                if not helds:
                    break
                p, q = helds[int(rng.integers(len(helds)))]
                kind, trial, eng2 = rng.random(), list(part), eng
                ip, iq = part.index(p), part.index(q)
                if rng.random() < TUNE["anew"]:
                    ip = max(0, ip - int(rng.integers(0, TUNE["run"])))
                    iq = min(len(part), iq + 1 + int(rng.integers(0, TUNE["run"])))
                    hop, free, done, eng2 = cases[0][2], dict(states[0][0]), list(ends_), dict(eng)
                    for z in part[:ip]:
                        free[eng[z]] = ends_[z] - hop - lats[0][z]
                    sd, taken, starts = TUNE["sd"][i % 3], {e: [] for e in free}, {}
                    rank_ = {z: ends_[z] - lats[0][z] - costs[0][eng[z]][z] + sd * float(rng.normal()) for z in part[ip:iq]}
                    for z in part[iq - 1:ip - 1 if ip else None:-1]:
                        for y in pre[z]:
                            if y in rank_ and rank_[y] >= rank_[z]:
                                rank_[y] = rank_[z] - 0.001
                    for z in sorted(rank_, key=rank_.get):
                        t, found = max([done[y] for y in pre[z]] + [0.0]), []
                        for e in ways[z]:
                            s, c = max(t, free[e]), costs[0][e][z]
                            for (s0, s1) in taken[e]:
                                if s0 >= s + c - 1e-9:
                                    break
                                s = max(s, s1)
                            found.append((s + c + (TUNE["bias"] if e == "v" else 0.0), e, s, c))
                        _, e, s, c = min(found)
                        taken[e].append((s, s + c))
                        taken[e].sort()
                        eng2[z], starts[z], done[z] = e, s, s + c + lats[0][z] + hop
                    trial[ip:iq] = sorted(starts, key=lambda z: (starts[z], rank_[z]))
                    if any(ops[z]["behind"] for z in starts):
                        continue
                elif kind < 0.3:
                    z = p if len(ways[p]) > 1 and (rng.random() < 0.6 or len(ways[q]) == 1) else q
                    if len(ways[z]) == 1:
                        continue
                    eng2 = dict(eng)
                    eng2[z] = [e for e in ways[z] if e != eng[z]][0]
                elif kind < 0.65:
                    iq = min(len(part) - 1, iq + int(rng.integers(0, 16)) * (rng.random() < 0.4))
                    late = [z for z in part[ip:iq + 1] if z == p or above[z] >> p & 1]
                    trial[ip:iq + 1] = [z for z in part[ip:iq + 1] if z not in late] + late
                else:
                    ip = max(0, ip - int(rng.integers(0, 16)) * (rng.random() < 0.4))
                    soon = [z for z in part[ip:iq + 1] if z == q or above[q] >> z & 1]
                    trial[ip:iq + 1] = soon + [z for z in part[ip:iq + 1] if z not in soon]
                bar, new_ = heat * (1 - i / moves) * rng.random(), []
                for c in range(len(cases)):
                    new_.append(fast(trial, eng2, c, states[c], whole))
                    if new_[0] > each[0] + bar + 0.03:
                        break
                end = sum(new_)
                if len(new_) == len(cases) and end <= now + bar:
                    part, eng, each, now, helds = trial, eng2, new_, end, None
                    if end < best:
                        best, kept_ = end, (part, eng)
            return order[:i0] + kept_[0] + order[i1:], kept_[1], best

        order, eng = [q for q, e in PLAN["order"]], {q: e for q, e in PLAN["order"]}
        for mark, back in TUNE["marks"]:
            cuts = [0] + [i + 1 for i, q in enumerate(order) if ops[q].get("mark") == mark] + [n]
            for i0, i1 in zip(cuts, cuts[1:]):
                order, eng, best = improve(order, eng, max(0, i0 - back), i1, TUNE["moves"] * (i1 - i0) // n, TUNE["heat"])
        order, eng, best = improve(order, eng, 0, n, TUNE["last"], 0.0)
        PLAN["order"] = [(z, eng[z]) for z in order]
        PLAN["time"] = best
    order = []
    for (q, e) in PLAN["order"]:
        order.append(ops[q])
        if "ways" in ops[q]:
            ops[q].update(eng=e, sem=ENG_SEM[e], fn=ops[q]["ways"][e][0])

    queue = {"v": g.vector, "a": g.scalar, "p": g, "t": g.tensor, "s": g.sync}
    total = {}
    for o in order:
        total[o["sem"]] = total.get(o["sem"], 0) + abs(o["inc"])
        o["n"] = total[o["sem"]]
    known = {e: {} for e in queue}
    for o in order:
        need = {}
        for q in o["dep"]:
            q = ops[q]
            cnt = total[q["sem"]] if q["dma"] else q["n"]
            if cnt > need.get(q["sem"], (0, None))[0]:
                need[q["sem"]] = (cnt, q)
        if o["ext"]:
            need[o["ext"]] = (count[o["ext"]], None)
        kn = known[o["eng"]]
        for s in sorted(need):
            cnt, q = need[s]
            if any(s2 != s and q2 is not None and q2["kn"].get(s, 0) >= cnt for s2, (c2, q2) in need.items()):
                continue
            if kn.get(s, 0) < cnt:
                queue[o["eng"]].wait_ge(T.sem[s], cnt)
        for s, (cnt, q) in need.items():
            kn[s] = max(kn.get(s, 0), cnt)
            if q is not None:
                for s2, c2 in q["kn"].items():
                    kn[s2] = max(kn.get(s2, 0), c2)
        o["kn"] = dict(kn)
        ins = o["fn"]()
        if o["inc"] > 0:
            ins.then_inc(T.sem[o["sem"]], o["inc"])
    total.update(count)
    for s in sorted(total):
        g.wait_ge(T.sem[s], total[s])
